import numpy as np, ml_dtypes
CORES = [16,17,18,19,32,33,34,35]
N = 8
BF = ml_dtypes.bfloat16
L, W, E, D, RO, EPS = 256, 3072, 4096, 256, 3, 4
def pack(S, EF, OT, Q, K, P, G, M):
    bf = lambda a: np.ascontiguousarray(a.reshape(N, 128, -1)).astype(np.float32).astype(BF)
    li = lambda a: np.ascontiguousarray(a.transpose(0, 1, 3, 2, 4)).reshape(N, 128, 3 * L).astype(np.int32)
    return {"st0": bf(S), "ef": bf(EF), "ot": bf(OT), "qn": li(Q), "qk": li(K), "tu": np.ascontiguousarray(P.reshape(N, 8, 3 * L)).astype(np.int32), "gl": bf(G), "rm": bf(M)}
def with15(v, last):
    return np.concatenate([v, np.broadcast_to(last, v.shape[:2] + (1, v.shape[3]))], axis=2).astype(np.int64)
def base(rng):
    cen = rng.integers(8, 56, (N, 8, 15, 1))
    def near(n):
        return np.clip(np.rint(cen + rng.standard_normal((N, 8, 15, n), dtype=np.float32) * rng.choice(np.array([1.5, 3.0, 6.0, 16.0]), (N, 8, 1, n))), 0, 63)
    S = with15(near(W), rng.random((N, 8, 1, W)) < rng.choice(np.array([0.1, 0.3, 0.5, 0.85]), (N, 8, 1, 1))); S[:, :, 15, W - 1] = 1
    EF = with15(np.rint((2 * rng.random((N, 8, 15, E)) - 1) * rng.integers(1, 9, (N, 8, 1, E))), 0)
    OT = rng.integers(0, 256, (N, 8, 16, D)); Q = rng.integers(0, W, (N, 8, 3, 16, L)); K = rng.integers(0, 946, (N, 8, 3, 16, L))
    kind = rng.integers(0, 3, (N, 8, 1, 1, L)); K = np.where(kind == 1, np.maximum(K, 300), np.where(kind == 2, K - K % 64, K))
    P = rng.integers(-3, 4, (N, 8, 3, L)); G = with15(near(L), 0); M = with15(rng.random((N, 8, 15, 1)) < 0.5, 0)
    for q in range(N):
        for g in range(8):
            Q[q, g, :, :, 5::16] = rng.choice(np.flatnonzero(S[q, g, 15]), (3, 16, L // 16))
    return S, EF, OT, Q, K, P, G, M
def setup_inputs(rng):
    return pack(*base(rng))
def setup_inputs_spread(rng):
    def un(hi, shape, eshape):
        return np.minimum(((hi + 1) * rng.random(shape) ** np.exp2(rng.integers(-2, 4, eshape))).astype(np.int64), hi)
    S = with15(un(63, (N, 8, 15, W), (N, 8, 1, W)), rng.random((N, 8, 1, W)) < rng.random((N, 8, 1, 1)))
    EF = with15(un(8, (N, 8, 15, E), (N, 8, 1, E)) * (2 * rng.integers(0, 2, (N, 8, 15, E)) - 1), 0)
    OT = un(255, (N, 8, 16, D), (N, 8, 1, D)); Q = un(W - 1, (N, 8, 3, 16, L), (N, 8, 3, 1, L)); K = un(945, (N, 8, 3, 16, L), (N, 8, 3, 1, L))
    P = rng.integers(-6, 7, (N, 8, 3, L)); G = with15(un(63, (N, 8, 15, L), (N, 8, 1, L)), 0)
    M = with15(rng.random((N, 8, 15, 1)) < rng.random((N, 8, 1, 1)), 0)
    return pack(S, EF, OT, Q, K, P, G, M)
def setup_inputs_ends(rng):
    def bits(n):
        r = rng.integers(0, 4, (N, 8, 1, n))
        return np.where(r == 0, 0, np.where(r == 1, 1, rng.integers(0, 2, (N, 8, 15, n))))
    S = with15(63 * bits(W), rng.integers(0, 2, (N, 8, 1, W))); EF = with15(16 * bits(E) - 8, 0); G = with15(63 * bits(L), 0)
    OT = 255 * rng.integers(0, 2, (N, 8, 16, D)); K = 945 * rng.integers(0, 2, (N, 8, 3, 16, L)); P = 12 * rng.integers(0, 2, (N, 8, 3, L)) - 6
    Q = np.where(rng.random((N, 8, 3, 16, L)) < 0.8, (W - 1) * rng.integers(0, 2, (N, 8, 3, 16, L)), rng.integers(0, W, (N, 8, 3, 16, L)))
    M = with15(rng.integers(0, 2, (N, 8, 15, 1)), 0)
    q, g = N - 1, 7
    S[q, g, :15, W - 1] = 63; S[q, g, :15, 0] = 0; S[q, g, 15, W - 1] = 0; S[q, g, 15, 0] = 0; EF[q, g, :15, E - 1] = 8; EF[q, g, :15, 0] = -8
    Q[q, g, :, :, L - 4:] = 0; Q[q, g, :, 15, L - 1] = W - 1; Q[q, g, :, 14, L - 2] = W - 1
    K[q, g, :, :, L - 2:] = 945; K[q, g, :, 15, L - 1] = 0; K[q, g, :, 14:, L - 2] = 0; K[q, g, :, :, L - 3] = 0; K[q, g, :, :, L - 4] = 945
    G[q, g, :15, L - 1] = 0; G[q, g, :15, L - 2] = 63; G[q, g, :15, L - 3] = 0; G[q, g, :15, L - 4] = 63
    P[q, g, :, L - 4:] = -6; P[q, g, 0, L - 2] = 6
    M[q, g, :15, 0] = 1; OT[q, g, :, 15120 % D] = 255
    return pack(S, EF, OT, Q, K, P, G, M)
def setup_inputs_corners(rng):
    S, EF, OT, Q, K, P, G, M = base(rng); i = np.arange(L); n8 = L // 8
    EF[:, 1::2] = np.take_along_axis(EF[:, 1::2], rng.integers(0, 4, (N, 4, 1, E)), 3)
    for q in range(N):
        for g in range(8):
            mode = (q + g) % 4; B = Q[q, g]; C = K[q, g]; c = (0, W - 1, L, int(rng.integers(0, W)))[int(rng.integers(0, 4))]
            S[q, g, 15] = 0 if mode == 0 else 1 if mode < 3 else (rng.random(W) < 0.5)
            B[:, :, 0::8] = rng.integers(0, W, (3, 1, n8)); B[:, :, 1::8] = L * rng.integers(0, 2 * RO, (3, 16, n8)) + i[1::8]
            B[:, :, 2::8] = (W - 1) * rng.integers(0, 2, (3, 16, n8)); B[:, :, 6::8] = L * rng.integers(0, 2 * RO, (3, 16, n8)) + i[6::8] + 1
            C[:, :, 3::8] = C[:, :1, 3::8].copy(); C[:, :, 4::8] = 945 * rng.integers(0, 2, (3, 16, n8)); C[:, :15, 5::8] = 945
            if mode == 2:
                S[q, g, 15, c] = 0; sl = rng.choice(np.array([0, 7, 15]), (3, L)); o = i[rng.random(L) < 0.5]
                for l in range(3): B[l, sl[l, o], o] = c
            m = (g // 2 + q) % 4
            if m < 3: M[q, g, :15, 0] = 0 if m != 1 else 1
            if m == 2: M[q, g, int(rng.integers(0, 15)), 0] = 1
            P[q, g, :, 0::4] = P[q, g, :1, 0::4].copy(); P[q, g, :, 1::4] = 12 * rng.integers(0, 2, (3, L // 4)) - 6; P[q, g, 2, 2::4] = P[q, g, 1, 2::4]
            G[q, g, :15, 3::8] = S[q, g][:15, B[0, 0, 3::8]]
    return pack(S, EF, OT, Q, K, P, G, M)
def setup_inputs_crowd(rng):
    S, EF, OT, Q, K, P, G, M = base(rng); i = np.arange(L); first = int(rng.integers(0, 8)); flip = int(rng.integers(0, 2))
    o = [int(g) for g in rng.permutation(8) if g not in (first, 7 - first)]
    for m, g in enumerate((first, o[0], 7 - first, o[1], o[2], o[3])):
        if m > 3: c = int(rng.integers(L, W - 2))
        elif m // 2 == flip: c = int(rng.integers(L, RO * L - 2))
        else: c = int(rng.integers(2 * RO * L, W - 2))
        z = L - 1 if m == 1 else int(rng.integers(0, L))
        S[:, g, 15, c:c + 3] = 0; P[:, g, 0] = -6; P[:, g, 1:] = 6
        if m < 4:
            EF[:, g, :15] = rng.integers(1, 9, (N, 15, E)); G[:, g, :15] = 63
            if m < 2: Q[:, g, 0] = c
            else:
                sl = rng.integers(0, 16, L); K[:, g, 0] = 945; K[:, g, 0, sl, i] = 0; Q[:, g, 0, sl, i] = c
            if m % 2 == 1:
                Q[:, g, 0, :, z] = c + 1; G[:, g, :15, z] = 0
        else:
            Q[:, g, 0] = c + rng.integers(0, 3, (N, 16, L))
            if m == 5:
                EF[:, g, :15] = rng.integers(1, 9, (N, 15, E)); G[:, g, :15] = 0; P[:, g, 0, ::2] = 6
    return pack(S, EF, OT, Q, K, P, G, M)
def check_inputs(d):
    bad = []
    for k, lo, hi in (("st0", 0, 63), ("ef", -8, 8), ("ot", 0, 255), ("qn", 0, W - 1), ("qk", 0, 945), ("tu", -6, 6), ("gl", 0, 63), ("rm", 0, 1)):
        v = np.asarray(d[k]).astype(np.float64)
        if not (np.min(v) >= lo and np.max(v) <= hi): bad.append("range of " + k)
        elif np.any(v != np.rint(v)): bad.append("whole numbers in " + k)
    for k in ("st0", "ef", "gl", "rm"):
        v = np.asarray(d[k]).astype(np.float64).reshape(N, 8, 16, -1)[:, :, 15]
        if not (np.min(v) >= 0 and np.max(v) <= (1 if k == "st0" else 0)): bad.append("last row of the groups in " + k)
    return bad
def ints(a):
    return a.astype(np.float32).astype(np.int32)
def reference(st0, ef, ot, qn, qk, tu, gl, rm):
    S = ints(st0).reshape(N, 8, 16, W); EF = ints(ef).reshape(N, 8, 16, E)[:, :, :15]; OT = ints(ot).reshape(N, 8, 16, D); M = ints(rm).reshape(N, 8, 16, 1, 1)[:, :, :15]
    Q = np.ascontiguousarray(ints(qn).reshape(N, 8, 16, 3, L).transpose(0, 1, 3, 2, 4)); K = np.ascontiguousarray(ints(qk).reshape(N, 8, 16, 3, L).transpose(0, 1, 3, 2, 4))
    P = ints(tu).reshape(N, 8, 3, L); G = ints(gl).reshape(N, 8, 16, 1, L)[:, :, :15]; A = np.zeros((N, 8, 1, 1), np.int64)
    cf = (2 * np.arange(15) + 1)[:, None]; kk = np.arange(16)[:, None]; lane = np.arange(L)
    def hs(y, g):
        dd = np.abs(y - g)
        return np.stack([np.add.reduce(dd, axis=2), 16 * np.add.reduce((dd > EPS).astype(np.int32), axis=2), np.add.reduce(dd * M, axis=2)], axis=2)
    for t in range(RO):
        if t > 0:
            Q, K, P, G = (np.roll(a, 1, axis=0) for a in (Q, K, P, G))
        j = np.argmin(P, axis=2); jj = j[:, :, None, None, :]
        q = np.take_along_axis(Q, jj, 2)[:, :, 0]; key = np.take_along_axis(K, jj, 2)[:, :, 0]
        s = np.take_along_axis(S, q.reshape(N, 8, 1, 16 * L), 3).reshape(N, 8, 16, 16, L)
        key = np.where(s[:, :, 15] == 1, 1023, key)
        k0 = np.argmin(key, axis=2)
        x = np.take_along_axis(s, k0[:, :, None, None, :], 3)[:, :, :15, 0]; xn = np.take_along_axis(q, k0[:, :, None], 2)[:, :, 0]
        u = np.add.reduce(cf * x, axis=2); v = np.add.reduce(np.maximum.reduce(s[:, :, :15], axis=3), axis=2)
        o = np.take_along_axis(OT, ((u + v) & (D - 1))[:, :, None, :], 3)
        n = (((o * u[:, :, None]) >> 5) + o + 37 * kk + A) & (E - 1)
        e = np.take_along_axis(EF, n.reshape(N, 8, 1, 16 * L), 3).reshape(N, 8, 15, 16, L)
        y = np.clip(x[:, :, :, None] + e, 0, 63)
        h = hs(y, G); hx = hs(x[:, :, :, None], G)[:, :, :, 0]
        ha = np.take_along_axis(h, jj, 2)[:, :, 0]; hb = np.take_along_axis(h, (jj + 1) % 3, 2)[:, :, 0]
        a = np.argmin(ha, axis=2); b = np.argmin(hb, axis=2)
        ya = np.take_along_axis(y, a[:, :, None, None, :], 3)[:, :, :, 0]; yb = np.take_along_axis(y, b[:, :, None, None, :], 3)[:, :, :, 0]
        np.put_along_axis(S[:, :, 15], xn, 1, 2)
        S[:, :, :15, t * L:(t + 1) * L] = ya; S[:, :, 15, t * L:(t + 1) * L] = 0
        S[:, :, :15, (RO + t) * L:(RO + t + 1) * L] = np.roll(yb, 1, axis=0); S[:, :, 15, (RO + t) * L:(RO + t + 1) * L] = 0
        np.put_along_axis(K, jj, key[:, :, None], 2)
        w = np.argmax(K, axis=3)[:, :, :, None]
        np.put_along_axis(Q, w, t * L + lane, 3); np.put_along_axis(K, w, hx[:, :, :, None], 3)
        go = (np.min(ha, axis=2) < np.take_along_axis(hx, j[:, :, None], 2)[:, :, 0]).astype(np.int32)
        np.put_along_axis(P, j[:, :, None], np.take_along_axis(P, j[:, :, None], 2) + 1 - 3 * go[:, :, None], 2)
        A = (np.add.reduce(go, axis=2) & 63)[:, :, None, None]
    yq = np.ascontiguousarray((4096 * K + Q).transpose(0, 1, 3, 2, 4)).reshape(N, 128, 3 * L)
    return {"ys": np.ascontiguousarray(S[..., :2 * RO * L]).reshape(N, 128, 2 * RO * L).astype(np.float32).astype(BF), "ym": np.ascontiguousarray(S[:, :, 15, 2 * RO * L:]).astype(np.float32).astype(BF),
            "yq": yq.astype(np.float32), "yp": P.reshape(N, 8, 3 * L).astype(np.float32)}

@@ -1,0 +1,783 @@
+import numpy as np
+from concourse.bass import DstId, RemoteDMATransfer
+from concourse.mybir import AluOpType, ActivationFunctionType
+
+ALU = AluOpType
+AF = ActivationFunctionType
+BF, F32, I32, U16, F16 = "bfloat16", "float32", "int32", "uint16", "float16"
+RO = 3
+BIG = float(1 << 23)
+
+SCRATCH = {}
+
+
+def _sb(name, n, dt, where="sbuf"):
+    SCRATCH[name] = (where, [128, n], dt)
+
+
+for _n, _c, _d in (
+    ("St", 3088, BF), ("Ef", 4096, BF), ("Ot", 256, BF), ("Qn", 768, I32), ("Qk", 768, I32), ("Tu", 768, I32),
+    ("Tub", 768, BF), ("Rm", 16, BF), ("Gl0", 256, BF), ("Gl1", 256, BF), ("Gl2", 256, BF),
+    ("Cw0", 768, I32), ("Cw1", 768, I32), ("Cw2", 768, I32), ("Cs0", 768, I32), ("Cs1", 768, I32), ("Cf", 768, F32),
+    ("C1", 768, I32), ("C2", 768, I32), ("K16", 768, F16), ("wsc", 768, F32),
+    ("Sb0", 400, BF), ("Sb1", 400, BF), ("Sb2", 400, BF), ("Lb0", 400, BF), ("Lb1", 400, BF), ("Lb2", 256, BF),
+    ("sg", 4096, BF), ("smx", 4096, BF), ("eg", 4096, BF), ("yy", 4096, BF), ("dd", 4096, BF), ("ind", 4096, BF),
+    ("P40", 48, BF), ("pmin", 48, F32), ("mj", 48, BF), ("mm", 48, BF), ("ji", 16, I32), ("jj", 16, I32),
+    ("mj4", 48, BF), ("pm2", 48, F32), ("ji2", 16, I32), ("jalt", 16, I32),
+    ("dj", 16, F32), ("LJ", 16, U16), ("R0j", 256, BF), ("t12", 48, BF), ("Pfin", 48, BF), ("Pout", 768, F32),
+    ("q32", 256, I32), ("q16", 256, U16), ("qf", 256, F16), ("key", 256, F16), ("msc", 256, F32),
+    ("mi", 16, I32), ("k0", 16, I32), ("Dk", 256, BF), ("Lk", 16, U16), ("xx", 256, BF), ("xm", 256, BF),
+    ("uvi", 16, I32), ("uva", 16, I32), ("Du", 256, BF), ("Lo", 16, U16), ("u32", 256, F32), ("tO", 256, F32),
+    ("nr", 256, I32), ("na", 256, I32), ("n16", 256, U16), ("dx", 256, BF), ("ix", 256, BF),
+    ("hxm", 48, F32), ("hxs", 48, F32), ("hsc", 768, F32), ("t48", 96, F32), ("ss", 96, F32), ("ai", 32, I32),
+    ("jba", 64, I32), ("gt", 16, F32), ("Dj", 768, BF), ("Lab", 32, U16), ("ya", 256, BF),
+    ("mT", 256, BF), ("wi", 48, I32), ("wa", 48, I32), ("wT", 128, BF), ("R0w", 256, BF),
+    ("kT", 64, BF), ("R0k", 256, BF), ("xsc", 256, F32), ("Dx", 256, F16), ("RT", 256, F32), ("eq", 256, F16),
+    ("Lx", 32, U16), ("cnt", 16, BF), ("Ai", 16, I32), ("Aa", 16, I32), ("cA", 16, F32),
+    ("ci", 16, I32), ("cf", 32, F32), ("cb", 2560, BF), ("ch", 1536, F16), ("ce", 1920, BF), ("d0", 1680, BF),
+    ("d0c", 128, F32), ("cl", 64, U16), ("tf", 768, F32), ("tb", 768, BF), ("ti", 16, I32), ("m2", 256, BF), ("kz", 256, BF),
+):
+    _sb(_n, _c, _d)
+for _n in ("PA0", "PA1", "PB0", "PB1", "PH", "PT0", "PT1", "PQ"):
+    _sb(_n, 512, F32, "psum")
+
+LOADS = ("tu", "qn", "qk", "st0", "gl", "rm", "ot", "ef")
+STORES = ("o1", "o2", "o3", "o4", "o5", "o6", "o7")
+SEMAPHORES = (["cV", "cS", "cP", "cG", "lsem", "rG1", "rG2", "rC00", "rC01", "rC10", "rC11", "rB0", "rB1", "rB2"]
+              + ["l" + n for n in LOADS] + list(STORES))
+
+G1ENG = ("VSSS", "SSSS")
+G2ENG = ("SSSS", "SSSS")
+INDENG = ("SSSS", "SSVV")
+ADDENG = ("VVVV", "VVVV")
+YBENG = "SS"
+VC = 1.0
+BASE = (0.52, 1.56, 3.8)
+CASES = ((0.8, 1.56, 3.8, 1.0), (0.52, 1.1, 2.0, 1.0), (0.52, 2.0, 5.5, 1.0), (0.52, 1.56, 3.8, 2.0))
+LAT, LATS = 100.0, 60.0
+SEED, ROUNDS, JIT, WAITW, LOOK = 0, 60, 3000.0, 1.0, 0.0
+TRY = (400, 1000)
+KINS = ("q32 q16 sg", "key msc mi k0 Dk Lk xx uvi uva Du Lo u32 tO nr na n16", "smx", "eg", "yy dd PA0 PA1 PB0 PB1", "ind",
+        "dx ix hxm hxs", "xm kT R0k xsc Dx RT eq Lx", "St", "R0j mT qf C1 K16 wsc wi wa wT R0w C2 Cs Cf PQ",
+        "hsc t48 ss ai jba gt Dj Lab Sb", "PT0", "PT1", "PH", "t12 P40 mj mm mj4 pm2 ji2 jalt dj")
+TIMES = []
+
+
+def R(name, a, b, step=1, p0=0, p1=128):
+    return ("r", name, a, b, step, p0, p1)
+
+
+def IND(win, off):
+    return ("i", win, off)
+
+
+def nel(r):
+    if r[0] == "i":
+        return 16 * nel(r[2])
+    return (r[3] - r[2] + r[4] - 1) // r[4]
+
+
+def dty(r):
+    return SCRATCH[(r[1] if r[0] == "r" else r[1][1])][2]
+
+
+def inps(r):
+    return r[0] == "r" and SCRATCH[r[1]][0] == "psum"
+
+
+def flat(rs):
+    o = []
+    for r in rs:
+        if isinstance(r, tuple):
+            o += [r] if r[0] == "r" else [r[1], r[2]]
+    return o
+
+
+def clash(a, b):
+    if a[1] != b[1] or a[3] <= b[2] or b[3] <= a[2]:
+        return False
+    return not (a[4] == b[4] and a[4] > 1 and (a[2] - b[2]) % a[4] != 0)
+
+
+def ap(T, r):
+    if not isinstance(r, tuple):
+        return r
+    if r[0] == "i":
+        return ap(T, r[1]).indirect(ap(T, r[2]))
+    if r[4] == 1:
+        return T[r[1]][r[5]:r[6], r[2]:r[3]]
+    return T[r[1]][r[5]:r[6], r[2]:r[3]:r[4]]
+
+
+def build(case=None):
+    ops = []
+    PC, GC, SC = case or BASE
+
+    def add(q, kind, args, rd, wr, cost, **kw):
+        o = dict(q=q, kind=kind, args=args, rd=flat(rd), wr=flat(wr), cost=cost, n=len(ops))
+        o.update(kw)
+        ops.append(o)
+        return o
+
+    def vcost(out, ins, two=False):
+        if out[0] == "i":
+            return 50 + SC * nel(out) * VC
+        if ins[0][0] == "i":
+            return 50 + GC * nel(out) * VC
+        n = nel(out)
+        if two:
+            f = 1.0 if (inps(ins[0]) or inps(ins[1])) else 2.0
+        else:
+            f = 0.5 if all(dty(r) in (BF, F16, U16) for r in [out] + ins) else 1.0
+        return max(64, n * f) * VC
+
+    def cp(out, a):
+        wr = [out[1]] if out[0] == "i" else [out]
+        rd = [a, out[2]] if out[0] == "i" else [a]
+        add("V", "cp", (out, a), rd, wr, vcost(out, [a]))
+
+    def tt(out, a, b, op):
+        add("V", "tt", (out, a, b, op), [a, b], [out], vcost(out, [a, b], True))
+
+    def ts(out, a, s1, op0, s2=None, op1=None):
+        add("V", "ts", (out, a, s1, s2, op0, op1), [a, s1, s2], [out], vcost(out, [a]))
+
+    def scan(out, d0, d1, op0, op1):
+        add("V", "scan", (out, d0, d1, op0, op1), [d0, d1], [out], vcost(out, [d0, d1]))
+
+    def ms(out, v):
+        add("V", "ms", (out, v), [], [out], max(64, nel(out) * 0.5) * VC)
+
+    def act(out, a, f=AF.Identity, bias=0.0, scale=1.0):
+        c = 65 + GC * nel(out) * VC if a[0] == "i" else max(64, nel(out)) * VC + 30
+        add("S", "act", (out, a, f, bias, scale), [a, bias, scale], [out], c)
+
+    def mov(eng, out, a):
+        if eng == "V":
+            cp(out, a)
+        else:
+            act(out, a)
+
+    def mm(lst, chain=True):
+        c = sum(max(min(64, nel(l)), nel(r)) for (_, l, r) in lst) * PC + 30
+        add("P", "mm", (lst, chain), [x for (_, l, r) in lst for x in (l, r)], [o for (o, _, _) in lst], c)
+
+    def iota(out, pat, base, cm):
+        add("G", "iota", (out, pat, base, cm), [], [out], 130 + 2 * nel(out) * VC)
+
+    def asel(out, a, pat, base, cm, op=ALU.is_equal, fill=0.0):
+        add("G", "asel", (out, a, pat, base, cm, op, fill), [a], [out], 170 + 2 * nel(out) * VC)
+
+    def load(q, name, out, kb, behind=()):
+        add(q, "load", (name, out), list(behind), [out], 60, sem="l" + name, lat=1800 + kb * 5.0)
+
+    def store(sem, fn, rd, kb):
+        add("Y", "store", (sem, fn), rd, [], 60, sem=sem, lat=1800 + kb * 5.0)
+
+    def send(kind, src, dst, sem, kb):
+        s = add("G", "send", (kind, src, dst, sem), [src], [], 500 + kb * 14.0)
+        for d, sm in zip(dst, sem):
+            add("R", "recv", (kind,), [], [d], 0, sem=sm, lat=0, after=(s["n"], 1500.0))
+
+    add_, sub_, mul_, max_, min_ = ALU.add, ALU.subtract, ALU.mult, ALU.max, ALU.min
+    eq_, and_ = ALU.is_equal, ALU.bitwise_and
+
+    load("Y", "tu", R("Tu", 0, 128, 1, 0, 48), 24)
+    load("Y", "qn", R("Qn", 0, 768), 400)
+    load("S", "st0", R("St", 0, 3072), 800)
+    load("Y", "qk", R("Qk", 0, 768), 800)
+    load("Y", "gl", R("Gl0", 0, 256), 800)
+    load("Y", "rm", R("Rm", 0, 1), 800)
+    load("Y", "ot", R("Ot", 0, 256), 800)
+    load("Y", "ef", R("Ef", 0, 4096), 800, [R("Qn", 0, 768)])
+    send("G", R("Gl0", 0, 256), [R("Gl1", 0, 256), R("Gl2", 0, 256)], ["rG1", "rG2"], 128)
+
+    def col(j):
+        return R("cf", j, j + 1)
+    cP, cB, cAa, cN15, cF15, cJ, cU, c16P, c16A, cM16, cM4k, cN16, cN4k, cN64k, cSg, cF64k, cK37 = [col(j) for j in range(17)]
+    iota(R("ci", 0, 1), [[0, 1]], 0, 1)
+    ts(R("ci", 4, 5), R("ci", 0, 1), 15, and_)
+    ts(R("ci", 8, 9), R("ci", 0, 1), 4, ALU.arith_shift_right)
+    cp(cP, R("ci", 0, 1)); cp(cB, R("ci", 4, 5)); cp(cAa, R("ci", 8, 9))
+    ts(cN15, cB, 15.0, ALU.is_lt); ts(cF15, cB, 15.0, eq_)
+    ts(cJ, cB, 3072.0, add_)
+    ts(col(20), cB, 2.0, mul_, 1.0, add_); ts(cU, col(20), cN15, mul_)
+    ts(c16P, cP, 16.0, mul_); ts(c16A, cAa, 16.0, mul_)
+    ts(cM16, R("Rm", 0, 1), 16.0, mul_); ts(cM4k, R("Rm", 0, 1), 4096.0, mul_)
+    ts(cN16, cN15, 16.0, mul_); ts(cN4k, cN15, 4096.0, mul_); ts(cN64k, cN15, 65536.0, mul_)
+    ts(cSg, cN15, 2048.0, mul_, -1920.0, add_)
+    ts(cF64k, cF15, 65536.0, mul_)
+    ts(cK37, cB, 37.0, mul_, -0.484375, add_)
+
+    def blk(buf, j, p1=128):
+        return R(buf, 128 * j, 128 * j + 128, 1, 0, p1)
+    Ib, I0, nI, IB, M16, kk, gg, B16, Wu, Wr0, Wr1, Wr2, One = [blk("cb", j) for j in range(13)]
+    ms(R("cb", 12 * 128, 15 * 128), 1.0)
+    ones3 = R("cb", 12 * 128, 15 * 128, 1, 0, 2)
+    ones31 = R("cb", 12 * 128, 15 * 128, 1, 0, 1)
+    asel(Ib, One, [[-1, 128]], 0, 1)
+    iota(kk, [[0, 8], [1, 16]], 0, 0)
+    iota(gg, [[1, 8], [0, 16]], 0, 0)
+    act(I0, Ib, scale=cN15); act(nI, Ib, scale=-1.0); act(IB, Ib, scale=BIG / 2)
+    ts(M16, kk, cB, eq_); ts(B16, gg, cAa, eq_)
+    kz = R("kz", 0, 256, 1, 0, 1)
+    ms(blk("kz", 1, 1), 0.0); cp(blk("kz", 0, 1), blk("cb", 5, 1))
+    act(Wu, B16, scale=cU); act(Wr0, B16, scale=cN4k); act(Wr1, B16, scale=cN64k); act(Wr2, B16, scale=cM4k)
+    o = 15 * 128
+
+    def sm(a, n=8, step=1):
+        return R("cb", o + a, o + a + n * step - (step - 1), step)
+    C8 = R("cb", 7 * 128, 8 * 128, 16)
+    C128, C256, Wu8, Wv8, C16p, Cp = sm(0), sm(8), sm(16), sm(24), sm(32), sm(56)
+    Cjb = sm(48, 16)
+    Wmk = sm(64, 16)
+    ts(C128, C8, 128.0, mul_); ts(C256, C8, 256.0, mul_); ts(Wu8, C8, cU, mul_); ts(Wv8, C8, cN15, mul_)
+    ts(C16p, C8, c16P, mul_); ts(sm(48), C8, c16A, mul_); ts(Cp, C8, cP, mul_)
+    ts(sm(64), C8, cF64k, mul_); ts(sm(72), C8, cF15, mul_)
+    Wd, Wi, Ws = sm(80, 24), sm(104, 24), sm(128, 24)
+    ms(sm(80, 72), 0.0)
+    ts(sm(80, 8, 3), C8, cN16, mul_); ts(sm(82, 8, 3), C8, cM16, mul_)
+    ts(sm(105, 8, 3), C8, cN16, mul_, 16.0, mul_); ts(sm(129, 8, 3), C8, cSg, mul_)
+    I4 = R("cb", o + 152, o + 200, 1, 0, 48)
+    ms(R("Tub", 128, 176, 1, 0, 48), 4.0)
+    asel(I4, R("Tub", 128, 176, 1, 0, 48), [[-1, 2], [-6, 8], [-2, 3]], 0, 1)
+    Iq = blk("cb", 17)
+    act(Iq, Ib, scale=0.25)
+    lv = R("cb", 18 * 128, 18 * 128 + 48)
+    iota(lv, [[0, 16], [1, 3]], 0, 0)
+    Ih, I16h, B16h, Tri, Oneh = [blk("ch", j) for j in range(5)]
+    cp(Ih, Ib); ts(I16h, Ib, 16.0, mul_); cp(B16h, B16); ts(Tri, kk, cB, ALU.is_le, 4096.0, mul_)
+    cp(blk("ch", 4, 1), blk("cb", 12, 1))
+    C8h, C4kh = R("ch", 640, 648), R("ch", 648, 656)
+    cp(C8h, C8); ts(C4kh, C8, 4096.0, mul_)
+    iota(R("tf", 0, 768, 1, 0, 1), [[1, 768]], 0, 0)
+    cp(R("ch", 768, 1536, 1, 0, 1), R("tf", 0, 768, 1, 0, 1))
+    Ej = [blk("ce", l, 24) for l in range(3)]
+    Ep = [blk("ce", 3 + l, 49) for l in range(3)]
+    En = [blk("ce", 6 + l, 49) for l in range(3)]
+    Ek, E8 = [blk("ce", 9, 33), blk("ce", 14, 33)], blk("ce", 10, 8)
+    B22 = float(1 << 22)
+    ta, tc = blk("ce", 11, 24), blk("ce", 12, 24)
+    ms(ta, -BIG)
+    asel(tc, ta, [[-3, 8], [0, 16]], 0, 1, ALU.is_ge)
+    asel(ta, tc, [[3, 8], [0, 16]], 2, -1, ALU.is_ge)
+    for l in range(3):
+        asel(Ej[l], ta, [[-3, 8], [0, 16]], -l, 1, ALU.not_equal, -2560.0)
+    asel(E8, blk("cb", 12, 8), [[-1, 8], [0, 16]], 0, 1)
+    t0, t1, t2 = [blk("tb", j, 49) for j in range(3)]
+    act(t0, blk("cb", 5, 49), bias=-30 * B22, scale=2 * B22)
+    ms(t1, B22)
+    for l in range(3):
+        asel(t2, t0, [[-1, 8], [0, 16]], -1 - 8 * l, 1)
+        asel(En[l], t1, [[-1, 8], [0, 16]], -25 - 8 * l, 1)
+        tt(Ep[l], En[l], t2, add_)
+        act(blk("ce", 3 + l, 1), blk("cb", 5, 1), AF.Square, bias=-15.0 * 2048, scale=2048.0)
+        act(En[l], Ep[l], scale=-1.0)
+    t0, t1, t2, t3 = blk("tb", 4, 33), blk("tb", 5, 33), blk("tb", 3, 33), blk("ce", 13, 33)
+    act(t0, blk("cb", 5, 33), scale=-8192.0)
+    ms(t1, 4096.0)
+    for h in range(2):
+        asel(t2, t0, [[-1, 8], [0, 16]], -17 - 8 * h, 1)
+        asel(t3, t1, [[-1, 8], [0, 16]], -1 - 8 * h, 1)
+        tt(Ek[h], t2, t3, add_)
+        act(blk("ce", 9 + 5 * h, 1), blk("cb", 5, 1), AF.Square, scale=64.0)
+    ms(R("wT", 0, 128, 64), 1.0); ms(R("kT", 0, 1), 1.0)
+    M2 = R("m2", 0, 256)
+    act(blk("m2", 0), M16); act(blk("m2", 1), M16)
+    lv2 = R("cb", 19 * 128, 19 * 128 + 48)
+    for l in range(3):
+        ms(R("cb", 19 * 128 + l, 19 * 128 + 48, 3), float((l + 2) % 3))
+    dMx, dH, dW, dX, dS3, dM3 = (R("d0", 0, 512), R("d0", 512, 896), R("d0", 896, 1280), R("d0", 1280, 1536),
+                                 R("d0", 1536, 1632), R("d0", 1632, 1680))
+    for r, body, head, st in ((dM3, 0.0, 1024.0, 3), (dMx, 1.0, 0.0, 16), (dH, -1.0, BIG, 16), (dW, 1.0, -BIG, 16),
+                              (dX, 0.0, BIG, 16), (dS3, 1.0, 0.0, 3), (R("d0c", 0, 128), -BIG, 32768.0, 16)):
+        ms(r, body); ms(R(r[1], r[2], r[3], st), head)
+    ms(R("St", 3072, 3088), 0.0)
+    Lb8, Lb16, Lend, Lgo = R("cl", 0, 8), R("cl", 0, 16), R("cl", 16, 32), R("cl", 32, 35)
+    cp(Lb16, R("cb", 5 * 128, 5 * 128 + 16))
+    ts(Lend, R("cb", 5 * 128, 5 * 128 + 16), 16.0, mul_, 15.0, add_)
+    jf, j3 = R("cf", 21, 24), R("ti", 0, 3)
+    ts(jf, R("cb", 5 * 128, 5 * 128 + 3), 16.0, mul_, cB, add_)
+    ts(j3, jf, -1.0, add_, 1.0 / 3.0, mul_)
+    cp(Lgo, j3)
+
+    def H(name, h, n=128, step=1, a=0):
+        return R(name, h * n + a, h * n + n, step)
+
+    cp(R("Tub", 0, 128, 1, 0, 48), R("Tu", 0, 128, 1, 0, 48))
+    mm([(R("PQ", 0, 48), R("Tub", 0, 128, 1, 0, 48), I4)])
+    tt(R("P40", 0, 48), R("PQ", 0, 48), lv, add_)
+
+    for t in range(RO):
+        last = t == RO - 1
+        P4 = R("P40", 0, 48)
+        Cw, Gl, Sb, Lp = "Cw%d" % t, "Gl%d" % t, "Sb%d" % t, "Lb%d" % (t - 1)
+        cA = cK37 if t == 0 else R("cA", 0, 1)
+        PT = ["PT0", "PT1"]
+        Pinc, mj12, go = R(Sb, 256, 304), R(Sb, 304, 352), R(Sb, 384, 400)
+        if t == 0:
+            jj = R("jj", 0, 16)
+            scan(R("pmin", 0, 48), dM3, P4, add_, min_)
+            cp(R("ji", 0, 16), R("pmin", 2, 48, 3)); ts(jj, R("ji", 0, 16), 3, and_)
+            for h in range(2):
+                tt(H("Dk", h), IND(H("jj", h, 8), Lb8), M16, mul_)
+                pl = R(PT[h], 384, 392)
+                mm([(pl, M16, Cp), (pl, H("Dk", h), C256)])
+                cp(H("LJ", h, 8), pl)
+        else:
+            jj = R(Lp, 368, 384)
+            ts(R("LJ", 0, 16), R(Lp, 352, 368), cB, add_)
+            tt(R("t12", 0, 48), IND(R(Lp, 384, 400), Lgo), R(Lp, 304, 352), mul_)
+            tt(P4, R(Lp, 256, 304), R("t12", 0, 48), add_)
+        tt(R("mj", 0, 48), IND(jj, Lgo), lv, eq_)
+        tt(R("mm", 0, 48), IND(jj, Lgo), lv2, eq_)
+        act(R("mj4", 0, 48), R("mj", 0, 48), scale=4.0); act(mj12, R("mj", 0, 48), scale=-12.0)
+        tt(Pinc, R("mj4", 0, 48), P4, add_)
+        if not last:
+            scan(R("pm2", 0, 48), dM3, Pinc, add_, min_)
+            cp(R("ji2", 0, 16), R("pm2", 2, 48, 3)); ts(R("jalt", 0, 16), R("ji2", 0, 16), 3, and_)
+            tt(R("dj", 0, 16), jj, R("jalt", 0, 16), sub_)
+        for h in range(2):
+            lj = H("LJ", h, 8)
+            if t == 0:
+                cp(H("q16", h), IND(R("Qn", 128 * h, 768), lj))
+                ts(H("key", h), IND(R("Qk", 128 * h, 768), lj), 1025.0, add_)
+            else:
+                ts(H("q32", h), IND(H(Cw, h, 384), lj), 4095, and_)
+                cp(H("q16", h), H("q32", h))
+                ts(H("key", h), IND(H(Cw, h, 384), lj), 1.0 / 4096, mul_, 1024.625, add_)
+            for c in range(4):
+                mov(G1ENG[h][c], H("sg", 4 * h + c, 512), IND(R("St", 0, 3072), H("q16", 4 * h + c, 32)))
+                scan(H("smx", 4 * h + c, 512), dMx, H("sg", 4 * h + c, 512), mul_, max_)
+            mm([(R(PT[h], 0, 256), blk("cb", 12, 1), kz), (R(PT[h], 0, 128), H("key", h), I16h)]
+               + [(R(PT[h], k, 256, 16), H("sg", h, 2048, 16, k), Wmk) for k in range(16)])
+            scan(H("msc", h), R("d0c", 0, 128), R(PT[h], 0, 128), max_, min_)
+            act(H("mT", h), R(PT[h], 128, 256))
+            cp(H("mi", h, 8), H("msc", h, 128, 16, 15)); ts(H("k0", h, 8), H("mi", h, 8), 15, and_)
+            tt(H("Dk", h), IND(H("k0", h, 8), Lb8), M16, mul_)
+            pl = R(PT[h], 392, 400)
+            mm([(pl, M16, C16p), (pl, H("Dk", h), C8)])
+            cp(H("Lk", h, 8), pl)
+            act(H("xx", h), IND(H("sg", h, 2048), H("Lk", h, 8)))
+            pl = R(PT[h], 400, 408)
+            mm([(pl, H("smx", h, 2048, 16, 15), Wv8), (pl, H("xx", h), Wu8)])
+            mm([(R(PT[h], 256, 384), Wu, H("xx", h))])
+            act(H("u32", h), R(PT[h], 256, 384), bias=32.0)
+            cp(H("uvi", h, 8), pl); ts(H("uva", h, 8), H("uvi", h, 8), 255, and_)
+            tt(H("Du", h), IND(H("uva", h, 8), Lb8), M16, mul_)
+            pl = R(PT[h], 408, 416)
+            mm([(pl, H("Du", h), C8)])
+            cp(H("Lo", h, 8), pl)
+            tt(H("tO", h), IND(R("Ot", 0, 256), H("Lo", h, 8)), H("u32", h), mul_)
+            ts(H("nr", h), H("tO", h), 1.0 / 32, mul_, cA, add_)
+            ts(H("na", h), H("nr", h), 4095, and_)
+            cp(H("n16", h), H("na", h))
+            for c in range(4):
+                mov(G2ENG[h][c], H("eg", 4 * h + c, 512), IND(R("Ef", 0, 4096), H("n16", 4 * h + c, 32)))
+            mm([(blk("PH", h), I0, H("xx", h)), (blk("PH", h), nI, H(Gl, h))])
+            act(H("dx", h), blk("PH", h), AF.Abs)
+            ts(H("ix", h), H("dx", h), 4.0, ALU.is_gt)
+            pl = R("PQ", 416 + 24 * h, 440 + 24 * h)
+            mm([(pl, H("dx", h), Wd), (pl, H("ix", h), Wi)])
+            ts(H("qf", h), H("q16", h), -1536.0, add_)
+        tt(R("hxm", 0, 48), R("PQ", 416, 464), R("mj", 0, 48), mul_)
+        scan(R("hxs", 0, 48), R("d0", 1536, 1584), R("hxm", 0, 48), mul_, add_)
+        act(R("xm", 0, 256), R("xx", 0, 256), bias=cF15, scale=cN15)
+        tt(R("kT", 1, 17), R("k0", 0, 16), R("k0", 0, 16), mul_)
+        cp(R("kT", 17, 33), R("k0", 0, 16))
+        mm([(blk("PH", 2, 33), R("kT", 0, 33), Ib)])
+        act(blk("R0k", 0, 33), blk("PH", 2, 33))
+        pl = R("PH", 256, 512)
+        mm([x for h in range(2) for x in ((blk("PH", 2 + h), blk("R0k", 0, 33), Ek[h]), (blk("PH", 2 + h), H("qf", h), Ih))], 2)
+        scan(R("xsc", 0, 256), dX, pl, add_, min_)
+        tt(R("Dx", 0, 256), IND(R("xsc", 0, 256), Lend), M2, mul_)
+        mm([(pl, B16h, R("Dx", 0, 256)), (blk("PH", 2), Ih, Tri), (blk("PH", 3), Ih, Tri)])
+        act(R("RT", 0, 256), pl)
+        tt(R("eq", 0, 256), IND(R("xsc", 0, 256), Lend), R("RT", 0, 256), eq_)
+        mm([x for h in range(2) for x in ((R("PH", 256 + 8 * h, 264 + 8 * h), H("Dx", h), C8h),
+                                          (R("PH", 256 + 8 * h, 264 + 8 * h), H("eq", h), C4kh))], 2)
+        ts(R("Lx", 0, 32, 2), R("PH", 256, 272), 1536.0, add_, cJ, min_)
+        for c in range(16):
+            cp(IND(R("St", 0, 3088), R("Lx", 2 * c, 2 * c + 1)), H("xm", c, 16))
+        for h in range(2):
+            PQ = "PA0" if h and "P" not in ADDENG[0] + ADDENG[1] else "PQ"
+            pq = R(PQ, 0, 384)
+            if t == 0:
+                for l in range(3):
+                    a = l * 256 + h * 128
+                    ts(blk(PQ, l), R("Qk", a, a + 128), 4096.0, mul_)
+                    tt(H(Cw, 3 * h + l), R("Qn", a, a + 128), blk(PQ, l), add_)
+            mm([(blk("PH", h, 24), H("mj", h, 24), Ib)])
+            r0 = blk("R0j", h, 24)
+            act(r0, blk("PH", h, 24))
+            lst = []
+            for l in range(3):
+                pl = blk(PQ, l)
+                lst += [(pl, Ej[l], r0), (pl, H("mT", h), IB), (pl, Ih, H("qf", h))]
+            mm(lst, 3)
+            tt(H("C1", h, 384), H(Cw, h, 384), pq, max_)
+            ts(H("K16", h, 384), H("C1", h, 384), 1.0 / 4096, mul_, 1024.625, add_)
+            mm([(blk(PQ, l), H("K16", 3 * h + l), I16h) for l in range(3)], False)
+            scan(H("wsc", h, 384), dW, pq, add_, max_)
+            cp(H("wi", h, 24), H("wsc", h, 384, 16, 15)); ts(H("wa", h, 24), H("wi", h, 24), 15, and_)
+            cp(R("wT", 64 * h + 1, 64 * h + 25), H("wa", h, 24))
+            tt(R("wT", 64 * h + 25, 64 * h + 49), H("wa", h, 24), H("wa", h, 24), mul_)
+            mm([(blk("PH", h, 49), R("wT", 64 * h, 64 * h + 49), Ib)])
+            r0 = blk("R0w", h, 49)
+            act(r0, blk("PH", h, 49))
+            mm([(blk(PQ, l), Ep[l], r0) for l in range(3)], False)
+            tt(H("C2", h, 384), H("C1", h, 384), pq, min_)
+            a = 768 + 256 * t + 128 * h
+            lst = []
+            for l, w, d in ((0, Wr0, "dx"), (1, Wr1, "ix"), (2, Wr2, "dx")):
+                pl = blk(PQ, l)
+                lst += [(pl, En[l], r0), (pl, blk("ch", 4, 1), R("ch", a, a + 128, 1, 0, 1)), (pl, w, H(d, h))]
+            mm(lst, 3)
+            if last:
+                for l in range(3):
+                    tt(H("Cf", 2 * l + h), H("C2", 3 * h + l), blk(PQ, l), max_)
+            else:
+                tt(H("Cs%d" % t, h, 384), H("C2", h, 384), pq, max_)
+                send("N", H("Cs%d" % t, h, 384), [H("Cw%d" % (t + 1), h, 384)], ["rC%d%d" % (t, h)], 192)
+        if last:
+            store("o1", ("yq", None, R("Cf", 0, 768)), [R("Cf", 0, 768)], 400)
+        for h in range(2):
+            vadd = "V" in ADDENG[0] + ADDENG[1]
+            if "V" in ADDENG[h]:
+                mm([(blk("PA1", h), I0, H("xx", h))])
+            for b in range(4):
+                pa, pb = "PA%d" % (0 if vadd else b % 2), "PB%d" % (b % 2)
+                yb, db, ib = H("yy", 4 * h + b, 512), H("dd", 4 * h + b, 512), H("ind", 4 * h + b, 512)
+                if ADDENG[h][b] == "V":
+                    for k in range(4 * b, 4 * b + 4):
+                        tt(H("ind", 16 * h + k), H("eg", h, 2048, 16, k), blk("PA1", h), add_)
+                    ts(yb, ib, 0.0, max_, 63.0, min_)
+                else:
+                    lst = []
+                    for kl in range(4):
+                        lst += [(blk(pa, kl), I0, H("xx", h)), (blk(pa, kl), Ib, H("eg", h, 2048, 16, 4 * b + kl))]
+                    mm(lst, 2)
+                    ts(yb, R(pa, 0, 512), 0.0, max_, 63.0, min_)
+                mm([(R(pb, 0, 512), Ib, yb)] + [(blk(pb, kl), nI, H(Gl, h)) for kl in range(4)])
+                act(db, R(pb, 0, 512), AF.Abs)
+                if INDENG[h][b] == "V":
+                    ts(ib, db, 4.0, ALU.is_gt)
+                else:
+                    act(ib, db, AF.Sign, bias=-4.5)
+                lst = []
+                for k in range(4 * b, 4 * b + 4):
+                    pl = R(PT[h], k, 384, 16)
+                    lst += [(pl, H("dd", 16 * h + k), Wd), (pl, H("ind", 16 * h + k), Wi if INDENG[h][b] == "V" else Ws)]
+                mm(lst, 2)
+            scan(H("hsc", h, 384), dH, R(PT[h], 0, 384), add_, min_)
+
+        def lanes(d, win, bank, a, c, out):
+            tt(H("Dj", d, 256), IND(win, Lb16), M2, mul_)
+            mm([x for h in range(2) for x in ((R(bank, a + 8 * h, a + 8 * h + 8), M16, c),
+                                              (R(bank, a + 8 * h, a + 8 * h + 8), H("Dj", 2 * d + h), C128))], 2)
+            cp(out, R(bank, a, a + 16))
+        ends = R("hsc", 15, 768, 16)
+        tt(R("t48", 0, 48), ends, R("mm", 0, 48), mul_)
+        tt(R("t48", 48, 96), ends, R("mj", 0, 48), mul_)
+        scan(R("ss", 0, 96), dS3, R("t48", 0, 96), mul_, add_)
+        ts(R("ai", 0, 32), R("ss", 2, 96, 3), 15.0, add_)
+        ts(R("jba", 0, 32), R("ai", 0, 32), 15, and_)
+        lanes(0, R("jba", 0, 16), "PT0", 448, Cp, R("Lab", 0, 16))
+        for h in range(2):
+            mov(YBENG[h], H(Sb, h), IND(H("yy", h, 2048), H("Lab", h, 8)))
+        tt(go, R("ai", 16, 32), R("hxs", 2, 48, 3), ALU.is_lt)
+        if not last:
+            tt(R("gt", 0, 16), go, R("dj", 0, 16), mul_)
+            tt(R(Sb, 368, 384), R("gt", 0, 16), R("jalt", 0, 16), add_)
+            lanes(1, R(Sb, 368, 384), "PT1", 448, sm(48), R(Sb, 352, 368))
+        w = 256 if last else 400
+        send("N", R(Sb, 0, w), [R("Lb%d" % t, 0, w)], ["rB%d" % t], w // 4)
+        lanes(2, R("jba", 16, 32), "PT0", 464, Cp, R("Lab", 16, 32))
+        for h in range(2):
+            act(H("St", 2 * t + h), IND(H("yy", h, 2048), H("Lab", 2 + h, 8)))
+        if last:
+            tt(R("t12", 0, 48), IND(go, Lgo), mj12, mul_)
+            tt(R("mj4", 0, 48), Pinc, lv, sub_)
+            for h in range(2):
+                tt(R("Pfin", h, 48, 2), H("mj4", h, 24), H("t12", h, 24), add_)
+        if not last:
+            pl = R("PQ", 384, 385, 1, 0, 8)
+            mm([(pl, R(Sb, 384 + 8 * h, 392 + 8 * h), R("cb", 12 * 128, 12 * 128 + 1)) for h in range(2)])
+            act(R("cnt", 0, 1, 1, 0, 8), pl)
+            mm([(R("PQ", 392, 393), E8, R("cnt", 0, 1, 1, 0, 8))])
+            cp(R("Ai", 0, 1), R("PQ", 392, 393)); ts(R("Aa", 0, 1), R("Ai", 0, 1), 63, and_)
+            ts(R("cA", 0, 1), R("Aa", 0, 1), cK37, add_)
+            act(R("St", 256 * (3 + t), 256 * (4 + t)), R("Lb%d" % t, 0, 256))
+        else:
+            mm([(blk("PA0", 0, 48), R("Pfin", 0, 48), Iq)])
+            act(blk("Pout", 0, 48), blk("PA0", 0, 48))
+            store("o2", ("yp", None, blk("Pout", 0, 48)), [blk("Pout", 0, 48)], 24)
+            store("o3", ("ym", None, "marks"), [R("St", 1536, 3072)], 24)
+            for s, a, b in (("o4", 0, 512), ("o6", 768, 1280), ("o7", 512, 768)):
+                store(s, ("ys", a, R("St", a, b)), [R("St", a, b)], (b - a) // 4)
+            store("o5", ("ys", 1280, R("Lb2", 0, 256)), [R("Lb2", 0, 256)], 64)
+    return ops
+
+
+def sched(ops, pre, pri, banks):
+    n = len(ops)
+    succ = [[] for _ in range(n)]
+    cnt = [len(p) for p in pre]
+    for i in range(n):
+        for j in pre[i]:
+            succ[j].append(i)
+    qq = [o["q"] for o in ops]
+    cost = [o["cost"] for o in ops]
+    free = dict((q, 0.0) for q in qq)
+    bank = {}
+    fin = [0.0] * n
+    est = [0.0] * n
+    t0 = [0.0] * n
+    ex = [None] * n
+    ready = [i for i in range(n) if cnt[i] == 0]
+    out = []
+    while ready:
+        st = {}
+        a, lim = -1, 1e30
+        for i in ready:
+            s = max(est[i], free[qq[i]])
+            for b in banks[i]:
+                for q, j in bank.get(b, {}).items():
+                    if q != qq[i] and fin[j] + LAT > s:
+                        s = fin[j] + LAT
+            st[i] = s
+            if s + cost[i] < lim:
+                a, lim = i, s + cost[i]
+        i = max([k for k in ready if qq[k] == qq[a] and st[k] < lim + LOOK or k == a],
+                key=lambda k: (pri[k] - WAITW * max(0.0, st[k] - st[a]), -k))
+        ready.remove(i)
+        t0[i] = st[i]
+        if qq[i] != "R":
+            free[qq[i]] = st[i] + cost[i]
+        fin[i] = st[i] + cost[i] + ops[i].get("lat", 0)
+        ex[i] = []
+        for b in banks[i]:
+            ex[i] += [j for q, j in bank.get(b, {}).items() if q != qq[i]]
+            bank.setdefault(b, {})[qq[i]] = i
+        out.append(i)
+        for k in succ[i]:
+            est[k] = max(est[k], fin[i] + pre[k][i])
+            cnt[k] -= 1
+            if cnt[k] == 0:
+                ready.append(k)
+    return out, t0, fin, ex
+
+
+def replay(ops, f, pre, cost, lat):
+    fin = [0.0] * len(ops)
+    free = {}
+    for i in f[0]:
+        q = ops[i]["q"]
+        s = free.get(q, 0.0)
+        for j, x in pre[i].items():
+            s = max(s, fin[j] + (x * lat if x <= LAT else x))
+        for j in f[3][i]:
+            s = max(s, fin[j] + LAT * lat)
+        if q != "R":
+            free[q] = s + cost[i]
+        fin[i] = s + cost[i] + ops[i].get("lat", 0)
+    return max(fin)
+
+
+def order(ops):
+    n = len(ops)
+    hard = [set() for _ in range(n)]
+    seen = {}
+    for o in ops:
+        i = o["n"]
+        for r in o["rd"]:
+            hard[i].update(j for (j, r2, w) in seen.get(r[1], []) if w and clash(r, r2))
+        for r in o["wr"]:
+            hard[i].update(j for (j, r2, w) in seen.get(r[1], []) if clash(r, r2))
+        for r in o["wr"]:
+            l = [e for e in seen.get(r[1], []) if not (r[4] == 1 and r[5] <= e[1][5] and e[1][6] <= r[6] and r[2] <= e[1][2] and e[1][3] <= r[3])]
+            seen[r[1]] = l + [(i, r, True)]
+        for r in o["rd"]:
+            seen.setdefault(r[1], []).append((i, r, False))
+        hard[i].discard(i)
+    pre = []
+    for i in range(n):
+        p = dict((j, LATS if ops[j]["q"] == ops[i]["q"] and "sem" not in ops[j] else LAT) for j in hard[i])
+        pre.append({ops[i]["after"][0]: ops[i]["after"][1]} if "after" in ops[i] else p)
+    post = [dict() for _ in range(n)]
+    for i in range(n):
+        for j in pre[i]:
+            post[j][i] = pre[i][j] + ops[j].get("lat", 0) - ops[i].get("lat", 0)
+    banks = [sorted(set(r[1] for r in o["rd"] + o["wr"] if inps(r))) for o in ops]
+    pri = [0.0] * n
+    for i in range(n - 1, -1, -1):
+        pri[i] = ops[i]["cost"] + ops[i].get("lat", 0) + max([pri[k] + pre[k][i] for k in post[i]] + [0.0])
+    cases = [([o["cost"] for o in build(c[:3])], c[3]) for c in CASES]
+    rng = np.random.default_rng(SEED)
+    fine, wide = [], []
+    for o in ops:
+        r = o["wr"][0] if o["wr"] else o["rd"][0]
+        nm = r[1][:2] if r[1][:2] in ("Cs", "Sb", "Cw", "Lb") else r[1]
+        h = int(2 * r[2] >= SCRATCH[r[1]][1][1]) if nm[0] != "P" else r[2] // 128
+        fine.append((nm, h, o["q"], o["kind"]))
+        wide.append([k for k, s in enumerate(KINS) if nm in s.split()] + [-1])
+    wide = [(w[0], f[1] if f[0][0] != "P" else 0) for w, f in zip(wide, fine)]
+    base = np.array(pri)
+    low = max(sched(ops, pre, pri, banks)[2])
+    for tags, rounds in ((wide, TRY[0]), (fine, TRY[1])):
+        names = sorted(set(tags))
+        tg = np.array([names.index(x) for x in tags])
+        for it in range(rounds):
+            off = np.zeros(len(names))
+            off[rng.integers(0, len(names), int(rng.integers(1, 4)))] = rng.normal(0.0, 2500.0)
+            v = max(sched(ops, pre, list(base + off[tg]), banks)[2])
+            if v <= low:
+                low, base = v, base + off[tg]
+    pri = list(base)
+    best = None
+    for it in range(ROUNDS):
+        f = sched(ops, pre, pri, banks)
+        if best is None or max(f[2]) < 1.02 * max(best[2]):
+            v = max(f[2]) + sum(replay(ops, f, pre, c, lat) for c, lat in cases)
+            if best is None or v < best[4]:
+                best = f + (v,)
+        jit = JIT * float(rng.random()) ** 2
+        if it % 2:
+            pri = [-x + float(z) * jit for x, z in zip(best[1], rng.random(n))]
+        else:
+            b = sched(ops, post, [x + float(z) * jit for x, z in zip(best[2], rng.random(n))], banks)
+            pri = [x + float(z) * jit for x, z in zip(b[2], rng.random(n))]
+    idx, t0, fin, ex = best[:4]
+    TIMES[:] = [max(fin)] + [replay(ops, best, pre, c, lat) for c, lat in cases]
+    out = [ops[i] for i in idx]
+    for o in out:
+        o["t0"], o["t1"] = t0[o["n"]], fin[o["n"]]
+        o["w"] = set() if o["q"] == "R" else hard[o["n"]] | set(ex[o["n"]])
+    pos = {}
+    for p, o in enumerate(out):
+        pos[o["n"]] = p
+    got = {}
+    for o in out:
+        need = {}
+        for j in o["w"]:
+            s = ops[j].get("sem") or "c" + ops[j]["q"]
+            if s not in need or pos[j] > pos[need[s]]:
+                need[s] = j
+        o["need"] = []
+        for s, j in sorted(need.items()):
+            if got.get((o["q"], s), -1) < pos[j]:
+                got[(o["q"], s)] = pos[j]
+                o["need"].append((s, j))
+                ops[j]["inc"] = True
+    tick = {}
+    for o in out:
+        if o.get("inc") and "sem" not in o:
+            tick[o["q"]] = tick.get(o["q"], 0) + 1
+            o["val"] = tick[o["q"]]
+    return out
+
+
+PLAN = []
+
+
+def bits(l):
+    m = 0
+    for e in l:
+        m |= 1 << e
+    return m
+
+
+def goal_engines(T, topo, r):
+    n = len(T.cores)
+    e1 = topo.engines(T.cores[r], T.cores[(r + 1) % n])
+    e2 = topo.engines(T.cores[r], T.cores[(r + 2) % n])
+    only1 = [e for e in e1 if e not in e2]
+    if only1:
+        return only1, e2
+    both = [e for e in e1 if e in e2]
+    return both[:len(both) // 2], both[len(both) // 2:]
+
+
+def rank_program(g, core, T, topo):
+    from_rank = T.rank_of(core)
+    if from_rank is None:
+        return
+    r = from_rank
+    n = len(T.cores)
+    if not PLAN:
+        ops = build()
+        PLAN.append(ops)
+        PLAN.append(order(ops))
+    ops, out = PLAN
+    Q = {"V": g.vector, "S": g.scalar, "P": g.tensor, "G": g, "Y": g.sync}
+    nxt, nx2, prv = T.cores[(r + 1) % n], T.cores[(r + 2) % n], T.cores[(r - 1) % n]
+    arr = {"rG1": len(goal_engines(T, topo, (r - 1) % n)[0]), "rG2": len(goal_engines(T, topo, (r - 2) % n)[1])}
+    nin = len(topo.engines(prv, core))
+    lsum = 0
+    for o in out:
+        if o["q"] == "R":
+            continue
+        q = Q[o["q"]]
+        for s, j in o["need"]:
+            p = ops[j]
+            v = p["val"] if "sem" not in p else (arr.get(s, nin) if p["q"] == "R" else 16)
+            q.wait_ge(T.sem[s], v)
+        k, a = o["kind"], o["args"]
+        if k == "cp":
+            ins = q.tensor_copy(ap(T, a[0]), ap(T, a[1]))
+        elif k == "tt":
+            ins = q.tensor_tensor(ap(T, a[0]), ap(T, a[1]), ap(T, a[2]), a[3])
+        elif k == "ts":
+            if a[5] is None:
+                ins = q.tensor_scalar(ap(T, a[0]), ap(T, a[1]), ap(T, a[2]), None, a[4])
+            else:
+                ins = q.tensor_scalar(ap(T, a[0]), ap(T, a[1]), ap(T, a[2]), ap(T, a[3]), a[4], a[5])
+        elif k == "scan":
+            ins = q.tensor_tensor_scan(ap(T, a[0]), ap(T, a[1]), ap(T, a[2]), 0.0, a[3], a[4])
+        elif k == "ms":
+            ins = q.memset(ap(T, a[0]), a[1])
+        elif k == "act":
+            ins = q.activation(ap(T, a[0]), ap(T, a[1]), a[2], bias=ap(T, a[3]), scale=ap(T, a[4]))
+        elif k == "mm":
+            m = len(a[0]) if a[1] is True else max(1, int(a[1]))
+            for i, (oo, l, rr) in enumerate(a[0]):
+                ins = q.matmul(ap(T, oo), ap(T, l), ap(T, rr), i % m == 0, i % m == m - 1)
+        elif k == "iota":
+            if dty(a[0]) == I32:
+                ins = q.iota(ap(T, a[0]), a[1], a[2], a[3])
+            else:
+                ins = q.iota(ap(T, a[0]), a[1], a[2], a[3], allow_small_or_imprecise_dtypes=True)
+        elif k == "asel":
+            ins = q.affine_select(ap(T, a[0]), ap(T, a[1]), a[2], a[5], a[6], a[3], a[4])
+        elif k == "load":
+            q.dma_start(ap(T, a[1]), T[a[0]][:]).then_inc(T.sem[o["sem"]], 16)
+            continue
+        elif k == "store":
+            name, c, src = a[1]
+            if src == "marks":
+                q.dma_start(T[name][:], T["St"][15:128:16, 1536:3072]).then_inc(T.sem[o["sem"]], 16)
+            elif c is None:
+                q.dma_start(T[name][:], ap(T, src)).then_inc(T.sem[o["sem"]], 16)
+            else:
+                q.dma_start(T[name][:, c:c + nel(src)], ap(T, src)).then_inc(T.sem[o["sem"]], 16)
+            continue
+        else:
+            if a[0] == "G":
+                e1, e2 = goal_engines(T, topo, r)
+                tr = []
+                for dst, d, s, e in ((nxt, a[2][0], a[3][0], e1), (nx2, a[2][1], a[3][1], e2)):
+                    rid, pid, _ = topo.addr(dst)
+                    tr.append(RemoteDMATransfer(dst_ids=[DstId(rid=rid, pnc=pid)], dma_engine_mask=bits(e),
+                                                remote_sem=T.sem[s], src=ap(T, a[1]), dst=ap(T, d)))
+                    lsum += len(e)
+                q.remote_dma_fused(tr, local_sem=T.sem["lsem"])
+            else:
+                rid, pid, _ = topo.addr(nxt)
+                q.remote_dma(ap(T, a[2][0]), ap(T, a[1]), T.sem[a[3][0]], T.sem["lsem"], pid, rid, topo.mask(core, nxt))
+                lsum += len(topo.engines(core, nxt))
+            continue
+        if o.get("inc"):
+            ins.then_inc(T.sem["c" + o["q"]], 1)
+    g.wait_ge(T.sem["lsem"], lsum)
+    for s in STORES:
+        g.sync.wait_ge(T.sem[s], 16)

@@ -16,7 +16,7 @@ def _sb(name, n, dt, where="sbuf"):
 
 
 for _n, _c, _d in (
-    ("St", 3088, BF), ("Ef", 4096, BF), ("Ot", 256, BF), ("Qn", 768, I32), ("Qk", 768, I32), ("Tu", 768, I32),
+    ("St", 3088, BF), ("Ef", 4720, BF), ("Ot", 256, BF), ("Qn", 768, I32), ("Qk", 768, I32), ("Tu", 768, I32),
     ("Tub", 768, BF), ("Rm", 16, BF), ("Gl0", 256, BF), ("Gl1", 256, BF), ("Gl2", 256, BF),
     ("Cw0", 768, I32), ("Cw1", 768, I32), ("Cw2", 768, I32), ("Cs0", 768, I32), ("Cs1", 768, I32), ("Cf", 768, F32),
     ("C1", 768, I32), ("C2", 768, I32), ("K16", 768, F16), ("wsc", 768, F32),
@@ -27,7 +27,7 @@ for _n, _c, _d in (
     ("dj", 16, F32), ("LJ", 16, U16), ("R0j", 256, BF), ("t12", 48, BF), ("Pfin", 48, BF), ("Pout", 768, F32),
     ("q32", 256, I32), ("q16", 256, U16), ("qf", 256, F16), ("key", 256, F16), ("msc", 256, F32),
     ("mi", 16, I32), ("k0", 16, I32), ("Dk", 256, BF), ("Lk", 16, U16), ("xx", 256, BF), ("xm", 256, BF),
-    ("uvi", 16, I32), ("uva", 16, I32), ("Du", 256, BF), ("Lo", 16, U16), ("u32", 256, F32), ("tO", 256, F32),
+    ("uvi", 16, I32), ("uva", 16, I32), ("Du", 256, BF), ("Lo", 16, U16), ("u32", 256, F32), ("tO", 256, I32),
     ("nr", 256, I32), ("na", 256, I32), ("n16", 256, U16), ("dx", 256, BF), ("ix", 256, BF),
     ("hxm", 48, F32), ("hxs", 48, F32), ("hsc", 768, F32), ("t48", 96, F32), ("ss", 96, F32), ("ai", 32, I32),
     ("jba", 64, I32), ("gt", 16, F32), ("Dj", 768, BF), ("Lab", 32, U16), ("ya", 256, BF),
@@ -41,20 +41,22 @@ for _n, _c, _d in (
 for _n in ("PA0", "PA1", "PB0", "PB1", "PH", "PT0", "PT1", "PQ"):
     _sb(_n, 512, F32, "psum")
 
-LOADS = ("tu", "qn", "qk", "st0", "gl", "rm", "ot", "ef")
+LOADS = ("tu", "qn", "qk", "st0", "gl", "rm", "ot", "ef", "ef2")
 STORES = ("o1", "o2", "o3", "o4", "o5", "o6", "o7")
 SEMAPHORES = (["cV", "cS", "cP", "cG", "lsem", "rG1", "rG2", "rC00", "rC01", "rC10", "rC11", "rB0", "rB1", "rB2"]
               + ["l" + n for n in LOADS] + list(STORES))
 
-G1ENG = ("VSSS", "SSSS")
+G1ENG = ("VVSS", "SSSS")
 G2ENG = ("SSSS", "SSSS")
-INDENG = ("SSSS", "SSVV")
+INDENG = ("SSSS", "SVVV")
 ADDENG = ("VVVV", "VVVV")
 YBENG = "SS"
 VC = 1.0
 BASE = (0.52, 1.56, 3.8)
-CASES = ((0.8, 1.56, 3.8, 1.0), (0.52, 1.1, 2.0, 1.0), (0.52, 2.0, 5.5, 1.0), (0.52, 1.56, 3.8, 2.0))
-LAT, LATS = 100.0, 60.0
+CASES = ((0.8, 1.56, 3.8, 1.0), (0.52, 1.1, 2.0, 1.0), (0.52, 2.0, 5.5, 1.0), (0.52, 1.56, 3.8, 0.55), (0.52, 1.3, 3.0, 1.6))
+LAT, LATS = 180.0, 110.0
+BACK = 3
+CFIRST = True
 SEED, ROUNDS, JIT, WAITW, LOOK = 0, 60, 3000.0, 1.0, 0.0
 TRY = (400, 1000)
 KINS = ("q32 q16 sg", "key msc mi k0 Dk Lk xx uvi uva Du Lo u32 tO nr na n16", "smx", "eg", "yy dd PA0 PA1 PB0 PB1", "ind",
@@ -175,7 +177,7 @@ def build(case=None):
         add("Y", "store", (sem, fn), rd, [], 60, sem=sem, lat=1800 + kb * 5.0)
 
     def send(kind, src, dst, sem, kb):
-        s = add("G", "send", (kind, src, dst, sem), [src], [], 500 + kb * 14.0)
+        s = add("G", "send", (kind, src, dst, sem), [src], [R("ya", 0, 1)] if CFIRST else [], 500 + kb * 14.0)
         for d, sm in zip(dst, sem):
             add("R", "recv", (kind,), [], [d], 0, sem=sm, lat=0, after=(s["n"], 1500.0))
 
@@ -190,6 +192,7 @@ def build(case=None):
     load("Y", "rm", R("Rm", 0, 1), 800)
     load("Y", "ot", R("Ot", 0, 256), 800)
     load("Y", "ef", R("Ef", 0, 4096), 800, [R("Qn", 0, 768)])
+    add("Y", "load", ("ef", R("Ef", 4096, 4720)), [R("Qn", 0, 768)], [R("Ef", 4096, 4720)], 60, sem="lef2", lat=5800)
     send("G", R("Gl0", 0, 256), [R("Gl1", 0, 256), R("Gl2", 0, 256)], ["rG1", "rG2"], 128)
 
     def col(j):
@@ -207,7 +210,7 @@ def build(case=None):
     ts(cN16, cN15, 16.0, mul_); ts(cN4k, cN15, 4096.0, mul_); ts(cN64k, cN15, 65536.0, mul_)
     ts(cSg, cN15, 2048.0, mul_, -1920.0, add_)
     ts(cF64k, cF15, 65536.0, mul_)
-    ts(cK37, cB, 37.0, mul_, -0.484375, add_)
+    ts(cK37, cB, 37.0, mul_)
 
     def blk(buf, j, p1=128):
         return R(buf, 128 * j, 128 * j + 128, 1, 0, p1)
@@ -369,11 +372,10 @@ def build(case=None):
             mm([(pl, H("Du", h), C8)])
             cp(H("Lo", h, 8), pl)
             tt(H("tO", h), IND(R("Ot", 0, 256), H("Lo", h, 8)), H("u32", h), mul_)
-            ts(H("nr", h), H("tO", h), 1.0 / 32, mul_, cA, add_)
-            ts(H("na", h), H("nr", h), 4095, and_)
-            cp(H("n16", h), H("na", h))
+            ts(H("na", h), H("tO", h), 5, ALU.arith_shift_right, 4095, and_)
+            ts(H("n16", h), H("na", h), cA, add_)
             for c in range(4):
-                mov(G2ENG[h][c], H("eg", 4 * h + c, 512), IND(R("Ef", 0, 4096), H("n16", 4 * h + c, 32)))
+                mov(G2ENG[h][c], H("eg", 4 * h + c, 512), IND(R("Ef", 0, 4720), H("n16", 4 * h + c, 32)))
             mm([(blk("PH", h), I0, H("xx", h)), (blk("PH", h), nI, H(Gl, h))])
             act(H("dx", h), blk("PH", h), AF.Abs)
             ts(H("ix", h), H("dx", h), 4.0, ALU.is_gt)
@@ -652,23 +654,34 @@ def order(ops):
     out = [ops[i] for i in idx]
     for o in out:
         o["t0"], o["t1"] = t0[o["n"]], fin[o["n"]]
-        o["w"] = set() if o["q"] == "R" else hard[o["n"]] | set(ex[o["n"]])
+        o["w"] = set() if o["q"] == "R" else set(j for j in hard[o["n"]] | set(ex[o["n"]]) if ops[j]["kind"] != "send")
     pos = {}
     for p, o in enumerate(out):
         pos[o["n"]] = p
     got = {}
+    past = {}
     for o in out:
         need = {}
         for j in o["w"]:
             s = ops[j].get("sem") or "c" + ops[j]["q"]
             if s not in need or pos[j] > pos[need[s]]:
                 need[s] = j
+        mine = got.setdefault(o["q"], {})
+        own = past.setdefault(o["q"], [])
+        s = "c" + o["q"]
+        if s in need and len(own) >= BACK and pos[need[s]] < pos[own[-BACK]]:
+            need[s] = own[-BACK]
         o["need"] = []
-        for s, j in sorted(need.items()):
-            if got.get((o["q"], s), -1) < pos[j]:
-                got[(o["q"], s)] = pos[j]
+        for s, j in sorted(need.items(), key=lambda e: -pos[e[1]]):
+            if mine.get(s, -1) < pos[j]:
+                mine[s] = pos[j]
+                for s2, p2 in ops[j]["know"].items():
+                    mine[s2] = max(mine.get(s2, -1), p2)
                 o["need"].append((s, j))
                 ops[j]["inc"] = True
+        o["know"] = dict(mine) if o["q"] != "R" else {}
+        if "sem" not in o and o["kind"] != "send":
+            own.append(o["n"])
     tick = {}
     for o in out:
         if o.get("inc") and "sem" not in o:
@@ -750,7 +763,8 @@ def rank_program(g, core, T, topo):
         elif k == "asel":
             ins = q.affine_select(ap(T, a[0]), ap(T, a[1]), a[2], a[5], a[6], a[3], a[4])
         elif k == "load":
-            q.dma_start(ap(T, a[1]), T[a[0]][:]).then_inc(T.sem[o["sem"]], 16)
+            src = T[a[0]][:, 0:nel(a[1])] if o["sem"] == "lef2" else T[a[0]][:]
+            q.dma_start(ap(T, a[1]), src).then_inc(T.sem[o["sem"]], 16)
             continue
         elif k == "store":
             name, c, src = a[1]

@@ -27,7 +27,7 @@ for _n, _c, _d in (
     ("dj", 16, F32), ("LJ", 16, U16), ("R0j", 256, BF), ("t12", 48, BF), ("Pfin", 48, BF), ("Pout", 768, F32),
     ("q32", 256, I32), ("q16", 256, U16), ("qf", 256, F16), ("key", 256, F16), ("msc", 256, F32),
     ("mi", 16, I32), ("k0", 16, I32), ("Dk", 256, BF), ("Lk", 16, U16), ("xx", 256, BF), ("xm", 256, BF),
-    ("uvi", 16, I32), ("uva", 16, I32), ("Du", 256, BF), ("Lo", 16, U16), ("u32", 256, F32), ("tO", 256, I32),
+    ("uvi", 16, I32), ("uva", 16, I32), ("Du", 288, BF), ("vl", 16, F32), ("Lo", 16, U16), ("u32", 256, F32), ("tO", 256, I32),
     ("nr", 256, I32), ("na", 256, I32), ("n16", 256, U16), ("dx", 256, BF), ("ix", 256, BF),
     ("hxm", 48, F32), ("hxs", 48, F32), ("hsc", 768, F32), ("t48", 96, F32), ("ss", 96, F32), ("ai", 32, I32),
     ("jba", 64, I32), ("gt", 16, F32), ("Dj", 768, BF), ("Lab", 32, U16), ("ya", 256, BF),
@@ -48,7 +48,7 @@ SEMAPHORES = (["cV", "cS", "cP", "cG", "lsem", "rG1", "rG2", "rC00", "rC01", "rC
 
 G1ENG = ("VVSS", "SSSS")
 G2ENG = ("SSSS", "SSSS")
-INDENG = ("SSSS", "SVVV")
+INDENG = ("SSSV", "SVVV")
 ADDENG = ("VVVV", "VVVV")
 YBENG = "SS"
 VC = 1.0
@@ -56,12 +56,16 @@ BASE = (0.52, 1.56, 3.8)
 CASES = ((0.8, 1.56, 3.8, 1.0), (0.52, 1.1, 2.0, 1.0), (0.52, 2.0, 5.5, 1.0), (0.52, 1.56, 3.8, 0.55), (0.52, 1.3, 3.0, 1.6))
 LAT, LATS = 180.0, 110.0
 BACK = 3
+SWAPS, HEAT, MIX = 26000, 600.0, (0, 1)
 CFIRST = True
-SEED, ROUNDS, JIT, WAITW, LOOK = 0, 60, 3000.0, 1.0, 0.0
-TRY = (400, 1000)
+DIRECT = False
+EARLY, XENG, UENG = -1, "VS", "SS"
+SEED, ROUNDS, JIT, WAITW, LOOK = 2, 20, 3000.0, 1.0, 0.0
+TRY = (300, 700)
 KINS = ("q32 q16 sg", "key msc mi k0 Dk Lk xx uvi uva Du Lo u32 tO nr na n16", "smx", "eg", "yy dd PA0 PA1 PB0 PB1", "ind",
         "dx ix hxm hxs", "xm kT R0k xsc Dx RT eq Lx", "St", "R0j mT qf C1 K16 wsc wi wa wT R0w C2 Cs Cf PQ",
         "hsc t48 ss ai jba gt Dj Lab Sb", "PT0", "PT1", "PH", "t12 P40 mj mm mj4 pm2 ji2 jalt dj")
+LEAD = [(0.0, 0.0)] * 15
 TIMES = []
 
 
@@ -186,13 +190,13 @@ def build(case=None):
 
     load("Y", "tu", R("Tu", 0, 128, 1, 0, 48), 24)
     load("Y", "qn", R("Qn", 0, 768), 400)
-    load("S", "st0", R("St", 0, 3072), 800)
-    load("Y", "qk", R("Qk", 0, 768), 800)
-    load("Y", "gl", R("Gl0", 0, 256), 800)
-    load("Y", "rm", R("Rm", 0, 1), 800)
-    load("Y", "ot", R("Ot", 0, 256), 800)
-    load("Y", "ef", R("Ef", 0, 4096), 800, [R("Qn", 0, 768)])
-    add("Y", "load", ("ef", R("Ef", 4096, 4720)), [R("Qn", 0, 768)], [R("Ef", 4096, 4720)], 60, sem="lef2", lat=5800)
+    load("S", "st0", R("St", 0, 3072), 600)
+    load("Y", "qk", R("Qk", 0, 768), 300, [R("Qn", 0, 768)])
+    load("Y", "gl", R("Gl0", 0, 256), 300, [R("Qn", 0, 768)])
+    load("Y", "rm", R("Rm", 0, 1), 300, [R("Qn", 0, 768)])
+    load("Y", "ot", R("Ot", 0, 256), 300, [R("Qn", 0, 768)])
+    load("Y", "ef", R("Ef", 0, 4096), 500, [R("St", 0, 3072)])
+    add("Y", "load", ("ef", R("Ef", 4096, 4720)), [R("St", 0, 3072)], [R("Ef", 4096, 4720)], 60, sem="lef2", lat=4300)
     send("G", R("Gl0", 0, 256), [R("Gl1", 0, 256), R("Gl2", 0, 256)], ["rG1", "rG2"], 128)
 
     def col(j):
@@ -205,12 +209,10 @@ def build(case=None):
     ts(cN15, cB, 15.0, ALU.is_lt); ts(cF15, cB, 15.0, eq_)
     ts(cJ, cB, 3072.0, add_)
     ts(col(20), cB, 2.0, mul_, 1.0, add_); ts(cU, col(20), cN15, mul_)
-    ts(c16P, cP, 16.0, mul_); ts(c16A, cAa, 16.0, mul_)
-    ts(cM16, R("Rm", 0, 1), 16.0, mul_); ts(cM4k, R("Rm", 0, 1), 4096.0, mul_)
-    ts(cN16, cN15, 16.0, mul_); ts(cN4k, cN15, 4096.0, mul_); ts(cN64k, cN15, 65536.0, mul_)
-    ts(cSg, cN15, 2048.0, mul_, -1920.0, add_)
-    ts(cF64k, cF15, 65536.0, mul_)
-    ts(cK37, cB, 37.0, mul_)
+    for d, a, c in ((c16P, cP, 16.0), (c16A, cAa, 16.0), (cM16, R("Rm", 0, 1), 16.0), (cM4k, R("Rm", 0, 1), 4096.0),
+                    (cN16, cN15, 16.0), (cN4k, cN15, 4096.0), (cN64k, cN15, 65536.0), (cF64k, cF15, 65536.0), (cK37, cB, 37.0)):
+        act(d, a, scale=c)
+    act(cSg, cN15, bias=-1920.0, scale=2048.0)
 
     def blk(buf, j, p1=128):
         return R(buf, 128 * j, 128 * j + 128, 1, 0, p1)
@@ -234,13 +236,16 @@ def build(case=None):
     C128, C256, Wu8, Wv8, C16p, Cp = sm(0), sm(8), sm(16), sm(24), sm(32), sm(56)
     Cjb = sm(48, 16)
     Wmk = sm(64, 16)
-    ts(C128, C8, 128.0, mul_); ts(C256, C8, 256.0, mul_); ts(Wu8, C8, cU, mul_); ts(Wv8, C8, cN15, mul_)
-    ts(C16p, C8, c16P, mul_); ts(sm(48), C8, c16A, mul_); ts(Cp, C8, cP, mul_)
-    ts(sm(64), C8, cF64k, mul_); ts(sm(72), C8, cF15, mul_)
+    for d, c in ((C256, 256.0), (Cp, cP), (sm(64), cF64k), (sm(72), cF15), (C16p, c16P), (Wu8, cU), (Wv8, cN15),
+                 (C128, 128.0), (sm(48), c16A)):
+        act(d, C8, scale=c)
+    if DIRECT:
+        ms(R("Du", 0, 288), 0.0)
+        ts(R("Du", 15, 143, 16), C8, cU, mul_); ts(R("Du", 159, 287, 16), C8, cN15, mul_)
     Wd, Wi, Ws = sm(80, 24), sm(104, 24), sm(128, 24)
     ms(sm(80, 72), 0.0)
-    ts(sm(80, 8, 3), C8, cN16, mul_); ts(sm(82, 8, 3), C8, cM16, mul_)
-    ts(sm(105, 8, 3), C8, cN16, mul_, 16.0, mul_); ts(sm(129, 8, 3), C8, cSg, mul_)
+    act(sm(80, 8, 3), C8, scale=cN16); act(sm(82, 8, 3), C8, scale=cM16)
+    act(sm(105, 8, 3), sm(80, 8, 3), scale=16.0); act(sm(129, 8, 3), C8, scale=cSg)
     I4 = R("cb", o + 152, o + 200, 1, 0, 48)
     ms(R("Tub", 128, 176, 1, 0, 48), 4.0)
     asel(I4, R("Tub", 128, 176, 1, 0, 48), [[-1, 2], [-6, 8], [-2, 3]], 0, 1)
@@ -253,8 +258,9 @@ def build(case=None):
     cp(blk("ch", 4, 1), blk("cb", 12, 1))
     C8h, C4kh = R("ch", 640, 648), R("ch", 648, 656)
     cp(C8h, C8); ts(C4kh, C8, 4096.0, mul_)
-    iota(R("tf", 0, 768, 1, 0, 1), [[1, 768]], 0, 0)
-    cp(R("ch", 768, 1536, 1, 0, 1), R("tf", 0, 768, 1, 0, 1))
+    iota(blk("tb", 0, 1), [[1, 128]], 0, 0)
+    for c in range(6):
+        ts(blk("ch", 6 + c, 1), blk("tb", 0, 1), 128.0 * c, add_)
     Ej = [blk("ce", l, 24) for l in range(3)]
     Ep = [blk("ce", 3 + l, 49) for l in range(3)]
     En = [blk("ce", 6 + l, 49) for l in range(3)]
@@ -361,16 +367,31 @@ def build(case=None):
             pl = R(PT[h], 392, 400)
             mm([(pl, M16, C16p), (pl, H("Dk", h), C8)])
             cp(H("Lk", h, 8), pl)
-            act(H("xx", h), IND(H("sg", h, 2048), H("Lk", h, 8)))
+            if XENG[h] == "S":
+                act(H("xx", h), IND(H("sg", h, 2048), H("Lk", h, 8)), bias=cF15, scale=cN15)
+            else:
+                ts(H("xx", h), IND(H("sg", h, 2048), H("Lk", h, 8)), cF15, max_)
             pl = R(PT[h], 400, 408)
-            mm([(pl, H("smx", h, 2048, 16, 15), Wv8), (pl, H("xx", h), Wu8)])
+            if DIRECT:
+                pv = R(PT[h], 408, 416)
+                mm([(pv, R("Du", 159 - b, 287 - b), H("smx", h, 2048, 256, 16 * b + 15)) for b in range(16)])
+                act(H("vl", h, 8), pv)
+                mm([(pl, R("Du", 15 - b, 143 - b), H("xx", h, 128, 16, b)) for b in range(16)])
+                tt(H("uvi", h, 8), pl, H("vl", h, 8), add_); ts(H("uva", h, 8), H("uvi", h, 8), 255, and_)
+                cp(H("Lo", h, 8), H("uva", h, 8))
+            else:
+                mm([(pl, H("smx", h, 2048, 16, 15), Wv8), (pl, H("xx", h), Wu8)])
             mm([(R(PT[h], 256, 384), Wu, H("xx", h))])
-            act(H("u32", h), R(PT[h], 256, 384), bias=32.0)
-            cp(H("uvi", h, 8), pl); ts(H("uva", h, 8), H("uvi", h, 8), 255, and_)
-            tt(H("Du", h), IND(H("uva", h, 8), Lb8), M16, mul_)
-            pl = R(PT[h], 408, 416)
-            mm([(pl, H("Du", h), C8)])
-            cp(H("Lo", h, 8), pl)
+            if UENG[h] == "S":
+                act(H("u32", h), R(PT[h], 256, 384), bias=32.0)
+            else:
+                ts(H("u32", h), R(PT[h], 256, 384), 32.0, add_)
+            if not DIRECT:
+                cp(H("uvi", h, 8), pl); ts(H("uva", h, 8), H("uvi", h, 8), 255, and_)
+                tt(H("Du", h), IND(H("uva", h, 8), Lb8), M16, mul_)
+                pl = R(PT[h], 408, 416)
+                mm([(pl, H("Du", h), C8)])
+                cp(H("Lo", h, 8), pl)
             tt(H("tO", h), IND(R("Ot", 0, 256), H("Lo", h, 8)), H("u32", h), mul_)
             ts(H("na", h), H("tO", h), 5, ALU.arith_shift_right, 4095, and_)
             ts(H("n16", h), H("na", h), cA, add_)
@@ -379,12 +400,11 @@ def build(case=None):
             mm([(blk("PH", h), I0, H("xx", h)), (blk("PH", h), nI, H(Gl, h))])
             act(H("dx", h), blk("PH", h), AF.Abs)
             ts(H("ix", h), H("dx", h), 4.0, ALU.is_gt)
-            pl = R("PQ", 416 + 24 * h, 440 + 24 * h)
+            pl = R("PT1", 464 + 24 * h, 488 + 24 * h)
             mm([(pl, H("dx", h), Wd), (pl, H("ix", h), Wi)])
             ts(H("qf", h), H("q16", h), -1536.0, add_)
-        tt(R("hxm", 0, 48), R("PQ", 416, 464), R("mj", 0, 48), mul_)
+        tt(R("hxm", 0, 48), R("PT1", 464, 512), R("mj", 0, 48), mul_)
         scan(R("hxs", 0, 48), R("d0", 1536, 1584), R("hxm", 0, 48), mul_, add_)
-        act(R("xm", 0, 256), R("xx", 0, 256), bias=cF15, scale=cN15)
         tt(R("kT", 1, 17), R("k0", 0, 16), R("k0", 0, 16), mul_)
         cp(R("kT", 17, 33), R("k0", 0, 16))
         mm([(blk("PH", 2, 33), R("kT", 0, 33), Ib)])
@@ -400,9 +420,9 @@ def build(case=None):
                                           (R("PH", 256 + 8 * h, 264 + 8 * h), H("eq", h), C4kh))], 2)
         ts(R("Lx", 0, 32, 2), R("PH", 256, 272), 1536.0, add_, cJ, min_)
         for c in range(16):
-            cp(IND(R("St", 0, 3088), R("Lx", 2 * c, 2 * c + 1)), H("xm", c, 16))
+            cp(IND(R("St", 0, 3088), R("Lx", 2 * c, 2 * c + 1)), H("xx", c, 16))
         for h in range(2):
-            PQ = "PA0" if h and "P" not in ADDENG[0] + ADDENG[1] else "PQ"
+            PQ = "PA0" if h else "PQ"
             pq = R(PQ, 0, 384)
             if t == 0:
                 for l in range(3):
@@ -444,15 +464,15 @@ def build(case=None):
         if last:
             store("o1", ("yq", None, R("Cf", 0, 768)), [R("Cf", 0, 768)], 400)
         for h in range(2):
-            vadd = "V" in ADDENG[0] + ADDENG[1]
+            xp = blk("PA1", h) if "P" not in ADDENG[0] + ADDENG[1] else blk("PA0" if h else "PQ", 3)
             if "V" in ADDENG[h]:
-                mm([(blk("PA1", h), I0, H("xx", h))])
+                mm([(xp, I0, H("xx", h))])
             for b in range(4):
-                pa, pb = "PA%d" % (0 if vadd else b % 2), "PB%d" % (b % 2)
+                pa, pb = "PA1", "PB%d" % (b % 2)
                 yb, db, ib = H("yy", 4 * h + b, 512), H("dd", 4 * h + b, 512), H("ind", 4 * h + b, 512)
                 if ADDENG[h][b] == "V":
                     for k in range(4 * b, 4 * b + 4):
-                        tt(H("ind", 16 * h + k), H("eg", h, 2048, 16, k), blk("PA1", h), add_)
+                        tt(H("ind", 16 * h + k), H("eg", h, 2048, 16, k), xp, add_)
                     ts(yb, ib, 0.0, max_, 63.0, min_)
                 else:
                     lst = []
@@ -472,6 +492,8 @@ def build(case=None):
                     lst += [(pl, H("dd", 16 * h + k), Wd), (pl, H("ind", 16 * h + k), Wi if INDENG[h][b] == "V" else Ws)]
                 mm(lst, 2)
             scan(H("hsc", h, 384), dH, R(PT[h], 0, 384), add_, min_)
+            if h == EARLY:
+                ops[-1]["rd"].append(R("St", 3072, 3088))
 
         def lanes(d, win, bank, a, c, out):
             tt(H("Dj", d, 256), IND(win, Lb16), M2, mul_)
@@ -503,11 +525,11 @@ def build(case=None):
             for h in range(2):
                 tt(R("Pfin", h, 48, 2), H("mj4", h, 24), H("t12", h, 24), add_)
         if not last:
-            pl = R("PQ", 384, 385, 1, 0, 8)
+            pl = R("PT0", 416, 417, 1, 0, 8)
             mm([(pl, R(Sb, 384 + 8 * h, 392 + 8 * h), R("cb", 12 * 128, 12 * 128 + 1)) for h in range(2)])
             act(R("cnt", 0, 1, 1, 0, 8), pl)
-            mm([(R("PQ", 392, 393), E8, R("cnt", 0, 1, 1, 0, 8))])
-            cp(R("Ai", 0, 1), R("PQ", 392, 393)); ts(R("Aa", 0, 1), R("Ai", 0, 1), 63, and_)
+            mm([(R("PT0", 424, 425), E8, R("cnt", 0, 1, 1, 0, 8))])
+            cp(R("Ai", 0, 1), R("PT0", 424, 425)); ts(R("Aa", 0, 1), R("Ai", 0, 1), 63, and_)
             ts(R("cA", 0, 1), R("Aa", 0, 1), cK37, add_)
             act(R("St", 256 * (3 + t), 256 * (4 + t)), R("Lb%d" % t, 0, 256))
         else:
@@ -586,6 +608,96 @@ def replay(ops, f, pre, cost, lat):
     return max(fin)
 
 
+def polish(ops, idx, pre, post, banks, cases, rng):
+    n = len(ops)
+    qn = [" VSPGY".find(o["q"]) for o in ops]
+    lat = [o.get("lat", 0) for o in ops]
+    names = sorted(set(b for l in banks for b in l))
+    bk = [[names.index(b) for b in l] for l in banks]
+    sets = [([o["cost"] for o in ops], 1.0)] + [cases[k] for k in MIX]
+    pl = [[[(j, x * f if x <= LAT else x) for j, x in pre[i].items()] for i in range(n)] for c, f in sets]
+
+    def run(idx, k):
+        cost, w, p = sets[k][0], LAT * sets[k][1], pl[k]
+        fin = [0.0] * n
+        why = [-1] * n
+        free = [0.0] * 6
+        who = [-1] * 6
+        bank = [[-1] * 6 for _ in names]
+        for i in idx:
+            q = qn[i]
+            s, y = (free[q], -2 - who[q]) if q > 0 else (0.0, -1)
+            for j, x in p[i]:
+                if fin[j] + x > s:
+                    s, y = fin[j] + x, j
+            for b in bk[i]:
+                l = bank[b]
+                for j in l:
+                    if j >= 0 and qn[j] != q and fin[j] + w > s:
+                        s, y = fin[j] + w, -2 - j
+                l[q] = i
+            if q > 0:
+                free[q], who[q] = s + cost[i], i
+            fin[i] = s + cost[i] + lat[i]
+            why[i] = y
+        return fin, why
+
+    def total(idx):
+        r = [run(idx, k) for k in range(len(sets))]
+        return sum(max(x[0]) for x in r), r
+
+    cur, res = total(idx)
+    low, keep = cur, idx
+    pairs = []
+    for it in range(SWAPS):
+        if not pairs:
+            fin, why = res[int(rng.integers(0, len(sets)))]
+            i = max(range(n), key=lambda k: fin[k])
+            while why[i] != -1:
+                j = why[i] if why[i] >= 0 else -2 - why[i]
+                if why[i] < -1 and j not in pre[i]:
+                    pairs.append((j, i))
+                i = j
+            pos = [0] * n
+            for p, k in enumerate(idx):
+                pos[k] = p
+            if not pairs:
+                break
+        j, i = pairs.pop(int(rng.integers(0, len(pairs))))
+        a, b = pos[j], pos[i]
+        mid = idx[a:b + 1]
+        if rng.random() < 0.5:
+            mv = {i}
+            for k in reversed(mid[:-1]):
+                if any(s in mv for s in post[k]):
+                    mv.add(k)
+            if j in mv:
+                continue
+            new = idx[:a] + [k for k in mid if k in mv] + [k for k in mid if k not in mv] + idx[b + 1:]
+        else:
+            mv = {j}
+            for k in mid[1:]:
+                if any(s in mv for s in pre[k]):
+                    mv.add(k)
+            if i in mv:
+                continue
+            new = idx[:a] + [k for k in mid if k not in mv] + [k for k in mid if k in mv] + idx[b + 1:]
+        v, r = total(new)
+        if v < cur + HEAT * (1.0 - it / SWAPS) * float(rng.random()) ** 3:
+            cur, res, idx, pairs = v, r, new, []
+            if v < low:
+                low, keep = v, new
+    fin = run(keep, 0)[0]
+    ex = [None] * n
+    bank = {}
+    for i in keep:
+        ex[i] = []
+        for b in banks[i]:
+            ex[i] += [j for q, j in bank.get(b, {}).items() if q != qn[i]]
+            bank.setdefault(b, {})[qn[i]] = i
+    return keep, [fin[i] - lat[i] - ops[i]["cost"] for i in range(n)], fin, ex
+
+
 def order(ops):
     n = len(ops)
     hard = [set() for _ in range(n)]
@@ -624,8 +736,8 @@ def order(ops):
         fine.append((nm, h, o["q"], o["kind"]))
         wide.append([k for k, s in enumerate(KINS) if nm in s.split()] + [-1])
     wide = [(w[0], f[1] if f[0][0] != "P" else 0) for w, f in zip(wide, fine)]
-    base = np.array(pri)
-    low = max(sched(ops, pre, pri, banks)[2])
+    base = np.array(pri) + np.array([LEAD[w[0]][w[1]] if w[0] >= 0 else 0.0 for w in wide])
+    low = max(sched(ops, pre, list(base), banks)[2])
     for tags, rounds in ((wide, TRY[0]), (fine, TRY[1])):
         names = sorted(set(tags))
         tg = np.array([names.index(x) for x in tags])
@@ -649,6 +761,7 @@ def order(ops):
         else:
             b = sched(ops, post, [x + float(z) * jit for x, z in zip(best[2], rng.random(n))], banks)
             pri = [x + float(z) * jit for x, z in zip(b[2], rng.random(n))]
+    best = polish(ops, best[0], pre, post, banks, cases, rng)
     idx, t0, fin, ex = best[:4]
     TIMES[:] = [max(fin)] + [replay(ops, best, pre, c, lat) for c, lat in cases]
     out = [ops[i] for i in idx]

@@ -16,56 +16,56 @@ def _sb(name, n, dt, where="sbuf"):
 
 
 for _n, _c, _d in (
-    ("St", 3088, BF), ("Ef", 4720, BF), ("Ot", 256, BF), ("Qn", 768, I32), ("Qk", 768, I32), ("Tu", 768, I32),
-    ("Tub", 768, BF), ("Rm", 16, BF), ("Gl0", 256, BF), ("Gl1", 256, BF), ("Gl2", 256, BF),
-    ("Cw0", 768, I32), ("Cw1", 768, I32), ("Cw2", 768, I32), ("Cs0", 768, I32), ("Cs1", 768, I32), ("Cf", 768, F32),
+    ("St", 3088, BF), ("Ef", 4720, BF), ("Ot", 256, BF), ("Qn", 768, I32), ("Qk", 768, I32), ("Tu", 128, I32),
+    ("Tub", 176, BF), ("Rm", 16, BF), ("Gl0", 256, BF), ("Gl1", 256, BF), ("Gl2", 256, BF),
+    ("Cw0", 768, I32), ("Cw1", 768, I32), ("Cw2", 768, I32), ("Cr0", 768, I32), ("Cr1", 768, I32),
+    ("In0", 1184, F16), ("In1", 1184, F16), ("In2", 1184, F16), ("Li0", 1184, F16), ("Li1", 1184, F16), ("Cf", 768, F32),
     ("C1", 768, I32), ("C2", 768, I32), ("K16", 768, F16), ("wsc", 768, F32),
     ("Sb0", 400, BF), ("Sb1", 400, BF), ("Sb2", 400, BF), ("Lb0", 400, BF), ("Lb1", 400, BF), ("Lb2", 256, BF),
     ("sg", 4096, BF), ("smx", 4096, BF), ("eg", 4096, BF), ("yy", 4096, BF), ("dd", 4096, BF), ("ind", 4096, BF),
     ("P40", 48, BF), ("pmin", 48, F32), ("mj", 48, BF), ("mm", 48, BF), ("ji", 16, I32), ("jj", 16, I32),
     ("mj4", 48, BF), ("pm2", 48, F32), ("ji2", 16, I32), ("jalt", 16, I32),
-    ("dj", 16, F32), ("LJ", 16, U16), ("R0j", 256, BF), ("t12", 48, BF), ("Pfin", 48, BF), ("Pout", 768, F32),
+    ("dj", 16, F32), ("LJ0", 16, U16), ("LJ1", 16, U16), ("LJ2", 16, U16), ("SL0", 16, U16), ("SL1", 16, U16), ("R0j", 256, BF),
+    ("wd", 240, BF), ("mb", 512, BF), ("t12", 48, BF), ("Pfin", 48, BF), ("Pout", 128, F32),
     ("q32", 256, I32), ("q16", 256, U16), ("qf", 256, F16), ("key", 256, F16), ("msc", 256, F32),
-    ("mi", 16, I32), ("k0", 16, I32), ("Dk", 256, BF), ("Lk", 16, U16), ("xx", 256, BF), ("xm", 256, BF),
-    ("uvi", 16, I32), ("uva", 16, I32), ("Du", 288, BF), ("vl", 16, F32), ("Lo", 16, U16), ("u32", 256, F32), ("tO", 256, I32),
-    ("nr", 256, I32), ("na", 256, I32), ("n16", 256, U16), ("dx", 256, BF), ("ix", 256, BF),
+    ("mi", 16, F16), ("k0", 32, BF), ("Dk", 256, BF), ("Lk", 16, U16), ("xx", 512, BF),
+    ("uvi", 16, I32), ("uva", 16, I32), ("Du", 288, BF), ("Lo", 16, U16), ("u32", 256, F32), ("tO", 256, I32),
+    ("na", 256, I32), ("n16", 256, U16), ("dx", 256, BF), ("ix", 256, BF), ("nf", 512, F16),
     ("hxm", 48, F32), ("hxs", 48, F32), ("hsc", 768, F32), ("t48", 96, F32), ("ss", 96, F32), ("ai", 32, I32),
-    ("jba", 64, I32), ("gt", 16, F32), ("Dj", 768, BF), ("Lab", 32, U16), ("ya", 256, BF),
-    ("mT", 256, BF), ("wi", 48, I32), ("wa", 48, I32), ("wT", 128, BF), ("R0w", 256, BF),
-    ("kT", 64, BF), ("R0k", 256, BF), ("xsc", 256, F32), ("Dx", 256, F16), ("RT", 256, F32), ("eq", 256, F16),
+    ("jba", 40, I32), ("gt", 16, F32), ("Dj", 384, BF), ("Lab", 32, U16), ("ya", 16, BF),
+    ("mT", 256, BF), ("wi", 48, F16), ("wT", 64, BF), ("R0w", 768, F16),
+    ("R0k", 128, BF), ("xsc", 256, F32), ("Dx", 256, F16), ("RT", 256, F32), ("eq", 256, BF),
     ("Lx", 32, U16), ("cnt", 16, BF), ("Ai", 16, I32), ("Aa", 16, I32), ("cA", 16, F32),
-    ("ci", 16, I32), ("cf", 32, F32), ("cb", 2560, BF), ("ch", 1536, F16), ("ce", 1920, BF), ("d0", 1680, BF),
-    ("d0c", 128, F32), ("cl", 64, U16), ("tf", 768, F32), ("tb", 768, BF), ("ti", 16, I32), ("m2", 256, BF), ("kz", 256, BF),
+    ("ci", 16, I32), ("cf", 48, F32), ("cb", 2560, BF), ("ce", 1792, BF), ("d0", 1296, BF), ("k37", 128, F16),
+    ("d0c", 128, F32), ("cl", 64, U16), ("tf", 768, F32), ("tb", 512, BF), ("m2", 256, BF), ("kz", 384, BF),
 ):
     _sb(_n, _c, _d)
-for _n in ("PA0", "PA1", "PB0", "PB1", "PH", "PT0", "PT1", "PQ"):
+for _n in ("PA0", "PA1", "PB0", "PB1", "PT0", "PT1", "PQ0", "PQ1"):
     _sb(_n, 512, F32, "psum")
 
 LOADS = ("tu", "qn", "qk", "st0", "gl", "rm", "ot", "ef", "ef2")
 STORES = ("o1", "o2", "o3", "o4", "o5", "o6", "o7")
-SEMAPHORES = (["cV", "cS", "cP", "cG", "lsem", "rG1", "rG2", "rC00", "rC01", "rC10", "rC11", "rB0", "rB1", "rB2"]
+SEMAPHORES = (["cV", "cS", "cP", "cG", "lsem", "rG1", "rG2", "rC0", "rC1", "rB0", "rB1", "rB2",
+               "rE00", "rE01", "rE10", "rE11", "rL0", "rL1"]
               + ["l" + n for n in LOADS] + list(STORES))
 
-G1ENG = ("VVSS", "SSSS")
-G2ENG = ("SSSS", "SSSS")
-INDENG = ("SSSV", "SVVV")
-ADDENG = ("VVVV", "VVVV")
-YBENG = "SS"
-VC = 1.0
-BASE = (0.52, 1.56, 3.8)
-CASES = ((0.8, 1.56, 3.8, 1.0), (0.52, 1.1, 2.0, 1.0), (0.52, 2.0, 5.5, 1.0), (0.52, 1.56, 3.8, 0.55), (0.52, 1.3, 3.0, 1.6))
+ENG = dict(sg="VVSSSSSS", eg="SSSSSSSS", ind="SVVVVVVV",
+           q16="VS", key="SV", mi="VV", Lk="VS", xx="VS", u32="SS", uvi="VV", Lo="VV", n16="SS", qf="VS", mT="SS",
+           K16="SS", wi="VS", R0j="SS", Lab="S", Laa="V", SL="S", yb="VS", ya="SS", Lb="V", Ai="S", cA="S", ji2="S",
+           RT="S", Cw="VS", cnt="S", LJ="VS", nf0="SS", nf1="VS", x2="VV", mj4="S", mj12="S",
+           Dk="SS", Db="S", Dj="S", Da="S", rm="S", c0="V" * 24, c1="S" * 60)
+PARTS = ("mT", "qf", "dx", "ix")
+WIDEK = "wn"
+ADD = "FPFPFPFP"
+BANKS = ("A0A0A0A0A0A0A0A0", "B0B1A1B0B1A1B0B1")
+DIRECT = False
+MKSPLIT = True
+MARKS = 1
+BASE = (0.52, 1.56, 3.8, 1.0)
+CASES = ((0.75, 1.56, 3.8, 1.0), (0.52, 1.2, 2.5, 1.5))
 LAT, LATS = 180.0, 110.0
 BACK = 3
-SWAPS, HEAT, MIX = 26000, 600.0, (0, 1)
-CFIRST = True
-DIRECT = False
-EARLY, XENG, UENG = -1, "VS", "SS"
-SEED, ROUNDS, JIT, WAITW, LOOK = 2, 20, 3000.0, 1.0, 0.0
-TRY = (300, 700)
-KINS = ("q32 q16 sg", "key msc mi k0 Dk Lk xx uvi uva Du Lo u32 tO nr na n16", "smx", "eg", "yy dd PA0 PA1 PB0 PB1", "ind",
-        "dx ix hxm hxs", "xm kT R0k xsc Dx RT eq Lx", "St", "R0j mT qf C1 K16 wsc wi wa wT R0w C2 Cs Cf PQ",
-        "hsc t48 ss ai jba gt Dj Lab Sb", "PT0", "PT1", "PH", "t12 P40 mj mm mj4 pm2 ji2 jalt dj")
-LEAD = [(0.0, 0.0)] * 15
+SEED, ROUNDS = 1, 8000
 TIMES = []
 
 
@@ -100,7 +100,7 @@ def flat(rs):
 
 
 def clash(a, b):
-    if a[1] != b[1] or a[3] <= b[2] or b[3] <= a[2]:
+    if a[1] != b[1] or a[3] <= b[2] or b[3] <= a[2] or a[6] <= b[5] or b[6] <= a[5]:
         return False
     return not (a[4] == b[4] and a[4] > 1 and (a[2] - b[2]) % a[4] != 0)
 
@@ -117,7 +117,7 @@ def ap(T, r):
 
 def build(case=None):
     ops = []
-    PC, GC, SC = case or BASE
+    PC, GC, SC = (case or BASE)[:3]
 
     def add(q, kind, args, rd, wr, cost, **kw):
         o = dict(q=q, kind=kind, args=args, rd=flat(rd), wr=flat(wr), cost=cost, n=len(ops))
@@ -127,15 +127,15 @@ def build(case=None):
 
     def vcost(out, ins, two=False):
         if out[0] == "i":
-            return 50 + SC * nel(out) * VC
+            return 50 + SC * nel(out)
         if ins[0][0] == "i":
-            return 50 + GC * nel(out) * VC
+            return 50 + GC * nel(out)
         n = nel(out)
         if two:
             f = 1.0 if (inps(ins[0]) or inps(ins[1])) else 2.0
         else:
             f = 0.5 if all(dty(r) in (BF, F16, U16) for r in [out] + ins) else 1.0
-        return max(64, n * f) * VC
+        return max(64, n * f)
 
     def cp(out, a):
         wr = [out[1]] if out[0] == "i" else [out]
@@ -152,27 +152,37 @@ def build(case=None):
         add("V", "scan", (out, d0, d1, op0, op1), [d0, d1], [out], vcost(out, [d0, d1]))
 
     def ms(out, v):
-        add("V", "ms", (out, v), [], [out], max(64, nel(out) * 0.5) * VC)
+        add("V", "ms", (out, v), [], [out], max(64, nel(out) * 0.5))
 
     def act(out, a, f=AF.Identity, bias=0.0, scale=1.0):
-        c = 65 + GC * nel(out) * VC if a[0] == "i" else max(64, nel(out)) * VC + 30
+        c = 65 + GC * nel(out) if a[0] == "i" else max(64, nel(out)) + 30
         add("S", "act", (out, a, f, bias, scale), [a, bias, scale], [out], c)
 
-    def mov(eng, out, a):
-        if eng == "V":
+    def aff(key, h, out, a, scale=1.0, bias=0.0):
+        if ENG[key][h] == "S":
+            act(out, a, bias=bias, scale=scale)
+        elif scale == 1.0 and bias == 0.0:
             cp(out, a)
+        elif scale == 1.0:
+            ts(out, a, bias, ALU.add)
         else:
-            act(out, a)
+            ts(out, a, scale, ALU.mult, bias, ALU.add)
+        ops[-1]["tag"] = (key, h)
 
-    def mm(lst, chain=True):
+    def mm(lst, chain=True, first=True, final=True):
         c = sum(max(min(64, nel(l)), nel(r)) for (_, l, r) in lst) * PC + 30
-        add("P", "mm", (lst, chain), [x for (_, l, r) in lst for x in (l, r)], [o for (o, _, _) in lst], c)
+        add("P", "mm", (lst, chain, first, final), [x for (_, l, r) in lst for x in (l, r)], [o for (o, _, _) in lst], c)
+
+    turn = R("ya", 2, 3)
 
     def iota(out, pat, base, cm):
-        add("G", "iota", (out, pat, base, cm), [], [out], 130 + 2 * nel(out) * VC)
+        add("G", "iota", (out, pat, base, cm), [turn], [out] + [turn] * (out[5] > 0), 130 + 2 * nel(out))
+
+    def fill(out, v):
+        iota(out, [[0, nel(out)]], int(v), 0)
 
     def asel(out, a, pat, base, cm, op=ALU.is_equal, fill=0.0):
-        add("G", "asel", (out, a, pat, base, cm, op, fill), [a], [out], 170 + 2 * nel(out) * VC)
+        add("G", "asel", (out, a, pat, base, cm, op, fill), [a, turn], [out] + [turn] * (out[5] > 0), 170 + 2 * nel(out))
 
     def load(q, name, out, kb, behind=()):
         add(q, "load", (name, out), list(behind), [out], 60, sem="l" + name, lat=1800 + kb * 5.0)
@@ -181,12 +191,15 @@ def build(case=None):
         add("Y", "store", (sem, fn), rd, [], 60, sem=sem, lat=1800 + kb * 5.0)
 
     def send(kind, src, dst, sem, kb):
-        s = add("G", "send", (kind, src, dst, sem), [src], [R("ya", 0, 1)] if CFIRST else [], 500 + kb * 14.0)
+        s = add("G", "send", (kind, src, dst, sem), [src], [R("ya", 0, 1)], 600)
+        after = dict((o["n"], 0.0) for o in ops if o["q"] == "L")
+        after[s["n"]] = 1000.0
+        w = add("L", "link", (kind,), [], [R("ya", 4, 5)], kb * 14.0, after=after)
         for d, sm in zip(dst, sem):
-            add("R", "recv", (kind,), [], [d], 0, sem=sm, lat=0, after=(s["n"], 1500.0))
+            add("R", "recv", (kind,), [], [d], 0, sem=sm, lat=0, after={w["n"]: 400.0})
 
     add_, sub_, mul_, max_, min_ = ALU.add, ALU.subtract, ALU.mult, ALU.max, ALU.min
-    eq_, and_ = ALU.is_equal, ALU.bitwise_and
+    eq_, and_, shr_ = ALU.is_equal, ALU.bitwise_and, ALU.arith_shift_right
 
     load("Y", "tu", R("Tu", 0, 128, 1, 0, 48), 24)
     load("Y", "qn", R("Qn", 0, 768), 400)
@@ -199,131 +212,154 @@ def build(case=None):
     add("Y", "load", ("ef", R("Ef", 4096, 4720)), [R("St", 0, 3072)], [R("Ef", 4096, 4720)], 60, sem="lef2", lat=4300)
     send("G", R("Gl0", 0, 256), [R("Gl1", 0, 256), R("Gl2", 0, 256)], ["rG1", "rG2"], 128)
 
-    def col(j):
-        return R("cf", j, j + 1)
-    cP, cB, cAa, cN15, cF15, cJ, cU, c16P, c16A, cM16, cM4k, cN16, cN4k, cN64k, cSg, cF64k, cK37 = [col(j) for j in range(17)]
-    iota(R("ci", 0, 1), [[0, 1]], 0, 1)
-    ts(R("ci", 4, 5), R("ci", 0, 1), 15, and_)
-    ts(R("ci", 8, 9), R("ci", 0, 1), 4, ALU.arith_shift_right)
-    cp(cP, R("ci", 0, 1)); cp(cB, R("ci", 4, 5)); cp(cAa, R("ci", 8, 9))
-    ts(cN15, cB, 15.0, ALU.is_lt); ts(cF15, cB, 15.0, eq_)
-    ts(cJ, cB, 3072.0, add_)
-    ts(col(20), cB, 2.0, mul_, 1.0, add_); ts(cU, col(20), cN15, mul_)
-    for d, a, c in ((c16P, cP, 16.0), (c16A, cAa, 16.0), (cM16, R("Rm", 0, 1), 16.0), (cM4k, R("Rm", 0, 1), 4096.0),
-                    (cN16, cN15, 16.0), (cN4k, cN15, 4096.0), (cN64k, cN15, 65536.0), (cF64k, cF15, 65536.0), (cK37, cB, 37.0)):
-        act(d, a, scale=c)
-    act(cSg, cN15, bias=-1920.0, scale=2048.0)
+    def col(j, p1=128):
+        return R("cf", j, j + 1, 1, 0, p1)
 
-    def blk(buf, j, p1=128):
-        return R(buf, 128 * j, 128 * j + 128, 1, 0, p1)
-    Ib, I0, nI, IB, M16, kk, gg, B16, Wu, Wr0, Wr1, Wr2, One = [blk("cb", j) for j in range(13)]
-    ms(R("cb", 12 * 128, 15 * 128), 1.0)
-    ones3 = R("cb", 12 * 128, 15 * 128, 1, 0, 2)
-    ones31 = R("cb", 12 * 128, 15 * 128, 1, 0, 1)
-    asel(Ib, One, [[-1, 128]], 0, 1)
+    def blk(buf, j, p1=128, p0=0):
+        return R(buf, 128 * j, 128 * j + 128, 1, p0, p1)
+    made = [0, 0]
+
+    def con(k, out, a, scale=1.0, bias=0.0):
+        aff("c%d" % k, made[k], out, a, scale, bias)
+        made[k] += 1
+    cP, cB, cAa, cN15, cF15, cJ, cU, c16P, cM16, cM4k, cN16, cN4k, cN64k, cSg, cF64k, cN63 = [col(j) for j in range(16)]
+    iP, iB, iA = R("ci", 0, 1), R("ci", 4, 5), R("ci", 8, 9)
+    iota(iP, [[0, 1]], 0, 1)
+    ts(iB, iP, 15, and_); ts(iA, iP, 4, shr_)
+    con(0, cP, iP); con(0, cB, iB); con(0, cAa, iA); con(0, c16P, iP, 16.0)
+    ts(cN15, iB, 15.0, ALU.is_lt); ts(cF15, iB, 15.0, eq_); ts(cF64k, iB, 15.0, eq_, 65536.0, mul_)
+    con(0, col(20), iB, 2.0, 1.0); con(0, cU, col(20), cN15)
+    for d, a, c in ((cM16, R("Rm", 0, 1), 16.0), (cM4k, R("Rm", 0, 1), 4096.0), (cN16, cN15, 16.0), (cN4k, cN15, 4096.0),
+                    (cN64k, cN15, 65536.0), (cN63, cN15, 63.0)):
+        con(1, d, a, c)
+    con(1, cJ, iB, 1.0, 3072.0); con(1, cSg, cN15, 2048.0, -1920.0)
+    Ib, I0, nI, IB, M16, kk, gg, B16, Wu, Wr0, Wr1, Wr2, One, I16, Tri = [blk("cb", j) for j in range(15)]
+    k8, k16, one1 = R("cb", 5 * 128, 5 * 128 + 8), R("cb", 5 * 128, 5 * 128 + 16), blk("cb", 12, 1)
     iota(kk, [[0, 8], [1, 16]], 0, 0)
     iota(gg, [[1, 8], [0, 16]], 0, 0)
-    act(I0, Ib, scale=cN15); act(nI, Ib, scale=-1.0); act(IB, Ib, scale=BIG / 2)
-    ts(M16, kk, cB, eq_); ts(B16, gg, cAa, eq_)
+    fill(One, 1)
+    asel(Ib, One, [[-1, 128]], 0, 1)
+    ts(M16, kk, cB, eq_); ts(B16, gg, cAa, eq_); ts(Tri, kk, cB, ALU.is_le, 4096.0, mul_)
+    con(0, I16, Ib, 16.0); con(0, I0, Ib, cN15); con(0, Wu, B16, cU); con(0, nI, Ib, -1.0)
+    con(1, IB, Ib, BIG / 2); con(1, Wr0, B16, cN4k); con(1, Wr1, B16, cN64k); con(1, Wr2, B16, cM4k)
     kz = R("kz", 0, 256, 1, 0, 1)
-    ms(blk("kz", 1, 1), 0.0); cp(blk("kz", 0, 1), blk("cb", 5, 1))
-    act(Wu, B16, scale=cU); act(Wr0, B16, scale=cN4k); act(Wr1, B16, scale=cN64k); act(Wr2, B16, scale=cM4k)
+    iota(blk("kz", 0, 1), [[0, 8], [1, 16]], 0, 0); fill(blk("kz", 1, 1), 0)
     o = 15 * 128
 
     def sm(a, n=8, step=1):
         return R("cb", o + a, o + a + n * step - (step - 1), step)
     C8 = R("cb", 7 * 128, 8 * 128, 16)
-    C128, C256, Wu8, Wv8, C16p, Cp = sm(0), sm(8), sm(16), sm(24), sm(32), sm(56)
-    Cjb = sm(48, 16)
-    Wmk = sm(64, 16)
-    for d, c in ((C256, 256.0), (Cp, cP), (sm(64), cF64k), (sm(72), cF15), (C16p, c16P), (Wu8, cU), (Wv8, cN15),
-                 (C128, 128.0), (sm(48), c16A)):
-        act(d, C8, scale=c)
+    C4k, C256, Wu8, Wv8, C16p, Cp, Cp2, Wmk = sm(0), sm(8), sm(16), sm(24), sm(32), sm(48), sm(48, 16), sm(64, 16)
+    for d, c in ((C256, 256.0), (Cp, cP), (sm(64), cF64k), (sm(72), cF15), (C16p, c16P), (Wu8, cU), (Wv8, cN15)):
+        con(0, d, C8, c)
+    con(1, sm(56), C8, cP); con(1, C4k, C8, 4096.0)
     if DIRECT:
-        ms(R("Du", 0, 288), 0.0)
-        ts(R("Du", 15, 143, 16), C8, cU, mul_); ts(R("Du", 159, 287, 16), C8, cN15, mul_)
+        fill(R("Du", 0, 288), 0)
+        con(1, R("Du", 15, 143, 16), C8, cU); con(1, R("Du", 159, 287, 16), C8, cN15)
     Wd, Wi, Ws = sm(80, 24), sm(104, 24), sm(128, 24)
-    ms(sm(80, 72), 0.0)
-    act(sm(80, 8, 3), C8, scale=cN16); act(sm(82, 8, 3), C8, scale=cM16)
-    act(sm(105, 8, 3), sm(80, 8, 3), scale=16.0); act(sm(129, 8, 3), C8, scale=cSg)
+    fill(sm(80, 72), 0)
+    con(1, sm(80, 8, 3), C8, cN16); con(1, sm(82, 8, 3), C8, cM16)
+    con(1, sm(105, 8, 3), sm(80, 8, 3), 16.0); con(1, sm(129, 8, 3), C8, cSg)
     I4 = R("cb", o + 152, o + 200, 1, 0, 48)
-    ms(R("Tub", 128, 176, 1, 0, 48), 4.0)
+    fill(R("Tub", 128, 176, 1, 0, 48), 4)
     asel(I4, R("Tub", 128, 176, 1, 0, 48), [[-1, 2], [-6, 8], [-2, 3]], 0, 1)
-    Iq = blk("cb", 17)
-    act(Iq, Ib, scale=0.25)
-    lv = R("cb", 18 * 128, 18 * 128 + 48)
-    iota(lv, [[0, 16], [1, 3]], 0, 0)
-    Ih, I16h, B16h, Tri, Oneh = [blk("ch", j) for j in range(5)]
-    cp(Ih, Ib); ts(I16h, Ib, 16.0, mul_); cp(B16h, B16); ts(Tri, kk, cB, ALU.is_le, 4096.0, mul_)
-    cp(blk("ch", 4, 1), blk("cb", 12, 1))
-    C8h, C4kh = R("ch", 640, 648), R("ch", 648, 656)
-    cp(C8h, C8); ts(C4kh, C8, 4096.0, mul_)
-    iota(blk("tb", 0, 1), [[1, 128]], 0, 0)
-    for c in range(6):
-        ts(blk("ch", 6 + c, 1), blk("tb", 0, 1), 128.0 * c, add_)
+    Iq, Wr3 = blk("cb", 17), blk("cb", 19)
+    con(1, Iq, Ib, 0.25)
+    lv, lv2 = R("cb", 18 * 128, 18 * 128 + 48), R("cb", 18 * 128 + 2, 18 * 128 + 50)
+    iota(R("cb", 18 * 128, 18 * 128 + 51), [[0, 17], [1, 3]], 0, 0)
     Ej = [blk("ce", l, 24) for l in range(3)]
-    Ep = [blk("ce", 3 + l, 49) for l in range(3)]
-    En = [blk("ce", 6 + l, 49) for l in range(3)]
-    Ek, E8 = [blk("ce", 9, 33), blk("ce", 14, 33)], blk("ce", 10, 8)
+    Ep = [blk("ce", 3 + l, 64) for l in range(3)]
+    En = [blk("ce", 6 + l, 65) for l in range(3)]
+    Ek, E8 = [blk("ce", 9, 65), blk("ce", 10, 65)], blk("ce", 11, 8)
     B22 = float(1 << 22)
-    ta, tc = blk("ce", 11, 24), blk("ce", 12, 24)
-    ms(ta, -BIG)
+    ta, tc = blk("ce", 12, 24), blk("ce", 13, 24)
+    fill(ta, -BIG)
     asel(tc, ta, [[-3, 8], [0, 16]], 0, 1, ALU.is_ge)
     asel(ta, tc, [[3, 8], [0, 16]], 2, -1, ALU.is_ge)
     for l in range(3):
         asel(Ej[l], ta, [[-3, 8], [0, 16]], -l, 1, ALU.not_equal, -2560.0)
     asel(E8, blk("cb", 12, 8), [[-1, 8], [0, 16]], 0, 1)
-    t0, t1, t2 = [blk("tb", j, 49) for j in range(3)]
-    act(t0, blk("cb", 5, 49), bias=-30 * B22, scale=2 * B22)
-    ms(t1, B22)
-    for l in range(3):
-        asel(t2, t0, [[-1, 8], [0, 16]], -1 - 8 * l, 1)
-        asel(En[l], t1, [[-1, 8], [0, 16]], -25 - 8 * l, 1)
-        tt(Ep[l], En[l], t2, add_)
-        act(blk("ce", 3 + l, 1), blk("cb", 5, 1), AF.Square, bias=-15.0 * 2048, scale=2048.0)
-        act(En[l], Ep[l], scale=-1.0)
-    t0, t1, t2, t3 = blk("tb", 4, 33), blk("tb", 5, 33), blk("tb", 3, 33), blk("ce", 13, 33)
-    act(t0, blk("cb", 5, 33), scale=-8192.0)
-    ms(t1, 4096.0)
-    for h in range(2):
-        asel(t2, t0, [[-1, 8], [0, 16]], -17 - 8 * h, 1)
-        asel(t3, t1, [[-1, 8], [0, 16]], -1 - 8 * h, 1)
-        tt(Ek[h], t2, t3, add_)
-        act(blk("ce", 9 + 5 * h, 1), blk("cb", 5, 1), AF.Square, scale=64.0)
-    ms(R("wT", 0, 128, 64), 1.0); ms(R("kT", 0, 1), 1.0)
+    fill(R("wT", 0, 64), 0); fill(R("k0", 0, 32), 0)
+    fill(R("wd", 0, 240), 0); con(1, R("wd", 112, 128), R("cb", 4 * 128, 4 * 128 + 16))
+    fill(R("jba", 32, 40), 0); fill(R("Sb0", 288, 304), 0); fill(R("Sb1", 288, 304), 0)
+    cOwn = col(26)
+    ts(col(25), iB, 8.0, ALU.is_ge, 8.0, mul_)
+    ts(R("ci", 15, 16), iP, 7, and_); ts(cOwn, R("ci", 15, 16), cAa, eq_)
+    Lz1, Lz2, Lz3 = R("cl", 8, 12), R("cl", 40, 48), R("cl", 48, 56)
+    for lst, src, step, hi, lo, zero in ((Lz1, R("cb", 5 * 128, 5 * 128 + 4), 2.0, 0.125, 0.0, 8.0), (Lz2, k8, 1.0, 1.0, 0.0, 32.0),
+                                         (Lz3, k8, 1.0, 1.0, 16.0, 32.0)):
+        con(1, col(38), col(25), hi, lo - zero)
+        con(1, R("cf", 40, 40 + nel(lst)), src, step, col(38))
+        con(1, lst, R("cf", 40, 40 + nel(lst)), cOwn, zero)
+    M16p, C8p, k37 = blk("mb", 2), R("mb", 384, 392), blk("k37", 0, 1)
+    ts(R("ci", 12, 13), iP, 1, and_); con(1, col(27), R("ci", 12, 13), 8.0, cAa)
+    ts(M16p, kk, col(27), eq_)
+    ts(R("ci", 13, 14), iB, 1, shr_); con(1, col(28), R("ci", 13, 14))
+    ts(C8p, k8, col(28), eq_)
+    cPar, cPb = (col(29), col(30)), (col(31), col(32))
+    ts(R("ci", 14, 15), iA, 1, and_)
+    con(1, cPar[1], R("ci", 14, 15)); con(1, cPar[0], R("ci", 14, 15), -1.0, 1.0)
+    con(1, cPb[1], R("ci", 14, 15), -2048.0); con(1, cPb[0], R("ci", 14, 15), 2048.0, -2048.0)
+    iota(blk("kz", 2, 1), [[1, 16], [0, 8]], 0, 0)
+    con(1, k37, blk("kz", 2, 1), 37.0)
     M2 = R("m2", 0, 256)
-    act(blk("m2", 0), M16); act(blk("m2", 1), M16)
-    lv2 = R("cb", 19 * 128, 19 * 128 + 48)
-    for l in range(3):
-        ms(R("cb", 19 * 128 + l, 19 * 128 + 48, 3), float((l + 2) % 3))
-    dMx, dH, dW, dX, dS3, dM3 = (R("d0", 0, 512), R("d0", 512, 896), R("d0", 896, 1280), R("d0", 1280, 1536),
-                                 R("d0", 1536, 1632), R("d0", 1632, 1680))
-    for r, body, head, st in ((dM3, 0.0, 1024.0, 3), (dMx, 1.0, 0.0, 16), (dH, -1.0, BIG, 16), (dW, 1.0, -BIG, 16),
-                              (dX, 0.0, BIG, 16), (dS3, 1.0, 0.0, 3), (R("d0c", 0, 128), -BIG, 32768.0, 16)):
+    asel(blk("m2", 0), M16, [[0, 128]], 0, 0); asel(blk("m2", 1), M16, [[0, 128]], 0, 0)
+    dMx, dH, dX, dS3, dM3 = R("d0", 0, 512), R("d0", 512, 896), R("d0", 896, 1152), R("d0", 1152, 1248), R("d0", 1248, 1296)
+    for r, body, head, st in ((dM3, 0.0, 1024.0, 3), (dMx, 1.0, 0.0, 16), (R("d0c", 0, 128), -BIG, 32768.0, 16)):
         ms(r, body); ms(R(r[1], r[2], r[3], st), head)
-    ms(R("St", 3072, 3088), 0.0)
-    Lb8, Lb16, Lend, Lgo = R("cl", 0, 8), R("cl", 0, 16), R("cl", 16, 32), R("cl", 32, 35)
-    cp(Lb16, R("cb", 5 * 128, 5 * 128 + 16))
-    ts(Lend, R("cb", 5 * 128, 5 * 128 + 16), 16.0, mul_, 15.0, add_)
-    jf, j3 = R("cf", 21, 24), R("ti", 0, 3)
-    ts(jf, R("cb", 5 * 128, 5 * 128 + 3), 16.0, mul_, cB, add_)
-    ts(j3, jf, -1.0, add_, 1.0 / 3.0, mul_)
-    cp(Lgo, j3)
+    for r, body, head, st in ((dH, -1.0, BIG, 16), (dX, 0.0, BIG, 16), (dS3, 1.0, 0.0, 3)):
+        fill(r, body); fill(R(r[1], r[2], r[3], st), head)
+    fill(R("St", 3072, 3088), 0)
+    Lb8, Lend, Lgo = R("cl", 0, 8), R("cl", 16, 32), R("cl", 32, 35)
+    con(0, Lb8, k8); con(1, Lend, k16, 16.0, 15.0)
+    con(0, R("cf", 21, 24), R("cb", 5 * 128, 5 * 128 + 3), 16.0, cB)
+    con(0, Lgo, R("cf", 21, 24), 1.0 / 3.0, -1.0 / 3.0)
+    cLo, k64 = col(24, 64), blk("cb", 5, 64)
+    ts(cLo, col(0, 64), 32.0, ALU.is_lt)
+    fill(R("ce", 768, 1152, 1, 0, 65), 1)
+    iota(R("R0w", 0, 768, 1, 0, 65), [[1, 768]], 0, 0)
+    fill(blk("R0k", 0, 65), 1)
+    con(1, col(34, 64), cLo, 2 * B22, -B22); con(1, col(35, 64), cLo, -31 * B22, 16 * B22)
+    con(1, blk("tb", 0, 64), k64, col(34, 64), col(35, 64))
+    for e in range(2):
+        for l in range(3):
+            asel(blk("ce", 3 + l, 32 * e + 32, 32 * e), blk("tb", 0, 32 * e + 32, 32 * e), [[-1, 8], [0, 16]], -1 - 8 * l, 1)
+    act(blk("tf", 0, 1), blk("cb", 5, 1), AF.Square, bias=-15.5 * 2048, scale=2048.0)
+    for l in range(3):
+        con(1, blk("ce", 3 + l, 1), blk("tf", 0, 1), 1.0, -B22 / 4)
+    con(1, R("ce", 768, 1152, 1, 0, 64), R("ce", 384, 768, 1, 0, 64), -1.0)
+    con(1, col(36, 64), cLo, -8192.0, 4096.0); con(1, col(37, 64), cLo, -4096.0, 4096.0)
+    con(1, blk("tb", 1, 64), k64, col(36, 64), col(37, 64))
+    for e in range(2):
+        for h in range(2):
+            asel(blk("ce", 9 + h, 32 * e + 32, 32 * e), blk("tb", 1, 32 * e + 32, 32 * e), [[-1, 8], [0, 16]], -16 * h, 1)
+    act(blk("Pout", 0, 65, 64), blk("cb", 5, 65, 64), AF.Square, bias=32.0, scale=64.0)
+    for h in range(2):
+        con(1, blk("ce", 9 + h, 65, 64), blk("Pout", 0, 65, 64), 1.0, -1024.0)
 
     def H(name, h, n=128, step=1, a=0):
         return R(name, h * n + a, h * n + n, step)
 
     cp(R("Tub", 0, 128, 1, 0, 48), R("Tu", 0, 128, 1, 0, 48))
-    mm([(R("PQ", 0, 48), R("Tub", 0, 128, 1, 0, 48), I4)])
-    tt(R("P40", 0, 48), R("PQ", 0, 48), lv, add_)
+    mm([(R("PQ0", 0, 48), R("Tub", 0, 128, 1, 0, 48), I4)])
+    tt(R("P40", 0, 48), R("PQ0", 0, 48), lv, add_)
+
+    def tolist(key, h, win, lst, D, pl, scale, c):
+        w = nel(pl)
+        aff(key, h, R(D[1], D[2], D[2] + 8 * w), IND(win, lst), scale)
+        mm([(pl, M16, c)] + [(pl, R("wd", 112 - 16 * g, 240 - 16 * g), R(D[1], D[2] + w * g, D[2] + w * g + w)) for g in range(8)])
 
     for t in range(RO):
         last = t == RO - 1
         P4 = R("P40", 0, 48)
-        Cw, Gl, Sb, Lp = "Cw%d" % t, "Gl%d" % t, "Sb%d" % t, "Lb%d" % (t - 1)
-        cA = cK37 if t == 0 else R("cA", 0, 1)
+        Cw, Gl, Sb, Lp, LJ = "Cw%d" % t, "Gl%d" % t, "Sb%d" % t, "Lb%d" % (t - 1), "LJ%d" % t
+        cA = 2048.0 if t == 0 else R("cA", 0, 1)
         PT = ["PT0", "PT1"]
-        Pinc, mj12, go = R(Sb, 256, 304), R(Sb, 304, 352), R(Sb, 384, 400)
+        In, Ip = "In%d" % t, "Li%d" % (t - 1)
+        mj, Pinc, mj12, go = R(In, 512, 560), R(In, 560, 608), R(In, 608, 656), R(Sb, 272, 288)
+
+        def part(name, h, buf=In):
+            return R(buf, 672 * h + 128 * PARTS.index(name), 672 * h + 128 * PARTS.index(name) + 128)
         if t == 0:
             jj = R("jj", 0, 16)
             scan(R("pmin", 0, 48), dM3, P4, add_, min_)
@@ -332,193 +368,208 @@ def build(case=None):
                 tt(H("Dk", h), IND(H("jj", h, 8), Lb8), M16, mul_)
                 pl = R(PT[h], 384, 392)
                 mm([(pl, M16, Cp), (pl, H("Dk", h), C256)])
-                cp(H("LJ", h, 8), pl)
+                aff("LJ", h, H(LJ, h, 8), pl)
         else:
-            jj = R(Lp, 368, 384)
-            ts(R("LJ", 0, 16), R(Lp, 352, 368), cB, add_)
-            tt(R("t12", 0, 48), IND(R(Lp, 384, 400), Lgo), R(Lp, 304, 352), mul_)
-            tt(P4, R(Lp, 256, 304), R("t12", 0, 48), add_)
-        tt(R("mj", 0, 48), IND(jj, Lgo), lv, eq_)
+            jj = R(Lp, 256, 272)
+            tt(R("t12", 0, 48), IND(R(Lp, 272, 288), Lgo), R(Ip, 608, 656), mul_)
+            tt(P4, R(Ip, 560, 608), R("t12", 0, 48), add_)
+        tt(mj, IND(jj, Lgo), lv, eq_)
         tt(R("mm", 0, 48), IND(jj, Lgo), lv2, eq_)
-        act(R("mj4", 0, 48), R("mj", 0, 48), scale=4.0); act(mj12, R("mj", 0, 48), scale=-12.0)
+        aff("mj4", 0, R("mj4", 0, 48), mj, 4.0); aff("mj12", 0, mj12, mj, -12.0)
         tt(Pinc, R("mj4", 0, 48), P4, add_)
         if not last:
             scan(R("pm2", 0, 48), dM3, Pinc, add_, min_)
-            cp(R("ji2", 0, 16), R("pm2", 2, 48, 3)); ts(R("jalt", 0, 16), R("ji2", 0, 16), 3, and_)
+            aff("ji2", 0, R("ji2", 0, 16), R("pm2", 2, 48, 3)); ts(R("jalt", 0, 16), R("ji2", 0, 16), 3, and_)
             tt(R("dj", 0, 16), jj, R("jalt", 0, 16), sub_)
-        for h in range(2):
-            lj = H("LJ", h, 8)
-            if t == 0:
-                cp(H("q16", h), IND(R("Qn", 128 * h, 768), lj))
-                ts(H("key", h), IND(R("Qk", 128 * h, 768), lj), 1025.0, add_)
-            else:
-                ts(H("q32", h), IND(H(Cw, h, 384), lj), 4095, and_)
-                cp(H("q16", h), H("q32", h))
-                ts(H("key", h), IND(H(Cw, h, 384), lj), 1.0 / 4096, mul_, 1024.625, add_)
-            for c in range(4):
-                mov(G1ENG[h][c], H("sg", 4 * h + c, 512), IND(R("St", 0, 3072), H("q16", 4 * h + c, 32)))
-                scan(H("smx", 4 * h + c, 512), dMx, H("sg", 4 * h + c, 512), mul_, max_)
-            mm([(R(PT[h], 0, 256), blk("cb", 12, 1), kz), (R(PT[h], 0, 128), H("key", h), I16h)]
-               + [(R(PT[h], k, 256, 16), H("sg", h, 2048, 16, k), Wmk) for k in range(16)])
-            scan(H("msc", h), R("d0c", 0, 128), R(PT[h], 0, 128), max_, min_)
-            act(H("mT", h), R(PT[h], 128, 256))
-            cp(H("mi", h, 8), H("msc", h, 128, 16, 15)); ts(H("k0", h, 8), H("mi", h, 8), 15, and_)
-            tt(H("Dk", h), IND(H("k0", h, 8), Lb8), M16, mul_)
-            pl = R(PT[h], 392, 400)
-            mm([(pl, M16, C16p), (pl, H("Dk", h), C8)])
-            cp(H("Lk", h, 8), pl)
-            if XENG[h] == "S":
-                act(H("xx", h), IND(H("sg", h, 2048), H("Lk", h, 8)), bias=cF15, scale=cN15)
-            else:
-                ts(H("xx", h), IND(H("sg", h, 2048), H("Lk", h, 8)), cF15, max_)
-            pl = R(PT[h], 400, 408)
-            if DIRECT:
-                pv = R(PT[h], 408, 416)
-                mm([(pv, R("Du", 159 - b, 287 - b), H("smx", h, 2048, 256, 16 * b + 15)) for b in range(16)])
-                act(H("vl", h, 8), pv)
-                mm([(pl, R("Du", 15 - b, 143 - b), H("xx", h, 128, 16, b)) for b in range(16)])
-                tt(H("uvi", h, 8), pl, H("vl", h, 8), add_); ts(H("uva", h, 8), H("uvi", h, 8), 255, and_)
-                cp(H("Lo", h, 8), H("uva", h, 8))
-            else:
-                mm([(pl, H("smx", h, 2048, 16, 15), Wv8), (pl, H("xx", h), Wu8)])
-            mm([(R(PT[h], 256, 384), Wu, H("xx", h))])
-            if UENG[h] == "S":
-                act(H("u32", h), R(PT[h], 256, 384), bias=32.0)
-            else:
-                ts(H("u32", h), R(PT[h], 256, 384), 32.0, add_)
-            if not DIRECT:
-                cp(H("uvi", h, 8), pl); ts(H("uva", h, 8), H("uvi", h, 8), 255, and_)
-                tt(H("Du", h), IND(H("uva", h, 8), Lb8), M16, mul_)
-                pl = R(PT[h], 408, 416)
-                mm([(pl, H("Du", h), C8)])
-                cp(H("Lo", h, 8), pl)
-            tt(H("tO", h), IND(R("Ot", 0, 256), H("Lo", h, 8)), H("u32", h), mul_)
-            ts(H("na", h), H("tO", h), 5, ALU.arith_shift_right, 4095, and_)
-            ts(H("n16", h), H("na", h), cA, add_)
-            for c in range(4):
-                mov(G2ENG[h][c], H("eg", 4 * h + c, 512), IND(R("Ef", 0, 4720), H("n16", 4 * h + c, 32)))
-            mm([(blk("PH", h), I0, H("xx", h)), (blk("PH", h), nI, H(Gl, h))])
-            act(H("dx", h), blk("PH", h), AF.Abs)
-            ts(H("ix", h), H("dx", h), 4.0, ALU.is_gt)
-            pl = R("PT1", 464 + 24 * h, 488 + 24 * h)
-            mm([(pl, H("dx", h), Wd), (pl, H("ix", h), Wi)])
-            ts(H("qf", h), H("q16", h), -1536.0, add_)
-        tt(R("hxm", 0, 48), R("PT1", 464, 512), R("mj", 0, 48), mul_)
-        scan(R("hxs", 0, 48), R("d0", 1536, 1584), R("hxm", 0, 48), mul_, add_)
-        tt(R("kT", 1, 17), R("k0", 0, 16), R("k0", 0, 16), mul_)
-        cp(R("kT", 17, 33), R("k0", 0, 16))
-        mm([(blk("PH", 2, 33), R("kT", 0, 33), Ib)])
-        act(blk("R0k", 0, 33), blk("PH", 2, 33))
-        pl = R("PH", 256, 512)
-        mm([x for h in range(2) for x in ((blk("PH", 2 + h), blk("R0k", 0, 33), Ek[h]), (blk("PH", 2 + h), H("qf", h), Ih))], 2)
-        scan(R("xsc", 0, 256), dX, pl, add_, min_)
-        tt(R("Dx", 0, 256), IND(R("xsc", 0, 256), Lend), M2, mul_)
-        mm([(pl, B16h, R("Dx", 0, 256)), (blk("PH", 2), Ih, Tri), (blk("PH", 3), Ih, Tri)])
-        act(R("RT", 0, 256), pl)
-        tt(R("eq", 0, 256), IND(R("xsc", 0, 256), Lend), R("RT", 0, 256), eq_)
-        mm([x for h in range(2) for x in ((R("PH", 256 + 8 * h, 264 + 8 * h), H("Dx", h), C8h),
-                                          (R("PH", 256 + 8 * h, 264 + 8 * h), H("eq", h), C4kh))], 2)
-        ts(R("Lx", 0, 32, 2), R("PH", 256, 272), 1536.0, add_, cJ, min_)
-        for c in range(16):
-            cp(IND(R("St", 0, 3088), R("Lx", 2 * c, 2 * c + 1)), H("xx", c, 16))
-        for h in range(2):
-            PQ = "PA0" if h else "PQ"
-            pq = R(PQ, 0, 384)
-            if t == 0:
+        if t == 0:
+            aff("rm", 0, R(In, 656, 657), R("Rm", 0, 1))
+            for h in range(2):
                 for l in range(3):
                     a = l * 256 + h * 128
-                    ts(blk(PQ, l), R("Qk", a, a + 128), 4096.0, mul_)
-                    tt(H(Cw, 3 * h + l), R("Qn", a, a + 128), blk(PQ, l), add_)
-            mm([(blk("PH", h, 24), H("mj", h, 24), Ib)])
+                    aff("Cw", h, blk("PQ%d" % h, l), R("Qk", a, a + 128), 4096.0)
+                    tt(H(Cw, 3 * h + l), R("Qn", a, a + 128), blk("PQ%d" % h, l), add_)
+        if not last:
+            send("N", R(Cw, 0, 768), [R("Cr%d" % t, 0, 768)], ["rC%d" % t], 384)
+        for h in range(2):
+            lj = H(LJ, h, 8)
+            if t == 0:
+                aff("q16", h, H("q16", h), IND(R("Qn", 128 * h, 768), lj))
+                aff("key", h, H("key", h), IND(R("Qk", 128 * h, 768), lj), bias=1025.0)
+            else:
+                ts(H("q32", h), IND(H(Cw, h, 384), lj), 4095, and_)
+                aff("q16", h, H("q16", h), H("q32", h))
+                aff("key", h, H("key", h), IND(H(Cw, h, 384), lj), 1.0 / 4096, 1024.625)
+            keys = [(R(PT[h], 0, 256), one1, kz), (R(PT[h], 0, 128), H("key", h), I16)]
+            if MKSPLIT:
+                mm(keys, final=False)
+            for c in range(4):
+                aff("sg", 4 * h + c, H("sg", 4 * h + c, 512), IND(R("St", 0, 3072), H("q16", 4 * h + c, 32)))
+                scan(H("smx", 4 * h + c, 512), dMx, H("sg", 4 * h + c, 512), mul_, max_)
+                if MKSPLIT:
+                    mm([(R(PT[h], k, 256, 16, 32 * c, 32 * c + 32), H("sg", 4 * h + c, 512, 16, k), Wmk) for k in range(16)],
+                       first=False, final=c == 3)
+            if not MKSPLIT:
+                mm(keys + [(R(PT[h], k, 256, 16), H("sg", h, 2048, 16, k), Wmk) for k in range(16)])
+            scan(H("msc", h), R("d0c", 0, 128), R(PT[h], 0, 128), max_, min_)
+            aff("mT", h, part("mT", h), R(PT[h], 128, 256))
+            k0, me = R("k0", 16 * h, 16 * h + 8), H("msc", h, 128, 16, 15)
+            aff("mi", h, H("mi", h, 8), me, bias=-7.5); tt(k0, me, H("mi", h, 8), sub_)
+            pl = R(PT[h], 392, 400)
+            if WIDEK[h] == "w":
+                tt(H("Dk", h), IND(k0, Lb8), M16, mul_)
+                mm([(pl, M16, C16p), (pl, H("Dk", h), C8)])
+            else:
+                tolist("Dk", h, H("k0", h, 16), Lz1, H("Dk", h), pl, 1.0, C16p)
+            aff("Lk", h, H("Lk", h, 8), pl)
+            xx = H("xx", 2 * h)
+            aff("xx", h, xx, IND(H("sg", h, 2048), H("Lk", h, 8)), cN15, cF15)
+            pl = R(PT[h], 400, 408)
+            if DIRECT:
+                la = [128 * h + 16 * (p % 8) + p // 8 for p in range(16)]
+                mm([(pl, R("Du", 159 - p, 287 - p), R("smx", 16 * la[p] + 15, 16 * la[p] + 240, 32)) for p in range(16)], final=False)
+                mm([(pl, R("Du", 15 - p, 143 - p), R("xx", 128 * h + la[p], 128 * h + la[p] + 15, 2)) for p in range(16)],
+                   first=False)
+            else:
+                mm([(pl, H("smx", h, 2048, 16, 15), Wv8), (pl, xx, Wu8)])
+            pn = R(PT[h], 256, 384)
+            mm([(R(PT[h], 256 + b, 384, 8), Wu, H("xx", 16 * h + b, 16)) for b in range(8)], False)
+            aff("u32", h, H("u32", h), pn, bias=32.0)
+            aff("uvi", h, H("uvi", h, 8), pl); ts(H("uva", h, 8), H("uvi", h, 8), 255, and_)
+            if DIRECT:
+                aff("Lo", h, H("Lo", h, 8), H("uva", h, 8))
+            else:
+                pl = R(PT[h], 408, 416)
+                tt(H("Du", h), IND(H("uva", h, 8), Lb8), M16p, mul_)
+                mm([(pl, H("Du", h), C8p)])
+                aff("Lo", h, H("Lo", h, 8), pl)
+            tt(H("tO", h), IND(R("Ot", 0, 256), H("Lo", h, 8)), H("u32", h), mul_)
+            ts(H("na", h), H("tO", h), 5, shr_, 4095, and_)
+            for e in range(2):
+                aff("nf%d" % e, h, H("nf", 2 * h + e), H("na", h), cPar[e], cPb[e])
+            mm([(pn, one1, k37)]
+               + [(R(PT[h], 256 + b, 384, 8, 32 * a, 32 * a + 32), R("nf", 256 * h + b, 256 * h + 256, 8, 32 * a, 32 * a + 32),
+                   R("cb", 4 * 128, 4 * 128 + 16, 1, 32 * a, 32 * a + 32)) for a in range(4) for b in range(8)])
+            aff("n16", h, H("n16", h), pn, bias=cA)
+            if "F" in ADD[4 * h:4 * h + 4]:
+                aff("x2", h, H("xx", 2 * h + 1), xx)
+            for c in range(4 * h, 4 * h + 4):
+                if ADD[c] == "F":
+                    for e in range(2):
+                        tt(H("eg", 2 * c + e, 256), IND(R("Ef", 0, 4720), H("n16", 2 * c + e, 16)), H("xx", h, 256), add_)
+                else:
+                    aff("eg", c, H("eg", c, 512), IND(R("Ef", 0, 4720), H("n16", c, 32)))
+            pd = blk("PQ%d" % h, 3)
+            mm([(pd, I0, xx), (pd, nI, H(Gl, h))])
+            act(part("dx", h), pd, AF.Abs)
+            ts(part("ix", h), part("dx", h), 4.0, ALU.is_gt)
+            pl = R("PT0", 464 + 24 * h, 488 + 24 * h)
+            mm([(pl, part("dx", h), Wd), (pl, part("ix", h), Wi)])
+            aff("qf", h, part("qf", h), H("q16", h), bias=-1536.0)
+            if not last:
+                a, b = ((0, 656 + (t == 0)), (672, 1184))[h]
+                send("N", R(In, a, b), [R("Li%d" % t, a, b)], ["rE%d%d" % (t, h)], (b - a) // 4)
+        tt(R("hxm", 0, 48), R("PT0", 464, 512), mj, mul_)
+        scan(R("hxs", 0, 48), R("d0", 1152, 1200), R("hxm", 0, 48), mul_, add_)
+
+        def marks(PM):
+            mm([(R(PM, 256, 384, 1, 32 * e, 32 * e + 32), R("k0", 0, 32), Ib) for e in range(2)], False)
+            act(blk("R0k", 0, 64), blk(PM, 2, 64), AF.Square, bias=cLo)
+            pl = R(PM, 0, 256)
+            mm([x for h in range(2) for x in ((blk(PM, h), blk("R0k", 0, 65), Ek[h]), (blk(PM, h), part("qf", h), Ib))], 2)
+            scan(R("xsc", 0, 256), dX, pl, add_, min_)
+            tt(R("Dx", 0, 256), IND(R("xsc", 0, 256), Lend), M2, mul_)
+            mm([(pl, B16, R("Dx", 0, 256)), (blk(PM, 0), Ib, Tri), (blk(PM, 1), Ib, Tri)])
+            aff("RT", 0, R("RT", 0, 256), pl)
+            tt(R("eq", 0, 256), IND(R("xsc", 0, 256), Lend), R("RT", 0, 256), eq_)
+            mm([x for h in range(2) for x in ((R(PM, 8 * h, 8 + 8 * h), H("Dx", h), C8),
+                                              (R(PM, 8 * h, 8 + 8 * h), H("eq", h), C4k))], 2)
+            ts(R("Lx", 0, 32, 2), R(PM, 0, 16), 1536.0, add_, cJ, min_)
+            for c in range(16):
+                cp(IND(R("St", 0, 3088), R("Lx", 2 * c, 2 * c + 1)), H("xx", c + 8 * (c // 8), 16))
+        marks("PQ%d" % MARKS)
+
+        def update(h, buf, old, Wm):
+            PQ = "PQ%d" % h
+            pq = R(PQ, 0, 384)
+            mm([(blk(PQ, 0, 24), R(buf, 512 + 24 * h, 536 + 24 * h), Ib)])
             r0 = blk("R0j", h, 24)
-            act(r0, blk("PH", h, 24))
+            aff("R0j", h, r0, blk(PQ, 0, 24))
             lst = []
             for l in range(3):
                 pl = blk(PQ, l)
-                lst += [(pl, Ej[l], r0), (pl, H("mT", h), IB), (pl, Ih, H("qf", h))]
+                lst += [(pl, Ej[l], r0), (pl, part("mT", h, buf), IB), (pl, Ib, part("qf", h, buf))]
             mm(lst, 3)
-            tt(H("C1", h, 384), H(Cw, h, 384), pq, max_)
-            ts(H("K16", h, 384), H("C1", h, 384), 1.0 / 4096, mul_, 1024.625, add_)
-            mm([(blk(PQ, l), H("K16", 3 * h + l), I16h) for l in range(3)], False)
-            scan(H("wsc", h, 384), dW, pq, add_, max_)
-            cp(H("wi", h, 24), H("wsc", h, 384, 16, 15)); ts(H("wa", h, 24), H("wi", h, 24), 15, and_)
-            cp(R("wT", 64 * h + 1, 64 * h + 25), H("wa", h, 24))
-            tt(R("wT", 64 * h + 25, 64 * h + 49), H("wa", h, 24), H("wa", h, 24), mul_)
-            mm([(blk("PH", h, 49), R("wT", 64 * h, 64 * h + 49), Ib)])
-            r0 = blk("R0w", h, 49)
-            act(r0, blk("PH", h, 49))
+            tt(H("C1", h, 384), H(old, h, 384), pq, max_)
+            aff("K16", h, H("K16", h, 384), H("C1", h, 384), -1.0 / 4096, -1024.625)
+            mm([(blk(PQ, l), H("K16", 3 * h + l), I16) for l in range(3)], False)
+            scan(H("wsc", h, 384), dH, pq, add_, min_)
+            we = H("wsc", h, 384, 16, 15)
+            aff("wi", h, H("wi", h, 24), we, bias=7.5)
+            tt(R("wT", 32 * h + 1, 32 * h + 25), H("wi", h, 24), we, sub_)
+            mm([(R(PQ, 0, 128, 1, 32 * e, 32 * e + 32), H("wT", h, 32), Ib) for e in range(2)], False)
+            r0 = blk("R0w", 2 * t + h, 64)
+            act(r0, blk(PQ, 0, 64), AF.Square, bias=cLo)
             mm([(blk(PQ, l), Ep[l], r0) for l in range(3)], False)
             tt(H("C2", h, 384), H("C1", h, 384), pq, min_)
-            a = 768 + 256 * t + 128 * h
             lst = []
-            for l, w, d in ((0, Wr0, "dx"), (1, Wr1, "ix"), (2, Wr2, "dx")):
-                pl = blk(PQ, l)
-                lst += [(pl, En[l], r0), (pl, blk("ch", 4, 1), R("ch", a, a + 128, 1, 0, 1)), (pl, w, H(d, h))]
-            mm(lst, 3)
+            for l, w, d in ((0, Wr0, "dx"), (1, Wr1, "ix"), (2, Wm, "dx")):
+                lst += [(blk(PQ, l), En[l], blk("R0w", 2 * t + h, 65)), (blk(PQ, l), w, part(d, h, buf))]
+            mm(lst, 2)
             if last:
                 for l in range(3):
                     tt(H("Cf", 2 * l + h), H("C2", 3 * h + l), blk(PQ, l), max_)
             else:
-                tt(H("Cs%d" % t, h, 384), H("C2", h, 384), pq, max_)
-                send("N", H("Cs%d" % t, h, 384), [H("Cw%d" % (t + 1), h, 384)], ["rC%d%d" % (t, h)], 192)
+                tt(H("Cw%d" % (t + 1), h, 384), H("C2", h, 384), pq, max_)
+        if t == 0:
+            con(1, col(39), R("Li0", 656, 657), 4096.0); con(1, Wr3, B16, col(39))
+        for h in range(2):
+            update(h, In, Cw, Wr2) if last else update(h, "Li%d" % t, "Cr%d" % t, Wr3)
         if last:
             store("o1", ("yq", None, R("Cf", 0, 768)), [R("Cf", 0, 768)], 400)
         for h in range(2):
-            xp = blk("PA1", h) if "P" not in ADDENG[0] + ADDENG[1] else blk("PA0" if h else "PQ", 3)
-            if "V" in ADDENG[h]:
-                mm([(xp, I0, H("xx", h))])
-            for b in range(4):
-                pa, pb = "PA1", "PB%d" % (b % 2)
-                yb, db, ib = H("yy", 4 * h + b, 512), H("dd", 4 * h + b, 512), H("ind", 4 * h + b, 512)
-                if ADDENG[h][b] == "V":
-                    for k in range(4 * b, 4 * b + 4):
-                        tt(H("ind", 16 * h + k), H("eg", h, 2048, 16, k), xp, add_)
-                    ts(yb, ib, 0.0, max_, 63.0, min_)
+            for c in range(4 * h, 4 * h + 4):
+                pa, pb = "P" + BANKS[0][2 * c:2 * c + 2], "P" + BANKS[1][2 * c:2 * c + 2]
+                yb, db, ib = H("yy", c, 512), H("dd", c, 512), H("ind", c, 512)
+                if ADD[c] == "F":
+                    ts(yb, H("eg", c, 512), 0.0, max_, cN63, min_)
                 else:
-                    lst = []
-                    for kl in range(4):
-                        lst += [(blk(pa, kl), I0, H("xx", h)), (blk(pa, kl), Ib, H("eg", h, 2048, 16, 4 * b + kl))]
-                    mm(lst, 2)
+                    mm([(R(pa, 0, 512), Ib, H("eg", c, 512))] + [(blk(pa, kl), I0, H("xx", 2 * h)) for kl in range(4)])
                     ts(yb, R(pa, 0, 512), 0.0, max_, 63.0, min_)
                 mm([(R(pb, 0, 512), Ib, yb)] + [(blk(pb, kl), nI, H(Gl, h)) for kl in range(4)])
                 act(db, R(pb, 0, 512), AF.Abs)
-                if INDENG[h][b] == "V":
+                if ENG["ind"][c] == "V":
                     ts(ib, db, 4.0, ALU.is_gt)
                 else:
                     act(ib, db, AF.Sign, bias=-4.5)
                 lst = []
-                for k in range(4 * b, 4 * b + 4):
-                    pl = R(PT[h], k, 384, 16)
-                    lst += [(pl, H("dd", 16 * h + k), Wd), (pl, H("ind", 16 * h + k), Wi if INDENG[h][b] == "V" else Ws)]
+                for k in range(4 * c, 4 * c + 4):
+                    pl = R(PT[h], k % 16, 384, 16)
+                    lst += [(pl, H("dd", k), Wd), (pl, H("ind", k), Wi if ENG["ind"][c] == "V" else Ws)]
                 mm(lst, 2)
             scan(H("hsc", h, 384), dH, R(PT[h], 0, 384), add_, min_)
-            if h == EARLY:
-                ops[-1]["rd"].append(R("St", 3072, 3088))
-
-        def lanes(d, win, bank, a, c, out):
-            tt(H("Dj", d, 256), IND(win, Lb16), M2, mul_)
-            mm([x for h in range(2) for x in ((R(bank, a + 8 * h, a + 8 * h + 8), M16, c),
-                                              (R(bank, a + 8 * h, a + 8 * h + 8), H("Dj", 2 * d + h), C128))], 2)
-            cp(out, R(bank, a, a + 16))
         ends = R("hsc", 15, 768, 16)
         tt(R("t48", 0, 48), ends, R("mm", 0, 48), mul_)
-        tt(R("t48", 48, 96), ends, R("mj", 0, 48), mul_)
+        tt(R("t48", 48, 96), ends, mj, mul_)
         scan(R("ss", 0, 96), dS3, R("t48", 0, 96), mul_, add_)
         ts(R("ai", 0, 32), R("ss", 2, 96, 3), 15.0, add_)
         ts(R("jba", 0, 32), R("ai", 0, 32), 15, and_)
-        lanes(0, R("jba", 0, 16), "PT0", 448, Cp, R("Lab", 0, 16))
+        tolist("Db", 0, R("jba", 0, 40), Lz2, H("Dj", 0), R("PT0", 448, 464), 128.0, Cp2)
+        aff("Lab", 0, R("Lab", 0, 16), R("PT0", 448, 464))
         for h in range(2):
-            mov(YBENG[h], H(Sb, h), IND(H("yy", h, 2048), H("Lab", h, 8)))
+            aff("yb", h, H(Sb, h), IND(H("yy", h, 2048), H("Lab", h, 8)))
         tt(go, R("ai", 16, 32), R("hxs", 2, 48, 3), ALU.is_lt)
         if not last:
             tt(R("gt", 0, 16), go, R("dj", 0, 16), mul_)
-            tt(R(Sb, 368, 384), R("gt", 0, 16), R("jalt", 0, 16), add_)
-            lanes(1, R(Sb, 368, 384), "PT1", 448, sm(48), R(Sb, 352, 368))
-        w = 256 if last else 400
+            tt(R(Sb, 256, 272), R("gt", 0, 16), R("jalt", 0, 16), add_)
+            tolist("Dj", 0, R(Sb, 256, 304), Lz2, H("Dj", 1), R("PT1", 448, 464), 128.0, Cp2)
+            aff("SL", 0, R("SL%d" % t, 0, 16), R("PT1", 448, 464))
+            send("N", R("SL%d" % t, 0, 16), [R("LJ%d" % (t + 1), 0, 16)], ["rL%d" % t], 4)
+        w = 256 if last else 288
         send("N", R(Sb, 0, w), [R("Lb%d" % t, 0, w)], ["rB%d" % t], w // 4)
-        lanes(2, R("jba", 16, 32), "PT0", 464, Cp, R("Lab", 16, 32))
+        tolist("Da", 0, R("jba", 0, 40), Lz3, H("Dj", 2), R("PT0", 432, 448), 128.0, Cp2)
+        aff("Laa", 0, R("Lab", 16, 32), R("PT0", 432, 448))
         for h in range(2):
-            act(H("St", 2 * t + h), IND(H("yy", h, 2048), H("Lab", 2 + h, 8)))
+            aff("ya", h, H("St", 2 * t + h), IND(H("yy", h, 2048), H("Lab", 2 + h, 8)))
         if last:
             tt(R("t12", 0, 48), IND(go, Lgo), mj12, mul_)
             tt(R("mj4", 0, 48), Pinc, lv, sub_)
@@ -526,12 +577,12 @@ def build(case=None):
                 tt(R("Pfin", h, 48, 2), H("mj4", h, 24), H("t12", h, 24), add_)
         if not last:
             pl = R("PT0", 416, 417, 1, 0, 8)
-            mm([(pl, R(Sb, 384 + 8 * h, 392 + 8 * h), R("cb", 12 * 128, 12 * 128 + 1)) for h in range(2)])
-            act(R("cnt", 0, 1, 1, 0, 8), pl)
+            mm([(pl, R(Sb, 272 + 8 * h, 280 + 8 * h), R("cb", 12 * 128, 12 * 128 + 1)) for h in range(2)])
+            aff("cnt", 0, R("cnt", 0, 1, 1, 0, 8), pl)
             mm([(R("PT0", 424, 425), E8, R("cnt", 0, 1, 1, 0, 8))])
-            cp(R("Ai", 0, 1), R("PT0", 424, 425)); ts(R("Aa", 0, 1), R("Ai", 0, 1), 63, and_)
-            ts(R("cA", 0, 1), R("Aa", 0, 1), cK37, add_)
-            act(R("St", 256 * (3 + t), 256 * (4 + t)), R("Lb%d" % t, 0, 256))
+            aff("Ai", 0, R("Ai", 0, 1), R("PT0", 424, 425)); ts(R("Aa", 0, 1), R("Ai", 0, 1), 63, and_)
+            aff("cA", 0, R("cA", 0, 1), R("Aa", 0, 1), bias=2048.0)
+            aff("Lb", 0, R("St", 256 * (3 + t), 256 * (4 + t)), R("Lb%d" % t, 0, 256))
         else:
             mm([(blk("PA0", 0, 48), R("Pfin", 0, 48), Iq)])
             act(blk("Pout", 0, 48), blk("PA0", 0, 48))
@@ -543,231 +594,196 @@ def build(case=None):
     return ops
 
 
-def sched(ops, pre, pri, banks):
-    n = len(ops)
-    succ = [[] for _ in range(n)]
-    cnt = [len(p) for p in pre]
-    for i in range(n):
-        for j in pre[i]:
-            succ[j].append(i)
-    qq = [o["q"] for o in ops]
-    cost = [o["cost"] for o in ops]
-    free = dict((q, 0.0) for q in qq)
-    bank = {}
-    fin = [0.0] * n
-    est = [0.0] * n
-    t0 = [0.0] * n
-    ex = [None] * n
-    ready = [i for i in range(n) if cnt[i] == 0]
-    out = []
-    while ready:
-        st = {}
-        a, lim = -1, 1e30
-        for i in ready:
-            s = max(est[i], free[qq[i]])
-            for b in banks[i]:
-                for q, j in bank.get(b, {}).items():
-                    if q != qq[i] and fin[j] + LAT > s:
-                        s = fin[j] + LAT
-            st[i] = s
-            if s + cost[i] < lim:
-                a, lim = i, s + cost[i]
-        i = max([k for k in ready if qq[k] == qq[a] and st[k] < lim + LOOK or k == a],
-                key=lambda k: (pri[k] - WAITW * max(0.0, st[k] - st[a]), -k))
-        ready.remove(i)
-        t0[i] = st[i]
-        if qq[i] != "R":
-            free[qq[i]] = st[i] + cost[i]
-        fin[i] = st[i] + cost[i] + ops[i].get("lat", 0)
-        ex[i] = []
-        for b in banks[i]:
-            ex[i] += [j for q, j in bank.get(b, {}).items() if q != qq[i]]
-            bank.setdefault(b, {})[qq[i]] = i
-        out.append(i)
-        for k in succ[i]:
-            est[k] = max(est[k], fin[i] + pre[k][i])
-            cnt[k] -= 1
-            if cnt[k] == 0:
-                ready.append(k)
-    return out, t0, fin, ex
-
-
-def replay(ops, f, pre, cost, lat):
-    fin = [0.0] * len(ops)
-    free = {}
-    for i in f[0]:
-        q = ops[i]["q"]
-        s = free.get(q, 0.0)
-        for j, x in pre[i].items():
-            s = max(s, fin[j] + (x * lat if x <= LAT else x))
-        for j in f[3][i]:
-            s = max(s, fin[j] + LAT * lat)
-        if q != "R":
-            free[q] = s + cost[i]
-        fin[i] = s + cost[i] + ops[i].get("lat", 0)
-    return max(fin)
-
-
-def polish(ops, idx, pre, post, banks, cases, rng):
-    n = len(ops)
-    qn = [" VSPGY".find(o["q"]) for o in ops]
-    lat = [o.get("lat", 0) for o in ops]
-    names = sorted(set(b for l in banks for b in l))
-    bk = [[names.index(b) for b in l] for l in banks]
-    sets = [([o["cost"] for o in ops], 1.0)] + [cases[k] for k in MIX]
-    pl = [[[(j, x * f if x <= LAT else x) for j, x in pre[i].items()] for i in range(n)] for c, f in sets]
-
-    def run(idx, k):
-        cost, w, p = sets[k][0], LAT * sets[k][1], pl[k]
-        fin = [0.0] * n
-        why = [-1] * n
-        free = [0.0] * 6
-        who = [-1] * 6
-        bank = [[-1] * 6 for _ in names]
-        for i in idx:
-            q = qn[i]
-            s, y = (free[q], -2 - who[q]) if q > 0 else (0.0, -1)
-            for j, x in p[i]:
-                if fin[j] + x > s:
-                    s, y = fin[j] + x, j
-            for b in bk[i]:
-                l = bank[b]
-                for j in l:
-                    if j >= 0 and qn[j] != q and fin[j] + w > s:
-                        s, y = fin[j] + w, -2 - j
-                l[q] = i
-            if q > 0:
-                free[q], who[q] = s + cost[i], i
-            fin[i] = s + cost[i] + lat[i]
-            why[i] = y
-        return fin, why
-
-    def total(idx):
-        r = [run(idx, k) for k in range(len(sets))]
-        return sum(max(x[0]) for x in r), r
-
-    cur, res = total(idx)
-    low, keep = cur, idx
-    pairs = []
-    for it in range(SWAPS):
-        if not pairs:
-            fin, why = res[int(rng.integers(0, len(sets)))]
-            i = max(range(n), key=lambda k: fin[k])
-            while why[i] != -1:
-                j = why[i] if why[i] >= 0 else -2 - why[i]
-                if why[i] < -1 and j not in pre[i]:
-                    pairs.append((j, i))
-                i = j
-            pos = [0] * n
-            for p, k in enumerate(idx):
-                pos[k] = p
-            if not pairs:
-                break
-        j, i = pairs.pop(int(rng.integers(0, len(pairs))))
-        a, b = pos[j], pos[i]
-        mid = idx[a:b + 1]
-        if rng.random() < 0.5:
-            mv = {i}
-            for k in reversed(mid[:-1]):
-                if any(s in mv for s in post[k]):
-                    mv.add(k)
-            if j in mv:
-                continue
-            new = idx[:a] + [k for k in mid if k in mv] + [k for k in mid if k not in mv] + idx[b + 1:]
-        else:
-            mv = {j}
-            for k in mid[1:]:
-                if any(s in mv for s in pre[k]):
-                    mv.add(k)
-            if i in mv:
-                continue
-            new = idx[:a] + [k for k in mid if k not in mv] + [k for k in mid if k in mv] + idx[b + 1:]
-        v, r = total(new)
-        if v < cur + HEAT * (1.0 - it / SWAPS) * float(rng.random()) ** 3:
-            cur, res, idx, pairs = v, r, new, []
-            if v < low:
-                low, keep = v, new
-    fin = run(keep, 0)[0]
-    ex = [None] * n
-    bank = {}
-    for i in keep:
-        ex[i] = []
-        for b in banks[i]:
-            ex[i] += [j for q, j in bank.get(b, {}).items() if q != qn[i]]
-            bank.setdefault(b, {})[qn[i]] = i
-    return keep, [fin[i] - lat[i] - ops[i]["cost"] for i in range(n)], fin, ex
-
-
-def order(ops):
+def depends(ops):
     n = len(ops)
     hard = [set() for _ in range(n)]
+    soft = [set() for _ in range(n)]
     seen = {}
     for o in ops:
         i = o["n"]
         for r in o["rd"]:
             hard[i].update(j for (j, r2, w) in seen.get(r[1], []) if w and clash(r, r2))
         for r in o["wr"]:
-            hard[i].update(j for (j, r2, w) in seen.get(r[1], []) if clash(r, r2))
+            for (j, r2, w) in seen.get(r[1], []):
+                if clash(r, r2):
+                    (soft if ops[j]["q"] == o["q"] == "P" and not o["args"][2] else hard)[i].add(j)
         for r in o["wr"]:
             l = [e for e in seen.get(r[1], []) if not (r[4] == 1 and r[5] <= e[1][5] and e[1][6] <= r[6] and r[2] <= e[1][2] and e[1][3] <= r[3])]
             seen[r[1]] = l + [(i, r, True)]
         for r in o["rd"]:
             seen.setdefault(r[1], []).append((i, r, False))
         hard[i].discard(i)
+    mms = [o for o in ops if o["kind"] == "mm"]
+    for a in mms:
+        if a["args"][2] != a["args"][3]:
+            for b in mms:
+                if b["wr"][0][1] == a["wr"][0][1]:
+                    if b["n"] < a["n"]:
+                        soft[a["n"]].add(b["n"])
+                    if b["n"] > a["n"] and a["args"][3]:
+                        soft[b["n"]].add(a["n"])
     pre = []
     for i in range(n):
         p = dict((j, LATS if ops[j]["q"] == ops[i]["q"] and "sem" not in ops[j] else LAT) for j in hard[i])
-        pre.append({ops[i]["after"][0]: ops[i]["after"][1]} if "after" in ops[i] else p)
-    post = [dict() for _ in range(n)]
+        p.update((j, 0.0) for j in soft[i] if j not in hard[i] and j != i)
+        pre.append(ops[i].get("after", p))
+    return hard, pre
+
+
+def above(l, x):
+    a, b = 0, len(l)
+    while a < b:
+        m = (a + b) // 2
+        if l[m] <= x:
+            a = m + 1
+        else:
+            b = m
+    return a
+
+
+def place(key, pre, rel, cost, qn, bk):
+    qs, qe = [[] for _ in range(6)], [[] for _ in range(6)]
+    bs, be, bq = [[] for _ in range(8)], [[] for _ in range(8)], [[] for _ in range(8)]
+    fin = [0.0] * len(key)
+    for i in key:
+        s = rel[i]
+        for j, d in pre[i]:
+            if fin[j] + d > s:
+                s = fin[j] + d
+        q, c = qn[i], cost[i]
+        if q:
+            S, E = qs[q], qe[q]
+            while True:
+                m = len(S)
+                k = m if not m or E[-1] <= s else above(E, s)
+                while k < m and S[k] < s + c:
+                    s = E[k]
+                    k += 1
+                s0 = s
+                for b in bk[i]:
+                    X, Y, Z = bs[b], be[b], bq[b]
+                    w = len(X)
+                    u = w if not w or Y[-1] <= s - LAT else above(Y, s - LAT)
+                    while u < w and X[u] < s + c + LAT:
+                        if Z[u] != q and Y[u] + LAT > s:
+                            s = Y[u] + LAT
+                        u += 1
+                if s == s0:
+                    break
+            S.insert(k, s); E.insert(k, s + c)
+            for b in bk[i]:
+                u = above(bs[b], s)
+                bs[b].insert(u, s); be[b].insert(u, s + c); bq[b].insert(u, q)
+        fin[i] = s + c
+    return np.array(fin)
+
+
+def replay(idx, pre, cost, lat, qn, bk, f):
+    fin = [0.0] * len(idx)
+    free = [0.0] * 6
+    bank = [[0.0] * 6 for _ in range(8)]
+    for i in idx:
+        q = qn[i]
+        s = free[q] if q else 0.0
+        for j, x in pre[i].items():
+            y = fin[j] + lat[j] + (x * f if x <= LAT else x)
+            if y > s:
+                s = y
+        for b in bk[i]:
+            for p, y in enumerate(bank[b]):
+                if p != q and y > s:
+                    s = y
+        fin[i] = free[q] = s + cost[i]
+        for b in bk[i]:
+            bank[b][q] = fin[i] + LAT * f
+    return max(x + y for x, y in zip(fin, lat))
+
+
+def search(ops, pre, rounds, start=None):
+    n = len(ops)
+    lat = [o.get("lat", 0) for o in ops]
+    cost = [o["cost"] for o in ops]
+    qn = [max(0, " VSPGY".find(o["q"])) for o in ops]
+    names = [k for k, v in SCRATCH.items() if v[0] == "psum"]
+    bk = [sorted(set(names.index(r[1]) for r in o["rd"] + o["wr"] if inps(r))) for o in ops]
+    fw = [[(j, d + lat[j]) for j, d in pre[i].items()] for i in range(n)]
+    bw = [[] for _ in range(n)]
     for i in range(n):
-        for j in pre[i]:
-            post[j][i] = pre[i][j] + ops[j].get("lat", 0) - ops[i].get("lat", 0)
-    banks = [sorted(set(r[1] for r in o["rd"] + o["wr"] if inps(r))) for o in ops]
-    pri = [0.0] * n
-    for i in range(n - 1, -1, -1):
-        pri[i] = ops[i]["cost"] + ops[i].get("lat", 0) + max([pri[k] + pre[k][i] for k in post[i]] + [0.0])
-    cases = [([o["cost"] for o in build(c[:3])], c[3]) for c in CASES]
-    rng = np.random.default_rng(SEED)
-    fine, wide = [], []
+        for j, d in fw[i]:
+            bw[j].append((i, d))
+    la, ca, zero, up = np.array(lat), np.array(cost), [0.0] * n, np.arange(n)
+    others = [([o["cost"] for o in build(c)], c[3]) for c in CASES]
+    kin = []
     for o in ops:
         r = o["wr"][0] if o["wr"] else o["rd"][0]
-        nm = r[1][:2] if r[1][:2] in ("Cs", "Sb", "Cw", "Lb") else r[1]
-        h = int(2 * r[2] >= SCRATCH[r[1]][1][1]) if nm[0] != "P" else r[2] // 128
-        fine.append((nm, h, o["q"], o["kind"]))
-        wide.append([k for k, s in enumerate(KINS) if nm in s.split()] + [-1])
-    wide = [(w[0], f[1] if f[0][0] != "P" else 0) for w, f in zip(wide, fine)]
-    base = np.array(pri) + np.array([LEAD[w[0]][w[1]] if w[0] >= 0 else 0.0 for w in wide])
-    low = max(sched(ops, pre, list(base), banks)[2])
-    for tags, rounds in ((wide, TRY[0]), (fine, TRY[1])):
-        names = sorted(set(tags))
-        tg = np.array([names.index(x) for x in tags])
-        for it in range(rounds):
-            off = np.zeros(len(names))
-            off[rng.integers(0, len(names), int(rng.integers(1, 4)))] = rng.normal(0.0, 2500.0)
-            v = max(sched(ops, pre, list(base + off[tg]), banks)[2])
-            if v <= low:
-                low, base = v, base + off[tg]
-    pri = list(base)
-    best = None
-    for it in range(ROUNDS):
-        f = sched(ops, pre, pri, banks)
-        if best is None or max(f[2]) < 1.02 * max(best[2]):
-            v = max(f[2]) + sum(replay(ops, f, pre, c, lat) for c, lat in cases)
-            if best is None or v < best[4]:
-                best = f + (v,)
-        jit = JIT * float(rng.random()) ** 2
-        if it % 2:
-            pri = [-x + float(z) * jit for x, z in zip(best[1], rng.random(n))]
+        ps = inps(r)
+        kin.append((r[1] if ps else r[1].rstrip("012"), r[2] // 128 if ps else int(2 * r[2] >= SCRATCH[r[1]][1][1]), o["q"], o["kind"]))
+    kinds = sorted(set(kin))
+    kin = np.array([kinds.index(x) for x in kin])
+
+    def forward(key):
+        key = list(key)
+        for i in range(n):
+            for j, d in fw[i]:
+                if key[j] > key[i]:
+                    key[i] = key[j]
+        return place(np.lexsort((up, key)).tolist(), fw, zero, cost, qn, bk)
+
+    def turn(f):
+        b = place(np.lexsort((-up, -f)).tolist(), bw, lat, cost, qn, bk)
+        return place(np.lexsort((up, -b)).tolist(), fw, zero, cost, qn, bk)
+
+    def worth(f):
+        idx = np.lexsort((up, f - ca)).tolist()
+        return [float((f + la).max())] + [replay(idx, pre, c, lat, qn, bk, w) for c, w in others]
+
+    if start is None:
+        tail = [0.0] * n
+        for i in range(n - 1, -1, -1):
+            tail[i] = cost[i] + max([lat[i]] + [tail[k] + d for k, d in bw[i]])
+        start = -np.array(tail)
+    f = turn(turn(forward(start)))
+    rng = np.random.default_rng(SEED)
+    v = worth(f)
+    cur, cf, low, best = v, f, v, f
+    for it in range(rounds):
+        key = cf - ca
+        m = rng.random()
+        if m < 0.5:
+            off = np.zeros(len(kinds))
+            off[rng.integers(0, len(kinds), int(rng.integers(1, 4)))] = rng.normal(0.0, 1500.0)
+            key = key + off[kin]
+        elif m < 0.8:
+            key = key + (np.abs(key - rng.random() * cur[0]) < 2500) * rng.normal(0.0, 500.0, n)
         else:
-            b = sched(ops, post, [x + float(z) * jit for x, z in zip(best[2], rng.random(n))], banks)
-            pri = [x + float(z) * jit for x, z in zip(b[2], rng.random(n))]
-    best = polish(ops, best[0], pre, post, banks, cases, rng)
-    idx, t0, fin, ex = best[:4]
-    TIMES[:] = [max(fin)] + [replay(ops, best, pre, c, lat) for c, lat in cases]
-    out = [ops[i] for i in idx]
+            key = key + rng.normal(0.0, 150.0, n)
+        f = forward(key)
+        if (f + la).max() < cur[0] + 3000:
+            g = turn(f)
+            if (g + la).max() <= (f + la).max():
+                f = g
+        if (f + la).max() < cur[0] + 600:
+            v = worth(f)
+            if sum(v) + v[0] < sum(cur) + cur[0] + 1500.0 * (1.0 - it / rounds) * rng.random() ** 2:
+                cur, cf = v, f
+                if sum(v) + v[0] < sum(low) + low[0]:
+                    low, best = v, f
+    TIMES[:] = low
+    return best - ca, qn, bk
+
+
+def order(ops):
+    hard, pre = depends(ops)
+    t0, qn, bk = search(ops, pre, ROUNDS)
+    out = [ops[i] for i in np.lexsort((np.arange(len(ops)), t0)).tolist()]
+    bank = {}
     for o in out:
-        o["t0"], o["t1"] = t0[o["n"]], fin[o["n"]]
-        o["w"] = set() if o["q"] == "R" else set(j for j in hard[o["n"]] | set(ex[o["n"]]) if ops[j]["kind"] != "send")
+        i = o["n"]
+        ex = set()
+        for b in bk[i]:
+            ex.update(j for q, j in bank.get(b, {}).items() if q != qn[i])
+            bank.setdefault(b, {})[qn[i]] = i
+        o["w"] = set() if o["q"] in "RL" else set(j for j in hard[i] | ex if ops[j]["kind"] != "send")
     pos = {}
     for p, o in enumerate(out):
         pos[o["n"]] = p
@@ -841,7 +857,7 @@ def rank_program(g, core, T, topo):
     nin = len(topo.engines(prv, core))
     lsum = 0
     for o in out:
-        if o["q"] == "R":
+        if o["q"] in "RL":
             continue
         q = Q[o["q"]]
         for s, j in o["need"]:
@@ -867,7 +883,8 @@ def rank_program(g, core, T, topo):
         elif k == "mm":
             m = len(a[0]) if a[1] is True else max(1, int(a[1]))
             for i, (oo, l, rr) in enumerate(a[0]):
-                ins = q.matmul(ap(T, oo), ap(T, l), ap(T, rr), i % m == 0, i % m == m - 1)
+                more = any(x[0][5] < oo[6] and oo[5] < x[0][6] for x in a[0][i + 1:i - i % m + m])
+                ins = q.matmul(ap(T, oo), ap(T, l), ap(T, rr), i % m == 0 and a[2], (a[3] or not a[2]) and not more)
         elif k == "iota":
             if dty(a[0]) == I32:
                 ins = q.iota(ap(T, a[0]), a[1], a[2], a[3])

@@ -23,49 +23,60 @@ for _n, _c, _d in (
     ("C1", 768, I32), ("C2", 768, I32), ("K16", 768, F16), ("wsc", 768, F32),
     ("Sb0", 400, BF), ("Sb1", 400, BF), ("Sb2", 400, BF), ("Lb0", 400, BF), ("Lb1", 400, BF), ("Lb2", 256, BF),
     ("sg", 4096, BF), ("smx", 4096, BF), ("eg", 4096, BF), ("yy", 4096, BF), ("dd", 4096, BF), ("ind", 4096, BF),
-    ("P40", 48, BF), ("pmin", 48, F32), ("mj", 48, BF), ("mm", 48, BF), ("ji", 16, I32), ("jj", 16, I32),
-    ("mj4", 48, BF), ("pm2", 48, F32), ("ji2", 16, I32), ("jalt", 16, I32),
-    ("dj", 16, F32), ("LJ0", 16, U16), ("LJ1", 16, U16), ("LJ2", 16, U16), ("SL0", 16, U16), ("SL1", 16, U16), ("R0j", 256, BF),
+    ("P40", 48, BF), ("pmin", 48, I32), ("mm", 48, BF), ("jj", 16, I32), ("mj4", 48, BF), ("pm2", 48, I32), ("jalt", 40, I32),
+    ("k0i", 32, I32), ("uvh", 16, BF), ("xn", 16, F16), ("rep", 16, F32), ("xu", 40, F32), ("sh", 272, BF),
+    ("dj", 40, F32), ("LJ0", 16, U16), ("LJ1", 16, U16), ("LJ2", 16, U16), ("SL0", 16, U16), ("SL1", 16, U16), ("R0j", 256, BF),
     ("wd", 240, BF), ("mb", 512, BF), ("t12", 48, BF), ("Pfin", 48, BF), ("Pout", 128, F32),
-    ("q32", 256, I32), ("q16", 256, U16), ("qf", 256, F16), ("key", 256, F16), ("msc", 256, F32),
-    ("mi", 16, F16), ("k0", 32, BF), ("Dk", 256, BF), ("Lk", 16, U16), ("xx", 512, BF),
-    ("uvi", 16, I32), ("uva", 16, I32), ("Du", 288, BF), ("Lo", 16, U16), ("u32", 256, F32), ("tO", 256, I32),
-    ("na", 256, I32), ("n16", 256, U16), ("dx", 256, BF), ("ix", 256, BF), ("nf", 512, F16),
-    ("hxm", 48, F32), ("hxs", 48, F32), ("hsc", 768, F32), ("t48", 96, F32), ("ss", 96, F32), ("ai", 32, I32),
-    ("jba", 40, I32), ("gt", 16, F32), ("Dj", 384, BF), ("Lab", 32, U16), ("ya", 16, BF),
+    ("q32", 256, I32), ("q16", 256, U16), ("key", 256, F16), ("msc", 256, I32),
+    ("k0", 32, BF), ("Dk", 256, BF), ("Lk", 16, U16), ("xx", 1024, BF),
+    ("uvi", 16, I32), ("uva", 32, I32), ("Du", 256, BF), ("Lo", 16, U16), ("u32", 256, F32), ("tO", 256, I32),
+    ("na", 256, I32), ("n16", 256, U16), ("dx", 256, BF), ("ix", 256, BF),
+    ("hxm", 48, F32), ("hxs", 48, F32), ("hsc", 768, F32), ("t48", 96, F32), ("ss", 96, I32),
+    ("jba", 72, I32), ("gt", 16, F32), ("Dj", 640, BF), ("Lab", 32, U16), ("ya", 16, BF),
     ("mT", 256, BF), ("wi", 48, F16), ("wT", 64, BF), ("R0w", 768, F16),
-    ("R0k", 128, BF), ("xsc", 256, F32), ("Dx", 256, F16), ("RT", 256, F32), ("eq", 256, BF),
+    ("R0k", 128, BF), ("xsc", 256, F32), ("Dx", 128, F16),
     ("Lx", 32, U16), ("cnt", 16, BF), ("Ai", 16, I32), ("Aa", 16, I32), ("cA", 16, F32),
-    ("ci", 16, I32), ("cf", 48, F32), ("cb", 2560, BF), ("ce", 1792, BF), ("d0", 1296, BF), ("k37", 128, F16),
-    ("d0c", 128, F32), ("cl", 64, U16), ("tf", 768, F32), ("tb", 512, BF), ("m2", 256, BF), ("kz", 384, BF),
+    ("ci", 16, I32), ("cf", 48, F32), ("cb", 2560, BF), ("ce", 1792, BF), ("d0", 1536, BF), ("k37", 128, F16),
+    ("d0c", 128, F32), ("cl", 64, U16), ("tf", 768, F32), ("tb", 640, BF), ("m2", 272, BF), ("kz", 384, BF),
 ):
     _sb(_n, _c, _d)
+SCRATCH["nf"] = ("sbuf", [128, 16, 32], F16)
 for _n in ("PA0", "PA1", "PB0", "PB1", "PT0", "PT1", "PQ0", "PQ1"):
     _sb(_n, 512, F32, "psum")
 
 LOADS = ("tu", "qn", "qk", "st0", "gl", "rm", "ot", "ef", "ef2")
-STORES = ("o1", "o2", "o3", "o4", "o5", "o6", "o7")
+STORES = ("o1", "o2", "o3", "o4", "o5", "o6")
+ISSUE = 300.0
+YQ = ((0, 768),)
 SEMAPHORES = (["cV", "cS", "cP", "cG", "lsem", "rG1", "rG2", "rC0", "rC1", "rB0", "rB1", "rB2",
                "rE00", "rE01", "rE10", "rE11", "rL0", "rL1"]
-              + ["l" + n for n in LOADS] + list(STORES))
+              + ["l" + n for n in LOADS] + list(STORES) + ["d%d%d" % (t, c) for t in range(RO) for c in range(8)])
 
-ENG = dict(sg="VVSSSSSS", eg="SSSSSSSS", ind="SVVVVVVV",
-           q16="VS", key="SV", mi="VV", Lk="VS", xx="VS", u32="SS", uvi="VV", Lo="VV", n16="SS", qf="VS", mT="SS",
-           K16="SS", wi="VS", R0j="SS", Lab="S", Laa="V", SL="S", yb="VS", ya="SS", Lb="V", Ai="S", cA="S", ji2="S",
-           RT="S", Cw="VS", cnt="S", LJ="VS", nf0="SS", nf1="VS", x2="VV", mj4="S", mj12="S",
-           Dk="SS", Db="S", Dj="S", Da="S", rm="S", c0="V" * 24, c1="S" * 60)
+ENG = dict(sg="VVSSVSSS", eg="SSSSSSSS", ind="VVVVVVVV",
+           q16="VS", key="SS", Lk="VS", xx="VS", u32="SS", uvi="VS", Lo="VS", n16="VS", qf="SS", mT="SS",
+           K16="SS", wi="SS", R0j="SS", Lab="SS", Laa="S", SL="S", yb="VS", ya="SS", Lb="VV", Dd="S", Ai="S", cA="S",
+           Cw="SS", cnt="S", LJ="VS", nf0="VV", nf1="SS", x2="VV", Pinc="S", mj12="S",
+           Dk="SS", Db="SS", Dj="S", Da="S", rm="S", k0="S", xn="S", Du="SS", x4="VV", Dx="S", c0="V" * 24, c1="S" * 60)
 PARTS = ("mT", "qf", "dx", "ix")
 WIDEK = "wn"
-ADD = "FPFPFPFP"
-BANKS = ("A0A0A0A0A0A0A0A0", "B0B1A1B0B1A1B0B1")
-DIRECT = False
+WIDEU = "ww"
+FOLD = False
+ADDS = ("DDFFDDFF",) * 3
+BANKS = ("A0A0A0A0A0A0A0A0", "B0B1A1A0B0B1A1A0")
+FILL = (0, 0)
+AHEAD = False
+SHARE = 0.3
+FOUR = True
+DMA = (1000.0, 800.0, 1100.0)
+LINK = (600.0, 1000.0, 150.0, 13.0)
 MKSPLIT = True
 MARKS = 1
-BASE = (0.52, 1.56, 3.8, 1.0)
-CASES = ((0.75, 1.56, 3.8, 1.0), (0.52, 1.2, 2.5, 1.5))
+BASE = (0.52, 1.56, 3.8, 1.0, 1.0)
+CASES = ((0.6, 1.9, 5.0, 0.8, 0.8), (0.52, 1.2, 2.5, 1.3, 1.3))
 LAT, LATS = 180.0, 110.0
 BACK = 3
-SEED, ROUNDS = 1, 8000
+SEED, ROUNDS = 1, 13000
+MOVES = (0.5, 1500.0, 1e9, 0.8, 2500.0, 500.0, 150.0, 3000.0, 500.0)
 TIMES = []
 
 
@@ -80,7 +91,7 @@ def IND(win, off):
 def nel(r):
     if r[0] == "i":
         return 16 * nel(r[2])
-    return (r[3] - r[2] + r[4] - 1) // r[4]
+    return (r[3] - r[2] + r[4] - 1) // r[4] * (r[7] if len(r) > 7 else 1)
 
 
 def dty(r):
@@ -110,6 +121,10 @@ def ap(T, r):
         return r
     if r[0] == "i":
         return ap(T, r[1]).indirect(ap(T, r[2]))
+    if r[1] == "nf":
+        if len(r) > 7:
+            return T["nf"][:, r[2] // 32:r[3] // 32, r[2] % 32:r[2] % 32 + r[7]]
+        return T["nf"][r[5]:r[6], r[2] // 32, :]
     if r[4] == 1:
         return T[r[1]][r[5]:r[6], r[2]:r[3]]
     return T[r[1]][r[5]:r[6], r[2]:r[3]:r[4]]
@@ -117,7 +132,7 @@ def ap(T, r):
 
 def build(case=None):
     ops = []
-    PC, GC, SC = (case or BASE)[:3]
+    PC, GC, SC, _, DF = case or BASE
 
     def add(q, kind, args, rd, wr, cost, **kw):
         o = dict(q=q, kind=kind, args=args, rd=flat(rd), wr=flat(wr), cost=cost, n=len(ops))
@@ -169,17 +184,21 @@ def build(case=None):
             ts(out, a, scale, ALU.mult, bias, ALU.add)
         ops[-1]["tag"] = (key, h)
 
-    def mm(lst, chain=True, first=True, final=True):
+    def mm(lst, chain=True, first=True, final=True, stop=False):
         c = sum(max(min(64, nel(l)), nel(r)) for (_, l, r) in lst) * PC + 30
-        add("P", "mm", (lst, chain, first, final), [x for (_, l, r) in lst for x in (l, r)], [o for (o, _, _) in lst], c)
+        add("P", "mm", (lst, chain, first, final, final or stop), [x for (_, l, r) in lst for x in (l, r)], [o for (o, _, _) in lst], c)
 
+    early = R("ya", 8, 9)
     turn = R("ya", 2, 3)
 
     def iota(out, pat, base, cm):
         add("G", "iota", (out, pat, base, cm), [turn], [out] + [turn] * (out[5] > 0), 130 + 2 * nel(out))
 
     def fill(out, v):
-        iota(out, [[0, nel(out)]], int(v), 0)
+        if FILL[0] <= nel(out) <= FILL[1]:
+            iota(out, [[0, nel(out)]], int(v), 0)
+        else:
+            ms(out, int(v) if dty(out) == I32 else float(v))
 
     def asel(out, a, pat, base, cm, op=ALU.is_equal, fill=0.0):
         add("G", "asel", (out, a, pat, base, cm, op, fill), [a, turn], [out] + [turn] * (out[5] > 0), 170 + 2 * nel(out))
@@ -188,15 +207,22 @@ def build(case=None):
         add(q, "load", (name, out), list(behind), [out], 60, sem="l" + name, lat=1800 + kb * 5.0)
 
     def store(sem, fn, rd, kb):
-        add("Y", "store", (sem, fn), rd, [], 60, sem=sem, lat=1800 + kb * 5.0)
+        s = add("Y", "store", (sem, fn), rd, [], ISSUE, sem=sem)
+        add("L", "work", (), [], [R("ya", 6, 7)], SHARE * (200.0 + kb * 5.0) * DF, after={s["n"]: 700.0},
+            lat=700.0 + (1 - SHARE) * (200.0 + kb * 5.0))
 
     def send(kind, src, dst, sem, kb):
-        s = add("G", "send", (kind, src, dst, sem), [src], [R("ya", 0, 1)], 600)
-        after = dict((o["n"], 0.0) for o in ops if o["q"] == "L")
-        after[s["n"]] = 1000.0
-        w = add("L", "link", (kind,), [], [R("ya", 4, 5)], kb * 14.0, after=after)
+        s = add("G", "send", (kind, src, dst, sem), [src] + [R("Qn", 0, 768)] * (kind == "A"), [R("ya", 0, 1)], LINK[0])
+        after = dict((o["n"], 0.0) for o in ops if o["kind"] == "link")
+        after[s["n"]] = LINK[1]
+        w = add("L", "link", (kind,), [], [R("ya", 4, 5)], (LINK[2] + kb * LINK[3]) * DF, after=after)
         for d, sm in zip(dst, sem):
             add("R", "recv", (kind,), [], [d], 0, sem=sm, lat=0, after={w["n"]: 400.0})
+
+    def total(out, a, sem):
+        s = add("G", "sum", (out, a, sem), [out, a], [], DMA[0] * DF)
+        w = add("L", "work", (), [], [R("ya", 6, 7)], SHARE * DMA[2] * DF, after={s["n"]: DMA[1] * DF})
+        add("R", "recv", (), [a], [out], 0, sem=sem, lat=0, after={w["n"]: 400.0 + (1 - SHARE) * DMA[2] * DF})
 
     add_, sub_, mul_, max_, min_ = ALU.add, ALU.subtract, ALU.mult, ALU.max, ALU.min
     eq_, and_, shr_ = ALU.is_equal, ALU.bitwise_and, ALU.arith_shift_right
@@ -229,17 +255,17 @@ def build(case=None):
     con(0, cP, iP); con(0, cB, iB); con(0, cAa, iA); con(0, c16P, iP, 16.0)
     ts(cN15, iB, 15.0, ALU.is_lt); ts(cF15, iB, 15.0, eq_); ts(cF64k, iB, 15.0, eq_, 65536.0, mul_)
     con(0, col(20), iB, 2.0, 1.0); con(0, cU, col(20), cN15)
-    for d, a, c in ((cM16, R("Rm", 0, 1), 16.0), (cM4k, R("Rm", 0, 1), 4096.0), (cN16, cN15, 16.0), (cN4k, cN15, 4096.0),
+    for d, a, c in ((cM16, R("Rm", 0, 1), -16.0), (cM4k, R("Rm", 0, 1), 4096.0), (cN16, cN15, -16.0), (cN4k, cN15, 4096.0),
                     (cN64k, cN15, 65536.0), (cN63, cN15, 63.0)):
         con(1, d, a, c)
-    con(1, cJ, iB, 1.0, 3072.0); con(1, cSg, cN15, 2048.0, -1920.0)
-    Ib, I0, nI, IB, M16, kk, gg, B16, Wu, Wr0, Wr1, Wr2, One, I16, Tri = [blk("cb", j) for j in range(15)]
+    con(1, cJ, iB, 1.0, 3072.0); con(1, cSg, cN15, -2048.0, 1920.0)
+    Ib, I0, nI, IB, M16, kk, gg, B16, Wu, Wr0, Wr1, Wr2, One, I16 = [blk("cb", j) for j in range(14)]
     k8, k16, one1 = R("cb", 5 * 128, 5 * 128 + 8), R("cb", 5 * 128, 5 * 128 + 16), blk("cb", 12, 1)
     iota(kk, [[0, 8], [1, 16]], 0, 0)
     iota(gg, [[1, 8], [0, 16]], 0, 0)
     fill(One, 1)
     asel(Ib, One, [[-1, 128]], 0, 1)
-    ts(M16, kk, cB, eq_); ts(B16, gg, cAa, eq_); ts(Tri, kk, cB, ALU.is_le, 4096.0, mul_)
+    ts(M16, kk, cB, eq_); ts(B16, gg, cAa, eq_)
     con(0, I16, Ib, 16.0); con(0, I0, Ib, cN15); con(0, Wu, B16, cU); con(0, nI, Ib, -1.0)
     con(1, IB, Ib, BIG / 2); con(1, Wr0, B16, cN4k); con(1, Wr1, B16, cN64k); con(1, Wr2, B16, cM4k)
     kz = R("kz", 0, 256, 1, 0, 1)
@@ -252,10 +278,7 @@ def build(case=None):
     C4k, C256, Wu8, Wv8, C16p, Cp, Cp2, Wmk = sm(0), sm(8), sm(16), sm(24), sm(32), sm(48), sm(48, 16), sm(64, 16)
     for d, c in ((C256, 256.0), (Cp, cP), (sm(64), cF64k), (sm(72), cF15), (C16p, c16P), (Wu8, cU), (Wv8, cN15)):
         con(0, d, C8, c)
-    con(1, sm(56), C8, cP); con(1, C4k, C8, 4096.0)
-    if DIRECT:
-        fill(R("Du", 0, 288), 0)
-        con(1, R("Du", 15, 143, 16), C8, cU); con(1, R("Du", 159, 287, 16), C8, cN15)
+    con(1, sm(56), C8, cP)
     Wd, Wi, Ws = sm(80, 24), sm(104, 24), sm(128, 24)
     fill(sm(80, 72), 0)
     con(1, sm(80, 8, 3), C8, cN16); con(1, sm(82, 8, 3), C8, cM16)
@@ -264,7 +287,8 @@ def build(case=None):
     fill(R("Tub", 128, 176, 1, 0, 48), 4)
     asel(I4, R("Tub", 128, 176, 1, 0, 48), [[-1, 2], [-6, 8], [-2, 3]], 0, 1)
     Iq, Wr3 = blk("cb", 17), blk("cb", 19)
-    con(1, Iq, Ib, 0.25)
+    I4x = blk("cb", 14)
+    con(1, Iq, Ib, 0.25); con(1, I4x, Ib, 4.0)
     lv, lv2 = R("cb", 18 * 128, 18 * 128 + 48), R("cb", 18 * 128 + 2, 18 * 128 + 50)
     iota(R("cb", 18 * 128, 18 * 128 + 51), [[0, 17], [1, 3]], 0, 0)
     Ej = [blk("ce", l, 24) for l in range(3)]
@@ -279,39 +303,42 @@ def build(case=None):
     for l in range(3):
         asel(Ej[l], ta, [[-3, 8], [0, 16]], -l, 1, ALU.not_equal, -2560.0)
     asel(E8, blk("cb", 12, 8), [[-1, 8], [0, 16]], 0, 1)
-    fill(R("wT", 0, 64), 0); fill(R("k0", 0, 32), 0)
+    fill(R("wT", 0, 64), 0); fill(R("k0i", 0, 32), 0)
     fill(R("wd", 0, 240), 0); con(1, R("wd", 112, 128), R("cb", 4 * 128, 4 * 128 + 16))
-    fill(R("jba", 32, 40), 0); fill(R("Sb0", 288, 304), 0); fill(R("Sb1", 288, 304), 0)
+    fill(R("jba", 0, 72), 15); fill(R("Sb0", 288, 320), 0); fill(R("Sb1", 288, 320), 0)
+    if AHEAD:
+        fill(R("dj", 32, 40), 0); fill(R("jalt", 32, 40), 0)
     cOwn = col(26)
     ts(col(25), iB, 8.0, ALU.is_ge, 8.0, mul_)
     ts(R("ci", 15, 16), iP, 7, and_); ts(cOwn, R("ci", 15, 16), cAa, eq_)
-    Lz1, Lz2, Lz3 = R("cl", 8, 12), R("cl", 40, 48), R("cl", 48, 56)
-    for lst, src, step, hi, lo, zero in ((Lz1, R("cb", 5 * 128, 5 * 128 + 4), 2.0, 0.125, 0.0, 8.0), (Lz2, k8, 1.0, 1.0, 0.0, 32.0),
-                                         (Lz3, k8, 1.0, 1.0, 16.0, 32.0)):
-        con(1, col(38), col(25), hi, lo - zero)
+    Lz1, Lz2 = R("cl", 8, 12), R("cl", 40, 48)
+    for lst, src, step, hi, zero in ((Lz1, R("cb", 5 * 128, 5 * 128 + 4), 2.0, 0.125, 8.0), (Lz2, k8, 1.0, 1.0, 32.0)):
+        con(1, col(38), col(25), hi, -zero)
         con(1, R("cf", 40, 40 + nel(lst)), src, step, col(38))
         con(1, lst, R("cf", 40, 40 + nel(lst)), cOwn, zero)
-    M16p, C8p, k37 = blk("mb", 2), R("mb", 384, 392), blk("k37", 0, 1)
-    ts(R("ci", 12, 13), iP, 1, and_); con(1, col(27), R("ci", 12, 13), 8.0, cAa)
-    ts(M16p, kk, col(27), eq_)
-    ts(R("ci", 13, 14), iB, 1, shr_); con(1, col(28), R("ci", 13, 14))
-    ts(C8p, k8, col(28), eq_)
+    k37 = blk("k37", 0, 1)
+    fill(R("uva", 0, 32), 0)
     cPar, cPb = (col(29), col(30)), (col(31), col(32))
     ts(R("ci", 14, 15), iA, 1, and_)
     con(1, cPar[1], R("ci", 14, 15)); con(1, cPar[0], R("ci", 14, 15), -1.0, 1.0)
     con(1, cPb[1], R("ci", 14, 15), -2048.0); con(1, cPb[0], R("ci", 14, 15), 2048.0, -2048.0)
     iota(blk("kz", 2, 1), [[1, 16], [0, 8]], 0, 0)
     con(1, k37, blk("kz", 2, 1), 37.0)
-    M2 = R("m2", 0, 256)
-    asel(blk("m2", 0), M16, [[0, 128]], 0, 0); asel(blk("m2", 1), M16, [[0, 128]], 0, 0)
-    dMx, dH, dX, dS3, dM3 = R("d0", 0, 512), R("d0", 512, 896), R("d0", 896, 1152), R("d0", 1152, 1248), R("d0", 1248, 1296)
-    for r, body, head, st in ((dM3, 0.0, 1024.0, 3), (dMx, 1.0, 0.0, 16), (R("d0c", 0, 128), -BIG, 32768.0, 16)):
+    dMx, dW, dX, dS3, dM3 = R("d0", 0, 512), R("d0", 512, 896), R("d0", 896, 1152), R("d0", 1152, 1248), R("d0", 1248, 1296)
+    dP = R("d0", 1296, 1536)
+    for r, body, head, st in ((dM3, 0.0, 1024.0, 3), (dMx, 1.0, 0.0, 16), (R("d0c", 0, 128), -BIG, 32768.0, 16),
+                              (dP, -2.0 ** 99, 2.0 ** 99, 15)):
         ms(r, body); ms(R(r[1], r[2], r[3], st), head)
-    for r, body, head, st in ((dH, -1.0, BIG, 16), (dX, 0.0, BIG, 16), (dS3, 1.0, 0.0, 3)):
+    for r, body, head, st in ((dW, 1.0, -BIG, 16), (dX, 0.0, BIG, 16), (dS3, 1.0, 0.0, 3)):
         fill(r, body); fill(R(r[1], r[2], r[3], st), head)
     fill(R("St", 3072, 3088), 0)
-    Lb8, Lend, Lgo = R("cl", 0, 8), R("cl", 16, 32), R("cl", 32, 35)
-    con(0, Lb8, k8); con(1, Lend, k16, 16.0, 15.0)
+    Tri, r15 = R("m2", 0, 240, 1, 0, 16), R("m2", 240, 264, 1, 0, 1)
+    fill(R("sh", 0, 16), 0); con(1, R("sh", 16, 144), Ib, 2.0 ** -13); con(1, R("sh", 144, 272), Ib, -2.0 ** -13)
+    fill(R("tb", 384, 624, 1, 0, 16), 0)
+    asel(Tri, R("tb", 384, 624, 1, 0, 16), [[0, 16], [-1, 15]], -1, 1, ALU.is_ge, 0.5)
+    fill(r15, 15); fill(R("xu", 32, 40), 0)
+    Lb8, Lgo = R("cl", 0, 8), R("cl", 32, 35)
+    con(0, Lb8, k8)
     con(0, R("cf", 21, 24), R("cb", 5 * 128, 5 * 128 + 3), 16.0, cB)
     con(0, Lgo, R("cf", 21, 24), 1.0 / 3.0, -1.0 / 3.0)
     cLo, k64 = col(24, 64), blk("cb", 5, 64)
@@ -344,16 +371,18 @@ def build(case=None):
     mm([(R("PQ0", 0, 48), R("Tub", 0, 128, 1, 0, 48), I4)])
     tt(R("P40", 0, 48), R("PQ0", 0, 48), lv, add_)
 
-    def tolist(key, h, win, lst, D, pl, scale, c):
+    def tolist(key, h, win, lst, D, pl, scale, c, bias=0.0, final=True):
         w = nel(pl)
-        aff(key, h, R(D[1], D[2], D[2] + 8 * w), IND(win, lst), scale)
-        mm([(pl, M16, c)] + [(pl, R("wd", 112 - 16 * g, 240 - 16 * g), R(D[1], D[2] + w * g, D[2] + w * g + w)) for g in range(8)])
+        aff(key, h, R(D[1], D[2], D[2] + 8 * w), IND(win, lst), scale, bias)
+        mm([(pl, M16, c)] * (c is not None) + [(pl, R("wd", 112 - 16 * g, 240 - 16 * g), R(D[1], D[2] + w * g, D[2] + w * g + w))
+                                               for g in range(8)], final=final)
 
     for t in range(RO):
         last = t == RO - 1
         P4 = R("P40", 0, 48)
         Cw, Gl, Sb, Lp, LJ = "Cw%d" % t, "Gl%d" % t, "Sb%d" % t, "Lb%d" % (t - 1), "LJ%d" % t
         cA = 2048.0 if t == 0 else R("cA", 0, 1)
+        ADD = ADDS[t]
         PT = ["PT0", "PT1"]
         In, Ip = "In%d" % t, "Li%d" % (t - 1)
         mj, Pinc, mj12, go = R(In, 512, 560), R(In, 560, 608), R(In, 608, 656), R(Sb, 272, 288)
@@ -363,7 +392,7 @@ def build(case=None):
         if t == 0:
             jj = R("jj", 0, 16)
             scan(R("pmin", 0, 48), dM3, P4, add_, min_)
-            cp(R("ji", 0, 16), R("pmin", 2, 48, 3)); ts(jj, R("ji", 0, 16), 3, and_)
+            ts(jj, R("pmin", 2, 48, 3), 3, and_)
             for h in range(2):
                 tt(H("Dk", h), IND(H("jj", h, 8), Lb8), M16, mul_)
                 pl = R(PT[h], 384, 392)
@@ -372,24 +401,28 @@ def build(case=None):
         else:
             jj = R(Lp, 256, 272)
             tt(R("t12", 0, 48), IND(R(Lp, 272, 288), Lgo), R(Ip, 608, 656), mul_)
-            tt(P4, R(Ip, 560, 608), R("t12", 0, 48), add_)
         tt(mj, IND(jj, Lgo), lv, eq_)
         tt(R("mm", 0, 48), IND(jj, Lgo), lv2, eq_)
-        aff("mj4", 0, R("mj4", 0, 48), mj, 4.0); aff("mj12", 0, mj12, mj, -12.0)
-        tt(Pinc, R("mj4", 0, 48), P4, add_)
+        aff("mj12", 0, mj12, mj, -12.0)
+        pl = R("PB1", 0, 48)
+        mm([(pl, Ib, x) for x in ((P4,) if t == 0 else (R(Ip, 560, 608), R("t12", 0, 48)))] + [(pl, I4x, mj)])
+        aff("Pinc", 0, Pinc, pl)
         if not last:
             scan(R("pm2", 0, 48), dM3, Pinc, add_, min_)
-            aff("ji2", 0, R("ji2", 0, 16), R("pm2", 2, 48, 3)); ts(R("jalt", 0, 16), R("ji2", 0, 16), 3, and_)
+            ts(R("jalt", 0, 16), R("pm2", 2, 48, 3), 3, and_)
             tt(R("dj", 0, 16), jj, R("jalt", 0, 16), sub_)
         if t == 0:
             aff("rm", 0, R(In, 656, 657), R("Rm", 0, 1))
             for h in range(2):
-                for l in range(3):
-                    a = l * 256 + h * 128
-                    aff("Cw", h, blk("PQ%d" % h, l), R("Qk", a, a + 128), 4096.0)
-                    tt(H(Cw, 3 * h + l), R("Qn", a, a + 128), blk("PQ%d" % h, l), add_)
-        if not last:
+                aff("Cw", h, H(Cw, h, 384) if FOLD else R("PQ%d" % h, 0, 384), H("Qk", h, 384), 4096.0)
+                if not FOLD:
+                    tt(H(Cw, h, 384), H("Qn", h, 384), R("PQ%d" % h, 0, 384), add_)
+            send("A" if FOLD else "N", R(Cw, 0, 768), [R("Cr0", 0, 768)], ["rC0"], 600 if FOLD else 384)
+        elif not last:
             send("N", R(Cw, 0, 768), [R("Cr%d" % t, 0, 768)], ["rC%d" % t], 384)
+        if last:
+            store("o6", ("ys", 0, R("St", 0, 1280)), [R("St", 0, 1280)], 320)
+            ops[-2].update(wr=[early], lat=3500.0)
         for h in range(2):
             lj = H(LJ, h, 8)
             if t == 0:
@@ -401,69 +434,73 @@ def build(case=None):
                 aff("key", h, H("key", h), IND(H(Cw, h, 384), lj), 1.0 / 4096, 1024.625)
             keys = [(R(PT[h], 0, 256), one1, kz), (R(PT[h], 0, 128), H("key", h), I16)]
             if MKSPLIT:
-                mm(keys, final=False)
+                mm(keys[:2 - (t == 0)], final=False)
             for c in range(4):
                 aff("sg", 4 * h + c, H("sg", 4 * h + c, 512), IND(R("St", 0, 3072), H("q16", 4 * h + c, 32)))
                 scan(H("smx", 4 * h + c, 512), dMx, H("sg", 4 * h + c, 512), mul_, max_)
                 if MKSPLIT:
                     mm([(R(PT[h], k, 256, 16, 32 * c, 32 * c + 32), H("sg", 4 * h + c, 512, 16, k), Wmk) for k in range(16)],
-                       first=False, final=c == 3)
+                       first=False, final=c == 3 and t > 0, stop=t > 0)
+            if MKSPLIT and t == 0:
+                mm(keys[1:], first=False)
             if not MKSPLIT:
                 mm(keys + [(R(PT[h], k, 256, 16), H("sg", h, 2048, 16, k), Wmk) for k in range(16)])
             scan(H("msc", h), R("d0c", 0, 128), R(PT[h], 0, 128), max_, min_)
             aff("mT", h, part("mT", h), R(PT[h], 128, 256))
-            k0, me = R("k0", 16 * h, 16 * h + 8), H("msc", h, 128, 16, 15)
-            aff("mi", h, H("mi", h, 8), me, bias=-7.5); tt(k0, me, H("mi", h, 8), sub_)
+            k0 = R("k0i", 16 * h, 16 * h + 8)
+            ts(k0, H("msc", h, 128, 16, 15), 15, and_)
             pl = R(PT[h], 392, 400)
             if WIDEK[h] == "w":
                 tt(H("Dk", h), IND(k0, Lb8), M16, mul_)
                 mm([(pl, M16, C16p), (pl, H("Dk", h), C8)])
             else:
-                tolist("Dk", h, H("k0", h, 16), Lz1, H("Dk", h), pl, 1.0, C16p)
+                tolist("Dk", h, H("k0i", h, 16), Lz1, H("Dk", h), pl, 1.0, C16p)
             aff("Lk", h, H("Lk", h, 8), pl)
-            xx = H("xx", 2 * h)
+            xx = H("xx", 4 * h)
             aff("xx", h, xx, IND(H("sg", h, 2048), H("Lk", h, 8)), cN15, cF15)
             pl = R(PT[h], 400, 408)
-            if DIRECT:
-                la = [128 * h + 16 * (p % 8) + p // 8 for p in range(16)]
-                mm([(pl, R("Du", 159 - p, 287 - p), R("smx", 16 * la[p] + 15, 16 * la[p] + 240, 32)) for p in range(16)], final=False)
-                mm([(pl, R("Du", 15 - p, 143 - p), R("xx", 128 * h + la[p], 128 * h + la[p] + 15, 2)) for p in range(16)],
-                   first=False)
-            else:
-                mm([(pl, H("smx", h, 2048, 16, 15), Wv8), (pl, xx, Wu8)])
+            mm([(pl, H("smx", h, 2048, 16, 15), Wv8), (pl, xx, Wu8)])
             pn = R(PT[h], 256, 384)
-            mm([(R(PT[h], 256 + b, 384, 8), Wu, H("xx", 16 * h + b, 16)) for b in range(8)], False)
+            mm([(pn, Wu, xx)])
             aff("u32", h, H("u32", h), pn, bias=32.0)
-            aff("uvi", h, H("uvi", h, 8), pl); ts(H("uva", h, 8), H("uvi", h, 8), 255, and_)
-            if DIRECT:
-                aff("Lo", h, H("Lo", h, 8), H("uva", h, 8))
+            uva = R("uva", 16 * h, 16 * h + 8)
+            aff("uvi", h, H("uvi", h, 8), pl); ts(uva, H("uvi", h, 8), 255, and_)
+            pl = R(PT[h], 408, 416)
+            if WIDEU[h] == "w":
+                tt(H("Du", h), IND(uva, Lb8), M16, mul_)
+                mm([(pl, H("Du", h), C8)])
             else:
-                pl = R(PT[h], 408, 416)
-                tt(H("Du", h), IND(H("uva", h, 8), Lb8), M16p, mul_)
-                mm([(pl, H("Du", h), C8p)])
-                aff("Lo", h, H("Lo", h, 8), pl)
+                tolist("Du", h, H("uva", h, 16), Lz1, H("Du", h), pl, 1.0, None)
+            aff("Lo", h, H("Lo", h, 8), pl)
             tt(H("tO", h), IND(R("Ot", 0, 256), H("Lo", h, 8)), H("u32", h), mul_)
             ts(H("na", h), H("tO", h), 5, shr_, 4095, and_)
             for e in range(2):
-                aff("nf%d" % e, h, H("nf", 2 * h + e), H("na", h), cPar[e], cPb[e])
+                aff("nf%d" % e, h, R("nf", 256 * h + 16 * e, 256 * h + 256, 32) + (16,), H("na", h), cPar[e], cPb[e])
             mm([(pn, one1, k37)]
-               + [(R(PT[h], 256 + b, 384, 8, 32 * a, 32 * a + 32), R("nf", 256 * h + b, 256 * h + 256, 8, 32 * a, 32 * a + 32),
+               + [(R(PT[h], 256 + b, 384, 8, 32 * a, 32 * a + 32), R("nf", 256 * h + 32 * b, 256 * h + 32 * b + 32, 1, 32 * a, 32 * a + 32),
                    R("cb", 4 * 128, 4 * 128 + 16, 1, 32 * a, 32 * a + 32)) for a in range(4) for b in range(8)])
             aff("n16", h, H("n16", h), pn, bias=cA)
-            if "F" in ADD[4 * h:4 * h + 4]:
-                aff("x2", h, H("xx", 2 * h + 1), xx)
+            four = "D" in ADD[4 * h:4 * h + 4]
+            if four or "F" in ADD[4 * h:4 * h + 4]:
+                aff("x2", h, H("xx", 4 * h + 1), xx)
+            if four:
+                aff("x4", h, H("xx", 2 * h + 1, 256), H("xx", 2 * h, 256))
             for c in range(4 * h, 4 * h + 4):
-                if ADD[c] == "F":
+                if ADD[c] == "F" and four and FOUR:
+                    tt(H("eg", c, 512), IND(R("Ef", 0, 4720), H("n16", c, 32)), H("xx", h, 512), add_)
+                elif ADD[c] == "F":
                     for e in range(2):
-                        tt(H("eg", 2 * c + e, 256), IND(R("Ef", 0, 4720), H("n16", 2 * c + e, 16)), H("xx", h, 256), add_)
+                        tt(H("eg", 2 * c + e, 256), IND(R("Ef", 0, 4720), H("n16", 2 * c + e, 16)), H("xx", 2 * h, 256), add_)
                 else:
                     aff("eg", c, H("eg", c, 512), IND(R("Ef", 0, 4720), H("n16", c, 32)))
+                if ADD[c] == "D":
+                    total(H("eg", c, 512), H("xx", h, 512), "d%d%d" % (t, c))
             pd = blk("PQ%d" % h, 3)
             mm([(pd, I0, xx), (pd, nI, H(Gl, h))])
             act(part("dx", h), pd, AF.Abs)
             ts(part("ix", h), part("dx", h), 4.0, ALU.is_gt)
             pl = R("PT0", 464 + 24 * h, 488 + 24 * h)
-            mm([(pl, part("dx", h), Wd), (pl, part("ix", h), Wi)])
+            mm([(pl, one1, r15), (pl, part("dx", h), Wd), (pl, part("ix", h), Wi)])
             aff("qf", h, part("qf", h), H("q16", h), bias=-1536.0)
             if not last:
                 a, b = ((0, 656 + (t == 0)), (672, 1184))[h]
@@ -472,20 +509,23 @@ def build(case=None):
         scan(R("hxs", 0, 48), R("d0", 1152, 1200), R("hxm", 0, 48), mul_, add_)
 
         def marks(PM):
+            aff("k0", 0, R("k0", 0, 32), R("k0i", 0, 32))
             mm([(R(PM, 256, 384, 1, 32 * e, 32 * e + 32), R("k0", 0, 32), Ib) for e in range(2)], False)
             act(blk("R0k", 0, 64), blk(PM, 2, 64), AF.Square, bias=cLo)
             pl = R(PM, 0, 256)
             mm([x for h in range(2) for x in ((blk(PM, h), blk("R0k", 0, 65), Ek[h]), (blk(PM, h), part("qf", h), Ib))], 2)
             scan(R("xsc", 0, 256), dX, pl, add_, min_)
-            tt(R("Dx", 0, 256), IND(R("xsc", 0, 256), Lend), M2, mul_)
-            mm([(pl, B16, R("Dx", 0, 256)), (blk(PM, 0), Ib, Tri), (blk(PM, 1), Ib, Tri)])
-            aff("RT", 0, R("RT", 0, 256), pl)
-            tt(R("eq", 0, 256), IND(R("xsc", 0, 256), Lend), R("RT", 0, 256), eq_)
-            mm([x for h in range(2) for x in ((R(PM, 8 * h, 8 + 8 * h), H("Dx", h), C8),
-                                              (R(PM, 8 * h, 8 + 8 * h), H("eq", h), C4k))], 2)
-            ts(R("Lx", 0, 32, 2), R(PM, 0, 16), 1536.0, add_, cJ, min_)
+            xn = R("xn", 0, 16)
+            aff("xn", 0, xn, R("xsc", 15, 256, 16))
+            mm([(R(PM, 0, 240), blk("cb", 0, 16), Tri)] + [(R(PM, s, 240, 15), R("sh", a, a + 128), xn) for s in range(15)
+                                                           for a in (15 - s, 144)])
+            scan(R("xsc", 0, 240), dP, R(PM, 0, 240), max_, mul_)
+            ts(R("rep", 0, 16), R("xsc", 14, 240, 15), 0.0, eq_, 4096.0, mul_)
+            tt(R("xu", 0, 16), R("rep", 0, 16), xn, add_)
+            tolist("Dx", 0, R("xu", 0, 40), Lz2, R("Dx", 0, 128), R(PM, 256, 272), 1.0, None)
+            ts(R("Lx", 0, 32, 2), R(PM, 256, 272), 1536.0, add_, cJ, min_)
             for c in range(16):
-                cp(IND(R("St", 0, 3088), R("Lx", 2 * c, 2 * c + 1)), H("xx", c + 8 * (c // 8), 16))
+                cp(IND(R("St", 0, 3088), R("Lx", 2 * c, 2 * c + 1)), H("xx", c + 24 * (c // 8), 16))
         marks("PQ%d" % MARKS)
 
         def update(h, buf, old, Wm):
@@ -499,13 +539,17 @@ def build(case=None):
                 pl = blk(PQ, l)
                 lst += [(pl, Ej[l], r0), (pl, part("mT", h, buf), IB), (pl, Ib, part("qf", h, buf))]
             mm(lst, 3)
-            tt(H("C1", h, 384), H(old, h, 384), pq, max_)
-            aff("K16", h, H("K16", h, 384), H("C1", h, 384), -1.0 / 4096, -1024.625)
+            if t == 0:
+                for l in range(3):
+                    tt(H("C1", 3 * h + l), H(old, 2 * l + h), blk(PQ, l), max_)
+            else:
+                tt(H("C1", h, 384), H(old, h, 384), pq, max_)
+            aff("K16", h, H("K16", h, 384), H("C1", h, 384), 1.0 / 4096, 1024.625)
             mm([(blk(PQ, l), H("K16", 3 * h + l), I16) for l in range(3)], False)
-            scan(H("wsc", h, 384), dH, pq, add_, min_)
+            scan(H("wsc", h, 384), dW, pq, add_, max_)
             we = H("wsc", h, 384, 16, 15)
-            aff("wi", h, H("wi", h, 24), we, bias=7.5)
-            tt(R("wT", 32 * h + 1, 32 * h + 25), H("wi", h, 24), we, sub_)
+            aff("wi", h, H("wi", h, 24), we, bias=-7.5)
+            tt(R("wT", 32 * h + 1, 32 * h + 25), we, H("wi", h, 24), sub_)
             mm([(R(PQ, 0, 128, 1, 32 * e, 32 * e + 32), H("wT", h, 32), Ib) for e in range(2)], False)
             r0 = blk("R0w", 2 * t + h, 64)
             act(r0, blk(PQ, 0, 64), AF.Square, bias=cLo)
@@ -525,15 +569,21 @@ def build(case=None):
         for h in range(2):
             update(h, In, Cw, Wr2) if last else update(h, "Li%d" % t, "Cr%d" % t, Wr3)
         if last:
-            store("o1", ("yq", None, R("Cf", 0, 768)), [R("Cf", 0, 768)], 400)
+            for a, b in YQ:
+                store("o1", ("yq", a, R("Cf", a, b)), [R("Cf", a, b)], (b - a) // 2)
         for h in range(2):
             for c in range(4 * h, 4 * h + 4):
                 pa, pb = "P" + BANKS[0][2 * c:2 * c + 2], "P" + BANKS[1][2 * c:2 * c + 2]
                 yb, db, ib = H("yy", c, 512), H("dd", c, 512), H("ind", c, 512)
-                if ADD[c] == "F":
+                if ADD[c] in "FD":
                     ts(yb, H("eg", c, 512), 0.0, max_, cN63, min_)
+                elif ADD[c] == "A":
+                    if "A" not in ADD[4 * h:c]:
+                        mm([(blk(pa, kl), I0, H("xx", 4 * h)) for kl in range(4)], False)
+                    tt(ib, H("eg", c, 512), R(pa, 0, 512), add_)
+                    ts(yb, ib, 0.0, max_, 63.0, min_)
                 else:
-                    mm([(R(pa, 0, 512), Ib, H("eg", c, 512))] + [(blk(pa, kl), I0, H("xx", 2 * h)) for kl in range(4)])
+                    mm([(R(pa, 0, 512), Ib, H("eg", c, 512))] + [(blk(pa, kl), I0, H("xx", 4 * h)) for kl in range(4)])
                     ts(yb, R(pa, 0, 512), 0.0, max_, 63.0, min_)
                 mm([(R(pb, 0, 512), Ib, yb)] + [(blk(pb, kl), nI, H(Gl, h)) for kl in range(4)])
                 act(db, R(pb, 0, 512), AF.Abs)
@@ -546,27 +596,33 @@ def build(case=None):
                     pl = R(PT[h], k % 16, 384, 16)
                     lst += [(pl, H("dd", k), Wd), (pl, H("ind", k), Wi if ENG["ind"][c] == "V" else Ws)]
                 mm(lst, 2)
-            scan(H("hsc", h, 384), dH, R(PT[h], 0, 384), add_, min_)
+            scan(H("hsc", h, 384), dW, R(PT[h], 0, 384), add_, max_)
         ends = R("hsc", 15, 768, 16)
         tt(R("t48", 0, 48), ends, R("mm", 0, 48), mul_)
         tt(R("t48", 48, 96), ends, mj, mul_)
         scan(R("ss", 0, 96), dS3, R("t48", 0, 96), mul_, add_)
-        ts(R("ai", 0, 32), R("ss", 2, 96, 3), 15.0, add_)
-        ts(R("jba", 0, 32), R("ai", 0, 32), 15, and_)
-        tolist("Db", 0, R("jba", 0, 40), Lz2, H("Dj", 0), R("PT0", 448, 464), 128.0, Cp2)
+        ts(R("jba", 0, 32), R("ss", 2, 96, 3), 15, and_)
+        tolist("Db", 0, R("jba", 0, 40), Lz2, H("Dj", 0), R("PT0", 448, 464), -128.0, Cp2, 1920.0)
         aff("Lab", 0, R("Lab", 0, 16), R("PT0", 448, 464))
         for h in range(2):
             aff("yb", h, H(Sb, h), IND(H("yy", h, 2048), H("Lab", h, 8)))
-        tt(go, R("ai", 16, 32), R("hxs", 2, 48, 3), ALU.is_lt)
+        tt(go, R("ss", 50, 96, 3), R("hxs", 2, 48, 3), ALU.is_gt)
         if not last:
+            pl = R("PB0", 0, 16)
+            if AHEAD:
+                aff("Dd", 0, H("Dj", 3), IND(R("dj", 0, 40), Lz2), 128.0)
+                tolist("Dj", 0, R("jalt", 0, 40), Lz2, H("Dj", 1), pl, 128.0, Cp2, final=False)
+                tt(H("Dj", 4), IND(R(Sb, 272, 320), Lz2), H("Dj", 3), mul_)
+                mm([(pl, R("wd", 112 - 16 * g, 240 - 16 * g), H("Dj", 32 + g, 16)) for g in range(8)], first=False)
             tt(R("gt", 0, 16), go, R("dj", 0, 16), mul_)
             tt(R(Sb, 256, 272), R("gt", 0, 16), R("jalt", 0, 16), add_)
-            tolist("Dj", 0, R(Sb, 256, 304), Lz2, H("Dj", 1), R("PT1", 448, 464), 128.0, Cp2)
-            aff("SL", 0, R("SL%d" % t, 0, 16), R("PT1", 448, 464))
+            if not AHEAD:
+                tolist("Dj", 0, R(Sb, 256, 304), Lz2, H("Dj", 1), pl, 128.0, Cp2)
+            aff("SL", 0, R("SL%d" % t, 0, 16), pl)
             send("N", R("SL%d" % t, 0, 16), [R("LJ%d" % (t + 1), 0, 16)], ["rL%d" % t], 4)
         w = 256 if last else 288
         send("N", R(Sb, 0, w), [R("Lb%d" % t, 0, w)], ["rB%d" % t], w // 4)
-        tolist("Da", 0, R("jba", 0, 40), Lz3, H("Dj", 2), R("PT0", 432, 448), 128.0, Cp2)
+        tolist("Da", 0, R("jba", 16, 56), Lz2, H("Dj", 2), R("PT0", 432, 448), -128.0, Cp2, 1920.0)
         aff("Laa", 0, R("Lab", 16, 32), R("PT0", 432, 448))
         for h in range(2):
             aff("ya", h, H("St", 2 * t + h), IND(H("yy", h, 2048), H("Lab", 2 + h, 8)))
@@ -582,14 +638,15 @@ def build(case=None):
             mm([(R("PT0", 424, 425), E8, R("cnt", 0, 1, 1, 0, 8))])
             aff("Ai", 0, R("Ai", 0, 1), R("PT0", 424, 425)); ts(R("Aa", 0, 1), R("Ai", 0, 1), 63, and_)
             aff("cA", 0, R("cA", 0, 1), R("Aa", 0, 1), bias=2048.0)
-            aff("Lb", 0, R("St", 256 * (3 + t), 256 * (4 + t)), R("Lb%d" % t, 0, 256))
+            aff("Lb", 0, H("St", 3 + t, 256), R("Lb%d" % t, 0, 256))
         else:
             mm([(blk("PA0", 0, 48), R("Pfin", 0, 48), Iq)])
             act(blk("Pout", 0, 48), blk("PA0", 0, 48))
             store("o2", ("yp", None, blk("Pout", 0, 48)), [blk("Pout", 0, 48)], 24)
             store("o3", ("ym", None, "marks"), [R("St", 1536, 3072)], 24)
-            for s, a, b in (("o4", 0, 512), ("o6", 768, 1280), ("o7", 512, 768)):
-                store(s, ("ys", a, R("St", a, b)), [R("St", a, b)], (b - a) // 4)
+            for a in (0, 768):
+                store("o3", ("ys", a, "marks"), [R("St", a, a + 512), early], 8)
+            store("o4", ("ys", 512, R("St", 512, 768)), [R("St", 512, 768), early], 64)
             store("o5", ("ys", 1280, R("Lb2", 0, 256)), [R("Lb2", 0, 256)], 64)
     return ops
 
@@ -642,7 +699,7 @@ def above(l, x):
 
 
 def place(key, pre, rel, cost, qn, bk):
-    qs, qe = [[] for _ in range(6)], [[] for _ in range(6)]
+    qs, qe = [[] for _ in range(7)], [[] for _ in range(7)]
     bs, be, bq = [[] for _ in range(8)], [[] for _ in range(8)], [[] for _ in range(8)]
     fin = [0.0] * len(key)
     for i in key:
@@ -680,8 +737,8 @@ def place(key, pre, rel, cost, qn, bk):
 
 def replay(idx, pre, cost, lat, qn, bk, f):
     fin = [0.0] * len(idx)
-    free = [0.0] * 6
-    bank = [[0.0] * 6 for _ in range(8)]
+    free = [0.0] * 7
+    bank = [[0.0] * 7 for _ in range(8)]
     for i in idx:
         q = qn[i]
         s = free[q] if q else 0.0
@@ -703,7 +760,7 @@ def search(ops, pre, rounds, start=None):
     n = len(ops)
     lat = [o.get("lat", 0) for o in ops]
     cost = [o["cost"] for o in ops]
-    qn = [max(0, " VSPGY".find(o["q"])) for o in ops]
+    qn = [max(0, " VSPGYL".find(o["q"])) for o in ops]
     names = [k for k, v in SCRATCH.items() if v[0] == "psum"]
     bk = [sorted(set(names.index(r[1]) for r in o["rd"] + o["wr"] if inps(r))) for o in ops]
     fw = [[(j, d + lat[j]) for j, d in pre[i].items()] for i in range(n)]
@@ -712,12 +769,14 @@ def search(ops, pre, rounds, start=None):
         for j, d in fw[i]:
             bw[j].append((i, d))
     la, ca, zero, up = np.array(lat), np.array(cost), [0.0] * n, np.arange(n)
-    others = [([o["cost"] for o in build(c)], c[3]) for c in CASES]
+    others = [([o["cost"] for o in l], [o.get("lat", 0) for o in l], w) for l, w in [(build(c), c[3]) for c in CASES]]
+    moves = np.array([o["n"] for o in ops if o["q"] == "L"])
+    ahead = np.array([cost[i - 1] + pre[i][i - 1] for i in moves])
     kin = []
     for o in ops:
         r = o["wr"][0] if o["wr"] else o["rd"][0]
         ps = inps(r)
-        kin.append((r[1] if ps else r[1].rstrip("012"), r[2] // 128 if ps else int(2 * r[2] >= SCRATCH[r[1]][1][1]), o["q"], o["kind"]))
+        kin.append((r[1] if ps else r[1].rstrip("012"), r[2] // 128 if ps else int(2 * r[2] >= np.prod(SCRATCH[r[1]][1][1:])), o["q"], o["kind"]))
     kinds = sorted(set(kin))
     kin = np.array([kinds.index(x) for x in kin])
 
@@ -733,9 +792,14 @@ def search(ops, pre, rounds, start=None):
         b = place(np.lexsort((-up, -f)).tolist(), bw, lat, cost, qn, bk)
         return place(np.lexsort((up, -b)).tolist(), fw, zero, cost, qn, bk)
 
+    def starts(f):
+        s = f - ca
+        s[moves - 1] = s[moves] = s[moves] - ahead
+        return s
+
     def worth(f):
-        idx = np.lexsort((up, f - ca)).tolist()
-        return [float((f + la).max())] + [replay(idx, pre, c, lat, qn, bk, w) for c, w in others]
+        idx = np.lexsort((up, starts(f))).tolist()
+        return [replay(idx, pre, c, l, qn, bk, w) for c, l, w in [(cost, lat, 1.0)] + others]
 
     if start is None:
         tail = [0.0] * n
@@ -749,27 +813,28 @@ def search(ops, pre, rounds, start=None):
     for it in range(rounds):
         key = cf - ca
         m = rng.random()
-        if m < 0.5:
+        near = np.abs(key - rng.random() * cur[0])
+        if m < MOVES[0]:
             off = np.zeros(len(kinds))
-            off[rng.integers(0, len(kinds), int(rng.integers(1, 4)))] = rng.normal(0.0, 1500.0)
-            key = key + off[kin]
-        elif m < 0.8:
-            key = key + (np.abs(key - rng.random() * cur[0]) < 2500) * rng.normal(0.0, 500.0, n)
+            off[rng.integers(0, len(kinds), int(rng.integers(1, 4)))] = rng.normal(0.0, MOVES[1])
+            key = key + off[kin] * (near < MOVES[2])
+        elif m < MOVES[3]:
+            key = key + (near < MOVES[4]) * rng.normal(0.0, MOVES[5], n)
         else:
-            key = key + rng.normal(0.0, 150.0, n)
+            key = key + rng.normal(0.0, MOVES[6], n)
         f = forward(key)
-        if (f + la).max() < cur[0] + 3000:
+        if (f + la).max() < cur[0] + MOVES[7]:
             g = turn(f)
             if (g + la).max() <= (f + la).max():
                 f = g
         if (f + la).max() < cur[0] + 600:
             v = worth(f)
-            if sum(v) + v[0] < sum(cur) + cur[0] + 1500.0 * (1.0 - it / rounds) * rng.random() ** 2:
+            if sum(v) + v[0] < sum(cur) + cur[0] + MOVES[8] * len(v) * (1.0 - it / rounds) * rng.random() ** 2:
                 cur, cf = v, f
                 if sum(v) + v[0] < sum(low) + low[0]:
                     low, best = v, f
     TIMES[:] = low
-    return best - ca, qn, bk
+    return starts(best), qn, bk
 
 
 def order(ops):
@@ -783,7 +848,7 @@ def order(ops):
         for b in bk[i]:
             ex.update(j for q, j in bank.get(b, {}).items() if q != qn[i])
             bank.setdefault(b, {})[qn[i]] = i
-        o["w"] = set() if o["q"] in "RL" else set(j for j in hard[i] | ex if ops[j]["kind"] != "send")
+        o["w"] = set() if o["q"] in "RL" else set(j for j in hard[i] | ex if ops[j]["kind"] not in ("send", "sum"))
     pos = {}
     for p, o in enumerate(out):
         pos[o["n"]] = p
@@ -809,7 +874,7 @@ def order(ops):
                 o["need"].append((s, j))
                 ops[j]["inc"] = True
         o["know"] = dict(mine) if o["q"] != "R" else {}
-        if "sem" not in o and o["kind"] != "send":
+        if "sem" not in o and o["kind"] not in ("send", "sum"):
             own.append(o["n"])
     tick = {}
     for o in out:
@@ -862,7 +927,7 @@ def rank_program(g, core, T, topo):
         q = Q[o["q"]]
         for s, j in o["need"]:
             p = ops[j]
-            v = p["val"] if "sem" not in p else (arr.get(s, nin) if p["q"] == "R" else 16)
+            v = p["val"] if "sem" not in p else (arr.get(s, nin) if s[0] == "r" else 16)
             q.wait_ge(T.sem[s], v)
         k, a = o["kind"], o["args"]
         if k == "cp":
@@ -884,7 +949,7 @@ def rank_program(g, core, T, topo):
             m = len(a[0]) if a[1] is True else max(1, int(a[1]))
             for i, (oo, l, rr) in enumerate(a[0]):
                 more = any(x[0][5] < oo[6] and oo[5] < x[0][6] for x in a[0][i + 1:i - i % m + m])
-                ins = q.matmul(ap(T, oo), ap(T, l), ap(T, rr), i % m == 0 and a[2], (a[3] or not a[2]) and not more)
+                ins = q.matmul(ap(T, oo), ap(T, l), ap(T, rr), i % m == 0 and a[2], a[4] and not more)
         elif k == "iota":
             if dty(a[0]) == I32:
                 ins = q.iota(ap(T, a[0]), a[1], a[2], a[3])
@@ -896,9 +961,14 @@ def rank_program(g, core, T, topo):
             src = T[a[0]][:, 0:nel(a[1])] if o["sem"] == "lef2" else T[a[0]][:]
             q.dma_start(ap(T, a[1]), src).then_inc(T.sem[o["sem"]], 16)
             continue
+        elif k == "sum":
+            q.dma_start(ap(T, a[0]), ap(T, a[1]), accum_op=ALU.add).then_inc(T.sem[a[2]], 16)
+            continue
         elif k == "store":
             name, c, src = a[1]
-            if src == "marks":
+            if src == "marks" and c is not None:
+                q.dma_start(T[name][15:128:16, c:c + 512], T["St"][15:128:16, c:c + 512]).then_inc(T.sem[o["sem"]], 16)
+            elif src == "marks":
                 q.dma_start(T[name][:], T["St"][15:128:16, 1536:3072]).then_inc(T.sem[o["sem"]], 16)
             elif c is None:
                 q.dma_start(T[name][:], ap(T, src)).then_inc(T.sem[o["sem"]], 16)
@@ -915,6 +985,12 @@ def rank_program(g, core, T, topo):
                                                 remote_sem=T.sem[s], src=ap(T, a[1]), dst=ap(T, d)))
                     lsum += len(e)
                 q.remote_dma_fused(tr, local_sem=T.sem["lsem"])
+            elif a[0] == "A":
+                rid, pid, _ = topo.addr(nxt)
+                q.remote_dma_fused([RemoteDMATransfer(dst_ids=[DstId(rid=rid, pnc=pid)], dma_engine_mask=topo.mask(core, nxt),
+                                                      remote_sem=T.sem[a[3][0]], srcs=[ap(T, a[1]), T["Qn"][:]],
+                                                      dsts=[ap(T, a[2][0])], alu_op=1)], local_sem=T.sem["lsem"])
+                lsum += len(topo.engines(core, nxt))
             else:
                 rid, pid, _ = topo.addr(nxt)
                 q.remote_dma(ap(T, a[2][0]), ap(T, a[1]), T.sem[a[3][0]], T.sem["lsem"], pid, rid, topo.mask(core, nxt))
@@ -924,4 +1000,4 @@ def rank_program(g, core, T, topo):
             ins.then_inc(T.sem["c" + o["q"]], 1)
     g.wait_ge(T.sem["lsem"], lsum)
     for s in STORES:
-        g.sync.wait_ge(T.sem[s], 16)
+        g.sync.wait_ge(T.sem[s], 16 * sum(o.get("sem") == s for o in ops))

@@ -32,12 +32,13 @@ for _n, _c, _d in (
     ("uvi", 16, I32), ("uva", 32, I32), ("Du", 256, BF), ("Lo", 16, U16), ("u32", 256, F32), ("tO", 256, I32),
     ("na", 256, I32), ("n16", 256, U16), ("dx", 256, BF), ("ix", 256, BF),
     ("hxm", 48, F32), ("hxs", 48, F32), ("hsc", 768, F32), ("t48", 96, F32), ("ss", 96, I32),
-    ("jba", 72, I32), ("gt", 16, F32), ("Dj", 640, BF), ("Lab", 32, U16), ("ya", 16, BF),
+    ("jba", 72, I32), ("gt", 16, F32), ("Dj", 768, BF), ("Lab", 32, U16), ("ya", 16, BF),
     ("mT", 256, BF), ("wi", 48, F16), ("wT", 64, BF), ("R0w", 768, F16),
     ("R0k", 128, BF), ("xsc", 256, F32), ("Dx", 128, F16),
     ("Lx", 32, U16), ("cnt", 16, BF), ("Ai", 16, I32), ("Aa", 16, I32), ("cA", 16, F32),
-    ("ci", 16, I32), ("cf", 48, F32), ("cb", 2560, BF), ("ce", 1792, BF), ("d0", 1536, BF), ("k37", 128, F16),
-    ("d0c", 128, F32), ("cl", 64, U16), ("tf", 768, F32), ("tb", 640, BF), ("m2", 272, BF), ("kz", 384, BF),
+    ("ci", 16, I32), ("cf", 48, F32), ("cb", 2816, BF), ("ce", 1792, BF), ("d0", 1824, BF), ("k37", 128, F16),
+    ("d0c", 128, F32), ("cl", 64, U16), ("tf", 768, F32), ("tb", 640, BF), ("m2", 352, BF), ("kz", 384, BF),
+    ("dAB", 240, F32), ("usc", 256, I32), ("sab", 240, I32),
 ):
     _sb(_n, _c, _d)
 SCRATCH["nf"] = ("sbuf", [128, 16, 32], F16)
@@ -52,30 +53,41 @@ SEMAPHORES = (["cV", "cS", "cP", "cG", "lsem", "rG1", "rG2", "rC0", "rC1", "rB0"
                "rE00", "rE01", "rE10", "rE11", "rL0", "rL1"]
               + ["l" + n for n in LOADS] + list(STORES) + ["d%d%d" % (t, c) for t in range(RO) for c in range(8)])
 
-ENG = dict(sg="VVSSVSSS", eg="SSSSSSSS", ind="VVVVVVVV",
+ENG = dict(sg="VSSVVSSS", eg="SSSSSSSS", ind="VVVSSVVS",
+           q16="SV", key="SS", Lk="SS", xx="SS", u32="SV", uvi="VS", Lo="VV", n16="SV", qf="SV", mT="SS",
+           K16="SS", wi="VV", R0j="VV", Lab="SS", Laa="V", SL="VS", yb="SS", ya="SS", Lb="VV", Ai="S", cA="S",
+           Cw="VV", cnt="V", LJ="SV", nf0="VS", nf1="SS", x2="SV", Pinc="V", mj12="S", dAB="S", pre="S",
+           Dk="SS", Db="SS", Dj="S", Da="S", rm="V", k0="S", xn="V", x4="SS", Dx="S", c0="V" * 24, c1="S" * 60)
+ENG.update(sg="VVSSVSSS", ind="VVVVVVVV",
            q16="VS", key="SS", Lk="VS", xx="VS", u32="SS", uvi="VS", Lo="VS", n16="VS", qf="SS", mT="SS",
-           K16="SS", wi="SS", R0j="SS", Lab="SS", Laa="S", SL="S", yb="VS", ya="SS", Lb="VV", Dd="S", Ai="S", cA="S",
+           K16="SS", wi="SS", R0j="SS", Lab="SS", Laa="S", SL="S", yb="VS", ya="SS", Lb="VV", Ai="S", cA="S",
            Cw="SS", cnt="S", LJ="VS", nf0="VV", nf1="SS", x2="VV", Pinc="S", mj12="S",
-           Dk="SS", Db="SS", Dj="S", Da="S", rm="S", k0="S", xn="S", Du="SS", x4="VV", Dx="S", c0="V" * 24, c1="S" * 60)
+           Dk="SS", Db="SS", Dj="S", Da="S", rm="S", k0="S", xn="S", x4="VV", Dx="S")
+ENG.update(ind="VVSVVVVV", key="VS", Lk="SS", xx="SS", mT="VV", Laa="V", SL="V", yb="SV", Ai="V", nf0="SS", nf1="VS",
+           x2="SS", rm="V", k0="V", x4="VS", Dx="V")
 PARTS = ("mT", "qf", "dx", "ix")
 WIDEK = "wn"
-WIDEU = "ww"
 FOLD = False
+TAIL, UD, SPLIT = 0, 1, 1
+JM = 0
+FB, LB = "PT1", "PT0"
 ADDS = ("DDFFDDFF",) * 3
 BANKS = ("A0A0A0A0A0A0A0A0", "B0B1A1A0B0B1A1A0")
 FILL = (0, 0)
-AHEAD = False
+LOAD = 2.8
 SHARE = 0.3
 FOUR = True
-DMA = (1000.0, 800.0, 1100.0)
-LINK = (600.0, 1000.0, 150.0, 13.0)
+DMA = (700.0, 600.0, 800.0)
+RELAY = ("rC",)
+GOALS = 1
+LINK = (600.0, 900.0, 120.0, 10.0, 6.0)
 MKSPLIT = True
 MARKS = 1
 BASE = (0.52, 1.56, 3.8, 1.0, 1.0)
-CASES = ((0.6, 1.9, 5.0, 0.8, 0.8), (0.52, 1.2, 2.5, 1.3, 1.3))
-LAT, LATS = 180.0, 110.0
-BACK = 3
-SEED, ROUNDS = 1, 13000
+CASES = ((0.6, 1.9, 5.0, 0.9, 0.8), (0.5, 1.2, 2.5, 1.2, 1.3), (0.52, 1.56, 3.8, 0.6, 1.0))
+LAT, LATS = 220.0, 220.0
+BACK = 9999
+SEED, ROUNDS = 1, 10500
 MOVES = (0.5, 1500.0, 1e9, 0.8, 2500.0, 500.0, 150.0, 3000.0, 500.0)
 TIMES = []
 
@@ -204,7 +216,11 @@ def build(case=None):
         add("G", "asel", (out, a, pat, base, cm, op, fill), [a, turn], [out] + [turn] * (out[5] > 0), 170 + 2 * nel(out))
 
     def load(q, name, out, kb, behind=()):
-        add(q, "load", (name, out), list(behind), [out], 60, sem="l" + name, lat=1800 + kb * 5.0)
+        s = add(q, "load", (name, out), list(behind), [R("ya", 10, 11)], 100)
+        after = dict((o["n"], 0.0) for o in ops if o["kind"] == "run")
+        after[s["n"]] = 1300.0
+        w = add("L", "run", (), [], [R("ya", 12, 13)], (150.0 + kb * LOAD) * DF, after=after)
+        add("R", "recv", (), [], [out], 0, sem="l" + name, lat=0, after={w["n"]: 400.0})
 
     def store(sem, fn, rd, kb):
         s = add("Y", "store", (sem, fn), rd, [], ISSUE, sem=sem)
@@ -215,9 +231,10 @@ def build(case=None):
         s = add("G", "send", (kind, src, dst, sem), [src] + [R("Qn", 0, 768)] * (kind == "A"), [R("ya", 0, 1)], LINK[0])
         after = dict((o["n"], 0.0) for o in ops if o["kind"] == "link")
         after[s["n"]] = LINK[1]
-        w = add("L", "link", (kind,), [], [R("ya", 4, 5)], (LINK[2] + kb * LINK[3]) * DF, after=after)
+        hop = sem[0][:len(RELAY[0])] in RELAY
+        w = add("L", "link", (kind,), [], [R("ya", 4, 5)], (LINK[2] + kb * LINK[3 + hop]) * DF, after=after)
         for d, sm in zip(dst, sem):
-            add("R", "recv", (kind,), [], [d], 0, sem=sm, lat=0, after={w["n"]: 400.0})
+            add("R", "recv", (kind,), [], [d], 0, sem=sm, lat=0, after={w["n"]: 400.0 + hop * (2400.0 + kb * LINK[3]) * DF})
 
     def total(out, a, sem):
         s = add("G", "sum", (out, a, sem), [out, a], [], DMA[0] * DF)
@@ -228,15 +245,16 @@ def build(case=None):
     eq_, and_, shr_ = ALU.is_equal, ALU.bitwise_and, ALU.arith_shift_right
 
     load("Y", "tu", R("Tu", 0, 128, 1, 0, 48), 24)
-    load("Y", "qn", R("Qn", 0, 768), 400)
-    load("S", "st0", R("St", 0, 3072), 600)
-    load("Y", "qk", R("Qk", 0, 768), 300, [R("Qn", 0, 768)])
-    load("Y", "gl", R("Gl0", 0, 256), 300, [R("Qn", 0, 768)])
-    load("Y", "rm", R("Rm", 0, 1), 300, [R("Qn", 0, 768)])
-    load("Y", "ot", R("Ot", 0, 256), 300, [R("Qn", 0, 768)])
-    load("Y", "ef", R("Ef", 0, 4096), 500, [R("St", 0, 3072)])
-    add("Y", "load", ("ef", R("Ef", 4096, 4720)), [R("St", 0, 3072)], [R("Ef", 4096, 4720)], 60, sem="lef2", lat=4300)
-    send("G", R("Gl0", 0, 256), [R("Gl1", 0, 256), R("Gl2", 0, 256)], ["rG1", "rG2"], 128)
+    load("Y", "qn", R("Qn", 0, 768), 384)
+    load("Y", "st0", R("St", 0, 3072), 768)
+    load("Y", "qk", R("Qk", 0, 768), 384, [R("Qn", 0, 768)])
+    load("Y", "ot", R("Ot", 0, 256), 64)
+    load("Y", "gl", R("Gl0", 0, 256), 64)
+    load("Y", "rm", R("Rm", 0, 1), 20)
+    load("Y", "ef", R("Ef", 0, 4096), 1024, [R("St", 0, 3072)])
+    load("Y", "ef2", R("Ef", 4096, 4720), 156)
+    if not GOALS:
+        send("G", R("Gl0", 0, 256), [R("Gl1", 0, 256), R("Gl2", 0, 256)], ["rG1", "rG2"], 128)
 
     def col(j, p1=128):
         return R("cf", j, j + 1, 1, 0, p1)
@@ -275,9 +293,17 @@ def build(case=None):
     def sm(a, n=8, step=1):
         return R("cb", o + a, o + a + n * step - (step - 1), step)
     C8 = R("cb", 7 * 128, 8 * 128, 16)
-    C4k, C256, Wu8, Wv8, C16p, Cp, Cp2, Wmk = sm(0), sm(8), sm(16), sm(24), sm(32), sm(48), sm(48, 16), sm(64, 16)
-    for d, c in ((C256, 256.0), (Cp, cP), (sm(64), cF64k), (sm(72), cF15), (C16p, c16P), (Wu8, cU), (Wv8, cN15)):
+    C256, C16p, Cp, Cp2, Wmk = sm(8), sm(32), sm(48), sm(48, 16), sm(64, 16)
+    for d, c in ((C256, 256.0), (Cp, cP), (sm(64), cF64k), (sm(72), cF15), (C16p, c16P)):
         con(0, d, C8, c)
+    Cn128, C128, Wv, Mbig = sm(0), sm(40), blk("cb", 20), blk("cb", 21)
+    Wu8, Wv8 = sm(16), sm(24)
+    if TAIL:
+        con(1, Cn128, C8, -128.0); con(1, C128, C8, 128.0)
+    if UD:
+        con(1, Wv, B16, cN15); con(1, Mbig, M16, -32768.0, 32768.0)
+    else:
+        con(0, Wu8, C8, cU); con(0, Wv8, C8, cN15)
     con(1, sm(56), C8, cP)
     Wd, Wi, Ws = sm(80, 24), sm(104, 24), sm(128, 24)
     fill(sm(80, 72), 0)
@@ -306,13 +332,11 @@ def build(case=None):
     fill(R("wT", 0, 64), 0); fill(R("k0i", 0, 32), 0)
     fill(R("wd", 0, 240), 0); con(1, R("wd", 112, 128), R("cb", 4 * 128, 4 * 128 + 16))
     fill(R("jba", 0, 72), 15); fill(R("Sb0", 288, 320), 0); fill(R("Sb1", 288, 320), 0)
-    if AHEAD:
-        fill(R("dj", 32, 40), 0); fill(R("jalt", 32, 40), 0)
     cOwn = col(26)
     ts(col(25), iB, 8.0, ALU.is_ge, 8.0, mul_)
     ts(R("ci", 15, 16), iP, 7, and_); ts(cOwn, R("ci", 15, 16), cAa, eq_)
-    Lz1, Lz2 = R("cl", 8, 12), R("cl", 40, 48)
-    for lst, src, step, hi, zero in ((Lz1, R("cb", 5 * 128, 5 * 128 + 4), 2.0, 0.125, 8.0), (Lz2, k8, 1.0, 1.0, 32.0)):
+    Lz1, Lz2, Lz3, k4 = R("cl", 8, 12), R("cl", 40, 48), R("cl", 12, 16), R("cb", 5 * 128, 5 * 128 + 4)
+    for lst, src, step, hi, zero in ((Lz1, k4, 2.0, 0.125, 8.0), (Lz2, k8, 1.0, 1.0, 32.0), (Lz3, k4, 2.0, 0.125, 32.0)):
         con(1, col(38), col(25), hi, -zero)
         con(1, R("cf", 40, 40 + nel(lst)), src, step, col(38))
         con(1, lst, R("cf", 40, 40 + nel(lst)), cOwn, zero)
@@ -329,7 +353,7 @@ def build(case=None):
     for r, body, head, st in ((dM3, 0.0, 1024.0, 3), (dMx, 1.0, 0.0, 16), (R("d0c", 0, 128), -BIG, 32768.0, 16),
                               (dP, -2.0 ** 99, 2.0 ** 99, 15)):
         ms(r, body); ms(R(r[1], r[2], r[3], st), head)
-    for r, body, head, st in ((dW, 1.0, -BIG, 16), (dX, 0.0, BIG, 16), (dS3, 1.0, 0.0, 3)):
+    for r, body, head, st in ((dW, 1.0, -BIG, 16), (dX, 0.0, BIG, 16), (dS3, 1.0, 0.0, 3), (R("d0", 1536, 1824), 1.0, -BIG, 12)):
         fill(r, body); fill(R(r[1], r[2], r[3], st), head)
     fill(R("St", 3072, 3088), 0)
     Tri, r15 = R("m2", 0, 240, 1, 0, 16), R("m2", 240, 264, 1, 0, 1)
@@ -339,6 +363,12 @@ def build(case=None):
     fill(r15, 15); fill(R("xu", 32, 40), 0)
     Lb8, Lgo = R("cl", 0, 8), R("cl", 32, 35)
     con(0, Lb8, k8)
+    Lb8h = R("cl", 48, 56)
+    rB, rN = R("m2", 272, 296, 1, 0, 1), R("m2", 296, 344, 1, 0, 1)
+    if TAIL:
+        con(1, Lb8h, k8, 1.0, 8.0)
+        fill(rB, 32768); fill(R("m2", 274, 320, 3, 0, 1), 0); fill(R("m2", 296, 320, 1, 0, 1), 0)
+        fill(R("m2", 320, 344, 1, 0, 1), -1); fill(R("dAB", 0, 240), 1)
     con(0, R("cf", 21, 24), R("cb", 5 * 128, 5 * 128 + 3), 16.0, cB)
     con(0, Lgo, R("cf", 21, 24), 1.0 / 3.0, -1.0 / 3.0)
     cLo, k64 = col(24, 64), blk("cb", 5, 64)
@@ -404,6 +434,10 @@ def build(case=None):
         tt(mj, IND(jj, Lgo), lv, eq_)
         tt(R("mm", 0, 48), IND(jj, Lgo), lv2, eq_)
         aff("mj12", 0, mj12, mj, -12.0)
+        j1, m1, pa, pb = R(In, 536, 560), R("mm", 24, 48), R("PB1", 48, 72), R("PB1", 72, 96)
+        if TAIL:
+            mm([(R("PB1", 48, 96), one1, rN), (pa, I4x, j1), (pa, nI, m1), (pb, Ib, j1), (pb, I4x, m1), (pb, Ib, m1)])
+            aff("dAB", 0, R("dAB", 0, 240, 5), R("PB1", 48, 96), -32768.0, -4.0)
         pl = R("PB1", 0, 48)
         mm([(pl, Ib, x) for x in ((P4,) if t == 0 else (R(Ip, 560, 608), R("t12", 0, 48)))] + [(pl, I4x, mj)])
         aff("Pinc", 0, Pinc, pl)
@@ -458,20 +492,26 @@ def build(case=None):
             aff("Lk", h, H("Lk", h, 8), pl)
             xx = H("xx", 4 * h)
             aff("xx", h, xx, IND(H("sg", h, 2048), H("Lk", h, 8)), cN15, cF15)
-            pl = R(PT[h], 400, 408)
-            mm([(pl, H("smx", h, 2048, 16, 15), Wv8), (pl, xx, Wu8)])
-            pn = R(PT[h], 256, 384)
-            mm([(pn, Wu, xx)])
-            aff("u32", h, H("u32", h), pn, bias=32.0)
-            uva = R("uva", 16 * h, 16 * h + 8)
-            aff("uvi", h, H("uvi", h, 8), pl); ts(uva, H("uvi", h, 8), 255, and_)
-            pl = R(PT[h], 408, 416)
-            if WIDEU[h] == "w":
+            pn, pu = R(PT[h], 256, 384), R(PT[h], 0, 128)
+            if UD:
+                mm([(pn, Ib, Mbig), (pn, Wv, H("smx", h, 2048, 16, 15))], final=False)
+                mm([(pn, Wu, xx)], first=False)
+                mm([(pu, Wu, xx)])
+                scan(H("usc", h), R("d0", 896, 1024), pn, add_, min_)
+                aff("u32", h, H("u32", h), pu, bias=32.0)
+                ts(H("uvi", h, 8), H("usc", h, 128, 16, 15), 255, and_)
+                aff("Lo", h, H("Lo", h, 8), H("uvi", h, 8))
+            else:
+                pl = R(PT[h], 400, 408)
+                mm([(pl, H("smx", h, 2048, 16, 15), Wv8), (pl, xx, Wu8)])
+                mm([(pn, Wu, xx)])
+                aff("u32", h, H("u32", h), pn, bias=32.0)
+                uva = R("uva", 16 * h, 16 * h + 8)
+                aff("uvi", h, H("uvi", h, 8), pl); ts(uva, H("uvi", h, 8), 255, and_)
+                pl = R(PT[h], 408, 416)
                 tt(H("Du", h), IND(uva, Lb8), M16, mul_)
                 mm([(pl, H("Du", h), C8)])
-            else:
-                tolist("Du", h, H("uva", h, 16), Lz1, H("Du", h), pl, 1.0, None)
-            aff("Lo", h, H("Lo", h, 8), pl)
+                aff("Lo", h, H("Lo", h, 8), pl)
             tt(H("tO", h), IND(R("Ot", 0, 256), H("Lo", h, 8)), H("u32", h), mul_)
             ts(H("na", h), H("tO", h), 5, shr_, 4095, and_)
             for e in range(2):
@@ -500,7 +540,7 @@ def build(case=None):
             act(part("dx", h), pd, AF.Abs)
             ts(part("ix", h), part("dx", h), 4.0, ALU.is_gt)
             pl = R("PT0", 464 + 24 * h, 488 + 24 * h)
-            mm([(pl, one1, r15), (pl, part("dx", h), Wd), (pl, part("ix", h), Wi)])
+            mm([(pl, one1, r15)] + [(pl, one1, rB)] * (h * TAIL) + [(pl, part("dx", h), Wd), (pl, part("ix", h), Wi)])
             aff("qf", h, part("qf", h), H("q16", h), bias=-1536.0)
             if not last:
                 a, b = ((0, 656 + (t == 0)), (672, 1184))[h]
@@ -585,44 +625,103 @@ def build(case=None):
                 else:
                     mm([(R(pa, 0, 512), Ib, H("eg", c, 512))] + [(blk(pa, kl), I0, H("xx", 4 * h)) for kl in range(4)])
                     ts(yb, R(pa, 0, 512), 0.0, max_, 63.0, min_)
-                mm([(R(pb, 0, 512), Ib, yb)] + [(blk(pb, kl), nI, H(Gl, h)) for kl in range(4)])
+                if SPLIT:
+                    mm([(blk(pb, kl), nI, H(Gl, h)) for kl in range(4)], final=False)
+                    mm([(R(pb, 0, 512), Ib, yb)], first=False)
+                else:
+                    mm([(R(pb, 0, 512), Ib, yb)] + [(blk(pb, kl), nI, H(Gl, h)) for kl in range(4)])
                 act(db, R(pb, 0, 512), AF.Abs)
                 if ENG["ind"][c] == "V":
                     ts(ib, db, 4.0, ALU.is_gt)
                 else:
                     act(ib, db, AF.Sign, bias=-4.5)
+                ops[-1]["tag"] = ("ind", c)
+                wi = Wi if ENG["ind"][c] == "V" else Ws
+                if c == 7 and TAIL:
+                    scan(R("hsc", 384, 672), R("d0", 1536, 1824), R(PT[1], 0, 288), add_, max_)
+                    pk = [R(FB, 288 + k, 408, 5) for k in range(5)]
+                    mm([(R(FB, 288, 408), one1, R("kz", 128, 248, 1, 0, 1))], final=False)
+                    aff("pre", 0, pk[0], R("hsc", 395, 672, 12))
+                    mm([(pk[1 + k], H("dd", 28 + k), Wd) for k in range(4)], first=False, final=False)
+                    mm([(pk[1 + k], H("ind", 28 + k), wi) for k in range(4)], first=False)
+                    continue
                 lst = []
                 for k in range(4 * c, 4 * c + 4):
-                    pl = R(PT[h], k % 16, 384, 16)
-                    lst += [(pl, H("dd", k), Wd), (pl, H("ind", k), Wi if ENG["ind"][c] == "V" else Ws)]
+                    pl = R(PT[1], k % 16, 288, 12) if h and TAIL else R(PT[h], k % 16, 384, 16)
+                    lst += [(pl, H("dd", k), Wd), (pl, H("ind", k), wi)]
                 mm(lst, 2)
-            scan(H("hsc", h, 384), dW, R(PT[h], 0, 384), add_, max_)
-        ends = R("hsc", 15, 768, 16)
-        tt(R("t48", 0, 48), ends, R("mm", 0, 48), mul_)
-        tt(R("t48", 48, 96), ends, mj, mul_)
-        scan(R("ss", 0, 96), dS3, R("t48", 0, 96), mul_, add_)
-        ts(R("jba", 0, 32), R("ss", 2, 96, 3), 15, and_)
-        tolist("Db", 0, R("jba", 0, 40), Lz2, H("Dj", 0), R("PT0", 448, 464), -128.0, Cp2, 1920.0)
-        aff("Lab", 0, R("Lab", 0, 16), R("PT0", 448, 464))
-        for h in range(2):
+            if not TAIL:
+                scan(H("hsc", h, 384), dW, R(PT[h], 0, 384), add_, max_)
+                continue
+            go, gt, jn = [R(n, a + 8 * h, a + 8 * h + 8) for n, a in ((Sb, 272), ("gt", 0), (Sb, 256))]
+            hx = H("hxs", h, 24, 3, 2)
+            if h == 0:
+                scan(H("hsc", 0, 384), dW, R(PT[0], 0, 384), add_, max_)
+                ends = R("hsc", 15, 384, 16)
+                tt(R("t48", 0, 24), ends, R("mm", 0, 24), mul_)
+                tt(R("t48", 24, 48), ends, R(In, 512, 536), mul_)
+                scan(R("ss", 0, 48), R("d0", 1152, 1200), R("t48", 0, 48), mul_, add_)
+                ts(R("jba", 0, 16), R("ss", 2, 48, 3), 15, and_)
+                pl = R(LB, 448, 456)
+                tolist("Db", 0, R("jba", 0, 40), Lz3, R("Dj", 0, 64), pl, -128.0, Cp, 1920.0)
+                aff("Lab", 0, R("Lab", 0, 8), pl)
+                tt(go, R("ss", 26, 48, 3), hx, ALU.is_gt)
+            else:
+                scan(R("sab", 0, 120), R("dAB", 0, 120), R(FB, 288, 408), add_, max_)
+                scan(R("sab", 120, 240), R("dAB", 120, 240), R(FB, 288, 408), add_, max_)
+                ts(R("jba", 24, 32), R("sab", 134, 240, 15), 15, and_)
+                tt(H("Dj", 3), IND(R("jba", 24, 32), Lb8), M16, mul_)
+                pl = R("PB1", 0, 8)
+                mm([(pl, M16, Cp), (pl, H("Dj", 3), Cn128)])
+                aff("Lab", 1, R("Lab", 8, 16), pl, bias=1920.0)
+                tt(go, R("sab", 14, 120, 15), hx, ALU.is_gt)
+                ts(R("jba", 16, 24), R("sab", 14, 120, 15), 15, and_)
             aff("yb", h, H(Sb, h), IND(H("yy", h, 2048), H("Lab", h, 8)))
-        tt(go, R("ss", 50, 96, 3), R("hxs", 2, 48, 3), ALU.is_gt)
-        if not last:
-            pl = R("PB0", 0, 16)
-            if AHEAD:
-                aff("Dd", 0, H("Dj", 3), IND(R("dj", 0, 40), Lz2), 128.0)
-                tolist("Dj", 0, R("jalt", 0, 40), Lz2, H("Dj", 1), pl, 128.0, Cp2, final=False)
-                tt(H("Dj", 4), IND(R(Sb, 272, 320), Lz2), H("Dj", 3), mul_)
-                mm([(pl, R("wd", 112 - 16 * g, 240 - 16 * g), H("Dj", 32 + g, 16)) for g in range(8)], first=False)
-            tt(R("gt", 0, 16), go, R("dj", 0, 16), mul_)
-            tt(R(Sb, 256, 272), R("gt", 0, 16), R("jalt", 0, 16), add_)
-            if not AHEAD:
+            if last:
+                continue
+            tt(gt, go, H("dj", h, 8), mul_)
+            tt(jn, gt, H("jalt", h, 8), add_)
+            if h == 0:
+                pl = R(LB, 440, 448)
+                tolist("Dj", 0, R(Sb, 256, 304), Lz3, R("Dj", 64, 128), pl, 128.0, Cp)
+            else:
+                pl = R("PB0", 0, 8)
+                if JM == 0:
+                    tt(H("Dj", 4), IND(R(Sb, 256, 272), Lb8h), M16, mul_)
+                if JM > 0:
+                    tt(H("Dj", 1), IND(R("jalt", 8, 16), Lb8), M16, mul_)
+                if JM == 1:
+                    tt(H("Dj", 4), IND(gt, Lb8), M16, mul_)
+                if JM == 2:
+                    tt(H("Dj", 5), IND(R("dj", 8, 16), Lb8), M16, mul_)
+                    tt(H("Dj", 4), IND(R(Sb, 272, 288), Lb8h), H("Dj", 5), mul_)
+                mm([(pl, M16, Cp)] + [(pl, H("Dj", 1), C128)] * (JM > 0) + [(pl, H("Dj", 4), C128)])
+            aff("SL", h, H("SL%d" % t, h, 8), pl)
+        go = R(Sb, 272, 288)
+        if not TAIL:
+            ends = R("hsc", 15, 768, 16)
+            tt(R("t48", 0, 48), ends, R("mm", 0, 48), mul_)
+            tt(R("t48", 48, 96), ends, mj, mul_)
+            scan(R("ss", 0, 96), dS3, R("t48", 0, 96), mul_, add_)
+            ts(R("jba", 0, 32), R("ss", 2, 96, 3), 15, and_)
+            tolist("Db", 0, R("jba", 0, 40), Lz2, H("Dj", 0), R("PT0", 448, 464), -128.0, Cp2, 1920.0)
+            aff("Lab", 0, R("Lab", 0, 16), R("PT0", 448, 464))
+            for h in range(2):
+                aff("yb", h, H(Sb, h), IND(H("yy", h, 2048), H("Lab", h, 8)))
+            tt(go, R("ss", 50, 96, 3), R("hxs", 2, 48, 3), ALU.is_gt)
+            if not last:
+                pl = R("PB0", 0, 16)
+                tt(R("gt", 0, 16), go, R("dj", 0, 16), mul_)
+                tt(R(Sb, 256, 272), R("gt", 0, 16), R("jalt", 0, 16), add_)
                 tolist("Dj", 0, R(Sb, 256, 304), Lz2, H("Dj", 1), pl, 128.0, Cp2)
-            aff("SL", 0, R("SL%d" % t, 0, 16), pl)
+                aff("SL", 0, R("SL%d" % t, 0, 16), pl)
+        if not last:
             send("N", R("SL%d" % t, 0, 16), [R("LJ%d" % (t + 1), 0, 16)], ["rL%d" % t], 4)
         w = 256 if last else 288
         send("N", R(Sb, 0, w), [R("Lb%d" % t, 0, w)], ["rB%d" % t], w // 4)
-        tolist("Da", 0, R("jba", 16, 56), Lz2, H("Dj", 2), R("PT0", 432, 448), -128.0, Cp2, 1920.0)
+        if t == 0 and GOALS:
+            send("G", R("Gl0", 0, 256), [R("Gl1", 0, 256), R("Gl2", 0, 256)], ["rG1", "rG2"], 128)
+        tolist("Da", 0, R("jba", 16 - 8 * TAIL, 56 - 8 * TAIL), Lz2, H("Dj", 2), R("PT0", 432, 448), -128.0, Cp2, 1920.0)
         aff("Laa", 0, R("Lab", 16, 32), R("PT0", 432, 448))
         for h in range(2):
             aff("ya", h, H("St", 2 * t + h), IND(H("yy", h, 2048), H("Lab", 2 + h, 8)))
@@ -848,7 +947,7 @@ def order(ops):
         for b in bk[i]:
             ex.update(j for q, j in bank.get(b, {}).items() if q != qn[i])
             bank.setdefault(b, {})[qn[i]] = i
-        o["w"] = set() if o["q"] in "RL" else set(j for j in hard[i] | ex if ops[j]["kind"] not in ("send", "sum"))
+        o["w"] = set() if o["q"] in "RL" else set(j for j in hard[i] | ex if ops[j]["kind"] not in ("send", "sum", "load"))
     pos = {}
     for p, o in enumerate(out):
         pos[o["n"]] = p
@@ -874,7 +973,7 @@ def order(ops):
                 o["need"].append((s, j))
                 ops[j]["inc"] = True
         o["know"] = dict(mine) if o["q"] != "R" else {}
-        if "sem" not in o and o["kind"] not in ("send", "sum"):
+        if "sem" not in o and o["kind"] not in ("send", "sum", "load"):
             own.append(o["n"])
     tick = {}
     for o in out:
@@ -905,17 +1004,41 @@ def goal_engines(T, topo, r):
     return both[:len(both) // 2], both[len(both) // 2:]
 
 
+def helper(T, topo, r):
+    c, nxt = T.cores[r], T.cores[(r + 1) % len(T.cores)]
+    if topo.chip(c) == topo.chip(nxt):
+        return None
+    free = [x for x in topo.cores_of(c) if T.rank_of(x) is None and topo.may_write(x, nxt)]
+    return ([x for x in free if topo.die(x) != topo.die(c)] + free + [None])[0]
+
+
+def handed(o):
+    return o["kind"] == "send" and o["args"][3][0][:len(RELAY[0])] in RELAY
+
+
 def rank_program(g, core, T, topo):
-    from_rank = T.rank_of(core)
-    if from_rank is None:
-        return
-    r = from_rank
+    r = T.rank_of(core)
     n = len(T.cores)
     if not PLAN:
         ops = build()
         PLAN.append(ops)
         PLAN.append(order(ops))
     ops, out = PLAN
+    if r is None:
+        for r in range(n):
+            if helper(T, topo, r) == core:
+                nxt, sent = T.cores[(r + 1) % n], 0
+                rid, pid, _ = topo.addr(nxt)
+                for o in out:
+                    if handed(o):
+                        d, s = ap(T, o["args"][2][0]), T.sem[o["args"][3][0]]
+                        g.wait_ge(s, len(topo.engines(T.cores[r], core)))
+                        g.remote_dma(d, d, s, T.sem["lsem"], pid, rid, topo.mask(core, nxt))
+                        sent += len(topo.engines(core, nxt))
+                if sent:
+                    g.wait_ge(T.sem["lsem"], sent)
+        return
+    hlp = helper(T, topo, r)
     Q = {"V": g.vector, "S": g.scalar, "P": g.tensor, "G": g, "Y": g.sync}
     nxt, nx2, prv = T.cores[(r + 1) % n], T.cores[(r + 2) % n], T.cores[(r - 1) % n]
     arr = {"rG1": len(goal_engines(T, topo, (r - 1) % n)[0]), "rG2": len(goal_engines(T, topo, (r - 2) % n)[1])}
@@ -958,8 +1081,8 @@ def rank_program(g, core, T, topo):
         elif k == "asel":
             ins = q.affine_select(ap(T, a[0]), ap(T, a[1]), a[2], a[5], a[6], a[3], a[4])
         elif k == "load":
-            src = T[a[0]][:, 0:nel(a[1])] if o["sem"] == "lef2" else T[a[0]][:]
-            q.dma_start(ap(T, a[1]), src).then_inc(T.sem[o["sem"]], 16)
+            src = T["ef"][:, 0:nel(a[1])] if a[0] == "ef2" else T[a[0]][:]
+            q.dma_start(ap(T, a[1]), src).then_inc(T.sem["l" + a[0]], 16)
             continue
         elif k == "sum":
             q.dma_start(ap(T, a[0]), ap(T, a[1]), accum_op=ALU.add).then_inc(T.sem[a[2]], 16)
@@ -992,9 +1115,10 @@ def rank_program(g, core, T, topo):
                                                       dsts=[ap(T, a[2][0])], alu_op=1)], local_sem=T.sem["lsem"])
                 lsum += len(topo.engines(core, nxt))
             else:
-                rid, pid, _ = topo.addr(nxt)
-                q.remote_dma(ap(T, a[2][0]), ap(T, a[1]), T.sem[a[3][0]], T.sem["lsem"], pid, rid, topo.mask(core, nxt))
-                lsum += len(topo.engines(core, nxt))
+                to = hlp if hlp is not None and handed(o) else nxt
+                rid, pid, _ = topo.addr(to)
+                q.remote_dma(ap(T, a[2][0]), ap(T, a[1]), T.sem[a[3][0]], T.sem["lsem"], pid, rid, topo.mask(core, to))
+                lsum += len(topo.engines(core, to))
             continue
         if o.get("inc"):
             ins.then_inc(T.sem["c" + o["q"]], 1)

@@ -7,6 +7,11 @@ AF = ActivationFunctionType
 BF, F32, I32, U16, F16 = "bfloat16", "float32", "int32", "uint16", "float16"
 RO = 3
 BIG = float(1 << 23)
+EIGHTS = float(3 << 25)
+SLPOS = 1
+
+MERGE = 1
+MSG = U16 if MERGE else BF
 
 SCRATCH = {}
 
@@ -19,26 +24,28 @@ for _n, _c, _d in (
     ("St", 3088, BF), ("Ef", 4720, BF), ("Ot", 256, BF), ("Qn", 768, I32), ("Qk", 768, I32), ("Tu", 128, I32),
     ("Tub", 176, BF), ("Rm", 16, BF), ("Gl0", 256, BF), ("Gl1", 256, BF), ("Gl2", 256, BF),
     ("Cw0", 768, I32), ("Cw1", 768, I32), ("Cw2", 768, I32), ("Cr0", 768, I32), ("Cr1", 768, I32),
-    ("In0", 1184, F16), ("In1", 1184, F16), ("In2", 1184, F16), ("Li0", 1184, F16), ("Li1", 1184, F16), ("Cf", 768, F32),
+    ("In0", 1440, F16), ("In1", 1440, F16), ("In2", 1440, F16), ("Li0", 1440, F16), ("Li1", 1440, F16), ("Cf", 768, F32),
+    ("Cs0", 768, I32), ("Cs1", 768, I32),
     ("C1", 768, I32), ("C2", 768, I32), ("K16", 768, F16), ("wsc", 768, F32),
-    ("Sb0", 400, BF), ("Sb1", 400, BF), ("Sb2", 400, BF), ("Lb0", 400, BF), ("Lb1", 400, BF), ("Lb2", 256, BF),
+    ("Sb0", 272, MSG), ("Sb1", 272, MSG), ("Sb2", 256, BF), ("Lb0", 272, MSG), ("Lb1", 272, MSG), ("Lb2", 256, BF),
+    ("Sc0", 64, BF), ("Sc1", 64, BF), ("Sc2", 64, BF), ("Lc0", 64, BF), ("Lc1", 64, BF),
     ("sg", 4096, BF), ("smx", 4096, BF), ("eg", 4096, BF), ("yy", 4096, BF), ("dd", 4096, BF), ("ind", 4096, BF),
-    ("P40", 48, BF), ("pmin", 48, I32), ("mm", 48, BF), ("jj", 16, I32), ("mj4", 48, BF), ("pm2", 48, I32), ("jalt", 40, I32),
-    ("k0i", 32, I32), ("uvh", 16, BF), ("xn", 16, F16), ("rep", 16, F32), ("xu", 40, F32), ("sh", 272, BF),
-    ("dj", 40, F32), ("LJ0", 16, U16), ("LJ1", 16, U16), ("LJ2", 16, U16), ("SL0", 16, U16), ("SL1", 16, U16), ("R0j", 256, BF),
-    ("wd", 240, BF), ("mb", 512, BF), ("t12", 48, BF), ("Pfin", 48, BF), ("Pout", 128, F32),
+    ("P40", 48, BF), ("pmin", 48, I32), ("kj", 48, BF), ("km", 48, BF), ("jj", 40, I32), ("mj4", 48, BF), ("pm2", 48, I32),
+    ("k0i", 32, I32), ("xn", 16, F16), ("rep", 16, F32), ("xu", 40, F32), ("sh", 272, BF),
+    ("dja", 32, I32), ("LJ0", 16, U16), ("LJ1", 16, U16), ("LJ2", 16, U16), ("SL0", 16, U16), ("SL1", 16, U16), ("R0j", 256, BF),
+    ("wd", 160, BF), ("t12", 48, BF), ("Pfin", 48, BF), ("Pout", 128, F32),
     ("q32", 256, I32), ("q16", 256, U16), ("key", 256, F16), ("msc", 256, I32),
-    ("k0", 32, BF), ("Dk", 256, BF), ("Lk", 16, U16), ("xx", 1024, BF),
-    ("uvi", 16, I32), ("uva", 32, I32), ("Du", 256, BF), ("Lo", 16, U16), ("u32", 256, F32), ("tO", 256, I32),
-    ("na", 256, I32), ("n16", 256, U16), ("dx", 256, BF), ("ix", 256, BF),
-    ("hxm", 48, F32), ("hxs", 48, F32), ("hsc", 768, F32), ("t48", 96, F32), ("ss", 96, I32),
-    ("jba", 72, I32), ("gt", 16, F32), ("Dj", 768, BF), ("Lab", 32, U16), ("ya", 16, BF),
-    ("mT", 256, BF), ("wi", 48, F16), ("wT", 64, BF), ("R0w", 768, F16),
-    ("R0k", 128, BF), ("xsc", 256, F32), ("Dx", 128, F16),
+    ("k0", 64, BF), ("Ds", 1920, BF), ("Dk", 256, BF), ("Lk", 16, U16), ("xx", 1024, BF),
+    ("uvi", 16, I32), ("Lo", 16, U16), ("u32", 256, F32), ("tO", 256, I32),
+    ("na", 256, I32), ("n16", 256, U16),
+    ("hxs", 48, F32), ("hsc", 768, F32), ("ss", 96, I32),
+    ("jba", 80, I32), ("Dj", 384, BF), ("Lab", 32, U16), ("ya", 16, BF),
+    ("wi", 48, F16), ("wT", 64, BF),
+    ("R0k", 256, BF), ("xsc", 256, F32), ("Dx", 128, F16),
     ("Lx", 32, U16), ("cnt", 16, BF), ("Ai", 16, I32), ("Aa", 16, I32), ("cA", 16, F32),
-    ("ci", 16, I32), ("cf", 48, F32), ("cb", 2816, BF), ("ce", 1792, BF), ("d0", 1824, BF), ("k37", 128, F16),
+    ("ci", 16, I32), ("cf", 64, F32), ("cb", 2816, BF), ("ce", 1792, BF), ("d0", 1536, BF), ("k37", 128, F16),
     ("d0c", 128, F32), ("cl", 64, U16), ("tf", 768, F32), ("tb", 640, BF), ("m2", 352, BF), ("kz", 384, BF),
-    ("dAB", 240, F32), ("usc", 256, I32), ("sab", 240, I32),
+    ("usc", 256, I32),
 ):
     _sb(_n, _c, _d)
 SCRATCH["nf"] = ("sbuf", [128, 16, 32], F16)
@@ -49,45 +56,49 @@ LOADS = ("tu", "qn", "qk", "st0", "gl", "rm", "ot", "ef", "ef2")
 STORES = ("o1", "o2", "o3", "o4", "o5", "o6")
 ISSUE = 300.0
 YQ = ((0, 768),)
-SEMAPHORES = (["cV", "cS", "cP", "cG", "lsem", "rG1", "rG2", "rC0", "rC1", "rB0", "rB1", "rB2",
-               "rE00", "rE01", "rE10", "rE11", "rL0", "rL1"]
-              + ["l" + n for n in LOADS] + list(STORES) + ["d%d%d" % (t, c) for t in range(RO) for c in range(8)])
+SEMAPHORES = (["cV", "cS", "cP", "cG", "lsem", "rG1", "rG2", "rC00", "rC01", "rC10", "rC11", "rB0", "rB1", "rB2",
+               "rE00", "rE01", "rE10", "rE11", "rL0", "rL1", "rJ0", "rJ1", "dq"]
+              + ["l" + n for n in LOADS] + list(STORES) + ["d%d%d" % (t, c) for t in range(RO) for c in range(8)]
+              + ["x%d%d" % (t, h) for t in range(RO) for h in range(2)])
 
-ENG = dict(sg="VSSVVSSS", eg="SSSSSSSS", ind="VVVSSVVS",
-           q16="SV", key="SS", Lk="SS", xx="SS", u32="SV", uvi="VS", Lo="VV", n16="SV", qf="SV", mT="SS",
-           K16="SS", wi="VV", R0j="VV", Lab="SS", Laa="V", SL="VS", yb="SS", ya="SS", Lb="VV", Ai="S", cA="S",
-           Cw="VV", cnt="V", LJ="SV", nf0="VS", nf1="SS", x2="SV", Pinc="V", mj12="S", dAB="S", pre="S",
-           Dk="SS", Db="SS", Dj="S", Da="S", rm="V", k0="S", xn="V", x4="SS", Dx="S", c0="V" * 24, c1="S" * 60)
-ENG.update(sg="VVSSVSSS", ind="VVVVVVVV",
-           q16="VS", key="SS", Lk="VS", xx="VS", u32="SS", uvi="VS", Lo="VS", n16="VS", qf="SS", mT="SS",
-           K16="SS", wi="SS", R0j="SS", Lab="SS", Laa="S", SL="S", yb="VS", ya="SS", Lb="VV", Ai="S", cA="S",
-           Cw="SS", cnt="S", LJ="VS", nf0="VV", nf1="SS", x2="VV", Pinc="S", mj12="S",
-           Dk="SS", Db="SS", Dj="S", Da="S", rm="S", k0="S", xn="S", x4="VV", Dx="S")
-ENG.update(ind="VVSVVVVV", key="VS", Lk="SS", xx="SS", mT="VV", Laa="V", SL="V", yb="SV", Ai="V", nf0="SS", nf1="VS",
-           x2="SS", rm="V", k0="V", x4="VS", Dx="V")
-PARTS = ("mT", "qf", "dx", "ix")
-WIDEK = "wn"
-FOLD = False
-TAIL, UD, SPLIT = 0, 1, 1
-JM = 0
-FB, LB = "PT1", "PT0"
+ENG = dict(sg="VVSSVSSS", eg="SSSSSSSS", ind="VVSVVVVV", q16="VS", key="VS", Lk="SS", xx="SS", u32="SS", Lo="VS", n16="VS",
+           qf="SS", mT="VV", K16="SS", wi="SS", R0j="SS", Lab="SS", Laa="V", SL="V", yb="SV", ya="SS", Lb="VV", Ai="V", cA="S",
+           Cw="SS", cnt="S", LJ="VS", nf0="SS", nf1="VS", x2="SS", Pinc="S", mj12="S", Dk="SS", Db="SS", Dj="S", Da="S",
+           km="VV", rm="V", k0="VV", xn="SS", x4="VS", Dx="SS", c0="V" * 24, c1="S" * 80)
+PARTS = ("mT", "qf", "dx", "ix", "rw")
+CUT = (1, 1)
+QSEND = 2
+WIDEK = "nn"
+XDMA = 1
+QSUM = 1
 ADDS = ("DDFFDDFF",) * 3
-BANKS = ("A0A0A0A0A0A0A0A0", "B0B1A1A0B0B1A1A0")
+BANKS = ("A0A0A0A0A0A0A0A0", "B0B1A1A0B0B1A1A0", "B1B0A0A1B1B0A0A1")
+COPY = (100.0, 1300.0, 300.0)
 FILL = (0, 0)
 LOAD = 2.8
 SHARE = 0.3
-FOUR = True
 DMA = (700.0, 600.0, 800.0)
 RELAY = ("rC",)
-GOALS = 1
 LINK = (600.0, 900.0, 120.0, 10.0, 6.0)
-MKSPLIT = True
-MARKS = 1
+LATE = 0
+MARKS = ("PA0", "PA0")
+LARGE = ("PQ0", "PQ1")
+MHALF = 0
+DSH = 3
+WAW = 1
 BASE = (0.52, 1.56, 3.8, 1.0, 1.0)
 CASES = ((0.6, 1.9, 5.0, 0.9, 0.8), (0.5, 1.2, 2.5, 1.2, 1.3), (0.52, 1.56, 3.8, 0.6, 1.0))
 LAT, LATS = 220.0, 220.0
 BACK = 9999
-SEED, ROUNDS = 1, 10500
+SEED = 1
+ROUNDS = 300
+STEPS = 450000
+WEIGHTS = (2.0, 1.0, 1.0, 1.0)
+HEAT = 30.0
+SLACK = 200.0
+FLIP = 0.15
+FAR = 0.3
+TIGHT = 0.9
 MOVES = (0.5, 1500.0, 1e9, 0.8, 2500.0, 500.0, 150.0, 3000.0, 500.0)
 TIMES = []
 
@@ -142,8 +153,12 @@ def ap(T, r):
     return T[r[1]][r[5]:r[6], r[2]:r[3]:r[4]]
 
 
-def build(case=None):
+def build(case=None, other=False):
     ops = []
+
+    def eng(key, h):
+        e = ENG[key][h]
+        return dict(V="S", S="V").get(e, e) if other is True or (other and len(ops) in other) else e
     PC, GC, SC, _, DF = case or BASE
 
     def add(q, kind, args, rd, wr, cost, **kw):
@@ -186,7 +201,7 @@ def build(case=None):
         add("S", "act", (out, a, f, bias, scale), [a, bias, scale], [out], c)
 
     def aff(key, h, out, a, scale=1.0, bias=0.0):
-        if ENG[key][h] == "S":
+        if eng(key, h) == "S":
             act(out, a, bias=bias, scale=scale)
         elif scale == 1.0 and bias == 0.0:
             cp(out, a)
@@ -227,19 +242,24 @@ def build(case=None):
         add("L", "work", (), [], [R("ya", 6, 7)], SHARE * (200.0 + kb * 5.0) * DF, after={s["n"]: 700.0},
             lat=700.0 + (1 - SHARE) * (200.0 + kb * 5.0))
 
-    def send(kind, src, dst, sem, kb):
-        s = add("G", "send", (kind, src, dst, sem), [src] + [R("Qn", 0, 768)] * (kind == "A"), [R("ya", 0, 1)], LINK[0])
-        after = dict((o["n"], 0.0) for o in ops if o["kind"] == "link")
-        after[s["n"]] = LINK[1]
+    def send(kind, src, dst, sem, kb, behind=(), mark=0):
+        s = add("G", "send", (kind, src, dst, sem), [src] + list(behind), [R("ya", 0, 1)] * mark, LINK[0])
+        after = {s["n"]: LINK[1]}
         hop = sem[0][:len(RELAY[0])] in RELAY
         w = add("L", "link", (kind,), [], [R("ya", 4, 5)], (LINK[2] + kb * LINK[3 + hop]) * DF, after=after)
         for d, sm in zip(dst, sem):
             add("R", "recv", (kind,), [], [d], 0, sem=sm, lat=0, after={w["n"]: 400.0 + hop * (2400.0 + kb * LINK[3]) * DF})
 
-    def total(out, a, sem):
+    def total(out, a, sem, size=1.0):
         s = add("G", "sum", (out, a, sem), [out, a], [], DMA[0] * DF)
-        w = add("L", "work", (), [], [R("ya", 6, 7)], SHARE * DMA[2] * DF, after={s["n"]: DMA[1] * DF})
-        add("R", "recv", (), [a], [out], 0, sem=sem, lat=0, after={w["n"]: 400.0 + (1 - SHARE) * DMA[2] * DF})
+        w = add("L", "work", (), [], [R("ya", 6, 7)], SHARE * DMA[2] * size * DF, after={s["n"]: DMA[1] * DF})
+        add("R", "recv", (), [a], [out], 0, sem=sem, lat=0, after={w["n"]: 400.0 + (1 - SHARE) * DMA[2] * size * DF})
+
+    def copies(outs, a, sem):
+        s = add("Y", "dup", (outs, a, sem), [a], outs, COPY[0] * len(outs))
+        w = add("L", "work", (), [], [R("ya", 6, 7)], SHARE * COPY[2] * len(outs) * DF, after={s["n"]: COPY[1] * DF})
+        add("R", "recv", (), [a], outs, 0, sem=sem, lat=0, count=16 * len(outs),
+            after={w["n"]: 400.0 + (1 - SHARE) * COPY[2] * len(outs) * DF})
 
     add_, sub_, mul_, max_, min_ = ALU.add, ALU.subtract, ALU.mult, ALU.max, ALU.min
     eq_, and_, shr_ = ALU.is_equal, ALU.bitwise_and, ALU.arith_shift_right
@@ -253,8 +273,6 @@ def build(case=None):
     load("Y", "rm", R("Rm", 0, 1), 20)
     load("Y", "ef", R("Ef", 0, 4096), 1024, [R("St", 0, 3072)])
     load("Y", "ef2", R("Ef", 4096, 4720), 156)
-    if not GOALS:
-        send("G", R("Gl0", 0, 256), [R("Gl1", 0, 256), R("Gl2", 0, 256)], ["rG1", "rG2"], 128)
 
     def col(j, p1=128):
         return R("cf", j, j + 1, 1, 0, p1)
@@ -273,9 +291,9 @@ def build(case=None):
     con(0, cP, iP); con(0, cB, iB); con(0, cAa, iA); con(0, c16P, iP, 16.0)
     ts(cN15, iB, 15.0, ALU.is_lt); ts(cF15, iB, 15.0, eq_); ts(cF64k, iB, 15.0, eq_, 65536.0, mul_)
     con(0, col(20), iB, 2.0, 1.0); con(0, cU, col(20), cN15)
-    for d, a, c in ((cM16, R("Rm", 0, 1), -16.0), (cM4k, R("Rm", 0, 1), 4096.0), (cN16, cN15, -16.0), (cN4k, cN15, 4096.0),
-                    (cN64k, cN15, 65536.0), (cN63, cN15, 63.0)):
+    for d, a, c in ((cM4k, R("Rm", 0, 1), 4096.0), (cN4k, cN15, 4096.0), (cN64k, cN15, 65536.0), (cN63, cN15, 63.0)):
         con(1, d, a, c)
+    con(1, cN16, cN15, -16.0 - 131072.0, 131072.0); con(1, col(27), cF64k, 1.5); con(1, cM16, R("Rm", 0, 1), -16.0, cF64k)
     con(1, cJ, iB, 1.0, 3072.0); con(1, cSg, cN15, -2048.0, 1920.0)
     Ib, I0, nI, IB, M16, kk, gg, B16, Wu, Wr0, Wr1, Wr2, One, I16 = [blk("cb", j) for j in range(14)]
     k8, k16, one1 = R("cb", 5 * 128, 5 * 128 + 8), R("cb", 5 * 128, 5 * 128 + 16), blk("cb", 12, 1)
@@ -296,18 +314,12 @@ def build(case=None):
     C256, C16p, Cp, Cp2, Wmk = sm(8), sm(32), sm(48), sm(48, 16), sm(64, 16)
     for d, c in ((C256, 256.0), (Cp, cP), (sm(64), cF64k), (sm(72), cF15), (C16p, c16P)):
         con(0, d, C8, c)
-    Cn128, C128, Wv, Mbig = sm(0), sm(40), blk("cb", 20), blk("cb", 21)
-    Wu8, Wv8 = sm(16), sm(24)
-    if TAIL:
-        con(1, Cn128, C8, -128.0); con(1, C128, C8, 128.0)
-    if UD:
-        con(1, Wv, B16, cN15); con(1, Mbig, M16, -32768.0, 32768.0)
-    else:
-        con(0, Wu8, C8, cU); con(0, Wv8, C8, cN15)
+    Wv, Mbig = blk("cb", 20), blk("cb", 21)
+    con(1, Wv, B16, cN15); con(1, Mbig, M16, -32768.0, 32768.0)
     con(1, sm(56), C8, cP)
     Wd, Wi, Ws = sm(80, 24), sm(104, 24), sm(128, 24)
-    fill(sm(80, 72), 0)
-    con(1, sm(80, 8, 3), C8, cN16); con(1, sm(82, 8, 3), C8, cM16)
+    fill(sm(104, 48), 0)
+    con(1, sm(80, 8, 3), C8, cN16); con(1, sm(81, 8, 3), C8, col(27)); con(1, sm(82, 8, 3), C8, cM16)
     con(1, sm(105, 8, 3), sm(80, 8, 3), 16.0); con(1, sm(129, 8, 3), C8, cSg)
     I4 = R("cb", o + 152, o + 200, 1, 0, 48)
     fill(R("Tub", 128, 176, 1, 0, 48), 4)
@@ -315,8 +327,8 @@ def build(case=None):
     Iq, Wr3 = blk("cb", 17), blk("cb", 19)
     I4x = blk("cb", 14)
     con(1, Iq, Ib, 0.25); con(1, I4x, Ib, 4.0)
-    lv, lv2 = R("cb", 18 * 128, 18 * 128 + 48), R("cb", 18 * 128 + 2, 18 * 128 + 50)
-    iota(R("cb", 18 * 128, 18 * 128 + 51), [[0, 17], [1, 3]], 0, 0)
+    lv = R("cb", 18 * 128, 18 * 128 + 48)
+    iota(lv, [[0, 16], [1, 3]], 0, 0)
     Ej = [blk("ce", l, 24) for l in range(3)]
     Ep = [blk("ce", 3 + l, 64) for l in range(3)]
     En = [blk("ce", 6 + l, 65) for l in range(3)]
@@ -330,52 +342,54 @@ def build(case=None):
         asel(Ej[l], ta, [[-3, 8], [0, 16]], -l, 1, ALU.not_equal, -2560.0)
     asel(E8, blk("cb", 12, 8), [[-1, 8], [0, 16]], 0, 1)
     fill(R("wT", 0, 64), 0); fill(R("k0i", 0, 32), 0)
-    fill(R("wd", 0, 240), 0); con(1, R("wd", 112, 128), R("cb", 4 * 128, 4 * 128 + 16))
-    fill(R("jba", 0, 72), 15); fill(R("Sb0", 288, 320), 0); fill(R("Sb1", 288, 320), 0)
+    fill(R("wd", 0, 48), 0); con(1, R("wd", 16, 32), R("cb", 4 * 128, 4 * 128 + 16))
+    fill(R("jba", 0, 80), 15); fill(R("jj", 32, 40), 0)
+    for t in range(RO):
+        fill(R("Sc%d" % t, 32, 64), 0)
     cOwn = col(26)
     ts(col(25), iB, 8.0, ALU.is_ge, 8.0, mul_)
     ts(R("ci", 15, 16), iP, 7, and_); ts(cOwn, R("ci", 15, 16), cAa, eq_)
-    Lz1, Lz2, Lz3, k4 = R("cl", 8, 12), R("cl", 40, 48), R("cl", 12, 16), R("cb", 5 * 128, 5 * 128 + 4)
-    for lst, src, step, hi, zero in ((Lz1, k4, 2.0, 0.125, 8.0), (Lz2, k8, 1.0, 1.0, 32.0), (Lz3, k4, 2.0, 0.125, 32.0)):
-        con(1, col(38), col(25), hi, -zero)
+    Lz1, Lz2, Lz3, k4 = R("cl", 8, 12), R("cl", 40, 48), R("cl", 16, 24), R("cb", 5 * 128, 5 * 128 + 4)
+    for lst, src, step, hi, zero, odd in ((Lz1, k4, 2.0, 0.125, 8.0, 0), (Lz2, k8, 1.0, 1.0, 32.0, 0), (Lz3, k8, 2.0, 2.0, 32.0, 1)):
+        con(1, col(38), col(25), hi, odd - zero)
         con(1, R("cf", 40, 40 + nel(lst)), src, step, col(38))
         con(1, lst, R("cf", 40, 40 + nel(lst)), cOwn, zero)
     k37 = blk("k37", 0, 1)
-    fill(R("uva", 0, 32), 0)
     cPar, cPb = (col(29), col(30)), (col(31), col(32))
     ts(R("ci", 14, 15), iA, 1, and_)
     con(1, cPar[1], R("ci", 14, 15)); con(1, cPar[0], R("ci", 14, 15), -1.0, 1.0)
     con(1, cPb[1], R("ci", 14, 15), -2048.0); con(1, cPb[0], R("ci", 14, 15), 2048.0, -2048.0)
     iota(blk("kz", 2, 1), [[1, 16], [0, 8]], 0, 0)
     con(1, k37, blk("kz", 2, 1), 37.0)
-    dMx, dW, dX, dS3, dM3 = R("d0", 0, 512), R("d0", 512, 896), R("d0", 896, 1152), R("d0", 1152, 1248), R("d0", 1248, 1296)
+    dMx, dW, dX, dM3 = R("d0", 0, 512), R("d0", 512, 896), R("d0", 896, 1152), R("d0", 1248, 1296)
     dP = R("d0", 1296, 1536)
     for r, body, head, st in ((dM3, 0.0, 1024.0, 3), (dMx, 1.0, 0.0, 16), (R("d0c", 0, 128), -BIG, 32768.0, 16),
                               (dP, -2.0 ** 99, 2.0 ** 99, 15)):
         ms(r, body); ms(R(r[1], r[2], r[3], st), head)
-    for r, body, head, st in ((dW, 1.0, -BIG, 16), (dX, 0.0, BIG, 16), (dS3, 1.0, 0.0, 3), (R("d0", 1536, 1824), 1.0, -BIG, 12)):
+    for r, body, head, st in ((dW, 1.0, -BIG, 16), (dX, 0.0, BIG, 16)):
         fill(r, body); fill(R(r[1], r[2], r[3], st), head)
     fill(R("St", 3072, 3088), 0)
     Tri, r15 = R("m2", 0, 240, 1, 0, 16), R("m2", 240, 264, 1, 0, 1)
     fill(R("sh", 0, 16), 0); con(1, R("sh", 16, 144), Ib, 2.0 ** -13); con(1, R("sh", 144, 272), Ib, -2.0 ** -13)
     fill(R("tb", 384, 624, 1, 0, 16), 0)
     asel(Tri, R("tb", 384, 624, 1, 0, 16), [[0, 16], [-1, 15]], -1, 1, ALU.is_ge, 0.5)
-    fill(r15, 15); fill(R("xu", 32, 40), 0)
-    Lb8, Lgo = R("cl", 0, 8), R("cl", 32, 35)
-    con(0, Lb8, k8)
-    Lb8h = R("cl", 48, 56)
-    rB, rN = R("m2", 272, 296, 1, 0, 1), R("m2", 296, 344, 1, 0, 1)
-    if TAIL:
-        con(1, Lb8h, k8, 1.0, 8.0)
-        fill(rB, 32768); fill(R("m2", 274, 320, 3, 0, 1), 0); fill(R("m2", 296, 320, 1, 0, 1), 0)
-        fill(R("m2", 320, 344, 1, 0, 1), -1); fill(R("dAB", 0, 240), 1)
-    con(0, R("cf", 21, 24), R("cb", 5 * 128, 5 * 128 + 3), 16.0, cB)
-    con(0, Lgo, R("cf", 21, 24), 1.0 / 3.0, -1.0 / 3.0)
+    fill(r15, 15); fill(R("xu", 0, 40), 0)
+    if MHALF:
+        fill(R("k0", 0, 64), 0)
+
+    Lb8, Lodd, Lgo = R("cl", 0, 8), R("cl", 24, 32), R("cl", 32, 35)
+    if "w" in WIDEK:
+        con(0, Lb8, k8)
+    con(0, Lodd, k8, 2.0, 1.0)
+    i48, third = R("cf", 21, 24), R("ci", 10, 13)
+    con(0, i48, R("cb", 5 * 128, 5 * 128 + 3), 16.0, cB)
+    con(0, third, i48, 1.0 / 3.0, -1.0 / 3.0)
+    con(0, Lgo, third, 2.0, 1.0)
+    fill(R("km", 0, 48), 0)
     cLo, k64 = col(24, 64), blk("cb", 5, 64)
     ts(cLo, col(0, 64), 32.0, ALU.is_lt)
     fill(R("ce", 768, 1152, 1, 0, 65), 1)
-    iota(R("R0w", 0, 768, 1, 0, 65), [[1, 768]], 0, 0)
-    fill(blk("R0k", 0, 65), 1)
+    fill(R("R0k", 0, 128 + 128 * MHALF, 1, 0, 65), 1)
     con(1, col(34, 64), cLo, 2 * B22, -B22); con(1, col(35, 64), cLo, -31 * B22, 16 * B22)
     con(1, blk("tb", 0, 64), k64, col(34, 64), col(35, 64))
     for e in range(2):
@@ -388,11 +402,14 @@ def build(case=None):
     con(1, col(36, 64), cLo, -8192.0, 4096.0); con(1, col(37, 64), cLo, -4096.0, 4096.0)
     con(1, blk("tb", 1, 64), k64, col(36, 64), col(37, 64))
     for e in range(2):
-        for h in range(2):
+        for h in range(2 - MHALF):
             asel(blk("ce", 9 + h, 32 * e + 32, 32 * e), blk("tb", 1, 32 * e + 32, 32 * e), [[-1, 8], [0, 16]], -16 * h, 1)
     act(blk("Pout", 0, 65, 64), blk("cb", 5, 65, 64), AF.Square, bias=32.0, scale=64.0)
-    for h in range(2):
+    for h in range(2 - MHALF):
         con(1, blk("ce", 9 + h, 65, 64), blk("Pout", 0, 65, 64), 1.0, -1024.0)
+
+    for s in range(15 * (DSH < RO)):
+        asel(blk("Ds", s), R("sh", 144, 272), [[-1, 128]], s + 1, 1, ALU.not_equal, 2.0 ** -13)
 
     def H(name, h, n=128, step=1, a=0):
         return R(name, h * n + a, h * n + n, step)
@@ -401,64 +418,65 @@ def build(case=None):
     mm([(R("PQ0", 0, 48), R("Tub", 0, 128, 1, 0, 48), I4)])
     tt(R("P40", 0, 48), R("PQ0", 0, 48), lv, add_)
 
-    def tolist(key, h, win, lst, D, pl, scale, c, bias=0.0, final=True):
+    def tolist(key, h, win, lst, D, pl, scale, c, bias=0.0):
         w = nel(pl)
         aff(key, h, R(D[1], D[2], D[2] + 8 * w), IND(win, lst), scale, bias)
-        mm([(pl, M16, c)] * (c is not None) + [(pl, R("wd", 112 - 16 * g, 240 - 16 * g), R(D[1], D[2] + w * g, D[2] + w * g + w))
-                                               for g in range(8)], final=final)
+        mm([(pl, M16, c) if c else (pl, one1, R("kz", 128, 128 + w, 1, 0, 1))]
+           + [(R(pl[1], pl[2], pl[3], 1, g // 2 * 32, g // 2 * 32 + 32), R("wd", 16 - g % 2 * 16, 48 - g % 2 * 16),
+               R(D[1], D[2] + w * g, D[2] + w * g + w)) for g in range(8)])
 
     for t in range(RO):
         last = t == RO - 1
         P4 = R("P40", 0, 48)
-        Cw, Gl, Sb, Lp, LJ = "Cw%d" % t, "Gl%d" % t, "Sb%d" % t, "Lb%d" % (t - 1), "LJ%d" % t
+        Cw, Gl, Sb, Sc, LJ = "Cw%d" % t, "Gl%d" % t, "Sb%d" % t, "Sc%d" % t, "LJ%d" % t
         cA = 2048.0 if t == 0 else R("cA", 0, 1)
         ADD = ADDS[t]
         PT = ["PT0", "PT1"]
         In, Ip = "In%d" % t, "Li%d" % (t - 1)
-        mj, Pinc, mj12, go = R(In, 512, 560), R(In, 560, 608), R(In, 608, 656), R(Sb, 272, 288)
+        mj, Pinc, mj12, go = R(In, 640, 688), R(In, 688, 736), R(In, 736, 784), R(Sc, 33, 64, 2)
+        kj, km = R("kj", 0, 48), R("km", 0, 48)
 
         def part(name, h, buf=In):
-            return R(buf, 672 * h + 128 * PARTS.index(name), 672 * h + 128 * PARTS.index(name) + 128)
+            return R(buf, 800 * h + 128 * PARTS.index(name), 800 * h + 128 * PARTS.index(name) + 128)
+        for h in range(2):
+            iota(part("rw", h), [[1, 128]], 256 * t + 128 * h, 0)
+        J = "jj" if t == 0 else "Lc%d" % (t - 1)
+        jj, jw = R(J, 1, 32, 2), R(J, 0, 40)
         if t == 0:
-            jj = R("jj", 0, 16)
             scan(R("pmin", 0, 48), dM3, P4, add_, min_)
             ts(jj, R("pmin", 2, 48, 3), 3, and_)
             for h in range(2):
-                tt(H("Dk", h), IND(H("jj", h, 8), Lb8), M16, mul_)
+                tt(H("Dk", h), IND(H("jj", h, 16), Lodd), M16, mul_)
                 pl = R(PT[h], 384, 392)
                 mm([(pl, M16, Cp), (pl, H("Dk", h), C256)])
                 aff("LJ", h, H(LJ, h, 8), pl)
         else:
-            jj = R(Lp, 256, 272)
-            tt(R("t12", 0, 48), IND(R(Lp, 272, 288), Lgo), R(Ip, 608, 656), mul_)
-        tt(mj, IND(jj, Lgo), lv, eq_)
-        tt(R("mm", 0, 48), IND(jj, Lgo), lv2, eq_)
+            tt(R("t12", 0, 48), IND(R(J, 32, 64), Lgo), R(Ip, 736, 784), mul_)
+        tt(mj, IND(jw, Lgo), lv, eq_)
+        tt(kj, IND(jw, Lgo), lv, ALU.is_lt)
+        for l in (1, 2):
+            aff("km", l - 1, R("km", l, 48, 3), R(In, 639 + l, 688, 3), -1.0, 1.0)
         aff("mj12", 0, mj12, mj, -12.0)
-        j1, m1, pa, pb = R(In, 536, 560), R("mm", 24, 48), R("PB1", 48, 72), R("PB1", 72, 96)
-        if TAIL:
-            mm([(R("PB1", 48, 96), one1, rN), (pa, I4x, j1), (pa, nI, m1), (pb, Ib, j1), (pb, I4x, m1), (pb, Ib, m1)])
-            aff("dAB", 0, R("dAB", 0, 240, 5), R("PB1", 48, 96), -32768.0, -4.0)
         pl = R("PB1", 0, 48)
-        mm([(pl, Ib, x) for x in ((P4,) if t == 0 else (R(Ip, 560, 608), R("t12", 0, 48)))] + [(pl, I4x, mj)])
+        mm([(pl, Ib, x) for x in ((P4,) if t == 0 else (R(Ip, 688, 736), R("t12", 0, 48)))] + [(pl, I4x, mj)])
         aff("Pinc", 0, Pinc, pl)
         if not last:
             scan(R("pm2", 0, 48), dM3, Pinc, add_, min_)
-            ts(R("jalt", 0, 16), R("pm2", 2, 48, 3), 3, and_)
-            tt(R("dj", 0, 16), jj, R("jalt", 0, 16), sub_)
+            ts(R("dja", 1, 32, 2), R("pm2", 2, 48, 3), 3, and_)
+            tt(R("dja", 0, 32, 2), jj, R("dja", 1, 32, 2), sub_)
         if t == 0:
-            aff("rm", 0, R(In, 656, 657), R("Rm", 0, 1))
+            aff("rm", 0, R(In, 784, 785), R("Rm", 0, 1))
             for h in range(2):
-                aff("Cw", h, H(Cw, h, 384) if FOLD else R("PQ%d" % h, 0, 384), H("Qk", h, 384), 4096.0)
-                if not FOLD:
+                aff("Cw", h, H(Cw, h, 384) if QSUM else R("PQ%d" % h, 0, 384), H("Qk", h, 384), 4096.0)
+                if not QSUM:
                     tt(H(Cw, h, 384), H("Qn", h, 384), R("PQ%d" % h, 0, 384), add_)
-            send("A" if FOLD else "N", R(Cw, 0, 768), [R("Cr0", 0, 768)], ["rC0"], 600 if FOLD else 384)
-        elif not last:
-            send("N", R(Cw, 0, 768), [R("Cr%d" % t, 0, 768)], ["rC%d" % t], 384)
+            if QSUM:
+                total(R(Cw, 0, 768), R("Qn", 0, 768), "dq", 2.0)
         if last:
             store("o6", ("ys", 0, R("St", 0, 1280)), [R("St", 0, 1280)], 320)
             ops[-2].update(wr=[early], lat=3500.0)
         for h in range(2):
-            lj = H(LJ, h, 8)
+            lj = R("Lb%d" % (t - 1), 256 + 8 * h, 264 + 8 * h) if MERGE and t else H(LJ, h, 8)
             if t == 0:
                 aff("q16", h, H("q16", h), IND(R("Qn", 128 * h, 768), lj))
                 aff("key", h, H("key", h), IND(R("Qk", 128 * h, 768), lj), bias=1025.0)
@@ -467,18 +485,14 @@ def build(case=None):
                 aff("q16", h, H("q16", h), H("q32", h))
                 aff("key", h, H("key", h), IND(H(Cw, h, 384), lj), 1.0 / 4096, 1024.625)
             keys = [(R(PT[h], 0, 256), one1, kz), (R(PT[h], 0, 128), H("key", h), I16)]
-            if MKSPLIT:
-                mm(keys[:2 - (t == 0)], final=False)
+            mm(keys[:2 - (t == 0)], final=False)
             for c in range(4):
                 aff("sg", 4 * h + c, H("sg", 4 * h + c, 512), IND(R("St", 0, 3072), H("q16", 4 * h + c, 32)))
                 scan(H("smx", 4 * h + c, 512), dMx, H("sg", 4 * h + c, 512), mul_, max_)
-                if MKSPLIT:
-                    mm([(R(PT[h], k, 256, 16, 32 * c, 32 * c + 32), H("sg", 4 * h + c, 512, 16, k), Wmk) for k in range(16)],
-                       first=False, final=c == 3 and t > 0, stop=t > 0)
-            if MKSPLIT and t == 0:
+                mm([(R(PT[h], k, 256, 16, 32 * c, 32 * c + 32), H("sg", 4 * h + c, 512, 16, k), Wmk) for k in range(16)],
+                   first=False, final=c == 3 and t > 0, stop=t > 0)
+            if t == 0:
                 mm(keys[1:], first=False)
-            if not MKSPLIT:
-                mm(keys + [(R(PT[h], k, 256, 16), H("sg", h, 2048, 16, k), Wmk) for k in range(16)])
             scan(H("msc", h), R("d0c", 0, 128), R(PT[h], 0, 128), max_, min_)
             aff("mT", h, part("mT", h), R(PT[h], 128, 256))
             k0 = R("k0i", 16 * h, 16 * h + 8)
@@ -493,60 +507,41 @@ def build(case=None):
             xx = H("xx", 4 * h)
             aff("xx", h, xx, IND(H("sg", h, 2048), H("Lk", h, 8)), cN15, cF15)
             pn, pu = R(PT[h], 256, 384), R(PT[h], 0, 128)
-            if UD:
-                mm([(pn, Ib, Mbig), (pn, Wv, H("smx", h, 2048, 16, 15))], final=False)
-                mm([(pn, Wu, xx)], first=False)
-                mm([(pu, Wu, xx)])
-                scan(H("usc", h), R("d0", 896, 1024), pn, add_, min_)
-                aff("u32", h, H("u32", h), pu, bias=32.0)
-                ts(H("uvi", h, 8), H("usc", h, 128, 16, 15), 255, and_)
-                aff("Lo", h, H("Lo", h, 8), H("uvi", h, 8))
-            else:
-                pl = R(PT[h], 400, 408)
-                mm([(pl, H("smx", h, 2048, 16, 15), Wv8), (pl, xx, Wu8)])
-                mm([(pn, Wu, xx)])
-                aff("u32", h, H("u32", h), pn, bias=32.0)
-                uva = R("uva", 16 * h, 16 * h + 8)
-                aff("uvi", h, H("uvi", h, 8), pl); ts(uva, H("uvi", h, 8), 255, and_)
-                pl = R(PT[h], 408, 416)
-                tt(H("Du", h), IND(uva, Lb8), M16, mul_)
-                mm([(pl, H("Du", h), C8)])
-                aff("Lo", h, H("Lo", h, 8), pl)
+            mm([(pn, Ib, Mbig), (pn, Wv, H("smx", h, 2048, 16, 15))], final=False)
+            mm([(pn, Wu, xx)], first=False)
+            mm([(pu, Wu, xx)])
+            scan(H("usc", h), R("d0", 896, 1024), pn, add_, min_)
+            aff("u32", h, H("u32", h), pu, bias=32.0)
+            ts(H("uvi", h, 8), H("usc", h, 128, 16, 15), 255, and_)
+            aff("Lo", h, H("Lo", h, 8), H("uvi", h, 8))
             tt(H("tO", h), IND(R("Ot", 0, 256), H("Lo", h, 8)), H("u32", h), mul_)
             ts(H("na", h), H("tO", h), 5, shr_, 4095, and_)
             for e in range(2):
                 aff("nf%d" % e, h, R("nf", 256 * h + 16 * e, 256 * h + 256, 32) + (16,), H("na", h), cPar[e], cPb[e])
-            mm([(pn, one1, k37)]
-               + [(R(PT[h], 256 + b, 384, 8, 32 * a, 32 * a + 32), R("nf", 256 * h + 32 * b, 256 * h + 32 * b + 32, 1, 32 * a, 32 * a + 32),
-                   R("cb", 4 * 128, 4 * 128 + 16, 1, 32 * a, 32 * a + 32)) for a in range(4) for b in range(8)])
+            mm([(pn, one1, k37)], final=False)
+            mm([(R(PT[h], 256 + b, 384, 8, 32 * a, 32 * a + 32), R("nf", 256 * h + 32 * b, 256 * h + 32 * b + 32, 1, 32 * a, 32 * a + 32),
+                 R("cb", 4 * 128, 4 * 128 + 16, 1, 32 * a, 32 * a + 32)) for a in range(4) for b in range(8)], first=False)
             aff("n16", h, H("n16", h), pn, bias=cA)
-            four = "D" in ADD[4 * h:4 * h + 4]
-            if four or "F" in ADD[4 * h:4 * h + 4]:
+            if XDMA:
+                copies([H("xx", 4 * h + e) for e in (1, 2, 3)], xx, "x%d%d" % (t, h))
+            else:
                 aff("x2", h, H("xx", 4 * h + 1), xx)
-            if four:
                 aff("x4", h, H("xx", 2 * h + 1, 256), H("xx", 2 * h, 256))
             for c in range(4 * h, 4 * h + 4):
-                if ADD[c] == "F" and four and FOUR:
+                if ADD[c] == "F":
                     tt(H("eg", c, 512), IND(R("Ef", 0, 4720), H("n16", c, 32)), H("xx", h, 512), add_)
-                elif ADD[c] == "F":
-                    for e in range(2):
-                        tt(H("eg", 2 * c + e, 256), IND(R("Ef", 0, 4720), H("n16", 2 * c + e, 16)), H("xx", 2 * h, 256), add_)
                 else:
                     aff("eg", c, H("eg", c, 512), IND(R("Ef", 0, 4720), H("n16", c, 32)))
                 if ADD[c] == "D":
                     total(H("eg", c, 512), H("xx", h, 512), "d%d%d" % (t, c))
             pd = blk("PQ%d" % h, 3)
             mm([(pd, I0, xx), (pd, nI, H(Gl, h))])
-            act(part("dx", h), pd, AF.Abs)
+            act(part("dx", h), pd, AF.Abs, bias=cF15)
             ts(part("ix", h), part("dx", h), 4.0, ALU.is_gt)
             pl = R("PT0", 464 + 24 * h, 488 + 24 * h)
-            mm([(pl, one1, r15)] + [(pl, one1, rB)] * (h * TAIL) + [(pl, part("dx", h), Wd), (pl, part("ix", h), Wi)])
+            mm([(pl, one1, r15), (pl, part("dx", h), Wd), (pl, part("ix", h), Wi)])
             aff("qf", h, part("qf", h), H("q16", h), bias=-1536.0)
-            if not last:
-                a, b = ((0, 656 + (t == 0)), (672, 1184))[h]
-                send("N", R(In, a, b), [R("Li%d" % t, a, b)], ["rE%d%d" % (t, h)], (b - a) // 4)
-        tt(R("hxm", 0, 48), R("PT0", 464, 512), mj, mul_)
-        scan(R("hxs", 0, 48), R("d0", 1152, 1200), R("hxm", 0, 48), mul_, add_)
+        scan(R("hxs", 0, 48), kj, R("PT0", 464, 512), mul_, max_)
 
         def marks(PM):
             aff("k0", 0, R("k0", 0, 32), R("k0i", 0, 32))
@@ -557,8 +552,9 @@ def build(case=None):
             scan(R("xsc", 0, 256), dX, pl, add_, min_)
             xn = R("xn", 0, 16)
             aff("xn", 0, xn, R("xsc", 15, 256, 16))
-            mm([(R(PM, 0, 240), blk("cb", 0, 16), Tri)] + [(R(PM, s, 240, 15), R("sh", a, a + 128), xn) for s in range(15)
-                                                           for a in (15 - s, 144)])
+            mm([(R(PM, 0, 240), blk("cb", 0, 16), Tri)]
+               + [(R(PM, s, 240, 15), a, xn) for s in range(15)
+                  for a in ([blk("Ds", s)] if t >= DSH else [R("sh", 15 - s, 143 - s), R("sh", 144, 272)])])
             scan(R("xsc", 0, 240), dP, R(PM, 0, 240), max_, mul_)
             ts(R("rep", 0, 16), R("xsc", 14, 240, 15), 0.0, eq_, 4096.0, mul_)
             tt(R("xu", 0, 16), R("rep", 0, 16), xn, add_)
@@ -566,12 +562,35 @@ def build(case=None):
             ts(R("Lx", 0, 32, 2), R(PM, 256, 272), 1536.0, add_, cJ, min_)
             for c in range(16):
                 cp(IND(R("St", 0, 3088), R("Lx", 2 * c, 2 * c + 1)), H("xx", c + 24 * (c // 8), 16))
-        marks("PQ%d" % MARKS)
 
-        def update(h, buf, old, Wm):
-            PQ = "PQ%d" % h
+        def marks1(h, PM):
+            aff("k0", h, R("k0", 32 * h, 32 * h + 8), R("k0i", 16 * h, 16 * h + 8))
+            mm([(R(PM, 256, 384, 1, 32 * e, 32 * e + 32), H("k0", h, 32), Ib) for e in range(2)], False)
+            act(blk("R0k", h, 64), blk(PM, 2, 64), AF.Square, bias=cLo)
+            mm([(blk(PM, 0), blk("R0k", h, 65), Ek[0]), (blk(PM, 0), part("qf", h), Ib)])
+            scan(H("xsc", h), R("d0", 896, 1024), blk(PM, 0), add_, min_)
+            xn = H("xn", h, 8)
+            aff("xn", h, xn, H("xsc", h, 128, 16, 15))
+            mm([(R(PM, 0, 120), blk("cb", 0, 16), R("m2", 0, 120, 1, 0, 16))]
+               + [(R(PM, s, 120, 15), a, xn) for s in range(15)
+                  for a in ([blk("Ds", s)] if t >= DSH else [R("sh", 15 - s, 143 - s), R("sh", 144, 272)])])
+            scan(R("xsc", 128 * h, 128 * h + 120), R("d0", 1296, 1416), R(PM, 0, 120), max_, mul_)
+            ts(H("rep", h, 8), R("xsc", 128 * h + 14, 128 * h + 120, 15), 0.0, eq_, 4096.0, mul_)
+            tt(R("xu", 16 * h, 16 * h + 8), H("rep", h, 8), xn, add_)
+            tolist("Dx", h, H("xu", h, 16), Lz1, H("Dx", h, 64), R(PM, 256, 264), 1.0, None)
+            ts(H("Lx", h, 16, 2), R(PM, 256, 264), 1536.0, add_, cJ, min_)
+            for c in range(8):
+                cp(IND(R("St", 0, 3088), R("Lx", 16 * h + 2 * c, 16 * h + 2 * c + 1)), H("xx", c + 32 * h, 16))
+        if MHALF:
+            for h in range(2):
+                marks1(h, MARKS[h])
+        else:
+            marks(MARKS[1])
+
+        def largest(h, buf, old, new):
+            PQ = LARGE[h]
             pq = R(PQ, 0, 384)
-            mm([(blk(PQ, 0, 24), R(buf, 512 + 24 * h, 536 + 24 * h), Ib)])
+            mm([(blk(PQ, 0, 24), R(buf, 640 + 24 * h, 664 + 24 * h), Ib)])
             r0 = blk("R0j", h, 24)
             aff("R0j", h, r0, blk(PQ, 0, 24))
             lst = []
@@ -581,158 +600,138 @@ def build(case=None):
             mm(lst, 3)
             if t == 0:
                 for l in range(3):
-                    tt(H("C1", 3 * h + l), H(old, 2 * l + h), blk(PQ, l), max_)
+                    tt(H(new, 3 * h + l), H(old, 2 * l + h), blk(PQ, l), max_)
             else:
-                tt(H("C1", h, 384), H(old, h, 384), pq, max_)
-            aff("K16", h, H("K16", h, 384), H("C1", h, 384), 1.0 / 4096, 1024.625)
+                tt(H(new, h, 384), H(old, h, 384), pq, max_)
+            aff("K16", h, H("K16", h, 384), H(new, h, 384), 1.0 / 4096, 1024.625)
             mm([(blk(PQ, l), H("K16", 3 * h + l), I16) for l in range(3)], False)
             scan(H("wsc", h, 384), dW, pq, add_, max_)
             we = H("wsc", h, 384, 16, 15)
             aff("wi", h, H("wi", h, 24), we, bias=-7.5)
             tt(R("wT", 32 * h + 1, 32 * h + 25), we, H("wi", h, 24), sub_)
             mm([(R(PQ, 0, 128, 1, 32 * e, 32 * e + 32), H("wT", h, 32), Ib) for e in range(2)], False)
-            r0 = blk("R0w", 2 * t + h, 64)
-            act(r0, blk(PQ, 0, 64), AF.Square, bias=cLo)
-            mm([(blk(PQ, l), Ep[l], r0) for l in range(3)], False)
-            tt(H("C2", h, 384), H("C1", h, 384), pq, min_)
+            act(part("rw", h, buf)[:6] + (64,), blk(PQ, 0, 64), AF.Square, bias=cLo)
+
+        def emptied(h, buf, old, new):
+            PQ = "PQ%d" % h
+            mm([(blk(PQ, l), Ep[l], part("rw", h, buf)[:6] + (64,)) for l in range(3)], False)
+            tt(H(new, h, 384), H(old, h, 384), R(PQ, 0, 384), min_)
+
+        def entered(h, buf, old, new):
+            PQ = "PQ%d" % h
             lst = []
-            for l, w, d in ((0, Wr0, "dx"), (1, Wr1, "ix"), (2, Wm, "dx")):
-                lst += [(blk(PQ, l), En[l], blk("R0w", 2 * t + h, 65)), (blk(PQ, l), w, part(d, h, buf))]
+            for l, w, d in ((0, Wr0, "dx"), (1, Wr1, "ix"), (2, Wr2 if buf == In else Wr3, "dx")):
+                lst += [(blk(PQ, l), En[l], part("rw", h, buf)[:6] + (65,)), (blk(PQ, l), w, part(d, h, buf))]
             mm(lst, 2)
             if last:
                 for l in range(3):
-                    tt(H("Cf", 2 * l + h), H("C2", 3 * h + l), blk(PQ, l), max_)
+                    tt(H(new, 2 * l + h), H(old, 3 * h + l), blk(PQ, l), max_)
             else:
-                tt(H("Cw%d" % (t + 1), h, 384), H("C2", h, 384), pq, max_)
-        if t == 0:
-            con(1, col(39), R("Li0", 656, 657), 4096.0); con(1, Wr3, B16, col(39))
+                tt(H(new, h, 384), H(old, h, 384), R(PQ, 0, 384), max_)
+        passes = (largest, emptied, entered)
+        cut = 3 if last else CUT[t]
+        new = ["C1", "C2", "Cf" if last else "Cw%d" % (t + 1)]
+        old = [Cw, "C1", "C2"]
+        if not last:
+            new[cut - 1], got = "Cs%d" % t, ("Cr%d" % t if cut < 3 else new[2])
         for h in range(2):
-            update(h, In, Cw, Wr2) if last else update(h, "Li%d" % t, "Cr%d" % t, Wr3)
-        if last:
-            for a, b in YQ:
-                store("o1", ("yq", a, R("Cf", a, b)), [R("Cf", a, b)], (b - a) // 2)
+            for p in range(1 if last else cut):
+                passes[p](h, In, old[p], new[p])
+            if not last:
+                a, b = ((256, 784 + (t == 0)), (1056, 1440))[h] if cut < 3 else (688, 784)
+                if cut < 3 or h == 0:
+                    send("N", R(In, a, b), [R("Li%d" % t, a, b)], ["rE%d%d" % (t, h)], (b - a) // 4)
+                if QSEND == 2:
+                    send("N", H(new[cut - 1], h, 384), [H(got, h, 384)], ["rC%d%d" % (t, h)], 192)
+        if not last and QSEND == 1:
+            send("N", R(new[cut - 1], 0, 768), [R(got, 0, 768)], ["rC%d0" % t], 384)
+        if t == 0 and min(CUT) < 3:
+            con(1, col(39), R("Li0", 784, 785), 4096.0); con(1, Wr3, B16, col(39))
+
+        def rest():
+            for h in range(2):
+                for p in range(1 if last else cut, 3):
+                    if last:
+                        passes[p](h, In, old[p], new[p])
+                    else:
+                        passes[p](h, "Li%d" % t, got if p == cut else old[p], new[p])
+            if last:
+                for a, b in YQ:
+                    store("o1", ("yq", a, R("Cf", a, b)), [R("Cf", a, b)], (b - a) // 2)
+        if not LATE:
+            rest()
         for h in range(2):
             for c in range(4 * h, 4 * h + 4):
                 pa, pb = "P" + BANKS[0][2 * c:2 * c + 2], "P" + BANKS[1][2 * c:2 * c + 2]
                 yb, db, ib = H("yy", c, 512), H("dd", c, 512), H("ind", c, 512)
                 if ADD[c] in "FD":
                     ts(yb, H("eg", c, 512), 0.0, max_, cN63, min_)
-                elif ADD[c] == "A":
-                    if "A" not in ADD[4 * h:c]:
-                        mm([(blk(pa, kl), I0, H("xx", 4 * h)) for kl in range(4)], False)
-                    tt(ib, H("eg", c, 512), R(pa, 0, 512), add_)
-                    ts(yb, ib, 0.0, max_, 63.0, min_)
                 else:
                     mm([(R(pa, 0, 512), Ib, H("eg", c, 512))] + [(blk(pa, kl), I0, H("xx", 4 * h)) for kl in range(4)])
                     ts(yb, R(pa, 0, 512), 0.0, max_, 63.0, min_)
-                if SPLIT:
-                    mm([(blk(pb, kl), nI, H(Gl, h)) for kl in range(4)], final=False)
-                    mm([(R(pb, 0, 512), Ib, yb)], first=False)
-                else:
-                    mm([(R(pb, 0, 512), Ib, yb)] + [(blk(pb, kl), nI, H(Gl, h)) for kl in range(4)])
-                act(db, R(pb, 0, 512), AF.Abs)
-                if ENG["ind"][c] == "V":
+                how = ENG["ind"][c]
+                for p in [pb] + ["P" + BANKS[2][2 * c:2 * c + 2]] * (how == "M"):
+                    mm([(blk(p, kl), nI, H(Gl, h)) for kl in range(4)], final=False)
+                    mm([(R(p, 0, 512), Ib, yb)], first=False)
+                act(db, R(pb, 0, 512), AF.Abs, bias=cF15)
+                how = eng("ind", c)
+                if how == "V":
                     ts(ib, db, 4.0, ALU.is_gt)
+                elif how == "M":
+                    ts(ib, R(p, 0, 512), EIGHTS, add_, EIGHTS, ALU.not_equal)
                 else:
                     act(ib, db, AF.Sign, bias=-4.5)
                 ops[-1]["tag"] = ("ind", c)
-                wi = Wi if ENG["ind"][c] == "V" else Ws
-                if c == 7 and TAIL:
-                    scan(R("hsc", 384, 672), R("d0", 1536, 1824), R(PT[1], 0, 288), add_, max_)
-                    pk = [R(FB, 288 + k, 408, 5) for k in range(5)]
-                    mm([(R(FB, 288, 408), one1, R("kz", 128, 248, 1, 0, 1))], final=False)
-                    aff("pre", 0, pk[0], R("hsc", 395, 672, 12))
-                    mm([(pk[1 + k], H("dd", 28 + k), Wd) for k in range(4)], first=False, final=False)
-                    mm([(pk[1 + k], H("ind", 28 + k), wi) for k in range(4)], first=False)
-                    continue
+                wi = Ws if how == "S" else Wi
                 lst = []
                 for k in range(4 * c, 4 * c + 4):
-                    pl = R(PT[1], k % 16, 288, 12) if h and TAIL else R(PT[h], k % 16, 384, 16)
+                    pl = R(PT[h], k % 16, 384, 16)
                     lst += [(pl, H("dd", k), Wd), (pl, H("ind", k), wi)]
                 mm(lst, 2)
-            if not TAIL:
-                scan(H("hsc", h, 384), dW, R(PT[h], 0, 384), add_, max_)
-                continue
-            go, gt, jn = [R(n, a + 8 * h, a + 8 * h + 8) for n, a in ((Sb, 272), ("gt", 0), (Sb, 256))]
-            hx = H("hxs", h, 24, 3, 2)
-            if h == 0:
-                scan(H("hsc", 0, 384), dW, R(PT[0], 0, 384), add_, max_)
-                ends = R("hsc", 15, 384, 16)
-                tt(R("t48", 0, 24), ends, R("mm", 0, 24), mul_)
-                tt(R("t48", 24, 48), ends, R(In, 512, 536), mul_)
-                scan(R("ss", 0, 48), R("d0", 1152, 1200), R("t48", 0, 48), mul_, add_)
-                ts(R("jba", 0, 16), R("ss", 2, 48, 3), 15, and_)
-                pl = R(LB, 448, 456)
-                tolist("Db", 0, R("jba", 0, 40), Lz3, R("Dj", 0, 64), pl, -128.0, Cp, 1920.0)
-                aff("Lab", 0, R("Lab", 0, 8), pl)
-                tt(go, R("ss", 26, 48, 3), hx, ALU.is_gt)
-            else:
-                scan(R("sab", 0, 120), R("dAB", 0, 120), R(FB, 288, 408), add_, max_)
-                scan(R("sab", 120, 240), R("dAB", 120, 240), R(FB, 288, 408), add_, max_)
-                ts(R("jba", 24, 32), R("sab", 134, 240, 15), 15, and_)
-                tt(H("Dj", 3), IND(R("jba", 24, 32), Lb8), M16, mul_)
-                pl = R("PB1", 0, 8)
-                mm([(pl, M16, Cp), (pl, H("Dj", 3), Cn128)])
-                aff("Lab", 1, R("Lab", 8, 16), pl, bias=1920.0)
-                tt(go, R("sab", 14, 120, 15), hx, ALU.is_gt)
-                ts(R("jba", 16, 24), R("sab", 14, 120, 15), 15, and_)
+            scan(H("hsc", h, 384), dW, R(PT[h], 0, 384), add_, max_)
+        if LATE:
+            rest()
+        ends = R("hsc", 15, 768, 16)
+        scan(R("ss", 0, 48), km, ends, mul_, max_)
+        scan(R("ss", 48, 96), kj, ends, mul_, max_)
+        ts(R("jba", 0, 16), R("ss", 2, 48, 3), 15, and_)
+        tolist("Db", 0, R("jba", 0, 40), Lz2, H("Dj", 0), R("PT0", 448, 464), -128.0, Cp2, 1920.0)
+        aff("Lab", 0, R("Lab", 0, 16), R("PT0", 448, 464))
+        for h in range(2):
             aff("yb", h, H(Sb, h), IND(H("yy", h, 2048), H("Lab", h, 8)))
-            if last:
-                continue
-            tt(gt, go, H("dj", h, 8), mul_)
-            tt(jn, gt, H("jalt", h, 8), add_)
-            if h == 0:
-                pl = R(LB, 440, 448)
-                tolist("Dj", 0, R(Sb, 256, 304), Lz3, R("Dj", 64, 128), pl, 128.0, Cp)
-            else:
-                pl = R("PB0", 0, 8)
-                if JM == 0:
-                    tt(H("Dj", 4), IND(R(Sb, 256, 272), Lb8h), M16, mul_)
-                if JM > 0:
-                    tt(H("Dj", 1), IND(R("jalt", 8, 16), Lb8), M16, mul_)
-                if JM == 1:
-                    tt(H("Dj", 4), IND(gt, Lb8), M16, mul_)
-                if JM == 2:
-                    tt(H("Dj", 5), IND(R("dj", 8, 16), Lb8), M16, mul_)
-                    tt(H("Dj", 4), IND(R(Sb, 272, 288), Lb8h), H("Dj", 5), mul_)
-                mm([(pl, M16, Cp)] + [(pl, H("Dj", 1), C128)] * (JM > 0) + [(pl, H("Dj", 4), C128)])
-            aff("SL", h, H("SL%d" % t, h, 8), pl)
-        go = R(Sb, 272, 288)
-        if not TAIL:
-            ends = R("hsc", 15, 768, 16)
-            tt(R("t48", 0, 48), ends, R("mm", 0, 48), mul_)
-            tt(R("t48", 48, 96), ends, mj, mul_)
-            scan(R("ss", 0, 96), dS3, R("t48", 0, 96), mul_, add_)
-            ts(R("jba", 0, 32), R("ss", 2, 96, 3), 15, and_)
-            tolist("Db", 0, R("jba", 0, 40), Lz2, H("Dj", 0), R("PT0", 448, 464), -128.0, Cp2, 1920.0)
-            aff("Lab", 0, R("Lab", 0, 16), R("PT0", 448, 464))
-            for h in range(2):
-                aff("yb", h, H(Sb, h), IND(H("yy", h, 2048), H("Lab", h, 8)))
-            tt(go, R("ss", 50, 96, 3), R("hxs", 2, 48, 3), ALU.is_gt)
-            if not last:
-                pl = R("PB0", 0, 16)
-                tt(R("gt", 0, 16), go, R("dj", 0, 16), mul_)
-                tt(R(Sb, 256, 272), R("gt", 0, 16), R("jalt", 0, 16), add_)
-                tolist("Dj", 0, R(Sb, 256, 304), Lz2, H("Dj", 1), pl, 128.0, Cp2)
-                aff("SL", 0, R("SL%d" % t, 0, 16), pl)
+        tt(go, R("ss", 50, 96, 3), R("hxs", 2, 48, 3), ALU.is_gt)
+        w = 256
         if not last:
-            send("N", R("SL%d" % t, 0, 16), [R("LJ%d" % (t + 1), 0, 16)], ["rL%d" % t], 4)
-        w = 256 if last else 288
-        send("N", R(Sb, 0, w), [R("Lb%d" % t, 0, w)], ["rB%d" % t], w // 4)
-        if t == 0 and GOALS:
-            send("G", R("Gl0", 0, 256), [R("Gl1", 0, 256), R("Gl2", 0, 256)], ["rG1", "rG2"], 128)
-        tolist("Da", 0, R("jba", 16 - 8 * TAIL, 56 - 8 * TAIL), Lz2, H("Dj", 2), R("PT0", 432, 448), -128.0, Cp2, 1920.0)
+            pl = R("PB0", 0, 16)
+            scan(R(Sc, 0, 32), R(Sc, 32, 64), R("dja", 0, 32), mul_, add_)
+            tolist("Dj", 0, R(Sc, 0, 40), Lz3, H("Dj", 1), pl, 128.0, Cp2)
+            if MERGE:
+                aff("SL", 0, R(Sb, 256, 272), pl)
+                w = 272
+            else:
+                aff("SL", 0, R("SL%d" % t, 0, 16), pl)
+        first = [lambda: send("N", R(Sb, 0, w), [R("Lb%d" % t, 0, w)], ["rB%d" % t], w // 4, mark=1)]
+        if not last and not MERGE:
+            first.insert(SLPOS, lambda: send("N", R("SL%d" % t, 0, 16), [R("LJ%d" % (t + 1), 0, 16)], ["rL%d" % t], 4))
+        for f in first:
+            f()
+        if not last:
+            send("N", R(Sc, 0, 64), [R("Lc%d" % t, 0, 64)], ["rJ%d" % t], 16, [R("ya", 0, 1)])
+        if t == 0:
+            send("G", R("Gl0", 0, 256), [R("Gl1", 0, 256), R("Gl2", 0, 256)], ["rG1", "rG2"], 128, [R("ya", 0, 1)])
+        ts(R("jba", 40, 56), R("ss", 50, 96, 3), 15, and_)
+        tolist("Da", 0, R("jba", 40, 80), Lz2, H("Dj", 2), R("PT0", 432, 448), -128.0, Cp2, 1920.0)
         aff("Laa", 0, R("Lab", 16, 32), R("PT0", 432, 448))
         for h in range(2):
             aff("ya", h, H("St", 2 * t + h), IND(H("yy", h, 2048), H("Lab", 2 + h, 8)))
         if last:
-            tt(R("t12", 0, 48), IND(go, Lgo), mj12, mul_)
+            tt(R("t12", 0, 48), IND(R(Sc, 32, 64), Lgo), mj12, mul_)
             tt(R("mj4", 0, 48), Pinc, lv, sub_)
             for h in range(2):
                 tt(R("Pfin", h, 48, 2), H("mj4", h, 24), H("t12", h, 24), add_)
         if not last:
             pl = R("PT0", 416, 417, 1, 0, 8)
-            mm([(pl, R(Sb, 272 + 8 * h, 280 + 8 * h), R("cb", 12 * 128, 12 * 128 + 1)) for h in range(2)])
+            mm([(pl, R(Sc, 33 + 16 * h, 48 + 16 * h, 2), R("cb", 12 * 128, 12 * 128 + 1)) for h in range(2)])
             aff("cnt", 0, R("cnt", 0, 1, 1, 0, 8), pl)
             mm([(R("PT0", 424, 425), E8, R("cnt", 0, 1, 1, 0, 8))])
             aff("Ai", 0, R("Ai", 0, 1), R("PT0", 424, 425)); ts(R("Aa", 0, 1), R("Ai", 0, 1), 63, and_)
@@ -762,7 +761,8 @@ def depends(ops):
         for r in o["wr"]:
             for (j, r2, w) in seen.get(r[1], []):
                 if clash(r, r2):
-                    (soft if ops[j]["q"] == o["q"] == "P" and not o["args"][2] else hard)[i].add(j)
+                    both = not WAW and o["kind"] == ops[j]["kind"] == "cp" and o["args"][0][0] == ops[j]["args"][0][0] == "i"
+                    (soft if both or ops[j]["q"] == o["q"] == "P" and not o["args"][2] else hard)[i].add(j)
         for r in o["wr"]:
             l = [e for e in seen.get(r[1], []) if not (r[4] == 1 and r[5] <= e[1][5] and e[1][6] <= r[6] and r[2] <= e[1][2] and e[1][3] <= r[3])]
             seen[r[1]] = l + [(i, r, True)]
@@ -936,10 +936,273 @@ def search(ops, pre, rounds, start=None):
     return starts(best), qn, bk
 
 
-def order(ops):
-    hard, pre = depends(ops)
+def polish(ops, pre, idx, rounds):
+    n = len(ops)
+    cases = [BASE] + list(CASES)
+    CS = range(len(cases))
+    built, other = [build(c) for c in cases], [build(c, True) for c in cases]
+    pres = [depends(b)[1] for b in built]
+    qn, qo = [[max(0, " VSPGYL".find(o["q"])) for o in l] + [0] for l in (ops, other[0])]
+    first = list(qn)
+    names = [k for k, v in SCRATCH.items() if v[0] == "psum"]
+    bk = [sorted(set(names.index(r[1]) for r in o["rd"] + o["wr"] if inps(r))) for o in ops]
+    anc, keep = [0] * n, []
+    for i in range(n):
+        m = 0
+        for j in pre[i]:
+            m |= anc[j]
+        keep.append([j for j, d in pre[i].items() if d > LAT or not m >> j & 1])
+        for j in pre[i]:
+            m |= 1 << j
+        anc[i] = m
+    cost, alt = [[[o["cost"] for o in b] for b in l] for l in (built, other)]
+    lat = [[o.get("lat", 0) for o in b] for b in built]
+    wait = [LAT * c[3] for c in cases]
+    P = [[[(j, lat[c][j] + pres[c][i][j] * (cases[c][3] if pres[c][i][j] <= LAT else 1.0)) for j in keep[i]] for i in range(n)] for c in CS]
+    S = [[[] for _ in range(n)] for c in CS]
+    for c in CS:
+        for i in range(n):
+            for j, d in P[c][i]:
+                S[c][j].append((i, d))
+    up = [keep[i] + [i + 1] * (qn[i + 1] == 6) for i in range(n)]
+    down = [[k for k, _ in S[0][i]] + [i - 1] * (qn[i] == 6) for i in range(n)]
+    after = [[k for k, _ in l] for l in S[0]]
+    sinks = [i for i in range(n) if not after[i] and lat[0][i]]
+    moves = np.array([i for i in range(n) if qn[i] == 6])
+    pos, qp, qx = [0] * n, [-1] * (n + 1), [-1] * (n + 1)
+    bp, bx = [{} for _ in range(n + 1)], [{} for _ in range(n + 1)]
+    fin, tail, span = [[0.0] * (n + 1) for _ in CS], [[0.0] * (n + 1) for _ in CS], [0.0 for _ in CS]
+
+    def exchange(v):
+        qn[v], qo[v] = qo[v], qn[v]
+        for c in CS:
+            cost[c][v], alt[c][v] = alt[c][v], cost[c][v]
+
+    def link(a, seq, ends):
+        lq, lb = dict(ends[0]), dict(ends[1])
+        for p, i in enumerate(seq):
+            pos[i] = a + p
+            if qn[i]:
+                j = qp[i] = lq[qn[i]]
+                qx[j] = lq[qn[i]] = i
+            for b in bk[i]:
+                j = bp[i][b] = lb[b]
+                bx[j][b] = lb[b] = i
+        for q, j in lq.items():
+            k = qx[j] = ends[2][q]
+            qp[k] = j
+        for b, j in lb.items():
+            k = bx[j][b] = ends[3][b]
+            bp[k][b] = j
+
+    def ahead(a, seeds):
+        log = []
+        fw = idx[a:]
+        for c in CS:
+            f, co, Pc, w, la = fin[c], cost[c], P[c], wait[c], lat[c]
+            dirty = [False] * (n + 1)
+            for i in seeds:
+                dirty[i] = True
+            for i in fw:
+                if dirty[i]:
+                    s = f[qp[i]]
+                    for j, d in Pc[i]:
+                        if f[j] + d > s:
+                            s = f[j] + d
+                    if bk[i]:
+                        for j in bp[i].values():
+                            if f[j] + w > s and j >= 0 and qn[j] != qn[i]:
+                                s = f[j] + w
+                    s += co[i]
+                    if s != f[i]:
+                        log.append((f, i, f[i]))
+                        f[i] = s
+                        dirty[qx[i]] = True
+                        for k in after[i]:
+                            dirty[k] = True
+                        if bk[i]:
+                            for k in bx[i].values():
+                                dirty[k] = True
+            log.append((span, c, span[c]))
+            span[c] = max(f[i] + la[i] for i in sinks)
+        return log
+
+    def back(b, seeds):
+        bw = idx[b::-1]
+        for c in CS:
+            t, co, Sc, w, la = tail[c], cost[c], S[c], wait[c], lat[c]
+            dirty = [False] * (n + 1)
+            for i in seeds:
+                dirty[i] = True
+            for i in bw:
+                if dirty[i]:
+                    s = t[qx[i]]
+                    if la[i] > s:
+                        s = la[i]
+                    for k, d in Sc[i]:
+                        if t[k] + d > s:
+                            s = t[k] + d
+                    if bk[i]:
+                        for k in bx[i].values():
+                            if t[k] + w > s and k >= 0 and qn[k] != qn[i]:
+                                s = t[k] + w
+                    s += co[i]
+                    if s != t[i]:
+                        t[i] = s
+                        dirty[qp[i]] = True
+                        for j in keep[i]:
+                            dirty[j] = True
+                        if bk[i]:
+                            for j in bp[i].values():
+                                dirty[j] = True
+
+    def worth():
+        return sum(w * s for w, s in zip(WEIGHTS, span))
+
+    def ends_of(a, b):
+        fq, fb, nq, nb = {}, {}, {}, {}
+        for i in idx[a:b + 1]:
+            if qn[i]:
+                fq.setdefault(qn[i], qp[i])
+                nq[qn[i]] = qx[i]
+            for x in bk[i]:
+                fb.setdefault(x, bp[i][x])
+                nb[x] = bx[i][x]
+        return fq, fb, nq, nb
+
+    def hopeful(b, seq, ends, bound):
+        fq, fb, nq, nb = ends
+        for c in CS:
+            f, t, co, Pc, Sc, w = fin[c], tail[c], cost[c], P[c], S[c], wait[c]
+            old = [f[i] for i in seq]
+            lq, lb = dict(fq), dict(fb)
+            best = 0.0
+            for i in seq:
+                q = qn[i]
+                s = 0.0
+                if q:
+                    s = f[lq[q]]
+                    lq[q] = i
+                for j, d in Pc[i]:
+                    if f[j] + d > s:
+                        s = f[j] + d
+                for x in bk[i]:
+                    j = lb[x]
+                    if f[j] + w > s and j >= 0 and qn[j] != q:
+                        s = f[j] + w
+                    lb[x] = i
+                s = f[i] = s + co[i]
+                if s + lat[c][i] > best:
+                    best = s + lat[c][i]
+                for k, d in Sc[i]:
+                    if s + d + t[k] > best and pos[k] > b:
+                        best = s + d + t[k]
+            for q, j in lq.items():
+                best = max(best, f[j] + t[nq[q]])
+            for x, j in lb.items():
+                if nb[x] >= 0 and qn[j] != qn[nb[x]]:
+                    best = max(best, f[j] + w + t[nb[x]])
+            for i, y in zip(seq, old):
+                f[i] = y
+            bound -= WEIGHTS[c] * max(best - span[c], -150.0)
+            if bound < -150.0 * sum(WEIGHTS[c + 1:]):
+                return False
+        return bound > 0
+
+    def whole():
+        e = dict.fromkeys(range(1, 7), -1), dict.fromkeys(range(8), -1)
+        link(0, idx, e + e)
+        ahead(0, idx)
+        back(n - 1, idx)
+        return worth()
+
+    def resort():
+        s = np.array(fin[0][:n]) - np.array(cost[0])
+        s[moves] = s[moves - 1]
+        idx[:] = np.lexsort((np.array(pos), s)).tolist()
+        return whole()
+
+    cur = whole()
+    rnd = np.random.default_rng(SEED).random((rounds, 4))
+    lims = (-np.log(rnd[:, 3] + 1e-12) * (HEAT * sum(WEIGHTS) * (1.0 - np.arange(rounds) / rounds) + 1.0)).tolist()
+    low, best, took = cur, (list(idx), set(), list(span)), 0
+    pick, p = np.random.default_rng(SEED + 1).integers(0, n, 100003).tolist(), 0
+    for it, (r0, r1, r2, _) in enumerate(rnd.tolist()):
+        c, v = it % len(cases), int(r0 * n)
+        while r1 < TIGHT and fin[c][v] - cost[c][v] + tail[c][v] < span[c] - SLACK:
+            p = (p + 1) % len(pick)
+            v = pick[p]
+        r1 = r1 % 0.1 * 10
+        if not qn[v]:
+            continue
+        turn = qo[v] != qn[v] and r2 < FLIP
+        if turn:
+            a = b = pos[v]
+            win = seq = [v]
+            ends = ends_of(a, b)
+            ends[0][qo[v]] = next((i for i in idx[a::-1] if qn[i] == qo[v]), -1)
+            ends[2][qo[v]] = next((i for i in idx[a:] if qn[i] == qo[v]), -1)
+            exchange(v)
+        else:
+            v -= qn[v] == 6
+            early = r2 < 0.575
+            near = [qp[v]] + list(bp[v].values()) if early else [qx[v]] + list(bx[v].values())
+            if qn[v + 1] == 6:
+                m = qp[v + 1] if early else qx[v + 1]
+                near.append(m - 1 if m >= 0 else -1)
+            u, hops = near[int(r1 * len(near))], r1 * len(near) % 1.0
+            while u >= 0 and hops < FAR:
+                hops /= FAR
+                u = qp[u] if early else qx[u]
+            if u < 0:
+                continue
+            a, b, nxt = (pos[u], pos[v] + (qn[v + 1] == 6), up) if early else (pos[v], pos[u] + (qn[u + 1] == 6), down)
+            if b - a > 120:
+                continue
+            grp, todo = {v}, [v]
+            while todo and u not in grp:
+                for j in nxt[todo.pop()]:
+                    if a <= pos[j] <= b and j not in grp:
+                        grp.add(j); todo.append(j)
+            if u in grp:
+                continue
+            win = idx[a:b + 1]
+            A, B = [i for i in win if i in grp], [i for i in win if i not in grp]
+            seq = A + B if early else B + A
+            ends = ends_of(a, b)
+        if hopeful(b, seq, ends, lims[it]):
+            idx[a:b + 1] = seq
+            link(a, seq, ends)
+            log = ahead(a, seq + list(ends[2].values()) + list(ends[3].values()))
+            new = worth()
+            if new - cur < lims[it]:
+                took += 1
+                back(b, seq + list(ends[0].values()) + list(ends[1].values()))
+                cur = resort() if took % 100 == 0 else new
+                if cur < low:
+                    low, best = cur, (list(idx), set(i for i in range(n) if qn[i] != first[i]), list(span))
+                continue
+            for l, i, y in log:
+                l[i] = y
+            idx[a:b + 1] = win
+            if turn:
+                exchange(v)
+            link(a, win, ends)
+        elif turn:
+            exchange(v)
+    TIMES[:] = best[2]
+    return best[:2]
+
+
+def order():
+    ops = build()
+    pre = depends(ops)[1]
     t0, qn, bk = search(ops, pre, ROUNDS)
-    out = [ops[i] for i in np.lexsort((np.arange(len(ops)), t0)).tolist()]
+    idx, turned = polish(ops, pre, np.lexsort((np.arange(len(ops)), t0)).tolist(), STEPS)
+    ops = build(None, turned)
+    hard = depends(ops)[0]
+    qn = [o["q"] for o in ops]
+    out = [ops[i] for i in idx]
     bank = {}
     for o in out:
         i = o["n"]
@@ -947,7 +1210,7 @@ def order(ops):
         for b in bk[i]:
             ex.update(j for q, j in bank.get(b, {}).items() if q != qn[i])
             bank.setdefault(b, {})[qn[i]] = i
-        o["w"] = set() if o["q"] in "RL" else set(j for j in hard[i] | ex if ops[j]["kind"] not in ("send", "sum", "load"))
+        o["w"] = set() if o["q"] in "RL" else set(j for j in hard[i] | ex if ops[j]["kind"] not in ("send", "sum", "load", "dup"))
     pos = {}
     for p, o in enumerate(out):
         pos[o["n"]] = p
@@ -973,14 +1236,14 @@ def order(ops):
                 o["need"].append((s, j))
                 ops[j]["inc"] = True
         o["know"] = dict(mine) if o["q"] != "R" else {}
-        if "sem" not in o and o["kind"] not in ("send", "sum", "load"):
+        if "sem" not in o and o["kind"] not in ("send", "sum", "load", "dup"):
             own.append(o["n"])
     tick = {}
     for o in out:
         if o.get("inc") and "sem" not in o:
             tick[o["q"]] = tick.get(o["q"], 0) + 1
             o["val"] = tick[o["q"]]
-    return out
+    return ops, out
 
 
 PLAN = []
@@ -1020,9 +1283,7 @@ def rank_program(g, core, T, topo):
     r = T.rank_of(core)
     n = len(T.cores)
     if not PLAN:
-        ops = build()
-        PLAN.append(ops)
-        PLAN.append(order(ops))
+        PLAN.extend(order())
     ops, out = PLAN
     if r is None:
         for r in range(n):
@@ -1050,7 +1311,7 @@ def rank_program(g, core, T, topo):
         q = Q[o["q"]]
         for s, j in o["need"]:
             p = ops[j]
-            v = p["val"] if "sem" not in p else (arr.get(s, nin) if s[0] == "r" else 16)
+            v = p["val"] if "sem" not in p else (arr.get(s, nin) if s[0] == "r" else p.get("count", 16))
             q.wait_ge(T.sem[s], v)
         k, a = o["kind"], o["args"]
         if k == "cp":
@@ -1087,6 +1348,10 @@ def rank_program(g, core, T, topo):
         elif k == "sum":
             q.dma_start(ap(T, a[0]), ap(T, a[1]), accum_op=ALU.add).then_inc(T.sem[a[2]], 16)
             continue
+        elif k == "dup":
+            for d in a[0]:
+                q.dma_start(ap(T, d), ap(T, a[1])).then_inc(T.sem[a[2]], 16)
+            continue
         elif k == "store":
             name, c, src = a[1]
             if src == "marks" and c is not None:
@@ -1108,12 +1373,6 @@ def rank_program(g, core, T, topo):
                                                 remote_sem=T.sem[s], src=ap(T, a[1]), dst=ap(T, d)))
                     lsum += len(e)
                 q.remote_dma_fused(tr, local_sem=T.sem["lsem"])
-            elif a[0] == "A":
-                rid, pid, _ = topo.addr(nxt)
-                q.remote_dma_fused([RemoteDMATransfer(dst_ids=[DstId(rid=rid, pnc=pid)], dma_engine_mask=topo.mask(core, nxt),
-                                                      remote_sem=T.sem[a[3][0]], srcs=[ap(T, a[1]), T["Qn"][:]],
-                                                      dsts=[ap(T, a[2][0])], alu_op=1)], local_sem=T.sem["lsem"])
-                lsum += len(topo.engines(core, nxt))
             else:
                 to = hlp if hlp is not None and handed(o) else nxt
                 rid, pid, _ = topo.addr(to)

@@ -57,14 +57,14 @@ STORES = ("o1", "o2", "o3", "o4", "o5", "o6")
 ISSUE = 300.0
 YQ = ((0, 768),)
 SEMAPHORES = (["cV", "cS", "cP", "cG", "lsem", "rG1", "rG2", "rC00", "rC01", "rC10", "rC11", "rB0", "rB1", "rB2",
-               "rE00", "rE01", "rE10", "rE11", "rL0", "rL1", "rJ0", "rJ1", "dq"]
+               "rE00", "rE01", "rE10", "rE11", "rL0", "rL1", "rJ0", "rJ1", "dq", "e00", "e01", "e10", "e11"]
               + ["l" + n for n in LOADS] + list(STORES) + ["d%d%d" % (t, c) for t in range(RO) for c in range(8)]
               + ["x%d%d" % (t, h) for t in range(RO) for h in range(2)])
 
 ENG = dict(sg="VVSSVSSS", eg="SSSSSSSS", ind="VVSVVVVV", q16="VS", key="VS", Lk="SS", xx="SS", u32="SS", Lo="VS", n16="VS",
            qf="SS", mT="VV", K16="SS", wi="SS", R0j="SS", Lab="SS", Laa="V", SL="V", yb="SV", ya="SS", Lb="VV", Ai="V", cA="S",
            Cw="SS", cnt="S", LJ="VS", nf0="SS", nf1="VS", x2="SS", Pinc="S", mj12="S", Dk="SS", Db="SS", Dj="S", Da="S",
-           km="VV", rm="V", k0="VV", xn="SS", x4="VS", Dx="SS", c0="V" * 24, c1="S" * 80)
+           km="SS", rm="V", k0="VV", xn="SS", x4="VS", Dx="SS", c0="V" * 24, c1="S" * 80)
 PARTS = ("mT", "qf", "dx", "ix", "rw")
 CUT = (1, 1)
 QSEND = 2
@@ -72,7 +72,14 @@ WIDEK = "nn"
 XDMA = 1
 QSUM = 1
 ADDS = ("DDFFDDFF",) * 3
-BANKS = ("A0A0A0A0A0A0A0A0", "B0B1A1A0B0B1A1A0", "B1B0A0A1B1B0A0A1")
+BANKS = "B0B1A1A0B0B1A1A0"
+PIECES = (0, 1, 2, 3, 4, 5, 6, 7)
+TURNS = (((0, 4),), ((0, 3), (3, 4)))
+GOALS = 0
+FIRST = 1500.0
+ENTER = (0, 0)
+NAMES = 0
+KJ = 1
 COPY = (100.0, 1300.0, 300.0)
 FILL = (0, 0)
 LOAD = 2.8
@@ -92,7 +99,7 @@ LAT, LATS = 220.0, 220.0
 BACK = 9999
 SEED = 1
 ROUNDS = 300
-STEPS = 450000
+STEPS = 500000
 WEIGHTS = (2.0, 1.0, 1.0, 1.0)
 HEAT = 30.0
 SLACK = 200.0
@@ -188,7 +195,7 @@ def build(case=None, other=False):
         add("V", "tt", (out, a, b, op), [a, b], [out], vcost(out, [a, b], True))
 
     def ts(out, a, s1, op0, s2=None, op1=None):
-        add("V", "ts", (out, a, s1, s2, op0, op1), [a, s1, s2], [out], vcost(out, [a]))
+        add("V", "ts", (out, a, s1, s2, op0, op1), [a, s1, s2], [out], vcost(out, [a] + flat([s1, s2])))
 
     def scan(out, d0, d1, op0, op1):
         add("V", "scan", (out, d0, d1, op0, op1), [d0, d1], [out], vcost(out, [d0, d1]))
@@ -243,12 +250,12 @@ def build(case=None, other=False):
             lat=700.0 + (1 - SHARE) * (200.0 + kb * 5.0))
 
     def send(kind, src, dst, sem, kb, behind=(), mark=0):
-        s = add("G", "send", (kind, src, dst, sem), [src] + list(behind), [R("ya", 0, 1)] * mark, LINK[0])
-        after = {s["n"]: LINK[1]}
+        s = add("G", "send", (kind, src, dst, sem), [src] + list(behind), [R("ya", 0, 1)] * mark, LINK[0] * DF)
+        after = {s["n"]: LINK[1] * DF}
         hop = sem[0][:len(RELAY[0])] in RELAY
         w = add("L", "link", (kind,), [], [R("ya", 4, 5)], (LINK[2] + kb * LINK[3 + hop]) * DF, after=after)
         for d, sm in zip(dst, sem):
-            add("R", "recv", (kind,), [], [d], 0, sem=sm, lat=0, after={w["n"]: 400.0 + hop * (2400.0 + kb * LINK[3]) * DF})
+            add("R", "recv", (kind,), [], [d], 0, sem=sm, lat=0, after={w["n"]: (400.0 + hop * (2400.0 + kb * LINK[3])) * DF})
 
     def total(out, a, sem, size=1.0):
         s = add("G", "sum", (out, a, sem), [out, a], [], DMA[0] * DF)
@@ -273,6 +280,9 @@ def build(case=None, other=False):
     load("Y", "rm", R("Rm", 0, 1), 20)
     load("Y", "ef", R("Ef", 0, 4096), 1024, [R("St", 0, 3072)])
     load("Y", "ef2", R("Ef", 4096, 4720), 156)
+    if GOALS:
+        send("G", R("Gl0", 0, 256), [R("Gl1", 0, 256), R("Gl2", 0, 256)], ["rG1", "rG2"], 128, [R("Ef", 0, 4096)], 1)
+        ops[-4]["cost"] += FIRST * DF
 
     def col(j, p1=128):
         return R("cf", j, j + 1, 1, 0, p1)
@@ -284,16 +294,17 @@ def build(case=None, other=False):
     def con(k, out, a, scale=1.0, bias=0.0):
         aff("c%d" % k, made[k], out, a, scale, bias)
         made[k] += 1
-    cP, cB, cAa, cN15, cF15, cJ, cU, c16P, cM16, cM4k, cN16, cN4k, cN64k, cSg, cF64k, cN63 = [col(j) for j in range(16)]
+    cP, cB, cAa, cN15, cF15, cJ, cU, c16P, cM16, cM4k, cN16, cN4k, cN64k, cSg, cF64k = [col(j) for j in range(15)]
     iP, iB, iA = R("ci", 0, 1), R("ci", 4, 5), R("ci", 8, 9)
     iota(iP, [[0, 1]], 0, 1)
     ts(iB, iP, 15, and_); ts(iA, iP, 4, shr_)
     con(0, cP, iP); con(0, cB, iB); con(0, cAa, iA); con(0, c16P, iP, 16.0)
     ts(cN15, iB, 15.0, ALU.is_lt); ts(cF15, iB, 15.0, eq_); ts(cF64k, iB, 15.0, eq_, 65536.0, mul_)
     con(0, col(20), iB, 2.0, 1.0); con(0, cU, col(20), cN15)
-    for d, a, c in ((cM4k, R("Rm", 0, 1), 4096.0), (cN4k, cN15, 4096.0), (cN64k, cN15, 65536.0), (cN63, cN15, 63.0)):
+    for d, a, c in ((cM4k, R("Rm", 0, 1), 4096.0), (cN4k, cN15, 4096.0), (cN64k, cN15, 65536.0)):
         con(1, d, a, c)
-    con(1, cN16, cN15, -16.0 - 131072.0, 131072.0); con(1, col(27), cF64k, 1.5); con(1, cM16, R("Rm", 0, 1), -16.0, cF64k)
+    con(1, cN16, cN15, -16.0 - 49152.0, 49152.0); con(1, col(27), cF15, 32768.0)
+    con(1, col(33), cF15, 16384.0); con(1, cM16, R("Rm", 0, 1), -16.0, col(33))
     con(1, cJ, iB, 1.0, 3072.0); con(1, cSg, cN15, -2048.0, 1920.0)
     Ib, I0, nI, IB, M16, kk, gg, B16, Wu, Wr0, Wr1, Wr2, One, I16 = [blk("cb", j) for j in range(14)]
     k8, k16, one1 = R("cb", 5 * 128, 5 * 128 + 8), R("cb", 5 * 128, 5 * 128 + 16), blk("cb", 12, 1)
@@ -302,7 +313,7 @@ def build(case=None, other=False):
     fill(One, 1)
     asel(Ib, One, [[-1, 128]], 0, 1)
     ts(M16, kk, cB, eq_); ts(B16, gg, cAa, eq_)
-    con(0, I16, Ib, 16.0); con(0, I0, Ib, cN15); con(0, Wu, B16, cU); con(0, nI, Ib, -1.0)
+    con(0, I16, Ib, 16.0); con(0, Wu, B16, cU); con(0, nI, Ib, -1.0)
     con(1, IB, Ib, BIG / 2); con(1, Wr0, B16, cN4k); con(1, Wr1, B16, cN64k); con(1, Wr2, B16, cM4k)
     kz = R("kz", 0, 256, 1, 0, 1)
     iota(blk("kz", 0, 1), [[0, 8], [1, 16]], 0, 0); fill(blk("kz", 1, 1), 0)
@@ -320,7 +331,7 @@ def build(case=None, other=False):
     Wd, Wi, Ws = sm(80, 24), sm(104, 24), sm(128, 24)
     fill(sm(104, 48), 0)
     con(1, sm(80, 8, 3), C8, cN16); con(1, sm(81, 8, 3), C8, col(27)); con(1, sm(82, 8, 3), C8, cM16)
-    con(1, sm(105, 8, 3), sm(80, 8, 3), 16.0); con(1, sm(129, 8, 3), C8, cSg)
+    con(1, sm(105, 8, 3), C8, -256.0); con(1, sm(129, 8, 3), C8, cSg)
     I4 = R("cb", o + 152, o + 200, 1, 0, 48)
     fill(R("Tub", 128, 176, 1, 0, 48), 4)
     asel(I4, R("Tub", 128, 176, 1, 0, 48), [[-1, 2], [-6, 8], [-2, 3]], 0, 1)
@@ -385,7 +396,7 @@ def build(case=None, other=False):
     con(0, i48, R("cb", 5 * 128, 5 * 128 + 3), 16.0, cB)
     con(0, third, i48, 1.0 / 3.0, -1.0 / 3.0)
     con(0, Lgo, third, 2.0, 1.0)
-    fill(R("km", 0, 48), 0)
+    fill(R("km", 0, 48), 0); fill(R("kj", 0, 48), 0)
     cLo, k64 = col(24, 64), blk("cb", 5, 64)
     ts(cLo, col(0, 64), 32.0, ALU.is_lt)
     fill(R("ce", 768, 1152, 1, 0, 65), 1)
@@ -453,7 +464,10 @@ def build(case=None, other=False):
         else:
             tt(R("t12", 0, 48), IND(R(J, 32, 64), Lgo), R(Ip, 736, 784), mul_)
         tt(mj, IND(jw, Lgo), lv, eq_)
-        tt(kj, IND(jw, Lgo), lv, ALU.is_lt)
+        if KJ:
+            aff("km", 0, R("kj", 1, 48, 3), R(In, 640, 688, 3)); aff("km", 1, R("kj", 2, 48, 3), R(In, 642, 688, 3), -1.0, 1.0)
+        else:
+            tt(kj, IND(jw, Lgo), lv, ALU.is_lt)
         for l in (1, 2):
             aff("km", l - 1, R("km", l, 48, 3), R(In, 639 + l, 688, 3), -1.0, 1.0)
         aff("mj12", 0, mj12, mj, -12.0)
@@ -481,16 +495,21 @@ def build(case=None, other=False):
                 aff("q16", h, H("q16", h), IND(R("Qn", 128 * h, 768), lj))
                 aff("key", h, H("key", h), IND(R("Qk", 128 * h, 768), lj), bias=1025.0)
             else:
-                ts(H("q32", h), IND(H(Cw, h, 384), lj), 4095, and_)
-                aff("q16", h, H("q16", h), H("q32", h))
+                if NAMES:
+                    ts(H("Qn", h, 384), H(Cw, h, 384), 4095, and_)
+                    aff("q16", h, H("q16", h), IND(H("Qn", h, 384), lj))
+                else:
+                    ts(H("q32", h), IND(H(Cw, h, 384), lj), 4095, and_)
+                    aff("q16", h, H("q16", h), H("q32", h))
                 aff("key", h, H("key", h), IND(H(Cw, h, 384), lj), 1.0 / 4096, 1024.625)
             keys = [(R(PT[h], 0, 256), one1, kz), (R(PT[h], 0, 128), H("key", h), I16)]
             mm(keys[:2 - (t == 0)], final=False)
             for c in range(4):
                 aff("sg", 4 * h + c, H("sg", 4 * h + c, 512), IND(R("St", 0, 3072), H("q16", 4 * h + c, 32)))
                 scan(H("smx", 4 * h + c, 512), dMx, H("sg", 4 * h + c, 512), mul_, max_)
-                mm([(R(PT[h], k, 256, 16, 32 * c, 32 * c + 32), H("sg", 4 * h + c, 512, 16, k), Wmk) for k in range(16)],
-                   first=False, final=c == 3 and t > 0, stop=t > 0)
+            for a, b in TURNS[h]:
+                mm([(R(PT[h], k, 256, 16, 32 * a, 32 * b), R("sg", 2048 * h + 512 * a + k, 2048 * h + 512 * b, 16), Wmk) for k in range(16)],
+                   first=False, final=b == 4 and t > 0, stop=t > 0)
             if t == 0:
                 mm(keys[1:], first=False)
             scan(H("msc", h), R("d0c", 0, 128), R(PT[h], 0, 128), max_, min_)
@@ -535,8 +554,8 @@ def build(case=None, other=False):
                 if ADD[c] == "D":
                     total(H("eg", c, 512), H("xx", h, 512), "d%d%d" % (t, c))
             pd = blk("PQ%d" % h, 3)
-            mm([(pd, I0, xx), (pd, nI, H(Gl, h))])
-            act(part("dx", h), pd, AF.Abs, bias=cF15)
+            mm([(pd, Ib, xx), (pd, nI, H(Gl, h))])
+            act(part("dx", h), pd, AF.Abs)
             ts(part("ix", h), part("dx", h), 4.0, ALU.is_gt)
             pl = R("PT0", 464 + 24 * h, 488 + 24 * h)
             mm([(pl, one1, r15), (pl, part("dx", h), Wd), (pl, part("ix", h), Wi)])
@@ -626,6 +645,9 @@ def build(case=None, other=False):
             if last:
                 for l in range(3):
                     tt(H(new, 2 * l + h), H(old, 3 * h + l), blk(PQ, l), max_)
+            elif ENTER[h]:
+                act(H(new, h, 384), R(PQ, 0, 384), AF.Relu)
+                total(H(new, h, 384), H(old, h, 384), "e%d%d" % (t, h), 1.5)
             else:
                 tt(H(new, h, 384), H(old, h, 384), R(PQ, 0, 384), max_)
         passes = (largest, emptied, entered)
@@ -640,9 +662,9 @@ def build(case=None, other=False):
             if not last:
                 a, b = ((256, 784 + (t == 0)), (1056, 1440))[h] if cut < 3 else (688, 784)
                 if cut < 3 or h == 0:
-                    send("N", R(In, a, b), [R("Li%d" % t, a, b)], ["rE%d%d" % (t, h)], (b - a) // 4)
+                    send("N", R(In, a, b), [R("Li%d" % t, a, b)], ["rE%d%d" % (t, h)], (b - a) // 4, [R("ya", 0, 1)])
                 if QSEND == 2:
-                    send("N", H(new[cut - 1], h, 384), [H(got, h, 384)], ["rC%d%d" % (t, h)], 192)
+                    send("N", H(new[cut - 1], h, 384), [H(got, h, 384)], ["rC%d%d" % (t, h)], 192, [R("ya", 0, 1)])
         if not last and QSEND == 1:
             send("N", R(new[cut - 1], 0, 768), [R(got, 0, 768)], ["rC%d0" % t], 384)
         if t == 0 and min(CUT) < 3:
@@ -660,34 +682,23 @@ def build(case=None, other=False):
                     store("o1", ("yq", a, R("Cf", a, b)), [R("Cf", a, b)], (b - a) // 2)
         if not LATE:
             rest()
+        for c in PIECES:
+            h, pb = c // 4, "P" + BANKS[2 * c:2 * c + 2]
+            yb, db, ib = H("yy", c, 512), H("dd", c, 512), H("ind", c, 512)
+            ts(yb, H("eg", c, 512), 0.0, max_, 63.0, min_)
+            mm([(blk(pb, kl), nI, H(Gl, h)) for kl in range(4)], final=False)
+            mm([(R(pb, 0, 512), Ib, yb)], first=False)
+            act(db, R(pb, 0, 512), AF.Abs)
+            how = eng("ind", c)
+            if how == "V":
+                ts(ib, db, 4.0, ALU.is_gt)
+            else:
+                act(ib, db, AF.Sign, bias=-4.5)
+            ops[-1].update(tag=("ind", c), rd=[db, Wi, Ws])
+            wi = Ws if how == "S" else Wi
+            mm([x for k in range(4 * c, 4 * c + 4)
+                for x in ((R(PT[h], k % 16, 384, 16), H("dd", k), Wd), (R(PT[h], k % 16, 384, 16), H("ind", k), wi))], 2)
         for h in range(2):
-            for c in range(4 * h, 4 * h + 4):
-                pa, pb = "P" + BANKS[0][2 * c:2 * c + 2], "P" + BANKS[1][2 * c:2 * c + 2]
-                yb, db, ib = H("yy", c, 512), H("dd", c, 512), H("ind", c, 512)
-                if ADD[c] in "FD":
-                    ts(yb, H("eg", c, 512), 0.0, max_, cN63, min_)
-                else:
-                    mm([(R(pa, 0, 512), Ib, H("eg", c, 512))] + [(blk(pa, kl), I0, H("xx", 4 * h)) for kl in range(4)])
-                    ts(yb, R(pa, 0, 512), 0.0, max_, 63.0, min_)
-                how = ENG["ind"][c]
-                for p in [pb] + ["P" + BANKS[2][2 * c:2 * c + 2]] * (how == "M"):
-                    mm([(blk(p, kl), nI, H(Gl, h)) for kl in range(4)], final=False)
-                    mm([(R(p, 0, 512), Ib, yb)], first=False)
-                act(db, R(pb, 0, 512), AF.Abs, bias=cF15)
-                how = eng("ind", c)
-                if how == "V":
-                    ts(ib, db, 4.0, ALU.is_gt)
-                elif how == "M":
-                    ts(ib, R(p, 0, 512), EIGHTS, add_, EIGHTS, ALU.not_equal)
-                else:
-                    act(ib, db, AF.Sign, bias=-4.5)
-                ops[-1]["tag"] = ("ind", c)
-                wi = Ws if how == "S" else Wi
-                lst = []
-                for k in range(4 * c, 4 * c + 4):
-                    pl = R(PT[h], k % 16, 384, 16)
-                    lst += [(pl, H("dd", k), Wd), (pl, H("ind", k), wi)]
-                mm(lst, 2)
             scan(H("hsc", h, 384), dW, R(PT[h], 0, 384), add_, max_)
         if LATE:
             rest()
@@ -698,7 +709,7 @@ def build(case=None, other=False):
         tolist("Db", 0, R("jba", 0, 40), Lz2, H("Dj", 0), R("PT0", 448, 464), -128.0, Cp2, 1920.0)
         aff("Lab", 0, R("Lab", 0, 16), R("PT0", 448, 464))
         for h in range(2):
-            aff("yb", h, H(Sb, h), IND(H("yy", h, 2048), H("Lab", h, 8)))
+            aff("yb", h, H(Sb, h), IND(H("yy", h, 2048), H("Lab", h, 8)), cN15)
         tt(go, R("ss", 50, 96, 3), R("hxs", 2, 48, 3), ALU.is_gt)
         w = 256
         if not last:
@@ -717,13 +728,13 @@ def build(case=None, other=False):
             f()
         if not last:
             send("N", R(Sc, 0, 64), [R("Lc%d" % t, 0, 64)], ["rJ%d" % t], 16, [R("ya", 0, 1)])
-        if t == 0:
+        if t == 0 and not GOALS:
             send("G", R("Gl0", 0, 256), [R("Gl1", 0, 256), R("Gl2", 0, 256)], ["rG1", "rG2"], 128, [R("ya", 0, 1)])
         ts(R("jba", 40, 56), R("ss", 50, 96, 3), 15, and_)
         tolist("Da", 0, R("jba", 40, 80), Lz2, H("Dj", 2), R("PT0", 432, 448), -128.0, Cp2, 1920.0)
         aff("Laa", 0, R("Lab", 16, 32), R("PT0", 432, 448))
         for h in range(2):
-            aff("ya", h, H("St", 2 * t + h), IND(H("yy", h, 2048), H("Lab", 2 + h, 8)))
+            aff("ya", h, H("St", 2 * t + h), IND(H("yy", h, 2048), H("Lab", 2 + h, 8)), cN15)
         if last:
             tt(R("t12", 0, 48), IND(R(Sc, 32, 64), Lgo), mj12, mul_)
             tt(R("mj4", 0, 48), Pinc, lv, sub_)
@@ -1123,6 +1134,7 @@ def polish(ops, pre, idx, rounds):
         return whole()
 
     cur = whole()
+    owed = [0, []]
     rnd = np.random.default_rng(SEED).random((rounds, 4))
     lims = (-np.log(rnd[:, 3] + 1e-12) * (HEAT * sum(WEIGHTS) * (1.0 - np.arange(rounds) / rounds) + 1.0)).tolist()
     low, best, took = cur, (list(idx), set(), list(span)), 0
@@ -1177,8 +1189,12 @@ def polish(ops, pre, idx, rounds):
             new = worth()
             if new - cur < lims[it]:
                 took += 1
-                back(b, seq + list(ends[0].values()) + list(ends[1].values()))
-                cur = resort() if took % 100 == 0 else new
+                owed[0] = max(owed[0], b)
+                owed[1] += seq + list(ends[0].values()) + list(ends[1].values())
+                if took % 5 == 0 or new != cur:
+                    back(*owed)
+                    owed[:] = 0, []
+                cur = resort() if took % 200 == 0 else new
                 if cur < low:
                     low, best = cur, (list(idx), set(i for i in range(n) if qn[i] != first[i]), list(span))
                 continue

import numpy as np
from concourse.bass import DstId, RemoteDMATransfer
from concourse.mybir import AluOpType, ActivationFunctionType

ALU = AluOpType
AF = ActivationFunctionType
BF, F32, I32, U16, F16 = "bfloat16", "float32", "int32", "uint16", "float16"
RO = 3
BIG = float(1 << 23)
EIGHTS = float(3 << 25)
SLPOS = 1

MERGE = 1
MSG = U16 if MERGE else BF

SCRATCH = {}


def _sb(name, n, dt, where="sbuf"):
    SCRATCH[name] = (where, [128, n], dt)


for _n, _c, _d in (
    ("St", 3088, BF), ("Ef", 4720, BF), ("Ot", 256, BF), ("Qn", 768, I32), ("Qk", 768, I32), ("Tu", 128, I32),
    ("Tub", 176, BF), ("Rm", 16, BF), ("Gl0", 256, BF), ("Gl1", 256, BF), ("Gl2", 256, BF),
    ("Cw0", 768, I32), ("Cw1", 768, I32), ("Cw2", 768, I32), ("Cr0", 768, I32), ("Cr1", 768, I32),
    ("In0", 1440, F16), ("In1", 1440, F16), ("In2", 1440, F16), ("Li0", 1440, F16), ("Li1", 1440, F16), ("Cf", 768, F32),
    ("Cs0", 768, I32), ("Cs1", 768, I32),
    ("C1", 768, I32), ("C2", 768, I32), ("K16", 768, F16), ("wsc", 768, F32),
    ("Sb0", 272, MSG), ("Sb1", 272, MSG), ("Sb2", 256, BF), ("Lb0", 272, MSG), ("Lb1", 272, MSG), ("Lb2", 256, BF),
    ("Sc0", 64, BF), ("Sc1", 64, BF), ("Sc2", 64, BF), ("Lc0", 64, BF), ("Lc1", 64, BF),
    ("sg", 4096, BF), ("smx", 4096, BF), ("eg", 4096, BF), ("yy", 4096, BF), ("dd", 4096, BF), ("ind", 4096, BF),
    ("P40", 48, BF), ("pmin", 48, I32), ("kj", 48, BF), ("km", 48, BF), ("jj", 40, I32), ("mj4", 48, BF), ("pm2", 48, I32),
    ("k0i", 32, I32), ("xn", 16, F16), ("rep", 16, F32), ("xu", 40, F32), ("sh", 272, BF),
    ("dja", 32, I32), ("LJ0", 16, U16), ("LJ1", 16, U16), ("LJ2", 16, U16), ("SL0", 16, U16), ("SL1", 16, U16), ("R0j", 256, BF),
    ("wd", 160, BF), ("t12", 48, BF), ("Pfin", 48, BF), ("Pout", 128, F32),
    ("q32", 256, I32), ("q16", 256, U16), ("key", 256, F16), ("msc", 256, I32),
    ("k0", 64, BF), ("Ds", 1920, BF), ("Dk", 256, BF), ("Lk", 16, U16), ("xx", 1024, BF),
    ("uvi", 16, I32), ("Lo", 16, U16), ("u32", 256, F32), ("tO", 256, I32),
    ("na", 256, I32), ("n16", 256, U16),
    ("hxs", 48, F32), ("hsc", 768, F32), ("ss", 96, I32),
    ("jba", 80, I32), ("Dj", 384, BF), ("Lab", 32, U16), ("ya", 16, BF),
    ("wi", 48, F16), ("wT", 64, BF),
    ("R0k", 256, BF), ("xsc", 256, F32), ("Dx", 128, F16),
    ("Lx", 32, U16), ("cnt", 16, BF), ("Ai", 16, I32), ("Aa", 16, I32), ("cA", 16, F32),
    ("ci", 16, I32), ("cf", 64, F32), ("cb", 2816, BF), ("ce", 1792, BF), ("d0", 1536, BF), ("k37", 128, F16),
    ("d0c", 128, F32), ("cl", 64, U16), ("tf", 768, F32), ("tb", 640, BF), ("m2", 352, BF), ("kz", 384, BF),
    ("usc", 256, I32),
):
    _sb(_n, _c, _d)
SCRATCH["nf"] = ("sbuf", [128, 16, 32], F16)
for _n in ("PA0", "PA1", "PB0", "PB1", "PT0", "PT1", "PQ0", "PQ1"):
    _sb(_n, 512, F32, "psum")

LOADS = ("tu", "qn", "qk", "st0", "gl", "rm", "ot", "ef", "ef2")
STORES = ("o1", "o2", "o3", "o4", "o5", "o6")
ISSUE = 300.0
YQ = ((0, 768),)
SEMAPHORES = (["cV", "cS", "cP", "cG", "lsem", "rG1", "rG2", "rC00", "rC01", "rC10", "rC11", "rB0", "rB1", "rB2",
               "rE00", "rE01", "rE10", "rE11", "rL0", "rL1", "rJ0", "rJ1", "dq", "e00", "e01", "e10", "e11"]
              + ["l" + n for n in LOADS] + list(STORES) + ["d%d%d" % (t, c) for t in range(RO) for c in range(8)]
              + ["x%d%d" % (t, h) for t in range(RO) for h in range(2)])

ENG = dict(sg="VVSSVSSS", eg="SSSSSSSS", ind="VVSVVVVV", q16="VS", key="VS", Lk="SS", xx="SS", u32="SS", Lo="VS", n16="VS",
           qf="SS", mT="VV", K16="SS", wi="SS", R0j="SS", Lab="SS", Laa="V", SL="V", yb="SV", ya="SS", Lb="VV", Ai="V", cA="S",
           Cw="SS", cnt="S", LJ="VS", nf0="SS", nf1="VS", x2="SS", Pinc="S", mj12="S", Dk="SS", Db="SS", Dj="S", Da="S",
           km="SS", rm="V", k0="VV", xn="SS", x4="VS", Dx="SS", c0="V" * 24, c1="S" * 80)
PARTS = ("mT", "qf", "dx", "ix", "rw")
CUT = (1, 1)
QSEND = 2
WIDEK = "nn"
XDMA = 1
QSUM = 1
ADDS = ("DDFFDDFF",) * 3
BANKS = "B0B1A1A0B0B1A1A0"
PIECES = (0, 1, 2, 3, 4, 5, 6, 7)
TURNS = (((0, 4),), ((0, 3), (3, 4)))
GOALS = 0
FIRST = 1500.0
ENTER = (0, 0)
NAMES = 0
KJ = 1
COPY = (100.0, 1300.0, 300.0)
FILL = (0, 0)
LOAD = 2.8
SHARE = 0.3
DMA = (700.0, 600.0, 800.0)
RELAY = ("rC",)
LINK = (600.0, 900.0, 120.0, 10.0, 6.0)
LATE = 0
MARKS = ("PA0", "PA0")
LARGE = ("PQ0", "PQ1")
MHALF = 0
DSH = 3
WAW = 1
BASE = (0.52, 1.56, 3.8, 1.0, 1.0)
CASES = ((0.6, 1.9, 5.0, 0.9, 0.8), (0.5, 1.2, 2.5, 1.2, 1.3), (0.52, 1.56, 3.8, 0.6, 1.0))
LAT, LATS = 220.0, 220.0
BACK = 9999
SEED = 1
ROUNDS = 300
STEPS = 500000
WEIGHTS = (2.0, 1.0, 1.0, 1.0)
HEAT = 30.0
SLACK = 200.0
FLIP = 0.15
FAR = 0.3
TIGHT = 0.9
MOVES = (0.5, 1500.0, 1e9, 0.8, 2500.0, 500.0, 150.0, 3000.0, 500.0)
TIMES = []


def R(name, a, b, step=1, p0=0, p1=128):
    return ("r", name, a, b, step, p0, p1)


def IND(win, off):
    return ("i", win, off)


def nel(r):
    if r[0] == "i":
        return 16 * nel(r[2])
    return (r[3] - r[2] + r[4] - 1) // r[4] * (r[7] if len(r) > 7 else 1)


def dty(r):
    return SCRATCH[(r[1] if r[0] == "r" else r[1][1])][2]


def inps(r):
    return r[0] == "r" and SCRATCH[r[1]][0] == "psum"


def flat(rs):
    o = []
    for r in rs:
        if isinstance(r, tuple):
            o += [r] if r[0] == "r" else [r[1], r[2]]
    return o


def clash(a, b):
    if a[1] != b[1] or a[3] <= b[2] or b[3] <= a[2] or a[6] <= b[5] or b[6] <= a[5]:
        return False
    return not (a[4] == b[4] and a[4] > 1 and (a[2] - b[2]) % a[4] != 0)


def ap(T, r):
    if not isinstance(r, tuple):
        return r
    if r[0] == "i":
        return ap(T, r[1]).indirect(ap(T, r[2]))
    if r[1] == "nf":
        if len(r) > 7:
            return T["nf"][:, r[2] // 32:r[3] // 32, r[2] % 32:r[2] % 32 + r[7]]
        return T["nf"][r[5]:r[6], r[2] // 32, :]
    if r[4] == 1:
        return T[r[1]][r[5]:r[6], r[2]:r[3]]
    return T[r[1]][r[5]:r[6], r[2]:r[3]:r[4]]


def build(case=None, other=False):
    ops = []

    def eng(key, h):
        e = ENG[key][h]
        return dict(V="S", S="V").get(e, e) if other is True or (other and len(ops) in other) else e
    PC, GC, SC, _, DF = case or BASE

    def add(q, kind, args, rd, wr, cost, **kw):
        o = dict(q=q, kind=kind, args=args, rd=flat(rd), wr=flat(wr), cost=cost, n=len(ops))
        o.update(kw)
        ops.append(o)
        return o

    def vcost(out, ins, two=False):
        if out[0] == "i":
            return 50 + SC * nel(out)
        if ins[0][0] == "i":
            return 50 + GC * nel(out)
        n = nel(out)
        if two:
            f = 1.0 if (inps(ins[0]) or inps(ins[1])) else 2.0
        else:
            f = 0.5 if all(dty(r) in (BF, F16, U16) for r in [out] + ins) else 1.0
        return max(64, n * f)

    def cp(out, a):
        wr = [out[1]] if out[0] == "i" else [out]
        rd = [a, out[2]] if out[0] == "i" else [a]
        add("V", "cp", (out, a), rd, wr, vcost(out, [a]))

    def tt(out, a, b, op):
        add("V", "tt", (out, a, b, op), [a, b], [out], vcost(out, [a, b], True))

    def ts(out, a, s1, op0, s2=None, op1=None):
        add("V", "ts", (out, a, s1, s2, op0, op1), [a, s1, s2], [out], vcost(out, [a] + flat([s1, s2])))

    def scan(out, d0, d1, op0, op1):
        add("V", "scan", (out, d0, d1, op0, op1), [d0, d1], [out], vcost(out, [d0, d1]))

    def ms(out, v):
        add("V", "ms", (out, v), [], [out], max(64, nel(out) * 0.5))

    def act(out, a, f=AF.Identity, bias=0.0, scale=1.0):
        c = 65 + GC * nel(out) if a[0] == "i" else max(64, nel(out)) + 30
        add("S", "act", (out, a, f, bias, scale), [a, bias, scale], [out], c)

    def aff(key, h, out, a, scale=1.0, bias=0.0):
        if eng(key, h) == "S":
            act(out, a, bias=bias, scale=scale)
        elif scale == 1.0 and bias == 0.0:
            cp(out, a)
        elif scale == 1.0:
            ts(out, a, bias, ALU.add)
        else:
            ts(out, a, scale, ALU.mult, bias, ALU.add)
        ops[-1]["tag"] = (key, h)

    def mm(lst, chain=True, first=True, final=True, stop=False):
        c = sum(max(min(64, nel(l)), nel(r)) for (_, l, r) in lst) * PC + 30
        add("P", "mm", (lst, chain, first, final, final or stop), [x for (_, l, r) in lst for x in (l, r)], [o for (o, _, _) in lst], c)

    early = R("ya", 8, 9)
    turn = R("ya", 2, 3)

    def iota(out, pat, base, cm):
        add("G", "iota", (out, pat, base, cm), [turn], [out] + [turn] * (out[5] > 0), 130 + 2 * nel(out))

    def fill(out, v):
        if FILL[0] <= nel(out) <= FILL[1]:
            iota(out, [[0, nel(out)]], int(v), 0)
        else:
            ms(out, int(v) if dty(out) == I32 else float(v))

    def asel(out, a, pat, base, cm, op=ALU.is_equal, fill=0.0):
        add("G", "asel", (out, a, pat, base, cm, op, fill), [a, turn], [out] + [turn] * (out[5] > 0), 170 + 2 * nel(out))

    def load(q, name, out, kb, behind=()):
        s = add(q, "load", (name, out), list(behind), [R("ya", 10, 11)], 100)
        after = dict((o["n"], 0.0) for o in ops if o["kind"] == "run")
        after[s["n"]] = 1300.0
        w = add("L", "run", (), [], [R("ya", 12, 13)], (150.0 + kb * LOAD) * DF, after=after)
        add("R", "recv", (), [], [out], 0, sem="l" + name, lat=0, after={w["n"]: 400.0})

    def store(sem, fn, rd, kb):
        s = add("Y", "store", (sem, fn), rd, [], ISSUE, sem=sem)
        add("L", "work", (), [], [R("ya", 6, 7)], SHARE * (200.0 + kb * 5.0) * DF, after={s["n"]: 700.0},
            lat=700.0 + (1 - SHARE) * (200.0 + kb * 5.0))

    def send(kind, src, dst, sem, kb, behind=(), mark=0):
        s = add("G", "send", (kind, src, dst, sem), [src] + list(behind), [R("ya", 0, 1)] * mark, LINK[0] * DF)
        after = {s["n"]: LINK[1] * DF}
        hop = sem[0][:len(RELAY[0])] in RELAY
        w = add("L", "link", (kind,), [], [R("ya", 4, 5)], (LINK[2] + kb * LINK[3 + hop]) * DF, after=after)
        for d, sm in zip(dst, sem):
            add("R", "recv", (kind,), [], [d], 0, sem=sm, lat=0, after={w["n"]: (400.0 + hop * (2400.0 + kb * LINK[3])) * DF})

    def total(out, a, sem, size=1.0):
        s = add("G", "sum", (out, a, sem), [out, a], [], DMA[0] * DF)
        w = add("L", "work", (), [], [R("ya", 6, 7)], SHARE * DMA[2] * size * DF, after={s["n"]: DMA[1] * DF})
        add("R", "recv", (), [a], [out], 0, sem=sem, lat=0, after={w["n"]: 400.0 + (1 - SHARE) * DMA[2] * size * DF})

    def copies(outs, a, sem):
        s = add("Y", "dup", (outs, a, sem), [a], outs, COPY[0] * len(outs))
        w = add("L", "work", (), [], [R("ya", 6, 7)], SHARE * COPY[2] * len(outs) * DF, after={s["n"]: COPY[1] * DF})
        add("R", "recv", (), [a], outs, 0, sem=sem, lat=0, count=16 * len(outs),
            after={w["n"]: 400.0 + (1 - SHARE) * COPY[2] * len(outs) * DF})

    add_, sub_, mul_, max_, min_ = ALU.add, ALU.subtract, ALU.mult, ALU.max, ALU.min
    eq_, and_, shr_ = ALU.is_equal, ALU.bitwise_and, ALU.arith_shift_right

    load("Y", "tu", R("Tu", 0, 128, 1, 0, 48), 24)
    load("Y", "qn", R("Qn", 0, 768), 384)
    load("Y", "st0", R("St", 0, 3072), 768)
    load("Y", "qk", R("Qk", 0, 768), 384, [R("Qn", 0, 768)])
    load("Y", "ot", R("Ot", 0, 256), 64)
    load("Y", "gl", R("Gl0", 0, 256), 64)
    load("Y", "rm", R("Rm", 0, 1), 20)
    load("Y", "ef", R("Ef", 0, 4096), 1024, [R("St", 0, 3072)])
    load("Y", "ef2", R("Ef", 4096, 4720), 156)
    if GOALS:
        send("G", R("Gl0", 0, 256), [R("Gl1", 0, 256), R("Gl2", 0, 256)], ["rG1", "rG2"], 128, [R("Ef", 0, 4096)], 1)
        ops[-4]["cost"] += FIRST * DF

    def col(j, p1=128):
        return R("cf", j, j + 1, 1, 0, p1)

    def blk(buf, j, p1=128, p0=0):
        return R(buf, 128 * j, 128 * j + 128, 1, p0, p1)
    made = [0, 0]

    def con(k, out, a, scale=1.0, bias=0.0):
        aff("c%d" % k, made[k], out, a, scale, bias)
        made[k] += 1
    cP, cB, cAa, cN15, cF15, cJ, cU, c16P, cM16, cM4k, cN16, cN4k, cN64k, cSg, cF64k = [col(j) for j in range(15)]
    iP, iB, iA = R("ci", 0, 1), R("ci", 4, 5), R("ci", 8, 9)
    iota(iP, [[0, 1]], 0, 1)
    ts(iB, iP, 15, and_); ts(iA, iP, 4, shr_)
    con(0, cP, iP); con(0, cB, iB); con(0, cAa, iA); con(0, c16P, iP, 16.0)
    ts(cN15, iB, 15.0, ALU.is_lt); ts(cF15, iB, 15.0, eq_); ts(cF64k, iB, 15.0, eq_, 65536.0, mul_)
    con(0, col(20), iB, 2.0, 1.0); con(0, cU, col(20), cN15)
    for d, a, c in ((cM4k, R("Rm", 0, 1), 4096.0), (cN4k, cN15, 4096.0), (cN64k, cN15, 65536.0)):
        con(1, d, a, c)
    con(1, cN16, cN15, -16.0 - 49152.0, 49152.0); con(1, col(27), cF15, 32768.0)
    con(1, col(33), cF15, 16384.0); con(1, cM16, R("Rm", 0, 1), -16.0, col(33))
    con(1, cJ, iB, 1.0, 3072.0); con(1, cSg, cN15, -2048.0, 1920.0)
    Ib, I0, nI, IB, M16, kk, gg, B16, Wu, Wr0, Wr1, Wr2, One, I16 = [blk("cb", j) for j in range(14)]
    k8, k16, one1 = R("cb", 5 * 128, 5 * 128 + 8), R("cb", 5 * 128, 5 * 128 + 16), blk("cb", 12, 1)
    iota(kk, [[0, 8], [1, 16]], 0, 0)
    iota(gg, [[1, 8], [0, 16]], 0, 0)
    fill(One, 1)
    asel(Ib, One, [[-1, 128]], 0, 1)
    ts(M16, kk, cB, eq_); ts(B16, gg, cAa, eq_)
    con(0, I16, Ib, 16.0); con(0, Wu, B16, cU); con(0, nI, Ib, -1.0)
    con(1, IB, Ib, BIG / 2); con(1, Wr0, B16, cN4k); con(1, Wr1, B16, cN64k); con(1, Wr2, B16, cM4k)
    kz = R("kz", 0, 256, 1, 0, 1)
    iota(blk("kz", 0, 1), [[0, 8], [1, 16]], 0, 0); fill(blk("kz", 1, 1), 0)
    o = 15 * 128

    def sm(a, n=8, step=1):
        return R("cb", o + a, o + a + n * step - (step - 1), step)
    C8 = R("cb", 7 * 128, 8 * 128, 16)
    C256, C16p, Cp, Cp2, Wmk = sm(8), sm(32), sm(48), sm(48, 16), sm(64, 16)
    for d, c in ((C256, 256.0), (Cp, cP), (sm(64), cF64k), (sm(72), cF15), (C16p, c16P)):
        con(0, d, C8, c)
    Wv, Mbig = blk("cb", 20), blk("cb", 21)
    con(1, Wv, B16, cN15); con(1, Mbig, M16, -32768.0, 32768.0)
    con(1, sm(56), C8, cP)
    Wd, Wi, Ws = sm(80, 24), sm(104, 24), sm(128, 24)
    fill(sm(104, 48), 0)
    con(1, sm(80, 8, 3), C8, cN16); con(1, sm(81, 8, 3), C8, col(27)); con(1, sm(82, 8, 3), C8, cM16)
    con(1, sm(105, 8, 3), C8, -256.0); con(1, sm(129, 8, 3), C8, cSg)
    I4 = R("cb", o + 152, o + 200, 1, 0, 48)
    fill(R("Tub", 128, 176, 1, 0, 48), 4)
    asel(I4, R("Tub", 128, 176, 1, 0, 48), [[-1, 2], [-6, 8], [-2, 3]], 0, 1)
    Iq, Wr3 = blk("cb", 17), blk("cb", 19)
    I4x = blk("cb", 14)
    con(1, Iq, Ib, 0.25); con(1, I4x, Ib, 4.0)
    lv = R("cb", 18 * 128, 18 * 128 + 48)
    iota(lv, [[0, 16], [1, 3]], 0, 0)
    Ej = [blk("ce", l, 24) for l in range(3)]
    Ep = [blk("ce", 3 + l, 64) for l in range(3)]
    En = [blk("ce", 6 + l, 65) for l in range(3)]
    Ek, E8 = [blk("ce", 9, 65), blk("ce", 10, 65)], blk("ce", 11, 8)
    B22 = float(1 << 22)
    ta, tc = blk("ce", 12, 24), blk("ce", 13, 24)
    fill(ta, -BIG)
    asel(tc, ta, [[-3, 8], [0, 16]], 0, 1, ALU.is_ge)
    asel(ta, tc, [[3, 8], [0, 16]], 2, -1, ALU.is_ge)
    for l in range(3):
        asel(Ej[l], ta, [[-3, 8], [0, 16]], -l, 1, ALU.not_equal, -2560.0)
    asel(E8, blk("cb", 12, 8), [[-1, 8], [0, 16]], 0, 1)
    fill(R("wT", 0, 64), 0); fill(R("k0i", 0, 32), 0)
    fill(R("wd", 0, 48), 0); con(1, R("wd", 16, 32), R("cb", 4 * 128, 4 * 128 + 16))
    fill(R("jba", 0, 80), 15); fill(R("jj", 32, 40), 0)
    for t in range(RO):
        fill(R("Sc%d" % t, 32, 64), 0)
    cOwn = col(26)
    ts(col(25), iB, 8.0, ALU.is_ge, 8.0, mul_)
    ts(R("ci", 15, 16), iP, 7, and_); ts(cOwn, R("ci", 15, 16), cAa, eq_)
    Lz1, Lz2, Lz3, k4 = R("cl", 8, 12), R("cl", 40, 48), R("cl", 16, 24), R("cb", 5 * 128, 5 * 128 + 4)
    for lst, src, step, hi, zero, odd in ((Lz1, k4, 2.0, 0.125, 8.0, 0), (Lz2, k8, 1.0, 1.0, 32.0, 0), (Lz3, k8, 2.0, 2.0, 32.0, 1)):
        con(1, col(38), col(25), hi, odd - zero)
        con(1, R("cf", 40, 40 + nel(lst)), src, step, col(38))
        con(1, lst, R("cf", 40, 40 + nel(lst)), cOwn, zero)
    k37 = blk("k37", 0, 1)
    cPar, cPb = (col(29), col(30)), (col(31), col(32))
    ts(R("ci", 14, 15), iA, 1, and_)
    con(1, cPar[1], R("ci", 14, 15)); con(1, cPar[0], R("ci", 14, 15), -1.0, 1.0)
    con(1, cPb[1], R("ci", 14, 15), -2048.0); con(1, cPb[0], R("ci", 14, 15), 2048.0, -2048.0)
    iota(blk("kz", 2, 1), [[1, 16], [0, 8]], 0, 0)
    con(1, k37, blk("kz", 2, 1), 37.0)
    dMx, dW, dX, dM3 = R("d0", 0, 512), R("d0", 512, 896), R("d0", 896, 1152), R("d0", 1248, 1296)
    dP = R("d0", 1296, 1536)
    for r, body, head, st in ((dM3, 0.0, 1024.0, 3), (dMx, 1.0, 0.0, 16), (R("d0c", 0, 128), -BIG, 32768.0, 16),
                              (dP, -2.0 ** 99, 2.0 ** 99, 15)):
        ms(r, body); ms(R(r[1], r[2], r[3], st), head)
    for r, body, head, st in ((dW, 1.0, -BIG, 16), (dX, 0.0, BIG, 16)):
        fill(r, body); fill(R(r[1], r[2], r[3], st), head)
    fill(R("St", 3072, 3088), 0)
    Tri, r15 = R("m2", 0, 240, 1, 0, 16), R("m2", 240, 264, 1, 0, 1)
    fill(R("sh", 0, 16), 0); con(1, R("sh", 16, 144), Ib, 2.0 ** -13); con(1, R("sh", 144, 272), Ib, -2.0 ** -13)
    fill(R("tb", 384, 624, 1, 0, 16), 0)
    asel(Tri, R("tb", 384, 624, 1, 0, 16), [[0, 16], [-1, 15]], -1, 1, ALU.is_ge, 0.5)
    fill(r15, 15); fill(R("xu", 0, 40), 0)
    if MHALF:
        fill(R("k0", 0, 64), 0)

    Lb8, Lodd, Lgo = R("cl", 0, 8), R("cl", 24, 32), R("cl", 32, 35)
    if "w" in WIDEK:
        con(0, Lb8, k8)
    con(0, Lodd, k8, 2.0, 1.0)
    i48, third = R("cf", 21, 24), R("ci", 10, 13)
    con(0, i48, R("cb", 5 * 128, 5 * 128 + 3), 16.0, cB)
    con(0, third, i48, 1.0 / 3.0, -1.0 / 3.0)
    con(0, Lgo, third, 2.0, 1.0)
    fill(R("km", 0, 48), 0); fill(R("kj", 0, 48), 0)
    cLo, k64 = col(24, 64), blk("cb", 5, 64)
    ts(cLo, col(0, 64), 32.0, ALU.is_lt)
    fill(R("ce", 768, 1152, 1, 0, 65), 1)
    fill(R("R0k", 0, 128 + 128 * MHALF, 1, 0, 65), 1)
    con(1, col(34, 64), cLo, 2 * B22, -B22); con(1, col(35, 64), cLo, -31 * B22, 16 * B22)
    con(1, blk("tb", 0, 64), k64, col(34, 64), col(35, 64))
    for e in range(2):
        for l in range(3):
            asel(blk("ce", 3 + l, 32 * e + 32, 32 * e), blk("tb", 0, 32 * e + 32, 32 * e), [[-1, 8], [0, 16]], -1 - 8 * l, 1)
    act(blk("tf", 0, 1), blk("cb", 5, 1), AF.Square, bias=-15.5 * 2048, scale=2048.0)
    for l in range(3):
        con(1, blk("ce", 3 + l, 1), blk("tf", 0, 1), 1.0, -B22 / 4)
    con(1, R("ce", 768, 1152, 1, 0, 64), R("ce", 384, 768, 1, 0, 64), -1.0)
    con(1, col(36, 64), cLo, -8192.0, 4096.0); con(1, col(37, 64), cLo, -4096.0, 4096.0)
    con(1, blk("tb", 1, 64), k64, col(36, 64), col(37, 64))
    for e in range(2):
        for h in range(2 - MHALF):
            asel(blk("ce", 9 + h, 32 * e + 32, 32 * e), blk("tb", 1, 32 * e + 32, 32 * e), [[-1, 8], [0, 16]], -16 * h, 1)
    act(blk("Pout", 0, 65, 64), blk("cb", 5, 65, 64), AF.Square, bias=32.0, scale=64.0)
    for h in range(2 - MHALF):
        con(1, blk("ce", 9 + h, 65, 64), blk("Pout", 0, 65, 64), 1.0, -1024.0)

    for s in range(15 * (DSH < RO)):
        asel(blk("Ds", s), R("sh", 144, 272), [[-1, 128]], s + 1, 1, ALU.not_equal, 2.0 ** -13)

    def H(name, h, n=128, step=1, a=0):
        return R(name, h * n + a, h * n + n, step)

    cp(R("Tub", 0, 128, 1, 0, 48), R("Tu", 0, 128, 1, 0, 48))
    mm([(R("PQ0", 0, 48), R("Tub", 0, 128, 1, 0, 48), I4)])
    tt(R("P40", 0, 48), R("PQ0", 0, 48), lv, add_)

    def tolist(key, h, win, lst, D, pl, scale, c, bias=0.0):
        w = nel(pl)
        aff(key, h, R(D[1], D[2], D[2] + 8 * w), IND(win, lst), scale, bias)
        mm([(pl, M16, c) if c else (pl, one1, R("kz", 128, 128 + w, 1, 0, 1))]
           + [(R(pl[1], pl[2], pl[3], 1, g // 2 * 32, g // 2 * 32 + 32), R("wd", 16 - g % 2 * 16, 48 - g % 2 * 16),
               R(D[1], D[2] + w * g, D[2] + w * g + w)) for g in range(8)])

    for t in range(RO):
        last = t == RO - 1
        P4 = R("P40", 0, 48)
        Cw, Gl, Sb, Sc, LJ = "Cw%d" % t, "Gl%d" % t, "Sb%d" % t, "Sc%d" % t, "LJ%d" % t
        cA = 2048.0 if t == 0 else R("cA", 0, 1)
        ADD = ADDS[t]
        PT = ["PT0", "PT1"]
        In, Ip = "In%d" % t, "Li%d" % (t - 1)
        mj, Pinc, mj12, go = R(In, 640, 688), R(In, 688, 736), R(In, 736, 784), R(Sc, 33, 64, 2)
        kj, km = R("kj", 0, 48), R("km", 0, 48)

        def part(name, h, buf=In):
            return R(buf, 800 * h + 128 * PARTS.index(name), 800 * h + 128 * PARTS.index(name) + 128)
        for h in range(2):
            iota(part("rw", h), [[1, 128]], 256 * t + 128 * h, 0)
        J = "jj" if t == 0 else "Lc%d" % (t - 1)
        jj, jw = R(J, 1, 32, 2), R(J, 0, 40)
        if t == 0:
            scan(R("pmin", 0, 48), dM3, P4, add_, min_)
            ts(jj, R("pmin", 2, 48, 3), 3, and_)
            for h in range(2):
                tt(H("Dk", h), IND(H("jj", h, 16), Lodd), M16, mul_)
                pl = R(PT[h], 384, 392)
                mm([(pl, M16, Cp), (pl, H("Dk", h), C256)])
                aff("LJ", h, H(LJ, h, 8), pl)
        else:
            tt(R("t12", 0, 48), IND(R(J, 32, 64), Lgo), R(Ip, 736, 784), mul_)
        tt(mj, IND(jw, Lgo), lv, eq_)
        if KJ:
            aff("km", 0, R("kj", 1, 48, 3), R(In, 640, 688, 3)); aff("km", 1, R("kj", 2, 48, 3), R(In, 642, 688, 3), -1.0, 1.0)
        else:
            tt(kj, IND(jw, Lgo), lv, ALU.is_lt)
        for l in (1, 2):
            aff("km", l - 1, R("km", l, 48, 3), R(In, 639 + l, 688, 3), -1.0, 1.0)
        aff("mj12", 0, mj12, mj, -12.0)
        pl = R("PB1", 0, 48)
        mm([(pl, Ib, x) for x in ((P4,) if t == 0 else (R(Ip, 688, 736), R("t12", 0, 48)))] + [(pl, I4x, mj)])
        aff("Pinc", 0, Pinc, pl)
        if not last:
            scan(R("pm2", 0, 48), dM3, Pinc, add_, min_)
            ts(R("dja", 1, 32, 2), R("pm2", 2, 48, 3), 3, and_)
            tt(R("dja", 0, 32, 2), jj, R("dja", 1, 32, 2), sub_)
        if t == 0:
            aff("rm", 0, R(In, 784, 785), R("Rm", 0, 1))
            for h in range(2):
                aff("Cw", h, H(Cw, h, 384) if QSUM else R("PQ%d" % h, 0, 384), H("Qk", h, 384), 4096.0)
                if not QSUM:
                    tt(H(Cw, h, 384), H("Qn", h, 384), R("PQ%d" % h, 0, 384), add_)
            if QSUM:
                total(R(Cw, 0, 768), R("Qn", 0, 768), "dq", 2.0)
        if last:
            store("o6", ("ys", 0, R("St", 0, 1280)), [R("St", 0, 1280)], 320)
            ops[-2].update(wr=[early], lat=3500.0)
        for h in range(2):
            lj = R("Lb%d" % (t - 1), 256 + 8 * h, 264 + 8 * h) if MERGE and t else H(LJ, h, 8)
            if t == 0:
                aff("q16", h, H("q16", h), IND(R("Qn", 128 * h, 768), lj))
                aff("key", h, H("key", h), IND(R("Qk", 128 * h, 768), lj), bias=1025.0)
            else:
                if NAMES:
                    ts(H("Qn", h, 384), H(Cw, h, 384), 4095, and_)
                    aff("q16", h, H("q16", h), IND(H("Qn", h, 384), lj))
                else:
                    ts(H("q32", h), IND(H(Cw, h, 384), lj), 4095, and_)
                    aff("q16", h, H("q16", h), H("q32", h))
                aff("key", h, H("key", h), IND(H(Cw, h, 384), lj), 1.0 / 4096, 1024.625)
            keys = [(R(PT[h], 0, 256), one1, kz), (R(PT[h], 0, 128), H("key", h), I16)]
            mm(keys[:2 - (t == 0)], final=False)
            for c in range(4):
                aff("sg", 4 * h + c, H("sg", 4 * h + c, 512), IND(R("St", 0, 3072), H("q16", 4 * h + c, 32)))
                scan(H("smx", 4 * h + c, 512), dMx, H("sg", 4 * h + c, 512), mul_, max_)
            for a, b in TURNS[h]:
                mm([(R(PT[h], k, 256, 16, 32 * a, 32 * b), R("sg", 2048 * h + 512 * a + k, 2048 * h + 512 * b, 16), Wmk) for k in range(16)],
                   first=False, final=b == 4 and t > 0, stop=t > 0)
            if t == 0:
                mm(keys[1:], first=False)
            scan(H("msc", h), R("d0c", 0, 128), R(PT[h], 0, 128), max_, min_)
            aff("mT", h, part("mT", h), R(PT[h], 128, 256))
            k0 = R("k0i", 16 * h, 16 * h + 8)
            ts(k0, H("msc", h, 128, 16, 15), 15, and_)
            pl = R(PT[h], 392, 400)
            if WIDEK[h] == "w":
                tt(H("Dk", h), IND(k0, Lb8), M16, mul_)
                mm([(pl, M16, C16p), (pl, H("Dk", h), C8)])
            else:
                tolist("Dk", h, H("k0i", h, 16), Lz1, H("Dk", h), pl, 1.0, C16p)
            aff("Lk", h, H("Lk", h, 8), pl)
            xx = H("xx", 4 * h)
            aff("xx", h, xx, IND(H("sg", h, 2048), H("Lk", h, 8)), cN15, cF15)
            pn, pu = R(PT[h], 256, 384), R(PT[h], 0, 128)
            mm([(pn, Ib, Mbig), (pn, Wv, H("smx", h, 2048, 16, 15))], final=False)
            mm([(pn, Wu, xx)], first=False)
            mm([(pu, Wu, xx)])
            scan(H("usc", h), R("d0", 896, 1024), pn, add_, min_)
            aff("u32", h, H("u32", h), pu, bias=32.0)
            ts(H("uvi", h, 8), H("usc", h, 128, 16, 15), 255, and_)
            aff("Lo", h, H("Lo", h, 8), H("uvi", h, 8))
            tt(H("tO", h), IND(R("Ot", 0, 256), H("Lo", h, 8)), H("u32", h), mul_)
            ts(H("na", h), H("tO", h), 5, shr_, 4095, and_)
            for e in range(2):
                aff("nf%d" % e, h, R("nf", 256 * h + 16 * e, 256 * h + 256, 32) + (16,), H("na", h), cPar[e], cPb[e])
            mm([(pn, one1, k37)], final=False)
            mm([(R(PT[h], 256 + b, 384, 8, 32 * a, 32 * a + 32), R("nf", 256 * h + 32 * b, 256 * h + 32 * b + 32, 1, 32 * a, 32 * a + 32),
                 R("cb", 4 * 128, 4 * 128 + 16, 1, 32 * a, 32 * a + 32)) for a in range(4) for b in range(8)], first=False)
            aff("n16", h, H("n16", h), pn, bias=cA)
            if XDMA:
                copies([H("xx", 4 * h + e) for e in (1, 2, 3)], xx, "x%d%d" % (t, h))
            else:
                aff("x2", h, H("xx", 4 * h + 1), xx)
                aff("x4", h, H("xx", 2 * h + 1, 256), H("xx", 2 * h, 256))
            for c in range(4 * h, 4 * h + 4):
                if ADD[c] == "F":
                    tt(H("eg", c, 512), IND(R("Ef", 0, 4720), H("n16", c, 32)), H("xx", h, 512), add_)
                else:
                    aff("eg", c, H("eg", c, 512), IND(R("Ef", 0, 4720), H("n16", c, 32)))
                if ADD[c] == "D":
                    total(H("eg", c, 512), H("xx", h, 512), "d%d%d" % (t, c))
            pd = blk("PQ%d" % h, 3)
            mm([(pd, Ib, xx), (pd, nI, H(Gl, h))])
            act(part("dx", h), pd, AF.Abs)
            ts(part("ix", h), part("dx", h), 4.0, ALU.is_gt)
            pl = R("PT0", 464 + 24 * h, 488 + 24 * h)
            mm([(pl, one1, r15), (pl, part("dx", h), Wd), (pl, part("ix", h), Wi)])
            aff("qf", h, part("qf", h), H("q16", h), bias=-1536.0)
        scan(R("hxs", 0, 48), kj, R("PT0", 464, 512), mul_, max_)

        def marks(PM):
            aff("k0", 0, R("k0", 0, 32), R("k0i", 0, 32))
            mm([(R(PM, 256, 384, 1, 32 * e, 32 * e + 32), R("k0", 0, 32), Ib) for e in range(2)], False)
            act(blk("R0k", 0, 64), blk(PM, 2, 64), AF.Square, bias=cLo)
            pl = R(PM, 0, 256)
            mm([x for h in range(2) for x in ((blk(PM, h), blk("R0k", 0, 65), Ek[h]), (blk(PM, h), part("qf", h), Ib))], 2)
            scan(R("xsc", 0, 256), dX, pl, add_, min_)
            xn = R("xn", 0, 16)
            aff("xn", 0, xn, R("xsc", 15, 256, 16))
            mm([(R(PM, 0, 240), blk("cb", 0, 16), Tri)]
               + [(R(PM, s, 240, 15), a, xn) for s in range(15)
                  for a in ([blk("Ds", s)] if t >= DSH else [R("sh", 15 - s, 143 - s), R("sh", 144, 272)])])
            scan(R("xsc", 0, 240), dP, R(PM, 0, 240), max_, mul_)
            ts(R("rep", 0, 16), R("xsc", 14, 240, 15), 0.0, eq_, 4096.0, mul_)
            tt(R("xu", 0, 16), R("rep", 0, 16), xn, add_)
            tolist("Dx", 0, R("xu", 0, 40), Lz2, R("Dx", 0, 128), R(PM, 256, 272), 1.0, None)
            ts(R("Lx", 0, 32, 2), R(PM, 256, 272), 1536.0, add_, cJ, min_)
            for c in range(16):
                cp(IND(R("St", 0, 3088), R("Lx", 2 * c, 2 * c + 1)), H("xx", c + 24 * (c // 8), 16))

        def marks1(h, PM):
            aff("k0", h, R("k0", 32 * h, 32 * h + 8), R("k0i", 16 * h, 16 * h + 8))
            mm([(R(PM, 256, 384, 1, 32 * e, 32 * e + 32), H("k0", h, 32), Ib) for e in range(2)], False)
            act(blk("R0k", h, 64), blk(PM, 2, 64), AF.Square, bias=cLo)
            mm([(blk(PM, 0), blk("R0k", h, 65), Ek[0]), (blk(PM, 0), part("qf", h), Ib)])
            scan(H("xsc", h), R("d0", 896, 1024), blk(PM, 0), add_, min_)
            xn = H("xn", h, 8)
            aff("xn", h, xn, H("xsc", h, 128, 16, 15))
            mm([(R(PM, 0, 120), blk("cb", 0, 16), R("m2", 0, 120, 1, 0, 16))]
               + [(R(PM, s, 120, 15), a, xn) for s in range(15)
                  for a in ([blk("Ds", s)] if t >= DSH else [R("sh", 15 - s, 143 - s), R("sh", 144, 272)])])
            scan(R("xsc", 128 * h, 128 * h + 120), R("d0", 1296, 1416), R(PM, 0, 120), max_, mul_)
            ts(H("rep", h, 8), R("xsc", 128 * h + 14, 128 * h + 120, 15), 0.0, eq_, 4096.0, mul_)
            tt(R("xu", 16 * h, 16 * h + 8), H("rep", h, 8), xn, add_)
            tolist("Dx", h, H("xu", h, 16), Lz1, H("Dx", h, 64), R(PM, 256, 264), 1.0, None)
            ts(H("Lx", h, 16, 2), R(PM, 256, 264), 1536.0, add_, cJ, min_)
            for c in range(8):
                cp(IND(R("St", 0, 3088), R("Lx", 16 * h + 2 * c, 16 * h + 2 * c + 1)), H("xx", c + 32 * h, 16))
        if MHALF:
            for h in range(2):
                marks1(h, MARKS[h])
        else:
            marks(MARKS[1])

        def largest(h, buf, old, new):
            PQ = LARGE[h]
            pq = R(PQ, 0, 384)
            mm([(blk(PQ, 0, 24), R(buf, 640 + 24 * h, 664 + 24 * h), Ib)])
            r0 = blk("R0j", h, 24)
            aff("R0j", h, r0, blk(PQ, 0, 24))
            lst = []
            for l in range(3):
                pl = blk(PQ, l)
                lst += [(pl, Ej[l], r0), (pl, part("mT", h, buf), IB), (pl, Ib, part("qf", h, buf))]
            mm(lst, 3)
            if t == 0:
                for l in range(3):
                    tt(H(new, 3 * h + l), H(old, 2 * l + h), blk(PQ, l), max_)
            else:
                tt(H(new, h, 384), H(old, h, 384), pq, max_)
            aff("K16", h, H("K16", h, 384), H(new, h, 384), 1.0 / 4096, 1024.625)
            mm([(blk(PQ, l), H("K16", 3 * h + l), I16) for l in range(3)], False)
            scan(H("wsc", h, 384), dW, pq, add_, max_)
            we = H("wsc", h, 384, 16, 15)
            aff("wi", h, H("wi", h, 24), we, bias=-7.5)
            tt(R("wT", 32 * h + 1, 32 * h + 25), we, H("wi", h, 24), sub_)
            mm([(R(PQ, 0, 128, 1, 32 * e, 32 * e + 32), H("wT", h, 32), Ib) for e in range(2)], False)
            act(part("rw", h, buf)[:6] + (64,), blk(PQ, 0, 64), AF.Square, bias=cLo)

        def emptied(h, buf, old, new):
            PQ = "PQ%d" % h
            mm([(blk(PQ, l), Ep[l], part("rw", h, buf)[:6] + (64,)) for l in range(3)], False)
            tt(H(new, h, 384), H(old, h, 384), R(PQ, 0, 384), min_)

        def entered(h, buf, old, new):
            PQ = "PQ%d" % h
            lst = []
            for l, w, d in ((0, Wr0, "dx"), (1, Wr1, "ix"), (2, Wr2 if buf == In else Wr3, "dx")):
                lst += [(blk(PQ, l), En[l], part("rw", h, buf)[:6] + (65,)), (blk(PQ, l), w, part(d, h, buf))]
            mm(lst, 2)
            if last:
                for l in range(3):
                    tt(H(new, 2 * l + h), H(old, 3 * h + l), blk(PQ, l), max_)
            elif ENTER[h]:
                act(H(new, h, 384), R(PQ, 0, 384), AF.Relu)
                total(H(new, h, 384), H(old, h, 384), "e%d%d" % (t, h), 1.5)
            else:
                tt(H(new, h, 384), H(old, h, 384), R(PQ, 0, 384), max_)
        passes = (largest, emptied, entered)
        cut = 3 if last else CUT[t]
        new = ["C1", "C2", "Cf" if last else "Cw%d" % (t + 1)]
        old = [Cw, "C1", "C2"]
        if not last:
            new[cut - 1], got = "Cs%d" % t, ("Cr%d" % t if cut < 3 else new[2])
        for h in range(2):
            for p in range(1 if last else cut):
                passes[p](h, In, old[p], new[p])
            if not last:
                a, b = ((256, 784 + (t == 0)), (1056, 1440))[h] if cut < 3 else (688, 784)
                if cut < 3 or h == 0:
                    send("N", R(In, a, b), [R("Li%d" % t, a, b)], ["rE%d%d" % (t, h)], (b - a) // 4, [R("ya", 0, 1)])
                if QSEND == 2:
                    send("N", H(new[cut - 1], h, 384), [H(got, h, 384)], ["rC%d%d" % (t, h)], 192, [R("ya", 0, 1)])
        if not last and QSEND == 1:
            send("N", R(new[cut - 1], 0, 768), [R(got, 0, 768)], ["rC%d0" % t], 384)
        if t == 0 and min(CUT) < 3:
            con(1, col(39), R("Li0", 784, 785), 4096.0); con(1, Wr3, B16, col(39))

        def rest():
            for h in range(2):
                for p in range(1 if last else cut, 3):
                    if last:
                        passes[p](h, In, old[p], new[p])
                    else:
                        passes[p](h, "Li%d" % t, got if p == cut else old[p], new[p])
            if last:
                for a, b in YQ:
                    store("o1", ("yq", a, R("Cf", a, b)), [R("Cf", a, b)], (b - a) // 2)
        if not LATE:
            rest()
        for c in PIECES:
            h, pb = c // 4, "P" + BANKS[2 * c:2 * c + 2]
            yb, db, ib = H("yy", c, 512), H("dd", c, 512), H("ind", c, 512)
            ts(yb, H("eg", c, 512), 0.0, max_, 63.0, min_)
            mm([(blk(pb, kl), nI, H(Gl, h)) for kl in range(4)], final=False)
            mm([(R(pb, 0, 512), Ib, yb)], first=False)
            act(db, R(pb, 0, 512), AF.Abs)
            how = eng("ind", c)
            if how == "V":
                ts(ib, db, 4.0, ALU.is_gt)
            else:
                act(ib, db, AF.Sign, bias=-4.5)
            ops[-1].update(tag=("ind", c), rd=[db, Wi, Ws])
            wi = Ws if how == "S" else Wi
            mm([x for k in range(4 * c, 4 * c + 4)
                for x in ((R(PT[h], k % 16, 384, 16), H("dd", k), Wd), (R(PT[h], k % 16, 384, 16), H("ind", k), wi))], 2)
        for h in range(2):
            scan(H("hsc", h, 384), dW, R(PT[h], 0, 384), add_, max_)
        if LATE:
            rest()
        ends = R("hsc", 15, 768, 16)
        scan(R("ss", 0, 48), km, ends, mul_, max_)
        scan(R("ss", 48, 96), kj, ends, mul_, max_)
        ts(R("jba", 0, 16), R("ss", 2, 48, 3), 15, and_)
        tolist("Db", 0, R("jba", 0, 40), Lz2, H("Dj", 0), R("PT0", 448, 464), -128.0, Cp2, 1920.0)
        aff("Lab", 0, R("Lab", 0, 16), R("PT0", 448, 464))
        for h in range(2):
            aff("yb", h, H(Sb, h), IND(H("yy", h, 2048), H("Lab", h, 8)), cN15)
        tt(go, R("ss", 50, 96, 3), R("hxs", 2, 48, 3), ALU.is_gt)
        w = 256
        if not last:
            pl = R("PB0", 0, 16)
            scan(R(Sc, 0, 32), R(Sc, 32, 64), R("dja", 0, 32), mul_, add_)
            tolist("Dj", 0, R(Sc, 0, 40), Lz3, H("Dj", 1), pl, 128.0, Cp2)
            if MERGE:
                aff("SL", 0, R(Sb, 256, 272), pl)
                w = 272
            else:
                aff("SL", 0, R("SL%d" % t, 0, 16), pl)
        first = [lambda: send("N", R(Sb, 0, w), [R("Lb%d" % t, 0, w)], ["rB%d" % t], w // 4, mark=1)]
        if not last and not MERGE:
            first.insert(SLPOS, lambda: send("N", R("SL%d" % t, 0, 16), [R("LJ%d" % (t + 1), 0, 16)], ["rL%d" % t], 4))
        for f in first:
            f()
        if not last:
            send("N", R(Sc, 0, 64), [R("Lc%d" % t, 0, 64)], ["rJ%d" % t], 16, [R("ya", 0, 1)])
        if t == 0 and not GOALS:
            send("G", R("Gl0", 0, 256), [R("Gl1", 0, 256), R("Gl2", 0, 256)], ["rG1", "rG2"], 128, [R("ya", 0, 1)])
        ts(R("jba", 40, 56), R("ss", 50, 96, 3), 15, and_)
        tolist("Da", 0, R("jba", 40, 80), Lz2, H("Dj", 2), R("PT0", 432, 448), -128.0, Cp2, 1920.0)
        aff("Laa", 0, R("Lab", 16, 32), R("PT0", 432, 448))
        for h in range(2):
            aff("ya", h, H("St", 2 * t + h), IND(H("yy", h, 2048), H("Lab", 2 + h, 8)), cN15)
        if last:
            tt(R("t12", 0, 48), IND(R(Sc, 32, 64), Lgo), mj12, mul_)
            tt(R("mj4", 0, 48), Pinc, lv, sub_)
            for h in range(2):
                tt(R("Pfin", h, 48, 2), H("mj4", h, 24), H("t12", h, 24), add_)
        if not last:
            pl = R("PT0", 416, 417, 1, 0, 8)
            mm([(pl, R(Sc, 33 + 16 * h, 48 + 16 * h, 2), R("cb", 12 * 128, 12 * 128 + 1)) for h in range(2)])
            aff("cnt", 0, R("cnt", 0, 1, 1, 0, 8), pl)
            mm([(R("PT0", 424, 425), E8, R("cnt", 0, 1, 1, 0, 8))])
            aff("Ai", 0, R("Ai", 0, 1), R("PT0", 424, 425)); ts(R("Aa", 0, 1), R("Ai", 0, 1), 63, and_)
            aff("cA", 0, R("cA", 0, 1), R("Aa", 0, 1), bias=2048.0)
            aff("Lb", 0, H("St", 3 + t, 256), R("Lb%d" % t, 0, 256))
        else:
            mm([(blk("PA0", 0, 48), R("Pfin", 0, 48), Iq)])
            act(blk("Pout", 0, 48), blk("PA0", 0, 48))
            store("o2", ("yp", None, blk("Pout", 0, 48)), [blk("Pout", 0, 48)], 24)
            store("o3", ("ym", None, "marks"), [R("St", 1536, 3072)], 24)
            for a in (0, 768):
                store("o3", ("ys", a, "marks"), [R("St", a, a + 512), early], 8)
            store("o4", ("ys", 512, R("St", 512, 768)), [R("St", 512, 768), early], 64)
            store("o5", ("ys", 1280, R("Lb2", 0, 256)), [R("Lb2", 0, 256)], 64)
    return ops


def depends(ops):
    n = len(ops)
    hard = [set() for _ in range(n)]
    soft = [set() for _ in range(n)]
    seen = {}
    for o in ops:
        i = o["n"]
        for r in o["rd"]:
            hard[i].update(j for (j, r2, w) in seen.get(r[1], []) if w and clash(r, r2))
        for r in o["wr"]:
            for (j, r2, w) in seen.get(r[1], []):
                if clash(r, r2):
                    both = not WAW and o["kind"] == ops[j]["kind"] == "cp" and o["args"][0][0] == ops[j]["args"][0][0] == "i"
                    (soft if both or ops[j]["q"] == o["q"] == "P" and not o["args"][2] else hard)[i].add(j)
        for r in o["wr"]:
            l = [e for e in seen.get(r[1], []) if not (r[4] == 1 and r[5] <= e[1][5] and e[1][6] <= r[6] and r[2] <= e[1][2] and e[1][3] <= r[3])]
            seen[r[1]] = l + [(i, r, True)]
        for r in o["rd"]:
            seen.setdefault(r[1], []).append((i, r, False))
        hard[i].discard(i)
    mms = [o for o in ops if o["kind"] == "mm"]
    for a in mms:
        if a["args"][2] != a["args"][3]:
            for b in mms:
                if b["wr"][0][1] == a["wr"][0][1]:
                    if b["n"] < a["n"]:
                        soft[a["n"]].add(b["n"])
                    if b["n"] > a["n"] and a["args"][3]:
                        soft[b["n"]].add(a["n"])
    pre = []
    for i in range(n):
        p = dict((j, LATS if ops[j]["q"] == ops[i]["q"] and "sem" not in ops[j] else LAT) for j in hard[i])
        p.update((j, 0.0) for j in soft[i] if j not in hard[i] and j != i)
        pre.append(ops[i].get("after", p))
    return hard, pre


def above(l, x):
    a, b = 0, len(l)
    while a < b:
        m = (a + b) // 2
        if l[m] <= x:
            a = m + 1
        else:
            b = m
    return a


def place(key, pre, rel, cost, qn, bk):
    qs, qe = [[] for _ in range(7)], [[] for _ in range(7)]
    bs, be, bq = [[] for _ in range(8)], [[] for _ in range(8)], [[] for _ in range(8)]
    fin = [0.0] * len(key)
    for i in key:
        s = rel[i]
        for j, d in pre[i]:
            if fin[j] + d > s:
                s = fin[j] + d
        q, c = qn[i], cost[i]
        if q:
            S, E = qs[q], qe[q]
            while True:
                m = len(S)
                k = m if not m or E[-1] <= s else above(E, s)
                while k < m and S[k] < s + c:
                    s = E[k]
                    k += 1
                s0 = s
                for b in bk[i]:
                    X, Y, Z = bs[b], be[b], bq[b]
                    w = len(X)
                    u = w if not w or Y[-1] <= s - LAT else above(Y, s - LAT)
                    while u < w and X[u] < s + c + LAT:
                        if Z[u] != q and Y[u] + LAT > s:
                            s = Y[u] + LAT
                        u += 1
                if s == s0:
                    break
            S.insert(k, s); E.insert(k, s + c)
            for b in bk[i]:
                u = above(bs[b], s)
                bs[b].insert(u, s); be[b].insert(u, s + c); bq[b].insert(u, q)
        fin[i] = s + c
    return np.array(fin)


def replay(idx, pre, cost, lat, qn, bk, f):
    fin = [0.0] * len(idx)
    free = [0.0] * 7
    bank = [[0.0] * 7 for _ in range(8)]
    for i in idx:
        q = qn[i]
        s = free[q] if q else 0.0
        for j, x in pre[i].items():
            y = fin[j] + lat[j] + (x * f if x <= LAT else x)
            if y > s:
                s = y
        for b in bk[i]:
            for p, y in enumerate(bank[b]):
                if p != q and y > s:
                    s = y
        fin[i] = free[q] = s + cost[i]
        for b in bk[i]:
            bank[b][q] = fin[i] + LAT * f
    return max(x + y for x, y in zip(fin, lat))


def search(ops, pre, rounds, start=None):
    n = len(ops)
    lat = [o.get("lat", 0) for o in ops]
    cost = [o["cost"] for o in ops]
    qn = [max(0, " VSPGYL".find(o["q"])) for o in ops]
    names = [k for k, v in SCRATCH.items() if v[0] == "psum"]
    bk = [sorted(set(names.index(r[1]) for r in o["rd"] + o["wr"] if inps(r))) for o in ops]
    fw = [[(j, d + lat[j]) for j, d in pre[i].items()] for i in range(n)]
    bw = [[] for _ in range(n)]
    for i in range(n):
        for j, d in fw[i]:
            bw[j].append((i, d))
    la, ca, zero, up = np.array(lat), np.array(cost), [0.0] * n, np.arange(n)
    others = [([o["cost"] for o in l], [o.get("lat", 0) for o in l], w) for l, w in [(build(c), c[3]) for c in CASES]]
    moves = np.array([o["n"] for o in ops if o["q"] == "L"])
    ahead = np.array([cost[i - 1] + pre[i][i - 1] for i in moves])
    kin = []
    for o in ops:
        r = o["wr"][0] if o["wr"] else o["rd"][0]
        ps = inps(r)
        kin.append((r[1] if ps else r[1].rstrip("012"), r[2] // 128 if ps else int(2 * r[2] >= np.prod(SCRATCH[r[1]][1][1:])), o["q"], o["kind"]))
    kinds = sorted(set(kin))
    kin = np.array([kinds.index(x) for x in kin])

    def forward(key):
        key = list(key)
        for i in range(n):
            for j, d in fw[i]:
                if key[j] > key[i]:
                    key[i] = key[j]
        return place(np.lexsort((up, key)).tolist(), fw, zero, cost, qn, bk)

    def turn(f):
        b = place(np.lexsort((-up, -f)).tolist(), bw, lat, cost, qn, bk)
        return place(np.lexsort((up, -b)).tolist(), fw, zero, cost, qn, bk)

    def starts(f):
        s = f - ca
        s[moves - 1] = s[moves] = s[moves] - ahead
        return s

    def worth(f):
        idx = np.lexsort((up, starts(f))).tolist()
        return [replay(idx, pre, c, l, qn, bk, w) for c, l, w in [(cost, lat, 1.0)] + others]

    if start is None:
        tail = [0.0] * n
        for i in range(n - 1, -1, -1):
            tail[i] = cost[i] + max([lat[i]] + [tail[k] + d for k, d in bw[i]])
        start = -np.array(tail)
    f = turn(turn(forward(start)))
    rng = np.random.default_rng(SEED)
    v = worth(f)
    cur, cf, low, best = v, f, v, f
    for it in range(rounds):
        key = cf - ca
        m = rng.random()
        near = np.abs(key - rng.random() * cur[0])
        if m < MOVES[0]:
            off = np.zeros(len(kinds))
            off[rng.integers(0, len(kinds), int(rng.integers(1, 4)))] = rng.normal(0.0, MOVES[1])
            key = key + off[kin] * (near < MOVES[2])
        elif m < MOVES[3]:
            key = key + (near < MOVES[4]) * rng.normal(0.0, MOVES[5], n)
        else:
            key = key + rng.normal(0.0, MOVES[6], n)
        f = forward(key)
        if (f + la).max() < cur[0] + MOVES[7]:
            g = turn(f)
            if (g + la).max() <= (f + la).max():
                f = g
        if (f + la).max() < cur[0] + 600:
            v = worth(f)
            if sum(v) + v[0] < sum(cur) + cur[0] + MOVES[8] * len(v) * (1.0 - it / rounds) * rng.random() ** 2:
                cur, cf = v, f
                if sum(v) + v[0] < sum(low) + low[0]:
                    low, best = v, f
    TIMES[:] = low
    return starts(best), qn, bk


def polish(ops, pre, idx, rounds):
    n = len(ops)
    cases = [BASE] + list(CASES)
    CS = range(len(cases))
    built, other = [build(c) for c in cases], [build(c, True) for c in cases]
    pres = [depends(b)[1] for b in built]
    qn, qo = [[max(0, " VSPGYL".find(o["q"])) for o in l] + [0] for l in (ops, other[0])]
    first = list(qn)
    names = [k for k, v in SCRATCH.items() if v[0] == "psum"]
    bk = [sorted(set(names.index(r[1]) for r in o["rd"] + o["wr"] if inps(r))) for o in ops]
    anc, keep = [0] * n, []
    for i in range(n):
        m = 0
        for j in pre[i]:
            m |= anc[j]
        keep.append([j for j, d in pre[i].items() if d > LAT or not m >> j & 1])
        for j in pre[i]:
            m |= 1 << j
        anc[i] = m
    cost, alt = [[[o["cost"] for o in b] for b in l] for l in (built, other)]
    lat = [[o.get("lat", 0) for o in b] for b in built]
    wait = [LAT * c[3] for c in cases]
    P = [[[(j, lat[c][j] + pres[c][i][j] * (cases[c][3] if pres[c][i][j] <= LAT else 1.0)) for j in keep[i]] for i in range(n)] for c in CS]
    S = [[[] for _ in range(n)] for c in CS]
    for c in CS:
        for i in range(n):
            for j, d in P[c][i]:
                S[c][j].append((i, d))
    up = [keep[i] + [i + 1] * (qn[i + 1] == 6) for i in range(n)]
    down = [[k for k, _ in S[0][i]] + [i - 1] * (qn[i] == 6) for i in range(n)]
    after = [[k for k, _ in l] for l in S[0]]
    sinks = [i for i in range(n) if not after[i] and lat[0][i]]
    moves = np.array([i for i in range(n) if qn[i] == 6])
    pos, qp, qx = [0] * n, [-1] * (n + 1), [-1] * (n + 1)
    bp, bx = [{} for _ in range(n + 1)], [{} for _ in range(n + 1)]
    fin, tail, span = [[0.0] * (n + 1) for _ in CS], [[0.0] * (n + 1) for _ in CS], [0.0 for _ in CS]

    def exchange(v):
        qn[v], qo[v] = qo[v], qn[v]
        for c in CS:
            cost[c][v], alt[c][v] = alt[c][v], cost[c][v]

    def link(a, seq, ends):
        lq, lb = dict(ends[0]), dict(ends[1])
        for p, i in enumerate(seq):
            pos[i] = a + p
            if qn[i]:
                j = qp[i] = lq[qn[i]]
                qx[j] = lq[qn[i]] = i
            for b in bk[i]:
                j = bp[i][b] = lb[b]
                bx[j][b] = lb[b] = i
        for q, j in lq.items():
            k = qx[j] = ends[2][q]
            qp[k] = j
        for b, j in lb.items():
            k = bx[j][b] = ends[3][b]
            bp[k][b] = j

    def ahead(a, seeds):
        log = []
        fw = idx[a:]
        for c in CS:
            f, co, Pc, w, la = fin[c], cost[c], P[c], wait[c], lat[c]
            dirty = [False] * (n + 1)
            for i in seeds:
                dirty[i] = True
            for i in fw:
                if dirty[i]:
                    s = f[qp[i]]
                    for j, d in Pc[i]:
                        if f[j] + d > s:
                            s = f[j] + d
                    if bk[i]:
                        for j in bp[i].values():
                            if f[j] + w > s and j >= 0 and qn[j] != qn[i]:
                                s = f[j] + w
                    s += co[i]
                    if s != f[i]:
                        log.append((f, i, f[i]))
                        f[i] = s
                        dirty[qx[i]] = True
                        for k in after[i]:
                            dirty[k] = True
                        if bk[i]:
                            for k in bx[i].values():
                                dirty[k] = True
            log.append((span, c, span[c]))
            span[c] = max(f[i] + la[i] for i in sinks)
        return log

    def back(b, seeds):
        bw = idx[b::-1]
        for c in CS:
            t, co, Sc, w, la = tail[c], cost[c], S[c], wait[c], lat[c]
            dirty = [False] * (n + 1)
            for i in seeds:
                dirty[i] = True
            for i in bw:
                if dirty[i]:
                    s = t[qx[i]]
                    if la[i] > s:
                        s = la[i]
                    for k, d in Sc[i]:
                        if t[k] + d > s:
                            s = t[k] + d
                    if bk[i]:
                        for k in bx[i].values():
                            if t[k] + w > s and k >= 0 and qn[k] != qn[i]:
                                s = t[k] + w
                    s += co[i]
                    if s != t[i]:
                        t[i] = s
                        dirty[qp[i]] = True
                        for j in keep[i]:
                            dirty[j] = True
                        if bk[i]:
                            for j in bp[i].values():
                                dirty[j] = True

    def worth():
        return sum(w * s for w, s in zip(WEIGHTS, span))

    def ends_of(a, b):
        fq, fb, nq, nb = {}, {}, {}, {}
        for i in idx[a:b + 1]:
            if qn[i]:
                fq.setdefault(qn[i], qp[i])
                nq[qn[i]] = qx[i]
            for x in bk[i]:
                fb.setdefault(x, bp[i][x])
                nb[x] = bx[i][x]
        return fq, fb, nq, nb

    def hopeful(b, seq, ends, bound):
        fq, fb, nq, nb = ends
        for c in CS:
            f, t, co, Pc, Sc, w = fin[c], tail[c], cost[c], P[c], S[c], wait[c]
            old = [f[i] for i in seq]
            lq, lb = dict(fq), dict(fb)
            best = 0.0
            for i in seq:
                q = qn[i]
                s = 0.0
                if q:
                    s = f[lq[q]]
                    lq[q] = i
                for j, d in Pc[i]:
                    if f[j] + d > s:
                        s = f[j] + d
                for x in bk[i]:
                    j = lb[x]
                    if f[j] + w > s and j >= 0 and qn[j] != q:
                        s = f[j] + w
                    lb[x] = i
                s = f[i] = s + co[i]
                if s + lat[c][i] > best:
                    best = s + lat[c][i]
                for k, d in Sc[i]:
                    if s + d + t[k] > best and pos[k] > b:
                        best = s + d + t[k]
            for q, j in lq.items():
                best = max(best, f[j] + t[nq[q]])
            for x, j in lb.items():
                if nb[x] >= 0 and qn[j] != qn[nb[x]]:
                    best = max(best, f[j] + w + t[nb[x]])
            for i, y in zip(seq, old):
                f[i] = y
            bound -= WEIGHTS[c] * max(best - span[c], -150.0)
            if bound < -150.0 * sum(WEIGHTS[c + 1:]):
                return False
        return bound > 0

    def whole():
        e = dict.fromkeys(range(1, 7), -1), dict.fromkeys(range(8), -1)
        link(0, idx, e + e)
        ahead(0, idx)
        back(n - 1, idx)
        return worth()

    def resort():
        s = np.array(fin[0][:n]) - np.array(cost[0])
        s[moves] = s[moves - 1]
        idx[:] = np.lexsort((np.array(pos), s)).tolist()
        return whole()

    cur = whole()
    owed = [0, []]
    rnd = np.random.default_rng(SEED).random((rounds, 4))
    lims = (-np.log(rnd[:, 3] + 1e-12) * (HEAT * sum(WEIGHTS) * (1.0 - np.arange(rounds) / rounds) + 1.0)).tolist()
    low, best, took = cur, (list(idx), set(), list(span)), 0
    pick, p = np.random.default_rng(SEED + 1).integers(0, n, 100003).tolist(), 0
    for it, (r0, r1, r2, _) in enumerate(rnd.tolist()):
        c, v = it % len(cases), int(r0 * n)
        while r1 < TIGHT and fin[c][v] - cost[c][v] + tail[c][v] < span[c] - SLACK:
            p = (p + 1) % len(pick)
            v = pick[p]
        r1 = r1 % 0.1 * 10
        if not qn[v]:
            continue
        turn = qo[v] != qn[v] and r2 < FLIP
        if turn:
            a = b = pos[v]
            win = seq = [v]
            ends = ends_of(a, b)
            ends[0][qo[v]] = next((i for i in idx[a::-1] if qn[i] == qo[v]), -1)
            ends[2][qo[v]] = next((i for i in idx[a:] if qn[i] == qo[v]), -1)
            exchange(v)
        else:
            v -= qn[v] == 6
            early = r2 < 0.575
            near = [qp[v]] + list(bp[v].values()) if early else [qx[v]] + list(bx[v].values())
            if qn[v + 1] == 6:
                m = qp[v + 1] if early else qx[v + 1]
                near.append(m - 1 if m >= 0 else -1)
            u, hops = near[int(r1 * len(near))], r1 * len(near) % 1.0
            while u >= 0 and hops < FAR:
                hops /= FAR
                u = qp[u] if early else qx[u]
            if u < 0:
                continue
            a, b, nxt = (pos[u], pos[v] + (qn[v + 1] == 6), up) if early else (pos[v], pos[u] + (qn[u + 1] == 6), down)
            if b - a > 120:
                continue
            grp, todo = {v}, [v]
            while todo and u not in grp:
                for j in nxt[todo.pop()]:
                    if a <= pos[j] <= b and j not in grp:
                        grp.add(j); todo.append(j)
            if u in grp:
                continue
            win = idx[a:b + 1]
            A, B = [i for i in win if i in grp], [i for i in win if i not in grp]
            seq = A + B if early else B + A
            ends = ends_of(a, b)
        if hopeful(b, seq, ends, lims[it]):
            idx[a:b + 1] = seq
            link(a, seq, ends)
            log = ahead(a, seq + list(ends[2].values()) + list(ends[3].values()))
            new = worth()
            if new - cur < lims[it]:
                took += 1
                owed[0] = max(owed[0], b)
                owed[1] += seq + list(ends[0].values()) + list(ends[1].values())
                if took % 5 == 0 or new != cur:
                    back(*owed)
                    owed[:] = 0, []
                cur = resort() if took % 200 == 0 else new
                if cur < low:
                    low, best = cur, (list(idx), set(i for i in range(n) if qn[i] != first[i]), list(span))
                continue
            for l, i, y in log:
                l[i] = y
            idx[a:b + 1] = win
            if turn:
                exchange(v)
            link(a, win, ends)
        elif turn:
            exchange(v)
    TIMES[:] = best[2]
    return best[:2]


def order():
    ops = build()
    pre = depends(ops)[1]
    t0, qn, bk = search(ops, pre, ROUNDS)
    idx, turned = polish(ops, pre, np.lexsort((np.arange(len(ops)), t0)).tolist(), STEPS)
    ops = build(None, turned)
    hard = depends(ops)[0]
    qn = [o["q"] for o in ops]
    out = [ops[i] for i in idx]
    bank = {}
    for o in out:
        i = o["n"]
        ex = set()
        for b in bk[i]:
            ex.update(j for q, j in bank.get(b, {}).items() if q != qn[i])
            bank.setdefault(b, {})[qn[i]] = i
        o["w"] = set() if o["q"] in "RL" else set(j for j in hard[i] | ex if ops[j]["kind"] not in ("send", "sum", "load", "dup"))
    pos = {}
    for p, o in enumerate(out):
        pos[o["n"]] = p
    got = {}
    past = {}
    for o in out:
        need = {}
        for j in o["w"]:
            s = ops[j].get("sem") or "c" + ops[j]["q"]
            if s not in need or pos[j] > pos[need[s]]:
                need[s] = j
        mine = got.setdefault(o["q"], {})
        own = past.setdefault(o["q"], [])
        s = "c" + o["q"]
        if s in need and len(own) >= BACK and pos[need[s]] < pos[own[-BACK]]:
            need[s] = own[-BACK]
        o["need"] = []
        for s, j in sorted(need.items(), key=lambda e: -pos[e[1]]):
            if mine.get(s, -1) < pos[j]:
                mine[s] = pos[j]
                for s2, p2 in ops[j]["know"].items():
                    mine[s2] = max(mine.get(s2, -1), p2)
                o["need"].append((s, j))
                ops[j]["inc"] = True
        o["know"] = dict(mine) if o["q"] != "R" else {}
        if "sem" not in o and o["kind"] not in ("send", "sum", "load", "dup"):
            own.append(o["n"])
    tick = {}
    for o in out:
        if o.get("inc") and "sem" not in o:
            tick[o["q"]] = tick.get(o["q"], 0) + 1
            o["val"] = tick[o["q"]]
    return ops, out


PLAN = []


def bits(l):
    m = 0
    for e in l:
        m |= 1 << e
    return m


def goal_engines(T, topo, r):
    n = len(T.cores)
    e1 = topo.engines(T.cores[r], T.cores[(r + 1) % n])
    e2 = topo.engines(T.cores[r], T.cores[(r + 2) % n])
    only1 = [e for e in e1 if e not in e2]
    if only1:
        return only1, e2
    both = [e for e in e1 if e in e2]
    return both[:len(both) // 2], both[len(both) // 2:]


def helper(T, topo, r):
    c, nxt = T.cores[r], T.cores[(r + 1) % len(T.cores)]
    if topo.chip(c) == topo.chip(nxt):
        return None
    free = [x for x in topo.cores_of(c) if T.rank_of(x) is None and topo.may_write(x, nxt)]
    return ([x for x in free if topo.die(x) != topo.die(c)] + free + [None])[0]


def handed(o):
    return o["kind"] == "send" and o["args"][3][0][:len(RELAY[0])] in RELAY


def rank_program(g, core, T, topo):
    r = T.rank_of(core)
    n = len(T.cores)
    if not PLAN:
        PLAN.extend(order())
    ops, out = PLAN
    if r is None:
        for r in range(n):
            if helper(T, topo, r) == core:
                nxt, sent = T.cores[(r + 1) % n], 0
                rid, pid, _ = topo.addr(nxt)
                for o in out:
                    if handed(o):
                        d, s = ap(T, o["args"][2][0]), T.sem[o["args"][3][0]]
                        g.wait_ge(s, len(topo.engines(T.cores[r], core)))
                        g.remote_dma(d, d, s, T.sem["lsem"], pid, rid, topo.mask(core, nxt))
                        sent += len(topo.engines(core, nxt))
                if sent:
                    g.wait_ge(T.sem["lsem"], sent)
        return
    hlp = helper(T, topo, r)
    Q = {"V": g.vector, "S": g.scalar, "P": g.tensor, "G": g, "Y": g.sync}
    nxt, nx2, prv = T.cores[(r + 1) % n], T.cores[(r + 2) % n], T.cores[(r - 1) % n]
    arr = {"rG1": len(goal_engines(T, topo, (r - 1) % n)[0]), "rG2": len(goal_engines(T, topo, (r - 2) % n)[1])}
    nin = len(topo.engines(prv, core))
    lsum = 0
    for o in out:
        if o["q"] in "RL":
            continue
        q = Q[o["q"]]
        for s, j in o["need"]:
            p = ops[j]
            v = p["val"] if "sem" not in p else (arr.get(s, nin) if s[0] == "r" else p.get("count", 16))
            q.wait_ge(T.sem[s], v)
        k, a = o["kind"], o["args"]
        if k == "cp":
            ins = q.tensor_copy(ap(T, a[0]), ap(T, a[1]))
        elif k == "tt":
            ins = q.tensor_tensor(ap(T, a[0]), ap(T, a[1]), ap(T, a[2]), a[3])
        elif k == "ts":
            if a[5] is None:
                ins = q.tensor_scalar(ap(T, a[0]), ap(T, a[1]), ap(T, a[2]), None, a[4])
            else:
                ins = q.tensor_scalar(ap(T, a[0]), ap(T, a[1]), ap(T, a[2]), ap(T, a[3]), a[4], a[5])
        elif k == "scan":
            ins = q.tensor_tensor_scan(ap(T, a[0]), ap(T, a[1]), ap(T, a[2]), 0.0, a[3], a[4])
        elif k == "ms":
            ins = q.memset(ap(T, a[0]), a[1])
        elif k == "act":
            ins = q.activation(ap(T, a[0]), ap(T, a[1]), a[2], bias=ap(T, a[3]), scale=ap(T, a[4]))
        elif k == "mm":
            m = len(a[0]) if a[1] is True else max(1, int(a[1]))
            for i, (oo, l, rr) in enumerate(a[0]):
                more = any(x[0][5] < oo[6] and oo[5] < x[0][6] for x in a[0][i + 1:i - i % m + m])
                ins = q.matmul(ap(T, oo), ap(T, l), ap(T, rr), i % m == 0 and a[2], a[4] and not more)
        elif k == "iota":
            if dty(a[0]) == I32:
                ins = q.iota(ap(T, a[0]), a[1], a[2], a[3])
            else:
                ins = q.iota(ap(T, a[0]), a[1], a[2], a[3], allow_small_or_imprecise_dtypes=True)
        elif k == "asel":
            ins = q.affine_select(ap(T, a[0]), ap(T, a[1]), a[2], a[5], a[6], a[3], a[4])
        elif k == "load":
            src = T["ef"][:, 0:nel(a[1])] if a[0] == "ef2" else T[a[0]][:]
            q.dma_start(ap(T, a[1]), src).then_inc(T.sem["l" + a[0]], 16)
            continue
        elif k == "sum":
            q.dma_start(ap(T, a[0]), ap(T, a[1]), accum_op=ALU.add).then_inc(T.sem[a[2]], 16)
            continue
        elif k == "dup":
            for d in a[0]:
                q.dma_start(ap(T, d), ap(T, a[1])).then_inc(T.sem[a[2]], 16)
            continue
        elif k == "store":
            name, c, src = a[1]
            if src == "marks" and c is not None:
                q.dma_start(T[name][15:128:16, c:c + 512], T["St"][15:128:16, c:c + 512]).then_inc(T.sem[o["sem"]], 16)
            elif src == "marks":
                q.dma_start(T[name][:], T["St"][15:128:16, 1536:3072]).then_inc(T.sem[o["sem"]], 16)
            elif c is None:
                q.dma_start(T[name][:], ap(T, src)).then_inc(T.sem[o["sem"]], 16)
            else:
                q.dma_start(T[name][:, c:c + nel(src)], ap(T, src)).then_inc(T.sem[o["sem"]], 16)
            continue
        else:
            if a[0] == "G":
                e1, e2 = goal_engines(T, topo, r)
                tr = []
                for dst, d, s, e in ((nxt, a[2][0], a[3][0], e1), (nx2, a[2][1], a[3][1], e2)):
                    rid, pid, _ = topo.addr(dst)
                    tr.append(RemoteDMATransfer(dst_ids=[DstId(rid=rid, pnc=pid)], dma_engine_mask=bits(e),
                                                remote_sem=T.sem[s], src=ap(T, a[1]), dst=ap(T, d)))
                    lsum += len(e)
                q.remote_dma_fused(tr, local_sem=T.sem["lsem"])
            else:
                to = hlp if hlp is not None and handed(o) else nxt
                rid, pid, _ = topo.addr(to)
                q.remote_dma(ap(T, a[2][0]), ap(T, a[1]), T.sem[a[3][0]], T.sem["lsem"], pid, rid, topo.mask(core, to))
                lsum += len(topo.engines(core, to))
            continue
        if o.get("inc"):
            ins.then_inc(T.sem["c" + o["q"]], 1)
    g.wait_ge(T.sem["lsem"], lsum)
    for s in STORES:
        g.sync.wait_ge(T.sem[s], 16 * sum(o.get("sem") == s for o in ops))
